import numpy as np, ml_dtypes
CORES = [24,25,26,27,28,29,30,31]
N = 8
BF = ml_dtypes.bfloat16
def gentries(a):
    return np.ascontiguousarray(a.reshape(8, 16, -1).transpose(0, 2, 1)).reshape(8, -1)
def gtable(e):
    e = np.asarray(e); return np.ascontiguousarray(e.reshape(8, -1, 16).transpose(0, 2, 1)).reshape(128, -1).astype(np.int32)
W, L, B, VI, PS, ST = 4096, 32, 128, 3, 3, 32
KAP = 113 * np.arange(L) + 37
def tables_of(rng):
    lv = rng.random((N, 8, 16, W), dtype=np.float32); x = rng.integers(0, 16, (N, 8, 16, W))
    h = rng.choice(np.array([0.15, 0.22, 0.3]), (N, 8, 1, 1)); w = rng.choice(np.array([0.12, 0.18]), (N, 8, 1, 1))
    e = np.where(lv < h, 12 + (x & 3), np.where(lv < h + w, x & 3, 4 + (x & 7)))
    nd = rng.choice(np.array([0.0, 0.05, 0.1, 0.2]), (N, 8, 1, W)); x = rng.integers(0, 12, (N, 8, 16, W))
    return e, np.where(rng.random((N, 8, 16, W), dtype=np.float32) < nd, 12 + (x & 3), x)
def own_steps(rng, s):
    return np.take_along_axis(s, rng.integers(0, L, (N, 8, L, B)), axis=2)
def pack(e, p, s, q, st, th):
    return {"eff": e.reshape(N, 128, W).astype(np.float32).astype(BF), "req": p.reshape(N, 128, W).astype(np.float32).astype(BF),
            "act": np.stack([gtable(a.reshape(8, L * B)) for a in s]), "why": np.stack([gtable(a.reshape(8, L * B)) for a in q]),
            "st0": np.ascontiguousarray(st).reshape(N, 128, B).astype(np.float32).astype(BF), "bar": np.stack([gtable(a) for a in th])}
def setup_inputs(rng):
    e, p = tables_of(rng); s = rng.integers(0, W, (N, 8, L, B)); w = rng.integers(0, 5, (N, 8, L, B))
    q = np.where(w < 2, -1, np.where(w < 4, own_steps(rng, s), rng.integers(0, W, (N, 8, L, B))))
    return pack(e, p, s, q, rng.integers(0, 16, (N, 8, 16, B)), rng.choice(np.array([0, 1, 2, 2, 3, 3, 4]), (N, 8, B)))
def setup_inputs_alike(rng):
    e, p = tables_of(rng)
    fw = np.concatenate([np.argsort(rng.random((N, 8, W - 2)), axis=-1)[..., :4] + 1, np.zeros((N, 8, 1), np.int64), np.full((N, 8, 1), W - 1)], axis=2)
    ix = np.broadcast_to(fw[:, :, None, :], (N, 8, 16, 6))
    np.put_along_axis(e, ix, rng.choice(np.array([0, 3, 4, 8, 11, 12, 15]), (N, 8, 16, 6)), axis=3)
    np.put_along_axis(p, ix, np.where(rng.random((N, 8, 16, 6)) < 0.2, 12, 11), axis=3)
    n = rng.integers(0, 6, (N, 8, L, B)); n[:, 1::2] = n[:, 1::2, :, :1]
    n = np.where(rng.random((N, 8, 1, B)) < 0.15, n[:, :, :1], n)
    s = np.take_along_axis(fw, n.reshape(N, 8, L * B), axis=2).reshape(N, 8, L, B)
    q = np.take_along_axis(fw, rng.integers(0, 6, (N, 8, L * B)), axis=2).reshape(N, 8, L, B)
    q = np.where(rng.random((N, 8, L, B)) < 0.4, -1, q)
    return pack(e, p, s, q, rng.integers(0, 16, (N, 8, 16, B)), rng.integers(0, 5, (N, 8, B)))
def setup_inputs_corners(rng):
    o = np.argsort(rng.random((N, 8, W)), axis=-1); kc = np.zeros((N, 8, W), np.int64)
    np.put_along_axis(kc, o, np.broadcast_to(np.arange(W) & 7, (N, 8, W)), axis=2)
    k4 = kc[:, :, None, :]; bit = rng.integers(0, 2, (N, 8, 16, W)) == 1
    e = np.where(bit, np.array([4, 0, 12, 4, 4, 4, 4, 4])[k4], np.array([11, 3, 15, 11, 11, 11, 11, 11])[k4])
    e = np.where(k4 == 7, np.array([3, 4, 11, 12])[rng.integers(0, 4, (N, 8, 16, W))], e)
    rk = ((2 * rng.integers(0, 8, (N, 8, 1, W)) + 1) * np.arange(16)[None, None, :, None] + rng.integers(0, 16, (N, 8, 1, W))) & 15
    nd = np.where(k4 == 7, rng.integers(0, 4, (N, 8, 1, W)), np.array([0, 0, 0, 1, 2, 3, 16, 0])[k4]); bit = rng.integers(0, 2, (N, 8, 16, W)) == 1
    p = np.where(rk < nd, np.where(bit, 12, 15), np.where(bit, 11, 0))
    tp = rng.integers(0, 8, (N, 8, 1, B)); y = rng.integers(4, 7, (N, 8, 1, B)); v = rng.integers(1, L, (N, 8, 1, B)); kk = np.arange(L)[None, None, :, None]
    j = rng.choice(np.array([0, L // 2, L - 2]), (N, 8, 1, B)); cp = np.zeros((N, 8, L, B), np.int64)
    cp = np.where((tp == 1) & (kk == 0), y, cp)
    cp = np.where((tp == 2) & (kk == j), 1, cp); cp = np.where((tp == 2) & (kk == L - 1), y, cp)
    cp = np.where(tp == 3, 3, cp)
    for a, b in ((L // 3, 4), (L // 2, 5), (L - 1, 6)): cp = np.where((tp == 4) & (kk == a), b, cp)
    cp = np.where(tp == 5, np.where(kk == v, y, 1), cp)
    cp = np.where((tp == 6) & (kk == 0), 2, cp); cp = np.where((tp == 6) & (kk == L - 1), 1, cp)
    cp = np.where(tp == 7, rng.integers(0, 8, (N, 8, L, B)), cp)
    s = np.take_along_axis(o, (8 * rng.integers(0, W // 8, (N, 8, L, B)) + cp).reshape(N, 8, L * B), axis=2).reshape(N, 8, L, B)
    st = np.array([7, 8, 0, 15])[rng.integers(0, 4, (N, 8, 16, B))]
    st = np.where((tp == 1) | (tp == 3) | (tp == 4), 7, np.where(tp == 2, 8, st))
    h = np.where(tp == 2, j, np.where(tp == 5, v - 1, np.where(tp == 4, L // 3, 0))); own = np.take_along_axis(s, h, axis=2)
    qm = rng.integers(0, 4, (N, 8, 1, B))
    q = np.where(qm == 0, -1, np.where(qm == 1, own, np.where(qm == 2, np.where(rng.random((N, 8, L, B)) < 0.5, own, -1), own_steps(rng, s))))
    return pack(e, p, s, q, st, rng.choice(np.array([0, 1, 2, 3, 16]), (N, 8, B)))
def setup_inputs_ends(rng):
    t = W - 1
    e = 15 * (rng.random((N, 8, 16, W), dtype=np.float32) < rng.choice(np.array([0.0, 0.1, 0.5, 0.9, 1.0]), (N, 8, 1, W))).astype(np.int64)
    p = 15 * (rng.random((N, 8, 16, W), dtype=np.float32) < rng.choice(np.array([0.0, 0.0, 0.1, 0.3, 1.0]), (N, 8, 1, W))).astype(np.int64)
    kk = np.arange(L)[None, None, :, None]; x = rng.choice(np.array([0, 1, L // 2, L - 2, L - 1, L]), (N, 8, 1, B)); x[..., B - 1] = L - 2; x[..., B - 2] = L - 1
    m = rng.random((N, 8, 1, B)) < 0.6; m[..., B - 2:] = True
    s = t * np.where(m, (kk >= x).astype(np.int64), rng.integers(0, 2, (N, 8, L, B)))
    q = np.where(rng.random((N, 8, L, B)) < rng.choice(np.array([0.0, 0.2, 0.5, 1.0]), (N, 8, 1, B)), t, -1)
    st = 15 * (rng.random((N, 8, 16, B)) < rng.choice(np.array([0.0, 0.5, 1.0]), (N, 8, 1, B))).astype(np.int64)
    th = 16 * rng.integers(0, 2, (N, 8, B)); th[..., B - 1] = 16; th[..., B - 2] = 0
    c0 = (KAP * t) & t; c1 = ((t * t >> 5) + KAP * t) & t
    for r in range(N):
        for g in range(8):
            k = (N + 7 - r - g) & 3; u = e[r, g]
            if k == 3: continue
            if k == 0:
                u[0, c0] = 0; u[:, c0[L - 1]] = 15; u[:, 0] = 0; u[:, t] = 15 * rng.integers(0, 2, 16)
            elif k == 1:
                u[:, c1[[1, 2, L - 1]]] = 15; u[5, c1[0]] = 0; u[:, 0] = 15; u[:, t] = 0
            else:
                u[:, c1] = 0; u[:, 0] = 15; u[:, t] = 15; u[rng.permutation(16)[:2], t] = 0
            p[r, g, :, 0] = 0; p[r, g, :, t] = 15
    return pack(e, p, s, q, st, th)
def setup_inputs_full(rng):
    e, p = tables_of(rng); s = rng.integers(0, W, (N, 8, L, B)); st = rng.integers(0, 16, (N, 8, 16, B)); th = rng.choice(np.array([0, 1, 2, 2, 3, 3, 4]), (N, 8, B)); kk = np.arange(L)[:, None]
    for r in range(N):
        for g in range(8):
            m = (g + r + 2 - N) & 7
            if m > 4: continue
            o = rng.permutation(W).reshape(32, W // 32); kc = np.zeros(W, np.int64); kc[o] = np.arange(32)[:, None]
            y = rng.integers(0, 4, (16, W)); e[r, g] = np.where(kc < 17, rng.integers(4, 12, (16, W)), np.where(kc < 20, y, 12 + y))
            rk = ((2 * rng.integers(0, 8, W) + 1) * np.arange(16)[:, None] + rng.integers(0, 16, W)) & 15
            p[r, g] = np.where((rk < kc) & (kc < 17), rng.integers(12, 16, (16, W)), rng.integers(0, 12, (16, W)))
            n = rng.integers(2, 16, B) if m == 0 else rng.integers(4, 17, B)
            x = rng.choice(np.array([0, L // 2, L - 1, L - 1]), B); j = rng.integers(0, L, B); low = (j < x) & (rng.random(B) < 0.5)
            calm = rng.random(B) < (0.1 if m else 0.0)
            if m: calm[B // 2] = True
            kd = np.where(kk == x, n, np.where(kk > x, rng.integers(0, 32, (L, B)), 0)); kd = np.where((kk == j) & low, rng.integers(17, 20, B), kd); kd = np.where(calm, 0, kd)
            s[r, g] = o[kd, rng.integers(0, W // 32, (L, B))]
            st[r, g] = rng.integers(0, 8, (16, B)) + 8 * (low | calm).astype(np.int64)
            up = np.ones(B, np.int64) if m == 0 else rng.integers(0, 2, B)
            th[r, g] = np.minimum(n + up, 16)
    w = rng.integers(0, 5, (N, 8, L, B))
    q = np.where(w < 2, -1, np.where(w < 4, own_steps(rng, s), rng.integers(0, W, (N, 8, L, B))))
    return pack(e, p, s, q, st, th)
def setup_inputs_spread(rng):
    def power(hi, pw, shape): return np.minimum((hi * rng.random(shape, dtype=np.float32) ** pw.astype(np.float32)).astype(np.int64), hi - 1)
    e = power(16, rng.choice(np.array([0.5, 1.0, 2.0]), (N, 8, 16, 1)), (N, 8, 16, W))
    p = power(16, rng.choice(np.array([1.0, 3.0, 8.0, 20.0, 20.0]), (N, 8, 1, W)), (N, 8, 16, W))
    s = power(W, rng.choice(np.array([0.25, 1.0, 4.0]), (N, 8, L, 1)), (N, 8, L, B))
    q = np.where(rng.random((N, 8, L, B)) < 0.5, own_steps(rng, s), rng.integers(-1, W, (N, 8, L, B)))
    return pack(e, p, s, q, power(16, rng.choice(np.array([0.3, 1.0, 3.0]), (N, 8, 1, B)), (N, 8, 16, B)), power(17, rng.choice(np.array([1.0, 3.0, 6.0]), (N, 8, 1)), (N, 8, B)))
def check_inputs(d):
    bad = []
    for k, lo, hi in (("eff", 0, 15), ("req", 0, 15), ("act", 0, W - 1), ("why", -1, W - 1), ("st0", 0, 15), ("bar", 0, 16)):
        v = np.asarray(d[k]).astype(np.float64)
        if not (np.min(v) >= lo and np.max(v) <= hi): bad.append("range of " + k)
        elif np.any(v != np.floor(v)): bad.append("whole numbers in " + k)
    return bad
def pick(tab, ix):
    return np.stack([tab[g][:, ix[g]] for g in range(8)])
def visit(E, P, S, Q, s, th, R, t):
    kk = np.arange(L)[None, :, None]
    es = pick(E, S.reshape(8, L * B)).reshape(8, 16, L, B); ps = pick(P, S.reshape(8, L * B)).reshape(8, 16, L, B)
    flaw = np.zeros((8, 16, L, B), bool)
    for k in range(L):
        flaw[:, :, k] = (ps[:, :, k] >= 12) & (s < 8)
        s = np.where((es[:, :, k] >= 12) | (es[:, :, k] <= 3), es[:, :, k], s)
    over = np.add.reduce(flaw.astype(np.int16), axis=1) >= 2 + (R & 1)
    found = np.any(over, axis=1); ks = np.argmax(over, axis=1)
    fl = np.take_along_axis(flaw, ks[:, None, None, :], 2); need = np.take_along_axis(ps, ks[:, None, None, :], 2) >= 12
    low = np.any((es <= 3) & fl, axis=1) & (kk < ks[:, None, :])
    d = np.where(np.any(low, axis=1), L - 1 - np.argmax(low[:, ::-1], axis=1), ks)
    a = np.take_along_axis(S, ks[:, None, :], 1); z = np.take_along_axis(S, d[:, None, :], 1)
    c = ((a * z >> 5) + KAP[None, :, None] * a + 97 * t) & (W - 1)
    ec = pick(E, c.reshape(8, L * B)).reshape(8, 16, L, B)
    score = np.add.reduce(((ec >= 12) & fl).astype(np.int64), axis=1) - np.add.reduce(((ec <= 3) & need & ~fl).astype(np.int64), axis=1)
    m = np.argmax(score, axis=1); best = np.max(score, axis=1); cm = np.take_along_axis(c, m[:, None, :], 1)
    put = (found & (best >= th))[:, None, :]; ret = (found & (best < th))[:, None, :]
    kb = ks[:, None, :]
    si = np.where(kk < kb, S, np.where(kk == kb, cm, np.concatenate([S[:, :1], S[:, :-1]], axis=1)))
    qi = np.where(kk < kb, Q, np.where(kk == kb, z, np.concatenate([Q[:, :1], Q[:, :-1]], axis=1)))
    go = (kk == d[:, None, :]) | (Q == z)
    order = np.argsort(go, axis=1, kind="stable"); kept = kk < L - np.add.reduce(go.astype(np.int64), axis=1)[:, None, :]
    sr = np.where(kept, np.take_along_axis(S, order, 1), c); qr = np.where(kept, np.take_along_axis(Q, order, 1), -1)
    at = ST * np.arange(B)[None, :] + (np.add.reduce(s.astype(np.int64), axis=1) & (ST - 1))
    e2 = np.array(E); np.put_along_axis(e2, np.broadcast_to(at[:, None, :], (8, 16, B)), (pick(E, at) + s) >> 1, axis=2)
    return np.where(put, si, np.where(ret, sr, S)), np.where(put, qi, np.where(ret, qr, Q)), s, e2, int(np.count_nonzero(ret))
def reference(eff, req, act, why, st0, bar):
    E = [x.astype(np.float32).astype(np.int16).reshape(8, 16, W) for x in eff]; P = [x.astype(np.float32).astype(np.int16).reshape(8, 16, W) for x in req]
    S = [gentries(x).astype(np.int64).reshape(8, L, B) for x in act]; Q = [gentries(x).astype(np.int64).reshape(8, L, B) for x in why]
    s = [x.astype(np.float32).astype(np.int16).reshape(8, 16, B) for x in st0]; th = [gentries(x).astype(np.int64) for x in bar]; R = [0] * N
    for t in range(VI):
        v = [visit(E[r], P[r], S[r], Q[r], s[r], th[r], R[r], t) for r in range(N)]
        E = [x[3] for x in v]; R = [x[4] for x in v]; go = PS if t < VI - 1 else 0
        S = [v[(r - go) % N][0] for r in range(N)]; Q = [v[(r - go) % N][1] for r in range(N)]; s = [v[(r - 1) % N][2] for r in range(N)]
    return {"ys": np.stack([gtable(x.reshape(8, L * B)) for x in S]).astype(np.float32), "yw": np.stack([gtable(x.reshape(8, L * B)) for x in Q]).astype(np.float32),
            "ye": np.stack([x.reshape(128, W) for x in E]).astype(np.float32).astype(BF)}

@@ -1,0 +1,665 @@
+from concourse.mybir import AluOpType, AxisListType, ActivationFunctionType
+
+A = AluOpType
+ACT = ActivationFunctionType
+AX = AxisListType.X
+W, L, B, VI = 4096, 32, 128, 3
+PLAN_GO, STATE_GO = 3, 1
+H, F, I, U = "bfloat16", "float32", "int32", "uint16"
+
+SCRATCH = {}
+
+
+def _buf(dtype, n, *names):
+    for x in names:
+        SCRATCH[x] = ("sbuf", [128, n], dtype)
+
+
+_buf(H, W, "E", "PT", "TT", "ND", "Gc", "FL", "EC")
+_buf(H, 33 * B, "Gn", "D0", "D1", "V0")
+_buf(H, 2048, "SEL", "SEL2")
+_buf(H, 128, "ID", "ONE", "MK16", "SC0", "FOUR", "LT", "vx", "t12", "y", "Mb", "sv", "sq", "eb", "sc0", "sc1", "sc2", "so0", "so1")
+_buf(H, 8, "G8", "retb")
+_buf(H, 32, "ONES32")
+_buf(H, 512, "W4", "pp", "IS")
+_buf(F, 128, "RM")
+_buf(H, 256, "o1", "kept")
+_buf(F, 256, "K1c", "K19", "K18", "K2c", "K2", "prod1", "key2", "cm64", "t64", "t64S")
+_buf(F, 32, "kc", "KAP")
+_buf(F, 512, "ysw")
+_buf(F, 8, "Cv", "Cn", "C32", "SG", "ncd", "xf", "d8", "sxf", "bsf", "barf", "barM", "fnd", "nr", "cbx", "cbr", "aq", "aqt")
+_buf(F, 24, "base24", "m24", "best24", "bar24", "ret24", "pr24", "a24")
+_buf(F, 16, "n16", "c16", "d16", "r16", "f16")
+_buf(F, 1, "rs", "thr")
+_buf(I, 2, "ri")
+_buf(I, 6 * 264, "tb")
+_buf(I, 256, "craw", "cm")
+_buf(I, 8, "M8i", "xr", "xm", "sx", "di", "dg", "Mdi", "sd", "pr0", "bs", "MBi", "cb", "ui", "ua", "uo")
+_buf(I, 16, "oi")
+_buf(I, 128, "vi", "e2", "es", "en")
+_buf(I, 264, "ZS", "ZQ")
+_buf(I, 256, "nS", "nQ")
+_buf(U, 512, "pl0", "pl1", "pl2", "plo0", "plo1")
+_buf(U, 256, "cu")
+_buf(U, 16, "ou")
+_buf(U, 8, "uu")
+for _b in range(8):
+    SCRATCH["ps%d" % _b] = ("psum", [128, 512], F)
+
+DMAS = ["ld%d" % k for k in range(12)] + ["ds%d" % k for k in range(3)]
+SEMAPHORES = ["qv", "qs", "qt", "qg"] + DMAS + ["ap1", "ap2", "aq1", "aq2", "as1", "as2", "lp1", "lp2", "lq1", "lq2", "ls1", "ls2"]
+NSC = 6
+EARLY = True
+NVD = 1
+NVG = 14
+
+
+def _tracker(g, T):
+    eng = {"v": g.vector, "s": g.scalar, "t": g.tensor, "g": g, "y": g.sync}
+    cnt, bank = {}, {}
+    known = {q: {} for q in eng}
+
+    def settle(q, toks):
+        best = {}
+        for sem, c, clk in toks:
+            if known[q].get(sem, 0) < c and (sem not in best or best[sem][0] < c):
+                best[sem] = (c, clk)
+        todo = sorted(best.items(), key=lambda x: -len(x[1][1]))
+        for sem, (c, clk) in todo:
+            if known[q].get(sem, 0) >= c:
+                continue
+            if any(s2 != sem and known[q].get(s2, 0) < c2 and k2.get(sem, 0) >= c for s2, (c2, k2) in todo):
+                continue
+            eng[q].wait_ge(T.sem[sem], c)
+            known[q][sem] = c
+            for s2, c2 in clk.items():
+                if known[q].get(s2, 0) < c2:
+                    known[q][s2] = c2
+
+    def op(q, fn, toks, P, sem, inc):
+        for b in P:
+            toks = toks + [t for q2, t in bank.get(b, {}).items() if q2 != q]
+        settle(q, toks)
+        ins = fn(eng[q])
+        name = sem or "q" + q
+        cnt[name] = cnt.get(name, 0) + inc
+        ins.then_inc(T.sem[name], inc)
+        tok = (name, cnt[name], dict(known[q]))
+        for b in P:
+            bank.setdefault(b, {})[q] = tok
+        return tok
+
+    def send(fn, toks, local, n):
+        settle("g", toks)
+        fn()
+        cnt[local] = n
+        return (local, n, dict(known["g"]))
+
+    def lands(sem, n):
+        cnt[sem] = n
+        return (sem, n, {})
+
+    def finish():
+        settle("g", [(s, c, {}) for s, c in cnt.items()])
+
+    return op, send, lands, finish
+
+
+SHARED = (("Sf", "K2", "dfS", "al"), ("prod1", "df", "dfQ"), ("key2", "kss"), ("o1", "e2p"), ("aqt", "dxs"), ("rg0", "e1", "ksh", "Fp"),
+          ("rg1", "sp", "shk", "alY"), ("rg2", "mvS"), ("rg3", "mvQ"), ("stin", "eb"), ("ai", "craw"), ("wi", "cm"), ("pi", "ui"), ("pb", "ua"), ("fx", "FL"), ("aq0", "aq"))
+TAKES = {"v": {"V0": 1.75, "y": .25, "W4a": .25, "t12": .25, "RM": .11, "es": .25, "eb": .11, "en": .11, "E": .42, "TT": .42, "sv": .11, "vi": .11, "e2": .11, "FL": .11,
+               "Gc": .21, "EC": .21, "fx": .21, "ND": .43, "LT": .053, "D": .053},
+         "s": {"Gc": .7, "Gn": .7, "EC": .7, "vx": .25, "TT": .43}, "t": {"rg": .43, "SP": .11, "DT": .11}}
+for _k in ("o1", "prod1", "K1", "kss", "cm64", "alY", "Sf", "t64S", "t64Q", "cm", "cu", "K2", "key2", "kept", "shk", "ksh", "ZS", "ZQ", "tb", "mvS", "mvQ", "nS", "nQ", "dfS", "fin",
+           "po", "ysw", "so"):
+    TAKES["v"][_k] = .2
+WAKE = 0.15
+REORDER = ("v",)
+
+
+def _takes(e):
+    kind, q, Wr = e[0], e[1], e[4]
+    if kind == "send":
+        return 0.5
+    if kind == "lands":
+        return 2.0
+    if e[6] is not None:
+        return 0.05
+    if q == "v" and len(Wr) == 4 and Wr[0].startswith("FL"):
+        return 0.7 if "cu" in e[3] else 0.43
+    if "plS" in e[3] and Wr[0].startswith("D1"):
+        return 0.22
+    if "plS" in e[3] and Wr[0].startswith("Gn"):
+        return 0.7
+    k = Wr[0] if Wr else ""
+    tab = TAKES.get(q, {})
+    return tab.get(k, tab.get(k.rstrip("0123456789"), .06 if q != "g" else .3))
+
+
+def _schedule(prog):
+    fam = {}
+    for f in SHARED:
+        for s in f:
+            fam[s] = f
+    stem = {}
+
+    def st(k):
+        if k not in stem:
+            stem[k] = k if k in fam else k.rstrip("0123456789")
+        return stem[k]
+
+    wr, rd, keys = {}, {}, {}
+    deps = []
+    for i, e in enumerate(prog):
+        d = set()
+        for k in e[3]:
+            if k in wr:
+                d.add(wr[k])
+        for k in e[4]:
+            if k in wr:
+                d.add(wr[k])
+            d.update(rd.get(k, ()))
+            for s in fam.get(st(k), ()):
+                if s != st(k):
+                    for k2 in keys.get(s, ()):
+                        if k2 in wr:
+                            d.add(wr[k2])
+                        d.update(rd.get(k2, ()))
+        for k in e[3]:
+            rd.setdefault(k, []).append(i)
+            keys.setdefault(st(k), set()).add(k)
+        for k in e[4]:
+            wr[k] = i
+            rd[k] = []
+            keys.setdefault(st(k), set()).add(k)
+        d.discard(i)
+        deps.append(d)
+    n = len(prog)
+    cost = [_takes(e) for e in prog]
+    nxt = [[] for _ in range(n)]
+    for i in range(n):
+        for j in deps[i]:
+            nxt[j].append(i)
+    rank = [0.0] * n
+    for i in range(n - 1, -1, -1):
+        m = 0.0
+        for j in nxt[i]:
+            m = max(m, rank[j] + WAKE)
+        lat = 5.0 if prog[i][6] is not None else 0.0
+        rank[i] = cost[i] + lat + m
+    left = [len(d) for d in deps]
+    ready = {}
+    fifo = {}
+    for i, e in enumerate(prog):
+        if e[1] not in REORDER and e[1] != "x":
+            fifo.setdefault(e[1], []).append(i)
+    head = {q: 0 for q in fifo}
+    at = [0.0] * n
+    free = {}
+    for i in range(n):
+        if not left[i]:
+            ready.setdefault(prog[i][1], set()).add(i)
+    order = []
+    while len(order) < n:
+        pick = None
+        for q, r in ready.items():
+            c = r
+            if q in fifo:
+                i = fifo[q][head[q]] if head[q] < len(fifo[q]) else None
+                c = (i,) if i in r else ()
+            if not c:
+                continue
+            f = free.get(q, 0.0) if q != "x" else 0.0
+            t0 = min(max(f, at[i]) for i in c)
+            b = min((-rank[i], i) for i in c if max(f, at[i]) <= t0 + 0.02)[1]
+            s = max(f, at[b])
+            if pick is None or s < pick[0]:
+                pick = (s, b, q)
+        s, i, q = pick
+        ready[q].discard(i)
+        if q in head:
+            head[q] += 1
+        end = s + cost[i]
+        free[q] = end
+        order.append((s, i))
+        lat = 5.0 if prog[i][6] is not None else 0.0
+        for j in nxt[i]:
+            at[j] = max(at[j], end + lat + WAKE)
+            left[j] -= 1
+            if not left[j]:
+                ready.setdefault(prog[j][1], set()).add(j)
+    return [i for _, i in order], deps
+
+
+def ks(x, n, a=0):
+    return [x + str(k) for k in range(a, n)]
+
+
+def rank_program(g, core, T, topo):
+    rank = T.rank_of(core)
+    if rank is None:
+        return
+    N = len(T.cores)
+    op_now, send_now, lands_now, finish = _tracker(g, T)
+    prog = []
+
+    def op(q, fn, R=(), Wr=(), P=(), sem=None, inc=1):
+        prog.append(("op", q, fn, tuple(R), tuple(Wr), tuple(P), sem, inc))
+
+    def send(fn, R, local, n):
+        prog.append(("send", "g", fn, tuple(R), ("@" + local[1:] + "x",), (), None, (local, n)))
+
+    def lands(sem, n, Wr):
+        prog.append(("lands", "x", None, ("@" + sem[1:] + "x",), tuple(Wr), (), None, (sem, n)))
+
+    def remote(out, src, there, here, dst):
+        rid, pid, _ = topo.addr(dst)
+        return lambda: g.remote_dma(out, src, T.sem[there], T.sem[here], pid, rid, topo.mask(core, dst))
+
+    def ts(out, in0, s1, o0, s2=None, o1=None, R=(), Wr=(), P=()):
+        if o1 is None:
+            op("v", lambda e: e.tensor_scalar(out, in0, s1, None, o0), R, Wr, P)
+        else:
+            op("v", lambda e: e.tensor_scalar(out, in0, s1, s2, o0, o1), R, Wr, P)
+
+    def tt(out, a, b, o, R=(), Wr=(), P=()):
+        op("v", lambda e: e.tensor_tensor(out, a, b, o), R, Wr, P)
+
+    def cp(out, a, R=(), Wr=(), P=()):
+        op("v", lambda e: e.tensor_copy(out, a), R, Wr, P)
+
+    def scan(out, a, b, o0, o1, R, Wr, P=()):
+        op("v", lambda e: e.tensor_tensor_scan(out, a, b, 0.0, o0, o1), R, Wr, P)
+
+    def fill(x, c, key=None):
+        op("v", lambda e: e.memset(x, c), (), [key or x.name])
+
+    def mm(out, l, r, start, stop, R, Wr, P):
+        op("t", lambda e: e.matmul(out, l, r, start, stop), R, Wr, P)
+
+    def act(out, a, fn, R, Wr, P=(), **kw):
+        op("s", lambda e: e.activation(out, a, fn, **kw), R, Wr, P)
+
+    def iota(out, pattern, base, cmul, key):
+        flag = {} if key in ("pi",) else {"allow_small_or_imprecise_dtypes": True}
+        op("g", lambda e: e.iota(out, pattern, base, cmul, **flag), (), [key])
+
+    def load(q, k, out, src, Wr):
+        op(q, lambda e: e.dma_start(out, src), (), Wr, (), "ld%d" % k, 16)
+
+    def gred(out, src, o, R, Wr, P=()):
+        for h in range(8):
+            op("v", lambda e, h=h: e.tensor_reduce(out[:, h:h + 1], src[:, h:256:8], AX, o), R, [Wr + str(h)], P)
+
+    load("s", 0, T.craw[:, :], T.act[:, :], ["ai"])
+    load("s", 1, T.cm[:, :], T.why[:, :], ["wi"])
+    load("s", 2, T.eb[:, :], T.st0[:, :], ["stin"])
+    load("s", 3, T.Mdi[:, :], T.bar[:, :], ["bari"])
+    for k in range(4):
+        load("y", 4 + k, T.E[:, k * 1024:k * 1024 + 1024], T.eff[:, k * 1024:k * 1024 + 1024], ["E%d" % k])
+    for k in range(4):
+        load("y", 8 + k, T.PT[:, k * 1024:k * 1024 + 1024], T.req[:, k * 1024:k * 1024 + 1024], ["P%d" % k])
+    EK = ks("E", 4)
+
+    fill(T.ONE[:, :], 1.0, "ONE")
+    op("g", lambda e: e.affine_select(T.ID[:, :], T.ONE[:, :], [[-1, 128]], A.is_equal, 0.0, 0, 1), ["ONE"], ["ID"])
+    op("g", lambda e: e.affine_select(T.G8[:, :], T.ONE[:, 0:8], [[-16, 8]], A.is_ge, 0.0, 0, 1), ["ONE"], ["G8"])
+    op("g", lambda e: e.affine_select(T.G8[:, :], T.G8[:, :], [[16, 8]], A.is_ge, 0.0, 15, -1), ["G8"], ["G8"])
+    iota(T.ui[:, :], [[0, 8]], 0, 1, "pi")
+    iota(T.kc[:, :], [[1, 32]], 0, 0, "kc")
+    iota(T.KAP[:, :], [[113, 32]], 37, 0, "KAP")
+    iota(T.K1c[:, :], [[-1, 32], [0, 8]], 32, 0, "K1c")
+    iota(T.K19[:, :], [[-1, 32], [0, 8]], -1, 0, "K19")
+    iota(T.K18[:, :], [[-1, 32], [0, 8]], -1, 0, "K18")
+    iota(T.K2c[:, :], [[-4096, 32], [0, 8]], 31 * 4096, 0, "K2c")
+    iota(T.C32[:, :], [[16, 8]], 0, 0, "C32")
+    fill(T.SEL[:, :], 0.0, "SELz")
+    fill(T.SEL2[:, :], 0.0, "SEL2z")
+    fill(T.D0[:, 0:33 * B:33], -30000.0, "D0i")
+    fill(T.Gn[:, W:W + B], 192.0, "Gnx")
+    fill(T.ONES32[:, :], 1.0, "ONES32")
+    fill(T.SC0[:, :], -1000.0, "SC0z")
+    fill(T.SC0[:, 0:128:16], 1000.0, "SC0z")
+    fill(T.thr[:, :], 2.0, "thr")
+
+    for k, w in enumerate((-6.0, 2.0, 2.0, -2.0)):
+        act(T.IS[:, k * 128:k * 128 + 128], T.ID[:, :], ACT.Copy, ["ID"], ["IS%d" % k], scale=w)
+    for k in range(16):
+        x = slice(k * 128 + k, k * 128 + 128, 16)
+        act(T.SEL[:, x], T.G8[:, :], ACT.Copy, ["G8", "SELz"], ["SEL%d" % k])
+        act(T.SEL2[:, x], T.G8[:, :], ACT.Copy, ["G8", "SEL2z"], ["SEL2%d" % k], scale=131072.0)
+
+    cp(T.pl0[:, 0:256], T.craw[:, :], ["ai"], ["plS"])
+    ts(T.pl0[:, 256:512], T.cm[:, :], 2, A.add, R=["wi"], Wr=["plQ"])
+    ts(T.sq[:, :], T.eb[:, :], 8.0, A.is_ge, -264.0, A.mult, ["stin"], ["sq"])
+    tt(T.sc0[:, :], T.eb[:, :], T.sq[:, :], A.add, ["stin", "sq"], ["st"])
+
+    for c in range(8):
+        x = slice(c * 512, c * 512 + 512)
+        e = "E%d" % (c // 2)
+        ts(T.Gc[:, x], T.E[:, x], 4.0, A.is_ge, -520.0, A.mult, [e], ["Gc%d" % c])
+        ts(T.EC[:, x], T.E[:, x], 12.0, A.is_ge, 252.0, A.mult, [e], ["EC%d" % c])
+        p = T["ps%d" % (c % 4)]
+        bk = ["b%d" % (c % 4)]
+        pk = ["rg%d" % (c % 4)]
+        scan(T.FL[:, x], T.EC[:, x], T.Gc[:, x], A.max, A.add, ["EC%d" % c, "Gc%d" % c], ["fx%d" % c])
+        mm(p[:, :], T.ID[:, :], T.E[:, x], True, False, [e, "ID"], pk, bk)
+        mm(p[:, :], T.ID[:, :], T.FL[:, x], False, True, ["fx%d" % c], pk, bk)
+        act(T.TT[:, x], p[:, :], ACT.Copy, pk, ["TT%d" % c], bk)
+    TK = ks("TT", 8)
+    ts(T.ua[:, :], T.ui[:, :], 15, A.bitwise_and, R=["pi"], Wr=["pb"])
+    tt(T.C32[:, :], T.C32[:, :], T.ua[:, :], A.add, ["C32", "pb"], ["C32"])
+    ts(T.Cv[:, :], T.C32[:, :], 33.0, A.mult, 32.0, A.add, ["C32"], ["Cv"])
+    ts(T.Cn[:, :], T.C32[:, :], 4096.0, A.add, R=["C32"], Wr=["Cn"])
+    ts(T.C32[:, :], T.C32[:, :], 32.0, A.mult, R=["C32", "Cv", "Cn"], Wr=["C32"])
+    ts(T.ps5[:, 128:384], T.K1c[:, :], 8192.0, A.mult, R=["K1c"], Wr=["K1c"], P=["b5"])
+    cp(T.ps6[:, 256:512], T.K2c[:, :], ["K2c"], ["K2c"], ["b6"])
+    fill(T.FOUR[:, :], 4.0, "FOUR")
+    for k, w in enumerate((0.5, 248.5, -7.5, -11.5, 5.0)):
+        fill(T.SG[:, k:k + 1], w, "sgn")
+    ts(T.K19[:, :], T.K19[:, :], 524288.0, A.mult, R=["K19"], Wr=["K19"])
+    ts(T.K18[:, :], T.K18[:, :], 262144.0, A.mult, R=["K18"], Wr=["K18"])
+    cp(T.barf[:, :], T.Mdi[:, :], ["bari"], ["barf"])
+    for k in range(4):
+        x = slice(k * 1024, k * 1024 + 1024)
+        ts(T.ND[:, x], T.PT[:, x], 12.0, A.is_lt, R=["P%d" % k], Wr=["ND%d" % k])
+    NK = ks("ND", 4)
+    tt(T.pp[:, 0:64], T.ID[:, 0:64], T.ID[:, 64:128], A.add, ["ID"], ["p1"])
+    tt(T.pp[:, 128:160], T.pp[:, 0:32], T.pp[:, 32:64], A.add, ["p1"], ["p2"])
+    tt(T.MK16[:, 0:16], T.pp[:, 128:144], T.pp[:, 144:160], A.add, ["p2"], ["MK16"])
+
+    for t in range(VI):
+        pl = T["pl%d" % t]
+        last = t == VI - 1
+        if t:
+            n = len(topo.engines(T.cores[(rank - PLAN_GO) % N], core))
+            lands("ap%d" % t, n, ["plS"])
+            lands("aq%d" % t, n, ["plQ"])
+            lands("as%d" % t, len(topo.engines(T.cores[(rank - STATE_GO) % N], core)), ["st"])
+
+        for k in range(32 - NVG):
+            act(T.D1[:, k + 1:33 * B:33], T.TT[:, :].indirect(pl[:, k * 8:k * 8 + 8]), ACT.Identity, TK + ["plS"], ["D1%d" % k], bias=12.0 + 4 * k)
+        for c in range(8):
+            out, src = T.Gn[:, c * 512:c * 512 + 512], T.ND[:, :].indirect(pl[:, c * 32:c * 32 + 32])
+            if c < NVD:
+                ts(out, src, 188.0, A.mult, 4.0, A.add, NK + ["plS"], ["Gn%d" % c])
+            else:
+                act(out, src, ACT.Identity, NK + ["plS"], ["Gn%d" % c], scale=188.0, bias=4.0)
+        for k in range(32 - NVG, 32):
+            ts(T.D1[:, k + 1:33 * B:33], T.TT[:, :].indirect(pl[:, k * 8:k * 8 + 8]), 12.0 + 4 * k, A.add, R=TK + ["plS"], Wr=["D1%d" % k])
+        ts(T.D1[:, 0:33 * B:33], T["sc%d" % t][:, :], 4.0, A.add, R=["st"], Wr=["D1i"])
+        for k in range(32):
+            ts(T.D0[:, k + 1:33 * B:33], T.D1[:, k + 1:33 * B:33], -16.0, A.mult, -4960.0, A.add, ["D1%d" % k], ["D0%d" % k])
+        op("v", lambda e: e.tensor_tensor_scan(T.V0[:, :], T.D0[:, :], T.D1[:, :], 0.0, A.min, A.max),
+           ks("D0", 32) + ks("D1", 32) + ["D0i", "D1i"], ["V0"])
+        if t:
+            op("v", lambda e: e.tensor_reduce(T.rs[:, :], T.ps7[:, 280:288], AX, A.add), ["RS"], ["rs"], ["b7"])
+            cp(T.ri[:, 0:1], T.rs[:, :], ["rs"], ["ri"])
+            ts(T.ri[:, 1:2], T.ri[:, 0:1], 1, A.bitwise_and, R=["ri"], Wr=["rj"])
+            ts(T.thr[:, :], T.ri[:, 1:2], 2, A.add, R=["rj"], Wr=["thr"])
+
+        def ndps(c):
+            r = c % 4
+            mm(T["ps%d" % r][:, :], T.ID[:, :], T.Gn[:, c * 512:c * 512 + 512], True, True, ["ID", "Gn%d" % c], ["rg%d" % r], ["b%d" % r])
+
+        def flaw(c):
+            r = c % 4
+            for k in range(4 * c, 4 * c + 4):
+                tt(T.FL[:, k * 128:k * 128 + 128], T.V0[:, k:33 * B:33], T["ps%d" % r][:, (k % 4) * 128:(k % 4) * 128 + 128], A.is_ge,
+                   ["V0", "rg%d" % r], ["FL%d" % k], ["b%d" % r])
+
+        def count(src, key, sel, dst, bk, c, wk):
+            for k in range(16):
+                mm(dst[:, c * 64:c * 64 + 64], T[sel][:, k * 128:k * 128 + 128], src[:, c * 1024 + k:(c + 1) * 1024:16], k == 0, k == 15,
+                   ks(key, 8 * c + 8, 8 * c) + [sel + str(k)], [wk + str(c)] if k in (0, 15) else (), [bk])
+
+        for c in range(4):
+            ndps(c)
+        flaw(0)
+        ndps(4)
+        flaw(1)
+        ndps(5)
+        if EARLY:
+            count(T.FL, "FL", "SEL", T.ps4, "b4", 0, "CN")
+        flaw(2)
+        ndps(6)
+        flaw(3)
+        ndps(7)
+        if not EARLY:
+            count(T.FL, "FL", "SEL", T.ps4, "b4", 0, "CN")
+        count(T.FL, "FL", "SEL", T.ps4, "b4", 1, "CN")
+        for c in (4, 5):
+            flaw(c)
+        count(T.FL, "FL", "SEL", T.ps4, "b4", 2, "CN")
+        for c in (6, 7):
+            flaw(c)
+        count(T.FL, "FL", "SEL", T.ps4, "b4", 3, "CN")
+
+        v32 = T.V0[:, 32:33 * B:33]
+        for k, cut in enumerate((0.5, 248.5, -7.5, -11.5)):
+            act(T.pp[:, k * 128:k * 128 + 128], v32, ACT.Sign, ["V0", "sgn"], ["p%d" % (k + 1)], bias=T.SG[:, k:k + 1])
+        cp(T.K2[:, :], pl[:, 0:256], ["plS"], ["Sf"])
+        act(T.t64S[:, :], T.K2[:, :], ACT.Copy, ["Sf"], ["t64S"], scale=64.0)
+        tt(T.ps6[:, 0:256], T.K2[:, :], T.ps5[:, 128:384], A.add, ["Sf", "K1c"], ["K1"], ["b6", "b5"])
+        for k in range(5):
+            mm(T.ps5[:, 384:512], T.IS[:, (k % 4) * 128:(k % 4) * 128 + 128] if k < 4 else T.ID[:, :], T.pp[:, k * 128:k * 128 + 128] if k < 4 else T.FOUR[:, :],
+               k == 0, k == 4, ["IS%d" % (k % 4), "ID", "FOUR", "p%d" % (k % 4 + 1)], ["SP"] if k in (0, 4) else (), ["b5"])
+        cp(T.vi[:, :], v32, ["V0"], ["vi"])
+        ts(T.e2[:, :], T.vi[:, :], 3, A.bitwise_and, R=["vi"], Wr=["e2"])
+
+        ts(T.o1[:, :], T.ps4[:, 0:256], T.thr[:, :], A.is_ge, R=ks("CN", 4) + ["thr"], Wr=["o1"], P=["b4"])
+        tt(T.prod1[:, :], T.o1[:, :], T.ps6[:, 0:256], A.mult, ["o1", "K1"], ["prod1"], ["b6"])
+        gred(T.M8i, T.prod1, A.max, ["prod1"], "M8")
+        ts(T.xr[:, :], T.M8i[:, :], 13, A.arith_shift_right, R=ks("M8", 8), Wr=["xr"])
+        ts(T.sx[:, :], T.M8i[:, :], 4095, A.bitwise_and, R=ks("M8", 8), Wr=["sx"])
+        ts(T.xm[:, :], T.M8i[:, :], 6, A.arith_shift_right, 0x7FF80, A.bitwise_and, ks("M8", 8), ["xm"])
+        tt(T.oi[:, 0:8], T.Cv[:, :], T.xr[:, :], A.subtract, ["Cv", "xr"], ["oi0"])
+        tt(T.oi[:, 8:16], T.Cn[:, :], T.xm[:, :], A.subtract, ["Cn", "xm"], ["oi1"])
+        cp(T.ou[:, :], T.oi[:, :], ["oi0", "oi1"], ["ou"])
+        GNK = ks("Gn", 8) + ["Gnx"]
+        act(T.vx[:, :], T.V0[:, :].indirect(T.ou[:, 0:8]), ACT.Copy, ["V0", "ou"], ["vx"])
+        ts(T.t12[:, :], T.V0[:, :].indirect(T.ou[:, 0:8]), 0.0, A.is_ge, 12.0, A.mult, ["V0", "ou"], ["t12"])
+        tt(T.y[:, :], T.Gn[:, :].indirect(T.ou[:, 8:16]), T.vx[:, :], A.subtract, GNK + ["ou", "vx"], ["y"])
+        mm(T.ps7[:, 0:128], T.y[:, :], T.ID[:, :], True, True, ["y", "ID"], ["DT"], ["b7"])
+        tt(T.W4[:, 0:128], T.Gn[:, :].indirect(T.ou[:, 8:16]), T.t12[:, :], A.max, GNK + ["ou", "t12"], ["W4a"])
+        op("v", lambda e: e.tensor_tensor_scan(T.RM[:, :], T.SC0[:, :], T.ps7[:, 0:128], 0.0, A.max, A.min), ["SC0z", "DT"], ["RM"], ["b7"])
+        ts(T.xf[:, :], T.xr[:, :], -1.0, A.mult, 32.0, A.add, ["xr"], ["xf"])
+        for h in range(8):
+            out, col = T.LT[:, h * 16:h * 16 + 16], T.RM[:, h * 16 + 15:h * 16 + 16]
+            if h < 5:
+                ts(out, T.MK16[:, 0:16], col, A.mult, R=["MK16", "RM"], Wr=["LT%d" % h])
+            else:
+                act(out, T.MK16[:, 0:16], ACT.Identity, ["MK16", "RM"], ["LT%d" % h], scale=col)
+        mm(T.ps7[:, 256:264], T.LT[:, :], T.G8[:, :], True, True, ks("LT", 8) + ["G8"], ["D8"], ["b7"])
+        for k in range(4):
+            mm(T.ps0[:, k * 128:k * 128 + 128], T.ID[:, :], T.W4[:, 0:128], True, True, ["ID", "W4a"], ["rg0"], ["b0"])
+        ts(T.ncd[:, :], T.xr[:, :], -8192.0, A.mult, 262144.0, A.add, ["xr"], ["xs"])
+        ts(T.di[:, :], T.ps7[:, 256:264], -2048.0, A.mult, -16384.0, A.add, ["D8"], ["di"], ["b7"])
+        ts(T.dg[:, :], T.di[:, :], 63 << 13, A.bitwise_and, R=["di"], Wr=["dg"])
+        tt(T.d8[:, :], T.dg[:, :], T.ncd[:, :], A.min, ["dg", "xs"], ["d8"])
+        cp(T.sxf[:, :], T.sx[:, :], ["sx"], ["sxf"])
+        for h in range(8):
+            ts(T.prod1[:, h:256:8], T.ps6[:, h:256:8], -262144.0, A.add, T.d8[:, h:h + 1], A.add, ["K1", "d8"], ["df%d" % h], ["b6"])
+        for h in range(8):
+            op("v", lambda e, h=h: e.tensor_reduce(T.sd[:, h:h + 1], T.prod1[:, h:256:8], AX, A.min, apply_absolute_value=True), ["df%d" % h], ["sd%d" % h])
+        SD = ks("sd", 8)
+        for k in range(2):
+            act(T.base24[:, k * 8:k * 8 + 8], T.xf[:, :], ACT.Copy, ["xf"], ["ba%d" % k])
+        act(T.c16[:, 8:16], T.xf[:, :], ACT.Copy, ["xf"], ["c161"])
+        act(T.m24[:, 0:8], T.xf[:, :], ACT.Copy, ["xf"], ["m240"], scale=-1.0, bias=99.0)
+        act(T.Mb[:, :], T.W4[:, 0:128], ACT.Relu, ["W4a", "sgn"], ["Mb"], scale=-1.0, bias=T.SG[:, 4:5])
+        for k in range(1, 4):
+            act(T.W4[:, k * 128:k * 128 + 128], T.W4[:, 0:128], ACT.Copy, ["W4a"], ["W4%d" % k])
+        tt(T.pr0[:, :], T.sx[:, :], T.sd[:, :], A.mult, ["sx"] + SD, ["pr0"])
+        ts(T.bs[:, :], T.pr0[:, :], 5, A.arith_shift_right, R=["pr0"], Wr=["bs"])
+        ts(T.bsf[:, :], T.bs[:, :], 97.0 * t, A.add, R=["bs"], Wr=["bsf"])
+        for h in range(8):
+            ts(T.craw[:, h:256:8], T.KAP[:, :], T.sxf[:, h:h + 1], A.mult, T.bsf[:, h:h + 1], A.add, ["KAP", "sxf", "bsf"], ["craw%d" % h])
+        ts(T.cm[:, :], T.craw[:, :], 4095, A.bitwise_and, R=ks("craw", 8), Wr=["cm"])
+        cp(T.cu[:, :], T.cm[:, :], ["cm"], ["cu"])
+
+        for c in range(NSC):
+            act(T.EC[:, c * 512:c * 512 + 512], T.E[:, :].indirect(T.cu[:, c * 32:c * 32 + 32]), ACT.Copy, EK + ["cu"], ["EC%d" % c])
+
+        def vfuse(c):
+            tt(T.FL[:, c * 512:c * 512 + 512], T.E[:, :].indirect(T.cu[:, c * 32:c * 32 + 32]), T.W4[:, :], A.is_ge,
+               EK + ["cu", "W4a"] + ks("W4", 4, 1), ks("FL", 4 * c + 4, 4 * c))
+
+        def hit(c):
+            tt(T.FL[:, c * 512:c * 512 + 512], T.EC[:, c * 512:c * 512 + 512], T.ps0[:, :], A.is_ge, ["EC%d" % c, "rg0"], ks("FL", 4 * c + 4, 4 * c), ["b0"])
+
+        def score(c):
+            count(T.FL, "FL", "SEL2", T.ps4, "b4", c, "CN")
+
+        vfuse(7)
+        tt(T.sv[:, :], T.e2[:, :], T.ps5[:, 384:512], A.add, ["e2", "SP"], ["sv"], ["b5"])
+        hit(0)
+        for k in range(16):
+            mm(T.ps7[:, 272:280], T.SEL[:, k * 128:k * 128 + 128], T.sv[:, k:128:16], k == 0, k == 15, ["sv", "SEL%d" % k], ["U8"] if k in (0, 15) else (), ["b7"])
+        for k in range(16):
+            mm(T.ps5[:, 0:8], T.SEL[:, k * 128:k * 128 + 128], T.Mb[:, k:128:16], k == 0, k == 15, ["Mb", "SEL%d" % k], ["NM"] if k in (0, 15) else (), ["b5"])
+        if not last:
+            so = T["so%d" % t]
+            ts(T.sq[:, :], T.sv[:, :], 8.0, A.is_ge, -264.0, A.mult, ["sv"], ["sq"])
+            tt(so[:, :], T.sv[:, :], T.sq[:, :], A.add, ["sv", "sq"], ["so"])
+            dst = T.cores[(rank + STATE_GO) % N]
+            n = len(topo.engines(core, dst))
+            send(remote(T["sc%d" % (t + 1)][:, :], so[:, :], "as%d" % (t + 1), "ls%d" % (t + 1), dst), ["so"], "ls%d" % (t + 1), n)
+        hit(1)
+        score(0)
+        if NSC == 6:
+            vfuse(6)
+            score(3)
+        tt(T.K2[:, :], T.cm[:, :], T.ps6[:, 256:512], A.add, ["K2c", "cm"], ["K2"], ["b6"])
+        hit(2)
+        if t == 0:
+            fill(T.base24[:, 16:24], 0.0, "ba2")
+        tt(T.aqt[:, :], T.d8[:, :], T.ncd[:, :], A.subtract, ["d8", "xs"], ["dxs"])
+        ts(T.m24[:, 8:16], T.aqt[:, :], 1.0 / 8192, A.mult, R=["dxs"], Wr=["m241"])
+        ts(T.cm64[:, :], T.cm[:, :], 64.0, A.mult, -16777216.0, A.add, ["cm"], ["cm64"])
+        ts(T.m24[:, 16:24], T.sd[:, :], 64.0, A.mult, 128.0, A.add, SD, ["m242"])
+        ts(T.fnd[:, :], T.xr[:, :], 1.0, A.is_ge, 131072.0, A.mult, ["xr"], ["fnd"])
+        tt(T.barM[:, :], T.barf[:, :], T.ps5[:, 0:8], A.add, ["barf", "NM"], ["barM"], ["b5"])
+        hit(3)
+        score(1)
+        for k in range(3):
+            tt(T.bar24[:, k * 8:k * 8 + 8], T.barM[:, :], T.fnd[:, :], A.mult, ["barM", "fnd"], ["br%d" % k])
+        hit(4)
+        cp(T.ui[:, :], T.ps7[:, 272:280], ["U8"], ["ui"], ["b7"])
+        ts(T.ua[:, :], T.ui[:, :], 31, A.bitwise_and, R=["ui"], Wr=["ua"])
+        tt(T.uo[:, :], T.ua[:, :], T.C32[:, :], A.add, ["ua", "C32"], ["uo"])
+        cp(T.uu[:, :], T.uo[:, :], ["uo"], ["uu"])
+        hit(5)
+        score(2)
+        ts(T.t64[:, :], pl[:, 256:512], 64.0, A.mult, R=["plQ"], Wr=["t64Q"])
+        if NSC == 7:
+            hit(6)
+            score(3)
+        tt(T.es[:, :], T.E[:, :].indirect(T.uu[:, :]), T.sv[:, :], A.add, EK + ["uu", "sv"], ["es"])
+        ts(T.en[:, :], T.es[:, :], 1, A.arith_shift_right, R=["es"], Wr=["en"])
+        cp(T.eb[:, :], T.en[:, :], ["en"], ["eb"])
+        op("v", lambda e: e.tensor_copy(T.E[:, :].indirect(T.uu[:, :]), T.eb[:, :]), ["eb", "uu"], EK)
+        if last:
+            op("y", lambda e: e.dma_start(T.ye[:, :], T.E[:, :]), EK, ["ye"], (), "ds0", 16)
+
+        tt(T.key2[:, :], T.K2[:, :], T.ps4[:, 0:256], A.add, ["K2"] + ks("CN", 4), ["key2"], ["b4"])
+        gred(T.MBi, T.key2, A.max, ["key2"], "MBi")
+        MB = ks("MBi", 8)
+        for k in range(3):
+            tt(T.ret24[:, k * 8:k * 8 + 8], T.MBi[:, :], T.bar24[:, k * 8:k * 8 + 8], A.is_lt, MB + ["br%d" % k], ["ret%d" % k])
+        tt(T.pr24[:, :], T.ret24[:, :], T.m24[:, :], A.mult, ks("ret", 3) + ks("m24", 3), ["pr24"])
+        ts(T.cb[:, :], T.MBi[:, :], 4095, A.bitwise_and, R=MB, Wr=["cb"])
+        ts(T.cbx[:, :], T.cb[:, :], 64.0, A.mult, -16777216.0, A.add, ["cb"], ["cbx"])
+        ts(T.nr[:, :], T.ret24[:, 0:8], -1.0, A.mult, 1.0, A.add, ["ret0"], ["nr"])
+        tt(T.a24[:, :], T.base24[:, :], T.pr24[:, :], A.add, ["pr24"] + ks("ba", 3), ["a24"])
+        for h in range(8):
+            ts(T.ps0[:, h:256:8], T.kc[:, :], T.a24[:, h:h + 1], A.min, T.a24[:, 8 + h:9 + h], A.not_equal, ["kc", "a24"], ["e1%d" % h], ["b0"])
+            ts(T.o1[:, h:256:8], T.t64[:, h:256:8], T.a24[:, 16 + h:17 + h], A.not_equal, R=["t64Q", "a24"], Wr=["e2p%d" % h])
+        tt(T.kept[:, :], T.o1[:, :], T.ps0[:, 0:256], A.min, ks("e1", 8) + ks("e2p", 8), ["kept"], ["b0"])
+        if not last:
+            cp(T.retb[:, :], T.ret24[:, 0:8], ["ret0"], ["retb"])
+            mm(T.ps7[:, 280:288], T.ONE[:, :], T.retb[:, :], True, True, ["ONE", "retb"], ["RS"], ["b7"])
+        for h in range(8):
+            op("v", lambda e, h=h: e.tensor_tensor_scan(T.ps1[:, h:256:8], T.ONES32[:, :], T.kept[:, h:256:8], 1.0, A.add, A.subtract),
+               ["ONES32", "kept"], ["sp%d" % h], ["b1"])
+        tt(T.ps1[:, 256:512], T.kept[:, :], T.ps1[:, 0:256], A.mult, ["kept"] + ks("sp", 8), ["shk"], ["b1"])
+        op("v", lambda e: e.memset(T.ZS[:, 0:8], 0), (), ["ZS0"])
+        op("v", lambda e: e.memset(T.ZQ[:, 0:8], 0), (), ["ZQ0"])
+        tt(T.ps0[:, 256:512], T.K19[:, :], T.ps1[:, 256:512], A.add, ["K19", "shk"], ["ksh"], ["b0", "b1"])
+        tt(T.key2[:, :], T.K18[:, :], T.ps1[:, 256:512], A.add, ["K18", "shk"], ["kss"], ["b1"])
+        tt(T.ZS[:, 8:264], T.t64S[:, :], T.key2[:, :], A.add, ["t64S", "kss"], ["ZS"])
+        tt(T.ZQ[:, 8:264], T.t64[:, :], T.ps0[:, 256:512], A.add, ["t64Q", "ksh"], ["ZQ"], ["b0"])
+        for k in range(2):
+            ts(T.n16[:, k * 8:k * 8 + 8], T.ps1[:, 248:256], -1.0, A.mult, 33.0, A.add, ks("sp", 8), ["n16%d" % k], ["b1"])
+        if t == 0:
+            fill(T.c16[:, 0:8], 99.0, "c160")
+        ts(T.aqt[:, :], T.sd[:, :], 1.0, A.add, R=SD, Wr=["aqt"])
+        tt(T.d16[:, :], T.n16[:, :], T.c16[:, :], A.subtract, ["n160", "n161", "c160", "c161"], ["d16"])
+        tt(T.cbr[:, :], T.cbx[:, :], T.nr[:, :], A.mult, ["cbx", "nr"], ["cbr"])
+        tt(T.aq[:, :], T.aqt[:, :], T.nr[:, :], A.mult, ["aqt", "nr"], ["aq0"])
+        tt(T.r16[:, :], T.d16[:, :], T.ret24[:, 0:16], A.mult, ["d16", "ret0", "ret1"], ["r16"])
+        ts(T.aq[:, :], T.aq[:, :], 1.0, A.add, R=["aq0"], Wr=["aq"])
+        tt(T.f16[:, :], T.r16[:, :], T.c16[:, :], A.add, ["r16", "c160", "c161"], ["f16"])
+        for h in range(8):
+            act(T.K2[:, h:256:8], T.cm64[:, h:256:8], ACT.Identity, ["cm64", "ret0", "cbr"], ["al%d" % h], scale=T.ret24[:, h:h + 1], bias=T.cbr[:, h:h + 1])
+        for h in range(8):
+            ts(T.ps0[:, h:256:8], T.kc[:, :], T.f16[:, h:h + 1], A.min, T.f16[:, 8 + h:9 + h], A.is_equal, ["kc", "f16"], ["Fp%d" % h], ["b0"])
+        tt(T.ps1[:, 0:256], T.K2[:, :], T.ps0[:, 0:256], A.mult, ks("al", 8) + ks("Fp", 8), ["alY"], ["b0", "b1"])
+        for b in range(6):
+            s = 1 << b
+            m = (33 - s) * 8
+            z = ["ZS", "ZS0"]
+            q = ["ZQ", "ZQ0"]
+            tb = T.tb[:, b * 264:b * 264 + m]
+            ts(tb, T.ZS[:, 8 * s:264], b, A.arith_shift_right, 1, A.bitwise_and, z, ["tb%d" % b])
+            scan(T.ps2[:, 0:m], tb, T.ZS[:, 8 * s:264], A.max, A.mult, ["tb%d" % b] + z, ["mvS"], ["b2"])
+            scan(T.ps3[:, 0:m], tb, T.ZQ[:, 8 * s:264], A.max, A.mult, ["tb%d" % b] + q, ["mvQ"], ["b3"])
+            tt(T.ZS[:, 0:m], T.ZS[:, 0:m], T.ps2[:, 0:m], A.min, z + ["mvS"], z, ["b2"])
+            tt(T.ZQ[:, 0:m], T.ZQ[:, 0:m], T.ps3[:, 0:m], A.min, q + ["mvQ"], q, ["b3"])
+        tt(T.ZS[:, 0:256], T.ZS[:, 0:256], T.ps1[:, 0:256], A.min, z + ["alY"], z, ["b1"])
+        ts(T.nS[:, :], T.ZS[:, 0:256], 6, A.arith_shift_right, 4095, A.bitwise_and, ["ZS", "ZS0"], ["nS"])
+
+        def reasons():
+            ts(T.nQ[:, :], T.ZQ[:, 0:256], 6, A.arith_shift_right, 8191, A.bitwise_and, ["ZQ", "ZQ0"], ["nQ"])
+            for h in range(8):
+                ts(T.prod1[:, h:256:8], T.nQ[:, h:256:8], -1.0, A.mult, T.aq[:, h:h + 1], A.add, ["nQ", "aq"], ["dfQ%d" % h])
+            tt(T.ps3[:, 0:256], T.prod1[:, :], T.ps0[:, 0:256], A.mult, ks("dfQ", 8) + ks("Fp", 8), ["mvQ"], ["b3", "b0"])
+
+        if not last:
+            po = T["plo%d" % t]
+            dst = T.cores[(rank + PLAN_GO) % N]
+            n = len(topo.engines(core, dst))
+
+            def go(half, s):
+                x = slice(half * 256, half * 256 + 256)
+                cp(po[:, x], (T.nS, T.nQ)[half][:, :], [("nS", "nQ")[half]], ["po%d" % half])
+                send(remote(T["pl%d" % (t + 1)][:, x], po[:, x], "a%s%d" % (s, t + 1), "l%s%d" % (s, t + 1), dst), ["po%d" % half],
+                     "l%s%d" % (s, t + 1), n)
+
+            go(0, "p")
+            ts(T.pp[:, 0:128], T.eb[:, :], 4.0, A.is_ge, -520.0, A.mult, ["eb"], ["p1"])
+            ts(T.pp[:, 128:256], T.eb[:, :], 12.0, A.is_ge, 252.0, A.mult, ["eb"], ["p2"])
+            tt(T.pp[:, 256:384], T.pp[:, 0:128], T.pp[:, 128:256], A.add, ["p1", "p2"], ["p3"])
+            tt(T.TT[:, :].indirect(T.uu[:, :]), T.eb[:, :], T.pp[:, 256:384], A.add, ["eb", "p3", "uu"], TK)
+            reasons()
+            tt(T.nQ[:, :], T.nQ[:, :], T.ps3[:, 0:256], A.add, ["nQ", "mvQ"], ["nQ"], ["b3"])
+            go(1, "q")
+        else:
+            cp(T.ysw[:, 0:256], T.nS[:, :], ["nS"], ["ysw0"])
+            op("y", lambda e: e.dma_start(T.ys[:, :], T.ysw[:, 0:256]), ["ysw0"], ["ys"], (), "ds1", 16)
+            reasons()
+            tt(T.K2[:, :], T.nQ[:, :], T.ps3[:, 0:256], A.add, ["nQ", "mvQ"], ["dfS"], ["b3"])
+            ts(T.ysw[:, 256:512], T.K2[:, :], 2.0, A.subtract, R=["dfS"], Wr=["ysw1"])
+            op("s", lambda e: e.dma_start(T.yw[:, :], T.ysw[:, 256:512]), ["ysw1"], ["yw"], (), "ds2", 16)
+    order, deps = _schedule(prog)
+    tok = {}
+    for i in order:
+        kind, q, fn, R, Wr, P, sem, inc = prog[i]
+        toks = [tok[j] for j in sorted(deps[i]) if not (q == "t" and prog[j][1] == "t")]
+        if kind == "op":
+            tok[i] = op_now(q, fn, toks, P, sem, inc)
+        elif kind == "send":
+            tok[i] = send_now(fn, toks, inc[0], inc[1])
+        else:
+            tok[i] = lands_now(inc[0], inc[1])
+    finish()

@@ -15,43 +15,54 @@ def _buf(dtype, n, *names):
         SCRATCH[x] = ("sbuf", [128, n], dtype)
 
 
-_buf(H, W, "E", "PT", "TT", "ND", "Gc", "FL", "EC")
-_buf(H, 33 * B, "Gn", "D0", "D1", "V0")
+PART = {}
+
+
+def _pool(name, dtype, n, *names):
+    _buf(dtype, n * len(names), name)
+    for k, x in enumerate(names):
+        PART[x] = (name, k * n, n)
+
+
+_buf(H, W, "E", "E2", "PT", "TT", "ND", "Gn", "EC")
+_buf(H, 33 * B, "D1", "V0", "FL")
 _buf(H, 2048, "SEL", "SEL2")
-_buf(H, 128, "ID", "ONE", "MK16", "SC0", "FOUR", "LT", "vx", "t12", "y", "Mb", "sv", "sq", "eb", "sc0", "sc1", "sc2", "so0", "so1")
-_buf(H, 8, "G8", "retb")
+_buf(H, 128, "ID", "ONE", "MK16", "SCM", "SCZ", "DM", "LT", "vx", "wm", "CW", "M130", "sg0", "r4", "sgn", "az", "iseq", "w8", "prw",
+     "es", "eb", "ea", "eu", "ew", "ef", "sc0", "sc1", "sc2", "so0", "so1", "so2")
+_buf(H, 7 * 128, "IS")
+_buf(H, 8, "G8", "G82", "HR", "retb")
 _buf(H, 32, "ONES32")
-_buf(H, 512, "W4", "pp", "IS")
-_buf(F, 128, "RM")
-_buf(H, 256, "o1", "kept")
-_buf(F, 256, "K1c", "K19", "K18", "K2c", "K2", "prod1", "key2", "cm64", "t64", "t64S")
-_buf(F, 32, "kc", "KAP")
-_buf(F, 512, "ysw")
-_buf(F, 8, "Cv", "Cn", "C32", "SG", "ncd", "xf", "d8", "sxf", "bsf", "barf", "barM", "fnd", "nr", "cbx", "cbr", "aq", "aqt")
-_buf(F, 24, "base24", "m24", "best24", "bar24", "ret24", "pr24", "a24")
-_buf(F, 16, "n16", "c16", "d16", "r16", "f16")
-_buf(F, 1, "rs", "thr")
+_buf(H, 64, "THR", "CS")
+_buf(H, 256, "K2c", "hi", "e2p")
+_buf(F, 128, "RM", "kd")
+_buf(F, 512, "W4", "ysw")
+_buf(F, 256, "d0", "cmZ", "key", "sp", "al", "alY", "tm", "Kf")
+_buf(F, 32, "kc", "kc1", "KAP")
+_pool("lf", F, 8, "Cv", "C32", "SG", "sxf", "bsf", "barf", "barK", "fnd", "ret", "nr", "A1", "A2", "A3", "xb", "x64", "dp1", "sd2", "sdZ", "c33x",
+      "nx", "rn", "f0", "f1", "nr99", "v1", "v2")
+_buf(F, 1, "thr", "lc")
 _buf(I, 2, "ri")
-_buf(I, 6 * 264, "tb")
-_buf(I, 256, "craw", "cm")
-_buf(I, 8, "M8i", "xr", "xm", "sx", "di", "dg", "Mdi", "sd", "pr0", "bs", "MBi", "cb", "ui", "ua", "uo")
-_buf(I, 16, "oi")
-_buf(I, 128, "vi", "e2", "es", "en")
-_buf(I, 264, "ZS", "ZQ")
-_buf(I, 256, "nS", "nQ")
-_buf(U, 512, "pl0", "pl1", "pl2", "plo0", "plo1")
-_buf(U, 256, "cu")
-_buf(U, 16, "ou")
+_buf(I, 6 * 256, "tb")
+_buf(I, 256, "craw", "cm", "Dz", "nS", "wi")
+_buf(I, 128, "rd")
+_buf(I, 8, "bari")
+_pool("li", I, 8, "pi", "pb", "qq", "xr", "sx", "oi", "sd", "dq", "pr0", "bs", "MBi", "cb", "ui", "ua", "uo")
+_buf(I, 1024, "KW0", "KW1", "KW2")
+_buf(I, 768, "ZO0", "ZO1", "ZO2")
+_buf(U, 256, "pl0", "pl1", "pl2", "plo0", "plo1", "cu")
+_buf(U, 24, "ou")
 _buf(U, 8, "uu")
 for _b in range(8):
     SCRATCH["ps%d" % _b] = ("psum", [128, 512], F)
 
-DMAS = ["ld%d" % k for k in range(12)] + ["ds%d" % k for k in range(3)]
+DMAS = ["ld%d" % k for k in range(12)] + ["ds%d" % k for k in range(4)]
 SEMAPHORES = ["qv", "qs", "qt", "qg"] + DMAS + ["ap1", "ap2", "aq1", "aq2", "as1", "as2", "lp1", "lp2", "lq1", "lq2", "ls1", "ls2"]
-NSC = 6
-EARLY = True
-NVD = 1
-NVG = 14
+NFUSE = 3
+DL = 2.0 ** -18
+B1, B2 = 49152, 98304
+WM, C0 = 760, 1304
+CYC, GATHER, SCATTER, WAKE = 0.83e-3, 1.56, 3.8, 0.1
+SIZE = {H: 2, F: 4, I: 4, U: 2}
 
 
 def _tracker(g, T):
@@ -105,134 +116,71 @@ def _tracker(g, T):
     return op, send, lands, finish
 
 
-SHARED = (("Sf", "K2", "dfS", "al"), ("prod1", "df", "dfQ"), ("key2", "kss"), ("o1", "e2p"), ("aqt", "dxs"), ("rg0", "e1", "ksh", "Fp"),
-          ("rg1", "sp", "shk", "alY"), ("rg2", "mvS"), ("rg3", "mvQ"), ("stin", "eb"), ("ai", "craw"), ("wi", "cm"), ("pi", "ui"), ("pb", "ua"), ("fx", "FL"), ("aq0", "aq"))
-TAKES = {"v": {"V0": 1.75, "y": .25, "W4a": .25, "t12": .25, "RM": .11, "es": .25, "eb": .11, "en": .11, "E": .42, "TT": .42, "sv": .11, "vi": .11, "e2": .11, "FL": .11,
-               "Gc": .21, "EC": .21, "fx": .21, "ND": .43, "LT": .053, "D": .053},
-         "s": {"Gc": .7, "Gn": .7, "EC": .7, "vx": .25, "TT": .43}, "t": {"rg": .43, "SP": .11, "DT": .11}}
-for _k in ("o1", "prod1", "K1", "kss", "cm64", "alY", "Sf", "t64S", "t64Q", "cm", "cu", "K2", "key2", "kept", "shk", "ksh", "ZS", "ZQ", "tb", "mvS", "mvQ", "nS", "nQ", "dfS", "fin",
-           "po", "ysw", "so"):
-    TAKES["v"][_k] = .2
-WAKE = 0.15
-REORDER = ("v",)
-
-
-def _takes(e):
-    kind, q, Wr = e[0], e[1], e[4]
-    if kind == "send":
-        return 0.5
-    if kind == "lands":
-        return 2.0
-    if e[6] is not None:
-        return 0.05
-    if q == "v" and len(Wr) == 4 and Wr[0].startswith("FL"):
-        return 0.7 if "cu" in e[3] else 0.43
-    if "plS" in e[3] and Wr[0].startswith("D1"):
-        return 0.22
-    if "plS" in e[3] and Wr[0].startswith("Gn"):
-        return 0.7
-    k = Wr[0] if Wr else ""
-    tab = TAKES.get(q, {})
-    return tab.get(k, tab.get(k.rstrip("0123456789"), .06 if q != "g" else .3))
-
-
-def _schedule(prog):
-    fam = {}
-    for f in SHARED:
-        for s in f:
-            fam[s] = f
-    stem = {}
-
-    def st(k):
-        if k not in stem:
-            stem[k] = k if k in fam else k.rstrip("0123456789")
-        return stem[k]
-
-    wr, rd, keys = {}, {}, {}
+def _depends(prog):
+    seen = {}
     deps = []
     for i, e in enumerate(prog):
         d = set()
-        for k in e[3]:
-            if k in wr:
-                d.add(wr[k])
-        for k in e[4]:
-            if k in wr:
-                d.add(wr[k])
-            d.update(rd.get(k, ()))
-            for s in fam.get(st(k), ()):
-                if s != st(k):
-                    for k2 in keys.get(s, ()):
-                        if k2 in wr:
-                            d.add(wr[k2])
-                        d.update(rd.get(k2, ()))
-        for k in e[3]:
-            rd.setdefault(k, []).append(i)
-            keys.setdefault(st(k), set()).add(k)
-        for k in e[4]:
-            wr[k] = i
-            rd[k] = []
-            keys.setdefault(st(k), set()).add(k)
+        for name, m in e["R"]:
+            d.update(j for m2, j, w in seen.get(name, ()) if w and m2 & m)
+        for name, m in e["W"]:
+            d.update(j for m2, j, w in seen.get(name, ()) if m2 & m)
+        for name, m in e["W"]:
+            seen[name] = [x for x in seen.get(name, ()) if x[0] & ~m] + [(m, i, True)]
+        for name, m in e["R"]:
+            seen.setdefault(name, []).append((m, i, False))
         d.discard(i)
         deps.append(d)
+    return deps
+
+
+def _schedule(prog):
+    deps = _depends(prog)
     n = len(prog)
-    cost = [_takes(e) for e in prog]
     nxt = [[] for _ in range(n)]
     for i in range(n):
         for j in deps[i]:
             nxt[j].append(i)
     rank = [0.0] * n
     for i in range(n - 1, -1, -1):
-        m = 0.0
-        for j in nxt[i]:
-            m = max(m, rank[j] + WAKE)
-        lat = 5.0 if prog[i][6] is not None else 0.0
-        rank[i] = cost[i] + lat + m
+        rank[i] = min(prog[i]["cost"].values()) + prog[i]["lat"] + max([rank[j] + WAKE for j in nxt[i]] + [0.0])
     left = [len(d) for d in deps]
-    ready = {}
-    fifo = {}
-    for i, e in enumerate(prog):
-        if e[1] not in REORDER and e[1] != "x":
-            fifo.setdefault(e[1], []).append(i)
-    head = {q: 0 for q in fifo}
-    at = [0.0] * n
-    free = {}
-    for i in range(n):
-        if not left[i]:
-            ready.setdefault(prog[i][1], set()).add(i)
-    order = []
-    while len(order) < n:
-        pick = None
-        for q, r in ready.items():
-            c = r
-            if q in fifo:
-                i = fifo[q][head[q]] if head[q] < len(fifo[q]) else None
-                c = (i,) if i in r else ()
-            if not c:
-                continue
-            f = free.get(q, 0.0) if q != "x" else 0.0
-            t0 = min(max(f, at[i]) for i in c)
-            b = min((-rank[i], i) for i in c if max(f, at[i]) <= t0 + 0.02)[1]
-            s = max(f, at[b])
-            if pick is None or s < pick[0]:
-                pick = (s, b, q)
-        s, i, q = pick
-        ready[q].discard(i)
-        if q in head:
-            head[q] += 1
-        end = s + cost[i]
+    at = [{} for _ in range(n)]
+    ready = set(i for i in range(n) if not left[i])
+    free, bank, queue, order = {}, {}, {}, []
+
+    def start(i, q):
+        s = max([free.get(q, 0.0) if q != "x" else 0.0] + [t + (0.0 if q == q2 == "t" else WAKE) for q2, t in at[i].items()])
+        for b in prog[i]["P"]:
+            s = max([s] + [t + WAKE for q2, t in bank.get(b, {}).items() if q2 != q])
+        return s
+
+    fifo = {q: [i for i in range(n) if q in prog[i]["cost"]] for q in ("g", "y")}
+    while ready:
+        c = [(start(i, q), i, q) for i in ready for q in prog[i]["cost"] if q not in fifo or fifo[q][0] == i]
+        first = {}
+        for s, i, q in c:
+            first[q] = min(first.get(q, s), s)
+        q = min(first, key=lambda x: first[x])
+        _, i, s = min((-rank[i], i, s) for s, i, q2 in c if q2 == q and s <= first[q] + 0.03)
+        ready.discard(i)
+        if q in fifo:
+            fifo[q].pop(0)
+        end = s + prog[i]["cost"][q]
         free[q] = end
-        order.append((s, i))
-        lat = 5.0 if prog[i][6] is not None else 0.0
+        queue[i] = q
+        order.append(i)
+        for b in prog[i]["P"]:
+            bank.setdefault(b, {})[q] = end
         for j in nxt[i]:
-            at[j] = max(at[j], end + lat + WAKE)
+            at[j][q] = max(at[j].get(q, 0.0), end + prog[i]["lat"])
             left[j] -= 1
             if not left[j]:
-                ready.setdefault(prog[j][1], set()).add(j)
-    return [i for _, i in order], deps
+                ready.add(j)
+    return order, queue, deps
 
 
-def ks(x, n, a=0):
-    return [x + str(k) for k in range(a, n)]
+PLANNED = {}
 
 
 def rank_program(g, core, T, topo):
@@ -243,423 +191,385 @@ def rank_program(g, core, T, topo):
     op_now, send_now, lands_now, finish = _tracker(g, T)
     prog = []
 
-    def op(q, fn, R=(), Wr=(), P=(), sem=None, inc=1):
-        prog.append(("op", q, fn, tuple(R), tuple(Wr), tuple(P), sem, inc))
-
-    def send(fn, R, local, n):
-        prog.append(("send", "g", fn, tuple(R), ("@" + local[1:] + "x",), (), None, (local, n)))
-
-    def lands(sem, n, Wr):
-        prog.append(("lands", "x", None, ("@" + sem[1:] + "x",), tuple(Wr), (), None, (sem, n)))
-
-    def remote(out, src, there, here, dst):
-        rid, pid, _ = topo.addr(dst)
-        return lambda: g.remote_dma(out, src, T.sem[there], T.sem[here], pid, rid, topo.mask(core, dst))
-
-    def ts(out, in0, s1, o0, s2=None, o1=None, R=(), Wr=(), P=()):
-        if o1 is None:
-            op("v", lambda e: e.tensor_scalar(out, in0, s1, None, o0), R, Wr, P)
+    def v(name, a=0, b=None, step=1, p=0):
+        if name in PART:
+            name, o, n = PART[name]
+            a, b = o + a, o + (n if b is None else b)
+        n = SCRATCH[name][1][1]
+        cols = range(n)[a:b:step]
+        m = 0
+        if step == 1:
+            m = ((1 << len(cols)) - 1) << a
         else:
-            op("v", lambda e: e.tensor_scalar(out, in0, s1, s2, o0, o1), R, Wr, P)
+            for c in cols:
+                m |= 1 << c
+        ap = T[name][p:128, a:b:step] if p else T[name][:, a:b:step]
+        return (ap, [(name, m)], len(cols), SIZE[SCRATCH[name][2]], SCRATCH[name][0] == "psum", None)
 
-    def tt(out, a, b, o, R=(), Wr=(), P=()):
-        op("v", lambda e: e.tensor_tensor(out, a, b, o), R, Wr, P)
+    def col(name, c, p=0):
+        return v(name, c, c + 1, 1, p)
 
-    def cp(out, a, R=(), Wr=(), P=()):
-        op("v", lambda e: e.tensor_copy(out, a), R, Wr, P)
+    def ind(win, off):
+        return (win[0].indirect(off[0]), win[1], 16 * off[2], win[3], False, off)
 
-    def scan(out, a, b, o0, o1, R, Wr, P=()):
-        op("v", lambda e: e.tensor_tensor_scan(out, a, b, 0.0, o0, o1), R, Wr, P)
+    def ap(x):
+        return x[0] if isinstance(x, tuple) else x
 
-    def fill(x, c, key=None):
-        op("v", lambda e: e.memset(x, c), (), [key or x.name])
+    def rec(fns, out, ins, kind, sem=None, inc=1, lat=0.0, R=(), Wr=()):
+        ins = [x for x in ins if isinstance(x, tuple)]
+        sides = [out] + ins
+        reads = [k for x in ins for k in x[1]] + [k for x in sides if x[5] for k in x[5][1]] + list(R)
+        n = max(x[2] for x in sides)
+        cost = {}
+        for q in fns:
+            if kind == "mm":
+                c = max(64, ins[1][2]) * CYC
+            elif kind in ("dma", "g"):
+                c = 0.05 if kind == "dma" else 0.15 + 2 * n * CYC
+            elif any(x[5] for x in sides):
+                c = (0.05 if q == "v" else 0.065) + n * CYC * (SCATTER if out[5] else GATHER)
+            elif kind == "tt":
+                c = max(64, n * (1 if any(x[4] for x in ins) else 2)) * CYC
+            else:
+                c = max(64, n * (0.5 if q == "v" and kind == "ts" and all(x[3] == 2 for x in sides if x[2] > 1) else 1)) * CYC
+            cost[q] = c
+        prog.append({"kind": "op", "fn": fns, "R": reads, "W": list(out[1]) + list(Wr), "P": sorted(set(x[1][0][0] for x in sides if x[4])),
+                     "sem": sem, "inc": inc, "cost": cost, "lat": lat})
 
-    def mm(out, l, r, start, stop, R, Wr, P):
-        op("t", lambda e: e.matmul(out, l, r, start, stop), R, Wr, P)
+    def ts_fn(out, a, s1, o0, s2, o1):
+        if o1 is None:
+            return lambda e: e.tensor_scalar(out[0], a[0], ap(s1), None, o0)
+        return lambda e: e.tensor_scalar(out[0], a[0], ap(s1), ap(s2), o0, o1)
 
-    def act(out, a, fn, R, Wr, P=(), **kw):
-        op("s", lambda e: e.activation(out, a, fn, **kw), R, Wr, P)
+    def ts(out, a, s1, o0, s2=None, o1=None):
+        rec({"v": ts_fn(out, a, s1, o0, s2, o1)}, out, [a, s1, s2], "ts")
 
-    def iota(out, pattern, base, cmul, key):
-        flag = {} if key in ("pi",) else {"allow_small_or_imprecise_dtypes": True}
-        op("g", lambda e: e.iota(out, pattern, base, cmul, **flag), (), [key])
+    def tt(out, a, b, o):
+        rec({"v": lambda e: e.tensor_tensor(out[0], a[0], b[0], o)}, out, [a, b], "tt")
 
-    def load(q, k, out, src, Wr):
-        op(q, lambda e: e.dma_start(out, src), (), Wr, (), "ld%d" % k, 16)
+    def cp(out, a):
+        rec({"v": lambda e: e.tensor_copy(out[0], a[0])}, out, [a], "ts")
 
-    def gred(out, src, o, R, Wr, P=()):
-        for h in range(8):
-            op("v", lambda e, h=h: e.tensor_reduce(out[:, h:h + 1], src[:, h:256:8], AX, o), R, [Wr + str(h)], P)
+    def scan(out, a, b, init, o0, o1):
+        rec({"v": lambda e: e.tensor_tensor_scan(out[0], a[0], b[0], init, o0, o1)}, out, [a, b], "ts")
 
-    load("s", 0, T.craw[:, :], T.act[:, :], ["ai"])
-    load("s", 1, T.cm[:, :], T.why[:, :], ["wi"])
-    load("s", 2, T.eb[:, :], T.st0[:, :], ["stin"])
-    load("s", 3, T.Mdi[:, :], T.bar[:, :], ["bari"])
+    def red(out, a, o):
+        rec({"v": lambda e: e.tensor_reduce(out[0], a[0], AX, o)}, out, [a], "red")
+
+    def fill(out, c):
+        rec({"v": lambda e: e.memset(out[0], c)}, out, [], "ts")
+
+    def act_fn(out, a, fn, scale, bias):
+        kw = {}
+        if scale is not None:
+            kw["scale"] = ap(scale)
+        if bias is not None:
+            kw["bias"] = ap(bias)
+        return lambda e: e.activation(out[0], a[0], fn, **kw)
+
+    def act(out, a, fn, scale=None, bias=None):
+        rec({"s": act_fn(out, a, fn, scale, bias)}, out, [a, scale, bias], "act")
+
+    def affine(out, a, scale, bias=None, qs="vs"):
+        fns = {"v": ts_fn(out, a, scale, A.mult, bias, None if bias is None else A.add), "s": act_fn(out, a, ACT.Identity, scale, bias)}
+        rec({q: fns[q] for q in qs}, out, [a, scale, bias], "ts")
+
+    def mms(out, pairs):
+        key = [("open" + out[1][0][0], 1)]
+        for k, (l, r) in enumerate(pairs):
+            first, last = k == 0, k == len(pairs) - 1
+            rec({"t": lambda e, l=l, r=r, first=first, last=last: e.matmul(out[0], l[0], r[0], first, last)}, out, [l, r], "mm", Wr=key)
+
+    def gp(fn, out, ins):
+        rec({"g": fn}, out, ins, "g")
+
+    def iota(out, pattern, base, cmul):
+        flag = {} if SCRATCH[out[1][0][0]][2] == I else {"allow_small_or_imprecise_dtypes": True}
+        gp(lambda e: e.iota(out[0], pattern, base, cmul, **flag), out, [])
+
+    def load(q, k, out, src, lat):
+        rec({q: lambda e: e.dma_start(out[0], src)}, out, [], "dma", "ld%d" % k, 16, lat)
+
+    def store(q, k, dst, src):
+        rec({q: lambda e: e.dma_start(dst, src[0])}, (None, [("out%d" % k, 1)], 1, 4, False, None), [src], "dma", "ds%d" % k, 16, 3.0)
+
+    def send(name, out, src, go, lat):
+        dst = T.cores[(rank + go) % N]
+        rid, pid, _ = topo.addr(dst)
+        fn = lambda: g.remote_dma(out[0], src[0], T.sem["a" + name], T.sem["l" + name], pid, rid, topo.mask(core, dst))
+        prog.append({"kind": "send", "fn": fn, "R": src[1], "W": [("sent" + name, 1)], "P": [], "sem": "l" + name,
+                     "inc": len(topo.engines(core, dst)), "cost": {"g": 0.5}, "lat": 0.0})
+        prog.append({"kind": "lands", "fn": None, "R": [("sent" + name, 1)], "W": out[1], "P": [], "sem": "a" + name,
+                     "inc": len(topo.engines(T.cores[(rank - go) % N], core)), "cost": {"x": lat}, "lat": 0.0})
+
+    def lanes(name, h, a=0):
+        return v(name, a + h, a + 256, 8)
+
+    def IS(k):
+        return v("IS", k * 128, k * 128 + 128)
+
+    load("s", 0, v("craw"), T.act[:, :], 3.0)
+    load("s", 2, v("sc0"), T.st0[:, :], 3.0)
+    load("s", 1, v("wi"), T.why[:, :], 3.5)
+    load("s", 3, v("bari"), T.bar[:, :], 3.5)
     for k in range(4):
-        load("y", 4 + k, T.E[:, k * 1024:k * 1024 + 1024], T.eff[:, k * 1024:k * 1024 + 1024], ["E%d" % k])
+        load("y", 4 + k, v("E", k * 1024, k * 1024 + 1024), T.eff[:, k * 1024:k * 1024 + 1024], 3.5 + k)
     for k in range(4):
-        load("y", 8 + k, T.PT[:, k * 1024:k * 1024 + 1024], T.req[:, k * 1024:k * 1024 + 1024], ["P%d" % k])
-    EK = ks("E", 4)
+        load("y", 8 + k, v("PT", k * 1024, k * 1024 + 1024), T.req[:, k * 1024:k * 1024 + 1024], 7.5 + k)
 
-    fill(T.ONE[:, :], 1.0, "ONE")
-    op("g", lambda e: e.affine_select(T.ID[:, :], T.ONE[:, :], [[-1, 128]], A.is_equal, 0.0, 0, 1), ["ONE"], ["ID"])
-    op("g", lambda e: e.affine_select(T.G8[:, :], T.ONE[:, 0:8], [[-16, 8]], A.is_ge, 0.0, 0, 1), ["ONE"], ["G8"])
-    op("g", lambda e: e.affine_select(T.G8[:, :], T.G8[:, :], [[16, 8]], A.is_ge, 0.0, 15, -1), ["G8"], ["G8"])
-    iota(T.ui[:, :], [[0, 8]], 0, 1, "pi")
-    iota(T.kc[:, :], [[1, 32]], 0, 0, "kc")
-    iota(T.KAP[:, :], [[113, 32]], 37, 0, "KAP")
-    iota(T.K1c[:, :], [[-1, 32], [0, 8]], 32, 0, "K1c")
-    iota(T.K19[:, :], [[-1, 32], [0, 8]], -1, 0, "K19")
-    iota(T.K18[:, :], [[-1, 32], [0, 8]], -1, 0, "K18")
-    iota(T.K2c[:, :], [[-4096, 32], [0, 8]], 31 * 4096, 0, "K2c")
-    iota(T.C32[:, :], [[16, 8]], 0, 0, "C32")
-    fill(T.SEL[:, :], 0.0, "SELz")
-    fill(T.SEL2[:, :], 0.0, "SEL2z")
-    fill(T.D0[:, 0:33 * B:33], -30000.0, "D0i")
-    fill(T.Gn[:, W:W + B], 192.0, "Gnx")
-    fill(T.ONES32[:, :], 1.0, "ONES32")
-    fill(T.SC0[:, :], -1000.0, "SC0z")
-    fill(T.SC0[:, 0:128:16], 1000.0, "SC0z")
-    fill(T.thr[:, :], 2.0, "thr")
-
-    for k, w in enumerate((-6.0, 2.0, 2.0, -2.0)):
-        act(T.IS[:, k * 128:k * 128 + 128], T.ID[:, :], ACT.Copy, ["ID"], ["IS%d" % k], scale=w)
+    ID, ONE, G8 = v("ID"), v("ONE"), v("G8")
+    fill(ONE, 1.0)
+    gp(lambda e: e.affine_select(ID[0], ONE[0], [[-1, 128]], A.is_equal, 0.0, 0, 1), ID, [ONE])
+    gp(lambda e: e.affine_select(G8[0], v("ONE", 0, 8)[0], [[-16, 8]], A.is_ge, 0.0, 0, 1), G8, [ONE])
+    gp(lambda e: e.affine_select(G8[0], G8[0], [[16, 8]], A.is_ge, 0.0, 15, -1), G8, [G8])
+    iota(v("pi"), [[0, 8]], 0, 1)
+    iota(v("C32"), [[16, 8]], 0, 0)
+    iota(v("Kf"), [[4096, 256]], 0, 0)
+    iota(v("kc"), [[1, 32]], 0, 0)
+    iota(v("kc1"), [[1, 32]], 1, 0)
+    iota(v("KAP"), [[113, 32]], 37, 0)
+    iota(v("HR"), [[1, 8]], 0, 0)
+    iota(v("K2c"), [[-4096, 32], [0, 8]], 31 * 4096, 0)
+    fill(v("SEL"), 0.0)
+    fill(v("SEL2"), 0.0)
+    fill(v("FL", W, W + B), B2 * DL)
+    fill(v("ONES32"), 1.0)
+    fill(v("SCM"), 10000.0)
+    fill(v("SCM", 0, 128, 16), -10000.0)
+    fill(v("SCZ"), 1.0)
+    fill(v("SCZ", 0, 128, 16), 0.0)
+    fill(v("CW"), -784.0)
+    fill(v("M130"), -130.0)
+    fill(v("THR"), 96.0 * 2 ** 22)
+    fill(v("THR", 0, 64, 1, 64), 1.5 * 2 ** 16)
+    fill(v("CS"), -32000.0 * 64)
+    slope = -(2 * WM + 20) / ((B2 - B1 + 256) * DL)
+    for k, w in enumerate((-7.5, 128.5, 1.0, WM + 12 - slope * (B1 - 256) * DL, 0.0)):
+        fill(col("SG", k), w)
+    for k, w in enumerate((-1.0, 6.0, 8.0, 64.0, 1 / DL, -1 / DL, -3 / 32 / DL)):
+        affine(IS(k), ID, w)
     for k in range(16):
-        x = slice(k * 128 + k, k * 128 + 128, 16)
-        act(T.SEL[:, x], T.G8[:, :], ACT.Copy, ["G8", "SELz"], ["SEL%d" % k])
-        act(T.SEL2[:, x], T.G8[:, :], ACT.Copy, ["G8", "SEL2z"], ["SEL2%d" % k], scale=131072.0)
+        affine(v("SEL", k * 128 + k, k * 128 + 128, 16), G8, 2.0 ** 32)
+        affine(v("SEL2", k * 128 + k, k * 128 + 128, 16), G8, 2.0 ** 13)
+    affine(v("G82"), G8, 2.0)
+    affine(v("HR"), v("HR"), 1 / 128)
+    ts(v("pb"), v("pi"), 15, A.bitwise_and)
+    cp(v("lc"), col("pb", 0))
+    tt(v("C32"), v("C32"), v("pb"), A.add)
+    affine(v("Cv"), v("C32"), 33.0)
+    affine(v("C32"), v("C32"), 32.0)
+    affine(v("ps6", 0, 256), v("Kf"), 1.0)
+    ts(v("barf"), v("bari"), 16.0, A.add)
+    tt(v("DM", 0, 64), v("ID", 0, 64), v("ID", 64, 128), A.add)
+    tt(v("DM", 64, 96), v("DM", 0, 32), v("DM", 32, 64), A.add)
+    tt(v("MK16", 0, 16), v("DM", 64, 80), v("DM", 80, 96), A.add)
+    for h in range(8):
+        affine(v("DM", 16 * h, 16 * h + 16), v("MK16", 0, 16), 1.0)
 
-    cp(T.pl0[:, 0:256], T.craw[:, :], ["ai"], ["plS"])
-    ts(T.pl0[:, 256:512], T.cm[:, :], 2, A.add, R=["wi"], Wr=["plQ"])
-    ts(T.sq[:, :], T.eb[:, :], 8.0, A.is_ge, -264.0, A.mult, ["stin"], ["sq"])
-    tt(T.sc0[:, :], T.eb[:, :], T.sq[:, :], A.add, ["stin", "sq"], ["st"])
+    cp(v("pl0"), v("craw"))
+    tt(v("KW0", 256, 512), v("craw"), v("ps6", 0, 256), A.add)
+    ts(v("KW0", 512, 768), v("wi"), -2047.0, A.add)
+    ts(v("ps5", 256, 512), v("wi"), -2047.0, A.add, 4096.0, A.mult)
+    tt(v("KW0", 768, 1024), v("craw"), v("ps5", 256, 512), A.add)
+
+    def classes(u, w, f, e, off):
+        ts(u, e, 4.0 + off, A.is_ge, -1 / DL, A.mult)
+        ts(w, e, 12.0 + off, A.is_ge, 1 + 116 * DL, A.subtract)
+        scan(f, u, w, 0.0, A.min, A.mult)
 
     for c in range(8):
-        x = slice(c * 512, c * 512 + 512)
-        e = "E%d" % (c // 2)
-        ts(T.Gc[:, x], T.E[:, x], 4.0, A.is_ge, -520.0, A.mult, [e], ["Gc%d" % c])
-        ts(T.EC[:, x], T.E[:, x], 12.0, A.is_ge, 252.0, A.mult, [e], ["EC%d" % c])
-        p = T["ps%d" % (c % 4)]
-        bk = ["b%d" % (c % 4)]
-        pk = ["rg%d" % (c % 4)]
-        scan(T.FL[:, x], T.EC[:, x], T.Gc[:, x], A.max, A.add, ["EC%d" % c, "Gc%d" % c], ["fx%d" % c])
-        mm(p[:, :], T.ID[:, :], T.E[:, x], True, False, [e, "ID"], pk, bk)
-        mm(p[:, :], T.ID[:, :], T.FL[:, x], False, True, ["fx%d" % c], pk, bk)
-        act(T.TT[:, x], p[:, :], ACT.Copy, pk, ["TT%d" % c], bk)
-    TK = ks("TT", 8)
-    ts(T.ua[:, :], T.ui[:, :], 15, A.bitwise_and, R=["pi"], Wr=["pb"])
-    tt(T.C32[:, :], T.C32[:, :], T.ua[:, :], A.add, ["C32", "pb"], ["C32"])
-    ts(T.Cv[:, :], T.C32[:, :], 33.0, A.mult, 32.0, A.add, ["C32"], ["Cv"])
-    ts(T.Cn[:, :], T.C32[:, :], 4096.0, A.add, R=["C32"], Wr=["Cn"])
-    ts(T.C32[:, :], T.C32[:, :], 32.0, A.mult, R=["C32", "Cv", "Cn"], Wr=["C32"])
-    ts(T.ps5[:, 128:384], T.K1c[:, :], 8192.0, A.mult, R=["K1c"], Wr=["K1c"], P=["b5"])
-    cp(T.ps6[:, 256:512], T.K2c[:, :], ["K2c"], ["K2c"], ["b6"])
-    fill(T.FOUR[:, :], 4.0, "FOUR")
-    for k, w in enumerate((0.5, 248.5, -7.5, -11.5, 5.0)):
-        fill(T.SG[:, k:k + 1], w, "sgn")
-    ts(T.K19[:, :], T.K19[:, :], 524288.0, A.mult, R=["K19"], Wr=["K19"])
-    ts(T.K18[:, :], T.K18[:, :], 262144.0, A.mult, R=["K18"], Wr=["K18"])
-    cp(T.barf[:, :], T.Mdi[:, :], ["bari"], ["barf"])
+        a, b = c * 512, c * 512 + 512
+        p = v(("ps0", "ps1", "ps2", "ps7")[c % 4])
+        classes(v("Gn", a, b), v("EC", a, b), v("D1", a, b), v("E", a, b), 0)
+        mms(p, [(ID, v("E", a, b)), (ID, v("D1", a, b))])
+        act(v("TT", a, b), p, ACT.Identity, None, -252.0)
     for k in range(4):
-        x = slice(k * 1024, k * 1024 + 1024)
-        ts(T.ND[:, x], T.PT[:, x], 12.0, A.is_lt, R=["P%d" % k], Wr=["ND%d" % k])
-    NK = ks("ND", 4)
-    tt(T.pp[:, 0:64], T.ID[:, 0:64], T.ID[:, 64:128], A.add, ["ID"], ["p1"])
-    tt(T.pp[:, 128:160], T.pp[:, 0:32], T.pp[:, 32:64], A.add, ["p1"], ["p2"])
-    tt(T.MK16[:, 0:16], T.pp[:, 128:144], T.pp[:, 144:160], A.add, ["p2"], ["MK16"])
+        ts(v("ND", k * 1024, k * 1024 + 1024), v("PT", k * 1024, k * 1024 + 1024), 12.0, A.is_lt)
+
+    def rows(dst, sel, src, a, n, first):
+        mms(dst, first + [(v(sel, k * 128, k * 128 + 128), v(src, a + k, a + n, 16)) for k in range(16)])
 
     for t in range(VI):
-        pl = T["pl%d" % t]
+        pl, KW, s0, sv, ZO = "pl%d" % t, "KW%d" % t, v("sc%d" % t), v("so%d" % t), "ZO%d" % t
         last = t == VI - 1
-        if t:
-            n = len(topo.engines(T.cores[(rank - PLAN_GO) % N], core))
-            lands("ap%d" % t, n, ["plS"])
-            lands("aq%d" % t, n, ["plQ"])
-            lands("as%d" % t, len(topo.engines(T.cores[(rank - STATE_GO) % N], core)), ["st"])
+        X0, V32 = v("D1", 0, None, 33), v("V0", 32, None, 33)
 
-        for k in range(32 - NVG):
-            act(T.D1[:, k + 1:33 * B:33], T.TT[:, :].indirect(pl[:, k * 8:k * 8 + 8]), ACT.Identity, TK + ["plS"], ["D1%d" % k], bias=12.0 + 4 * k)
-        for c in range(8):
-            out, src = T.Gn[:, c * 512:c * 512 + 512], T.ND[:, :].indirect(pl[:, c * 32:c * 32 + 32])
-            if c < NVD:
-                ts(out, src, 188.0, A.mult, 4.0, A.add, NK + ["plS"], ["Gn%d" % c])
-            else:
-                act(out, src, ACT.Identity, NK + ["plS"], ["Gn%d" % c], scale=188.0, bias=4.0)
-        for k in range(32 - NVG, 32):
-            ts(T.D1[:, k + 1:33 * B:33], T.TT[:, :].indirect(pl[:, k * 8:k * 8 + 8]), 12.0 + 4 * k, A.add, R=TK + ["plS"], Wr=["D1%d" % k])
-        ts(T.D1[:, 0:33 * B:33], T["sc%d" % t][:, :], 4.0, A.add, R=["st"], Wr=["D1i"])
+        act(v("sg0"), s0, ACT.Sign, None, col("SG", 0))
+        affine(X0, v("sg0"), 64 * DL, -192 * DL)
         for k in range(32):
-            ts(T.D0[:, k + 1:33 * B:33], T.D1[:, k + 1:33 * B:33], -16.0, A.mult, -4960.0, A.add, ["D1%d" % k], ["D0%d" % k])
-        op("v", lambda e: e.tensor_tensor_scan(T.V0[:, :], T.D0[:, :], T.D1[:, :], 0.0, A.min, A.max),
-           ks("D0", 32) + ks("D1", 32) + ["D0i", "D1i"], ["V0"])
-        if t:
-            op("v", lambda e: e.tensor_reduce(T.rs[:, :], T.ps7[:, 280:288], AX, A.add), ["RS"], ["rs"], ["b7"])
-            cp(T.ri[:, 0:1], T.rs[:, :], ["rs"], ["ri"])
-            ts(T.ri[:, 1:2], T.ri[:, 0:1], 1, A.bitwise_and, R=["ri"], Wr=["rj"])
-            ts(T.thr[:, :], T.ri[:, 1:2], 2, A.add, R=["rj"], Wr=["thr"])
-
-        def ndps(c):
-            r = c % 4
-            mm(T["ps%d" % r][:, :], T.ID[:, :], T.Gn[:, c * 512:c * 512 + 512], True, True, ["ID", "Gn%d" % c], ["rg%d" % r], ["b%d" % r])
-
-        def flaw(c):
-            r = c % 4
-            for k in range(4 * c, 4 * c + 4):
-                tt(T.FL[:, k * 128:k * 128 + 128], T.V0[:, k:33 * B:33], T["ps%d" % r][:, (k % 4) * 128:(k % 4) * 128 + 128], A.is_ge,
-                   ["V0", "rg%d" % r], ["FL%d" % k], ["b%d" % r])
-
-        def count(src, key, sel, dst, bk, c, wk):
-            for k in range(16):
-                mm(dst[:, c * 64:c * 64 + 64], T[sel][:, k * 128:k * 128 + 128], src[:, c * 1024 + k:(c + 1) * 1024:16], k == 0, k == 15,
-                   ks(key, 8 * c + 8, 8 * c) + [sel + str(k)], [wk + str(c)] if k in (0, 15) else (), [bk])
-
+            affine(v("D1", k + 1, None, 33), ind(v("TT"), v(pl, k * 8, k * 8 + 8)), DL, 4 * min(k, 30) * DL)
+        for c in range(8):
+            affine(v("Gn", c * 512, c * 512 + 512), ind(v("ND"), v(pl, c * 32, c * 32 + 32)), (B2 - B1) * DL, B1 * DL)
+        scan(v("V0"), v("D1"), v("D1"), 0.0, A.mult, A.min)
         for c in range(4):
-            ndps(c)
-        flaw(0)
-        ndps(4)
-        flaw(1)
-        ndps(5)
-        if EARLY:
-            count(T.FL, "FL", "SEL", T.ps4, "b4", 0, "CN")
-        flaw(2)
-        ndps(6)
-        flaw(3)
-        ndps(7)
-        if not EARLY:
-            count(T.FL, "FL", "SEL", T.ps4, "b4", 0, "CN")
-        count(T.FL, "FL", "SEL", T.ps4, "b4", 1, "CN")
-        for c in (4, 5):
-            flaw(c)
-        count(T.FL, "FL", "SEL", T.ps4, "b4", 2, "CN")
-        for c in (6, 7):
-            flaw(c)
-        count(T.FL, "FL", "SEL", T.ps4, "b4", 3, "CN")
-
-        v32 = T.V0[:, 32:33 * B:33]
-        for k, cut in enumerate((0.5, 248.5, -7.5, -11.5)):
-            act(T.pp[:, k * 128:k * 128 + 128], v32, ACT.Sign, ["V0", "sgn"], ["p%d" % (k + 1)], bias=T.SG[:, k:k + 1])
-        cp(T.K2[:, :], pl[:, 0:256], ["plS"], ["Sf"])
-        act(T.t64S[:, :], T.K2[:, :], ACT.Copy, ["Sf"], ["t64S"], scale=64.0)
-        tt(T.ps6[:, 0:256], T.K2[:, :], T.ps5[:, 128:384], A.add, ["Sf", "K1c"], ["K1"], ["b6", "b5"])
-        for k in range(5):
-            mm(T.ps5[:, 384:512], T.IS[:, (k % 4) * 128:(k % 4) * 128 + 128] if k < 4 else T.ID[:, :], T.pp[:, k * 128:k * 128 + 128] if k < 4 else T.FOUR[:, :],
-               k == 0, k == 4, ["IS%d" % (k % 4), "ID", "FOUR", "p%d" % (k % 4 + 1)], ["SP"] if k in (0, 4) else (), ["b5"])
-        cp(T.vi[:, :], v32, ["V0"], ["vi"])
-        ts(T.e2[:, :], T.vi[:, :], 3, A.bitwise_and, R=["vi"], Wr=["e2"])
-
-        ts(T.o1[:, :], T.ps4[:, 0:256], T.thr[:, :], A.is_ge, R=ks("CN", 4) + ["thr"], Wr=["o1"], P=["b4"])
-        tt(T.prod1[:, :], T.o1[:, :], T.ps6[:, 0:256], A.mult, ["o1", "K1"], ["prod1"], ["b6"])
-        gred(T.M8i, T.prod1, A.max, ["prod1"], "M8")
-        ts(T.xr[:, :], T.M8i[:, :], 13, A.arith_shift_right, R=ks("M8", 8), Wr=["xr"])
-        ts(T.sx[:, :], T.M8i[:, :], 4095, A.bitwise_and, R=ks("M8", 8), Wr=["sx"])
-        ts(T.xm[:, :], T.M8i[:, :], 6, A.arith_shift_right, 0x7FF80, A.bitwise_and, ks("M8", 8), ["xm"])
-        tt(T.oi[:, 0:8], T.Cv[:, :], T.xr[:, :], A.subtract, ["Cv", "xr"], ["oi0"])
-        tt(T.oi[:, 8:16], T.Cn[:, :], T.xm[:, :], A.subtract, ["Cn", "xm"], ["oi1"])
-        cp(T.ou[:, :], T.oi[:, :], ["oi0", "oi1"], ["ou"])
-        GNK = ks("Gn", 8) + ["Gnx"]
-        act(T.vx[:, :], T.V0[:, :].indirect(T.ou[:, 0:8]), ACT.Copy, ["V0", "ou"], ["vx"])
-        ts(T.t12[:, :], T.V0[:, :].indirect(T.ou[:, 0:8]), 0.0, A.is_ge, 12.0, A.mult, ["V0", "ou"], ["t12"])
-        tt(T.y[:, :], T.Gn[:, :].indirect(T.ou[:, 8:16]), T.vx[:, :], A.subtract, GNK + ["ou", "vx"], ["y"])
-        mm(T.ps7[:, 0:128], T.y[:, :], T.ID[:, :], True, True, ["y", "ID"], ["DT"], ["b7"])
-        tt(T.W4[:, 0:128], T.Gn[:, :].indirect(T.ou[:, 8:16]), T.t12[:, :], A.max, GNK + ["ou", "t12"], ["W4a"])
-        op("v", lambda e: e.tensor_tensor_scan(T.RM[:, :], T.SC0[:, :], T.ps7[:, 0:128], 0.0, A.max, A.min), ["SC0z", "DT"], ["RM"], ["b7"])
-        ts(T.xf[:, :], T.xr[:, :], -1.0, A.mult, 32.0, A.add, ["xr"], ["xf"])
-        for h in range(8):
-            out, col = T.LT[:, h * 16:h * 16 + 16], T.RM[:, h * 16 + 15:h * 16 + 16]
-            if h < 5:
-                ts(out, T.MK16[:, 0:16], col, A.mult, R=["MK16", "RM"], Wr=["LT%d" % h])
-            else:
-                act(out, T.MK16[:, 0:16], ACT.Identity, ["MK16", "RM"], ["LT%d" % h], scale=col)
-        mm(T.ps7[:, 256:264], T.LT[:, :], T.G8[:, :], True, True, ks("LT", 8) + ["G8"], ["D8"], ["b7"])
-        for k in range(4):
-            mm(T.ps0[:, k * 128:k * 128 + 128], T.ID[:, :], T.W4[:, 0:128], True, True, ["ID", "W4a"], ["rg0"], ["b0"])
-        ts(T.ncd[:, :], T.xr[:, :], -8192.0, A.mult, 262144.0, A.add, ["xr"], ["xs"])
-        ts(T.di[:, :], T.ps7[:, 256:264], -2048.0, A.mult, -16384.0, A.add, ["D8"], ["di"], ["b7"])
-        ts(T.dg[:, :], T.di[:, :], 63 << 13, A.bitwise_and, R=["di"], Wr=["dg"])
-        tt(T.d8[:, :], T.dg[:, :], T.ncd[:, :], A.min, ["dg", "xs"], ["d8"])
-        cp(T.sxf[:, :], T.sx[:, :], ["sx"], ["sxf"])
-        for h in range(8):
-            ts(T.prod1[:, h:256:8], T.ps6[:, h:256:8], -262144.0, A.add, T.d8[:, h:h + 1], A.add, ["K1", "d8"], ["df%d" % h], ["b6"])
-        for h in range(8):
-            op("v", lambda e, h=h: e.tensor_reduce(T.sd[:, h:h + 1], T.prod1[:, h:256:8], AX, A.min, apply_absolute_value=True), ["df%d" % h], ["sd%d" % h])
-        SD = ks("sd", 8)
-        for k in range(2):
-            act(T.base24[:, k * 8:k * 8 + 8], T.xf[:, :], ACT.Copy, ["xf"], ["ba%d" % k])
-        act(T.c16[:, 8:16], T.xf[:, :], ACT.Copy, ["xf"], ["c161"])
-        act(T.m24[:, 0:8], T.xf[:, :], ACT.Copy, ["xf"], ["m240"], scale=-1.0, bias=99.0)
-        act(T.Mb[:, :], T.W4[:, 0:128], ACT.Relu, ["W4a", "sgn"], ["Mb"], scale=-1.0, bias=T.SG[:, 4:5])
-        for k in range(1, 4):
-            act(T.W4[:, k * 128:k * 128 + 128], T.W4[:, 0:128], ACT.Copy, ["W4a"], ["W4%d" % k])
-        tt(T.pr0[:, :], T.sx[:, :], T.sd[:, :], A.mult, ["sx"] + SD, ["pr0"])
-        ts(T.bs[:, :], T.pr0[:, :], 5, A.arith_shift_right, R=["pr0"], Wr=["bs"])
-        ts(T.bsf[:, :], T.bs[:, :], 97.0 * t, A.add, R=["bs"], Wr=["bsf"])
-        for h in range(8):
-            ts(T.craw[:, h:256:8], T.KAP[:, :], T.sxf[:, h:h + 1], A.mult, T.bsf[:, h:h + 1], A.add, ["KAP", "sxf", "bsf"], ["craw%d" % h])
-        ts(T.cm[:, :], T.craw[:, :], 4095, A.bitwise_and, R=ks("craw", 8), Wr=["cm"])
-        cp(T.cu[:, :], T.cm[:, :], ["cm"], ["cu"])
-
-        for c in range(NSC):
-            act(T.EC[:, c * 512:c * 512 + 512], T.E[:, :].indirect(T.cu[:, c * 32:c * 32 + 32]), ACT.Copy, EK + ["cu"], ["EC%d" % c])
-
-        def vfuse(c):
-            tt(T.FL[:, c * 512:c * 512 + 512], T.E[:, :].indirect(T.cu[:, c * 32:c * 32 + 32]), T.W4[:, :], A.is_ge,
-               EK + ["cu", "W4a"] + ks("W4", 4, 1), ks("FL", 4 * c + 4, 4 * c))
-
-        def hit(c):
-            tt(T.FL[:, c * 512:c * 512 + 512], T.EC[:, c * 512:c * 512 + 512], T.ps0[:, :], A.is_ge, ["EC%d" % c, "rg0"], ks("FL", 4 * c + 4, 4 * c), ["b0"])
-
-        def score(c):
-            count(T.FL, "FL", "SEL2", T.ps4, "b4", c, "CN")
-
-        vfuse(7)
-        tt(T.sv[:, :], T.e2[:, :], T.ps5[:, 384:512], A.add, ["e2", "SP"], ["sv"], ["b5"])
-        hit(0)
-        for k in range(16):
-            mm(T.ps7[:, 272:280], T.SEL[:, k * 128:k * 128 + 128], T.sv[:, k:128:16], k == 0, k == 15, ["sv", "SEL%d" % k], ["U8"] if k in (0, 15) else (), ["b7"])
-        for k in range(16):
-            mm(T.ps5[:, 0:8], T.SEL[:, k * 128:k * 128 + 128], T.Mb[:, k:128:16], k == 0, k == 15, ["Mb", "SEL%d" % k], ["NM"] if k in (0, 15) else (), ["b5"])
-        if not last:
-            so = T["so%d" % t]
-            ts(T.sq[:, :], T.sv[:, :], 8.0, A.is_ge, -264.0, A.mult, ["sv"], ["sq"])
-            tt(so[:, :], T.sv[:, :], T.sq[:, :], A.add, ["sv", "sq"], ["so"])
-            dst = T.cores[(rank + STATE_GO) % N]
-            n = len(topo.engines(core, dst))
-            send(remote(T["sc%d" % (t + 1)][:, :], so[:, :], "as%d" % (t + 1), "ls%d" % (t + 1), dst), ["so"], "ls%d" % (t + 1), n)
-        hit(1)
-        score(0)
-        if NSC == 6:
-            vfuse(6)
-            score(3)
-        tt(T.K2[:, :], T.cm[:, :], T.ps6[:, 256:512], A.add, ["K2c", "cm"], ["K2"], ["b6"])
-        hit(2)
-        if t == 0:
-            fill(T.base24[:, 16:24], 0.0, "ba2")
-        tt(T.aqt[:, :], T.d8[:, :], T.ncd[:, :], A.subtract, ["d8", "xs"], ["dxs"])
-        ts(T.m24[:, 8:16], T.aqt[:, :], 1.0 / 8192, A.mult, R=["dxs"], Wr=["m241"])
-        ts(T.cm64[:, :], T.cm[:, :], 64.0, A.mult, -16777216.0, A.add, ["cm"], ["cm64"])
-        ts(T.m24[:, 16:24], T.sd[:, :], 64.0, A.mult, 128.0, A.add, SD, ["m242"])
-        ts(T.fnd[:, :], T.xr[:, :], 1.0, A.is_ge, 131072.0, A.mult, ["xr"], ["fnd"])
-        tt(T.barM[:, :], T.barf[:, :], T.ps5[:, 0:8], A.add, ["barf", "NM"], ["barM"], ["b5"])
-        hit(3)
-        score(1)
-        for k in range(3):
-            tt(T.bar24[:, k * 8:k * 8 + 8], T.barM[:, :], T.fnd[:, :], A.mult, ["barM", "fnd"], ["br%d" % k])
-        hit(4)
-        cp(T.ui[:, :], T.ps7[:, 272:280], ["U8"], ["ui"], ["b7"])
-        ts(T.ua[:, :], T.ui[:, :], 31, A.bitwise_and, R=["ui"], Wr=["ua"])
-        tt(T.uo[:, :], T.ua[:, :], T.C32[:, :], A.add, ["ua", "C32"], ["uo"])
-        cp(T.uu[:, :], T.uo[:, :], ["uo"], ["uu"])
-        hit(5)
-        score(2)
-        ts(T.t64[:, :], pl[:, 256:512], 64.0, A.mult, R=["plQ"], Wr=["t64Q"])
-        if NSC == 7:
-            hit(6)
-            score(3)
-        tt(T.es[:, :], T.E[:, :].indirect(T.uu[:, :]), T.sv[:, :], A.add, EK + ["uu", "sv"], ["es"])
-        ts(T.en[:, :], T.es[:, :], 1, A.arith_shift_right, R=["es"], Wr=["en"])
-        cp(T.eb[:, :], T.en[:, :], ["en"], ["eb"])
-        op("v", lambda e: e.tensor_copy(T.E[:, :].indirect(T.uu[:, :]), T.eb[:, :]), ["eb", "uu"], EK)
+            for k in range(8 * c, 8 * c + 8):
+                scan(v("FL", k * 128, k * 128 + 128), v("V0", k, None, 33), v("Gn", k * 128, k * 128 + 128), 1.0, A.min, A.add)
+            cn = v("ps%d" % (c % 2), c * 64, c * 64 + 64)
+            rows(cn, "SEL", "FL", c * 1024, 1024, [(ONE, v("THR"))])
+            affine(v("hi", c * 64, c * 64 + 64), cn, 1.0)
+            tt(v("d0", c * 64, c * 64 + 64), cn, v("hi", c * 64, c * 64 + 64), A.subtract)
         if last:
-            op("y", lambda e: e.dma_start(T.ye[:, :], T.E[:, :]), EK, ["ye"], (), "ds0", 16)
+            rec({"y": lambda e: e.dma_start(T.E2[:, :], T.E[:, :])}, v("E2"), [v("E"), v(pl)], "dma", "ds3", 16, 6.0)
 
-        tt(T.key2[:, :], T.K2[:, :], T.ps4[:, 0:256], A.add, ["K2"] + ks("CN", 4), ["key2"], ["b4"])
-        gred(T.MBi, T.key2, A.max, ["key2"], "MBi")
-        MB = ks("MBi", 8)
-        for k in range(3):
-            tt(T.ret24[:, k * 8:k * 8 + 8], T.MBi[:, :], T.bar24[:, k * 8:k * 8 + 8], A.is_lt, MB + ["br%d" % k], ["ret%d" % k])
-        tt(T.pr24[:, :], T.ret24[:, :], T.m24[:, :], A.mult, ks("ret", 3) + ks("m24", 3), ["pr24"])
-        ts(T.cb[:, :], T.MBi[:, :], 4095, A.bitwise_and, R=MB, Wr=["cb"])
-        ts(T.cbx[:, :], T.cb[:, :], 64.0, A.mult, -16777216.0, A.add, ["cb"], ["cbx"])
-        ts(T.nr[:, :], T.ret24[:, 0:8], -1.0, A.mult, 1.0, A.add, ["ret0"], ["nr"])
-        tt(T.a24[:, :], T.base24[:, :], T.pr24[:, :], A.add, ["pr24"] + ks("ba", 3), ["a24"])
         for h in range(8):
-            ts(T.ps0[:, h:256:8], T.kc[:, :], T.a24[:, h:h + 1], A.min, T.a24[:, 8 + h:9 + h], A.not_equal, ["kc", "a24"], ["e1%d" % h], ["b0"])
-            ts(T.o1[:, h:256:8], T.t64[:, h:256:8], T.a24[:, 16 + h:17 + h], A.not_equal, R=["t64Q", "a24"], Wr=["e2p%d" % h])
-        tt(T.kept[:, :], T.o1[:, :], T.ps0[:, 0:256], A.min, ks("e1", 8) + ks("e2p", 8), ["kept"], ["b0"])
+            scan(lanes(KW, h), v("d0", 248 + h, None, -8), v(KW, 504 + h, 255, -8), (256.0 + h) * 4096, A.min, A.max)
+        r = v(KW, 248, 256)
+        ts(v("qq"), r, 12, A.arith_shift_right)
+        ts(v("xr"), r, 15, A.arith_shift_right)
+        ts(v("sx"), r, 4095, A.bitwise_and)
+        ts(v("ou", 8, 16), v("qq"), 16.0, A.mult, v("lc"), A.add)
+        tt(v("oi"), v("xr"), v("Cv"), A.add)
+        cp(v("ou", 0, 8), v("oi"))
+        affine(v("vx"), ind(v("V0"), v("ou", 0, 8)), 1 / DL, 1022.5, "v")
+        act(v("wm"), ind(v("FL"), v("ou", 8, 16)), ACT.Abs, slope, col("SG", 3))
+
+        DT, D8 = v("ps2", 0, 128), v("ps2", 128, 136)
+        mms(DT, [(v("CW"), IS(3)), (v("wm"), IS(3)), (v("vx"), ID)])
+        scan(v("RM"), v("SCM"), DT, 0.0, A.min, A.max)
+        for h in range(8):
+            affine(v("LT", h * 16, h * 16 + 16), v("MK16", 0, 16), col("RM", h * 16 + 15))
+        mms(D8, [(ONE, v("HR")), (v("LT"), v("G82"))])
+        cp(v("ou", 16, 24), D8)
+        tt(v("kd"), ind(v(KW, 248, 512), v("ou", 16, 24)), v("DM"), A.mult)
+        scan(v("rd"), v("SCZ"), v("kd"), 0.0, A.mult, A.add)
+        rd = v("rd", 15, None, 16)
+        ts(v("sd"), rd, 4095, A.bitwise_and)
+        ts(v("dq"), rd, 15, A.arith_shift_right)
+        cp(v("sxf"), v("sx"))
+        for k in range(4):
+            act(v("W4", k * 128, k * 128 + 128), v("wm"), ACT.Identity, None, C0 + 0.5)
+
+        tt(v("pr0"), v("sx"), v("sd"), A.mult)
+        ts(v("bs"), v("pr0"), 5, A.arith_shift_right)
+        ts(v("bsf"), v("bs"), 97.0 * t, A.add)
+        for h in range(8):
+            ts(lanes("craw", h), v("KAP"), col("sxf", h), A.mult, col("bsf", h), A.add)
+        for a in (0, 128):
+            ts(v("cm", a, a + 128), v("craw", a, a + 128), 4095, A.bitwise_and)
+            cp(v("cu", a, a + 128), v("cm", a, a + 128))
+        ts(v("cmZ"), v("cm"), -2.0 ** 23, A.add)
+        fused = (1, 4, 6, 7)[:NFUSE]
+        for c in range(8):
+            a, src = c * 512, ind(v("E"), v("cu", c * 32, c * 32 + 32))
+            if c in fused:
+                tt(v("FL", a, a + 512), src, v("W4"), A.add)
+            else:
+                affine(v("EC", a, a + 512), src, 1.0, C0 + 0.5, "s")
+                for k in range(a, a + 512, 128):
+                    scan(v("FL", k, k + 128), v("EC", k, k + 128), v("wm"), 4000.0, A.min, A.add)
+            if c % 2:
+                x = (c // 2) * 64
+                cn = v("ps%d" % (c // 2 % 2), 256 + x, 320 + x)
+                rows(cn, "SEL2", "FL", a - 512, 1024, [(ONE, v("CS")), (ID, v("K2c", x, x + 64))])
+                tt(v("key", x, x + 64), v("cmZ", x, x + 64), cn, A.add)
+
+        act(v("r4"), V32, ACT.Identity, 1 / DL, 1022.5)
+        act(v("sgn"), V32, ACT.Sign, 1 / DL, col("SG", 1))
+        mms(v("ps3", 0, 128), [(IS(4), V32), (IS(5), X0)])
+        mms(v("ps3", 128, 256), [(ID, s0), (IS(6), X0)])
+        act(v("az"), v("ps3", 0, 128), ACT.Abs, None, col("SG", 4))
+        act(v("w8"), v("ps3", 128, 256), ACT.Identity, None, -32.0)
+        act(v("iseq"), v("az"), ACT.Relu, -1.0, col("SG", 2))
+        scan(v("prw"), v("iseq"), v("w8"), 0.0, A.max, A.mult)
+        mms(v("ps3", 256, 384), [(IS(4), V32), (IS(0), v("r4")), (IS(1), v("sgn")), (IS(2), v("iseq")), (ID, v("prw"))])
+        act(sv, v("ps3", 256, 384), ACT.Identity, None, 1030.0)
         if not last:
-            cp(T.retb[:, :], T.ret24[:, 0:8], ["ret0"], ["retb"])
-            mm(T.ps7[:, 280:288], T.ONE[:, :], T.retb[:, :], True, True, ["ONE", "retb"], ["RS"], ["b7"])
-        for h in range(8):
-            op("v", lambda e, h=h: e.tensor_tensor_scan(T.ps1[:, h:256:8], T.ONES32[:, :], T.kept[:, h:256:8], 1.0, A.add, A.subtract),
-               ["ONES32", "kept"], ["sp%d" % h], ["b1"])
-        tt(T.ps1[:, 256:512], T.kept[:, :], T.ps1[:, 0:256], A.mult, ["kept"] + ks("sp", 8), ["shk"], ["b1"])
-        op("v", lambda e: e.memset(T.ZS[:, 0:8], 0), (), ["ZS0"])
-        op("v", lambda e: e.memset(T.ZQ[:, 0:8], 0), (), ["ZQ0"])
-        tt(T.ps0[:, 256:512], T.K19[:, :], T.ps1[:, 256:512], A.add, ["K19", "shk"], ["ksh"], ["b0", "b1"])
-        tt(T.key2[:, :], T.K18[:, :], T.ps1[:, 256:512], A.add, ["K18", "shk"], ["kss"], ["b1"])
-        tt(T.ZS[:, 8:264], T.t64S[:, :], T.key2[:, :], A.add, ["t64S", "kss"], ["ZS"])
-        tt(T.ZQ[:, 8:264], T.t64[:, :], T.ps0[:, 256:512], A.add, ["t64Q", "ksh"], ["ZQ"], ["b0"])
-        for k in range(2):
-            ts(T.n16[:, k * 8:k * 8 + 8], T.ps1[:, 248:256], -1.0, A.mult, 33.0, A.add, ks("sp", 8), ["n16%d" % k], ["b1"])
-        if t == 0:
-            fill(T.c16[:, 0:8], 99.0, "c160")
-        ts(T.aqt[:, :], T.sd[:, :], 1.0, A.add, R=SD, Wr=["aqt"])
-        tt(T.d16[:, :], T.n16[:, :], T.c16[:, :], A.subtract, ["n160", "n161", "c160", "c161"], ["d16"])
-        tt(T.cbr[:, :], T.cbx[:, :], T.nr[:, :], A.mult, ["cbx", "nr"], ["cbr"])
-        tt(T.aq[:, :], T.aqt[:, :], T.nr[:, :], A.mult, ["aqt", "nr"], ["aq0"])
-        tt(T.r16[:, :], T.d16[:, :], T.ret24[:, 0:16], A.mult, ["d16", "ret0", "ret1"], ["r16"])
-        ts(T.aq[:, :], T.aq[:, :], 1.0, A.add, R=["aq0"], Wr=["aq"])
-        tt(T.f16[:, :], T.r16[:, :], T.c16[:, :], A.add, ["r16", "c160", "c161"], ["f16"])
-        for h in range(8):
-            act(T.K2[:, h:256:8], T.cm64[:, h:256:8], ACT.Identity, ["cm64", "ret0", "cbr"], ["al%d" % h], scale=T.ret24[:, h:h + 1], bias=T.cbr[:, h:h + 1])
-        for h in range(8):
-            ts(T.ps0[:, h:256:8], T.kc[:, :], T.f16[:, h:h + 1], A.min, T.f16[:, 8 + h:9 + h], A.is_equal, ["kc", "f16"], ["Fp%d" % h], ["b0"])
-        tt(T.ps1[:, 0:256], T.K2[:, :], T.ps0[:, 0:256], A.mult, ks("al", 8) + ks("Fp", 8), ["alY"], ["b0", "b1"])
-        for b in range(6):
-            s = 1 << b
-            m = (33 - s) * 8
-            z = ["ZS", "ZS0"]
-            q = ["ZQ", "ZQ0"]
-            tb = T.tb[:, b * 264:b * 264 + m]
-            ts(tb, T.ZS[:, 8 * s:264], b, A.arith_shift_right, 1, A.bitwise_and, z, ["tb%d" % b])
-            scan(T.ps2[:, 0:m], tb, T.ZS[:, 8 * s:264], A.max, A.mult, ["tb%d" % b] + z, ["mvS"], ["b2"])
-            scan(T.ps3[:, 0:m], tb, T.ZQ[:, 8 * s:264], A.max, A.mult, ["tb%d" % b] + q, ["mvQ"], ["b3"])
-            tt(T.ZS[:, 0:m], T.ZS[:, 0:m], T.ps2[:, 0:m], A.min, z + ["mvS"], z, ["b2"])
-            tt(T.ZQ[:, 0:m], T.ZQ[:, 0:m], T.ps3[:, 0:m], A.min, q + ["mvQ"], q, ["b3"])
-        tt(T.ZS[:, 0:256], T.ZS[:, 0:256], T.ps1[:, 0:256], A.min, z + ["alY"], z, ["b1"])
-        ts(T.nS[:, :], T.ZS[:, 0:256], 6, A.arith_shift_right, 4095, A.bitwise_and, ["ZS", "ZS0"], ["nS"])
-
-        def reasons():
-            ts(T.nQ[:, :], T.ZQ[:, 0:256], 6, A.arith_shift_right, 8191, A.bitwise_and, ["ZQ", "ZQ0"], ["nQ"])
-            for h in range(8):
-                ts(T.prod1[:, h:256:8], T.nQ[:, h:256:8], -1.0, A.mult, T.aq[:, h:h + 1], A.add, ["nQ", "aq"], ["dfQ%d" % h])
-            tt(T.ps3[:, 0:256], T.prod1[:, :], T.ps0[:, 0:256], A.mult, ks("dfQ", 8) + ks("Fp", 8), ["mvQ"], ["b3", "b0"])
-
-        if not last:
-            po = T["plo%d" % t]
-            dst = T.cores[(rank + PLAN_GO) % N]
-            n = len(topo.engines(core, dst))
-
-            def go(half, s):
-                x = slice(half * 256, half * 256 + 256)
-                cp(po[:, x], (T.nS, T.nQ)[half][:, :], [("nS", "nQ")[half]], ["po%d" % half])
-                send(remote(T["pl%d" % (t + 1)][:, x], po[:, x], "a%s%d" % (s, t + 1), "l%s%d" % (s, t + 1), dst), ["po%d" % half],
-                     "l%s%d" % (s, t + 1), n)
-
-            go(0, "p")
-            ts(T.pp[:, 0:128], T.eb[:, :], 4.0, A.is_ge, -520.0, A.mult, ["eb"], ["p1"])
-            ts(T.pp[:, 128:256], T.eb[:, :], 12.0, A.is_ge, 252.0, A.mult, ["eb"], ["p2"])
-            tt(T.pp[:, 256:384], T.pp[:, 0:128], T.pp[:, 128:256], A.add, ["p1", "p2"], ["p3"])
-            tt(T.TT[:, :].indirect(T.uu[:, :]), T.eb[:, :], T.pp[:, 256:384], A.add, ["eb", "p3", "uu"], TK)
-            reasons()
-            tt(T.nQ[:, :], T.nQ[:, :], T.ps3[:, 0:256], A.add, ["nQ", "mvQ"], ["nQ"], ["b3"])
-            go(1, "q")
+            send("s%d" % (t + 1), v("sc%d" % (t + 1)), sv, STATE_GO, 2.0)
+        rows(v("ps3", 384, 392), "SEL", "so%d" % t, 0, 128, [])
+        ts(v("ui"), v("ps3", 384, 392), 2.0 ** -32, A.mult)
+        ts(v("ua"), v("ui"), 31, A.bitwise_and)
+        tt(v("uo"), v("ua"), v("C32"), A.add)
+        cp(v("uu"), v("uo"))
+        tt(v("es"), ind(v("E"), v("uu")), sv, A.add)
+        act(v("eb"), v("es"), ACT.Identity, 0.5, 129.75)
+        tt(ind(v("E2" if last else "E"), v("uu")), v("eb"), v("M130"), A.add)
+        if last:
+            store("y", 0, T.ye[:, :], v("E2"))
         else:
-            cp(T.ysw[:, 0:256], T.nS[:, :], ["nS"], ["ysw0"])
-            op("y", lambda e: e.dma_start(T.ys[:, :], T.ysw[:, 0:256]), ["ysw0"], ["ys"], (), "ds1", 16)
-            reasons()
-            tt(T.K2[:, :], T.nQ[:, :], T.ps3[:, 0:256], A.add, ["nQ", "mvQ"], ["dfS"], ["b3"])
-            ts(T.ysw[:, 256:512], T.K2[:, :], 2.0, A.subtract, R=["dfS"], Wr=["ysw1"])
-            op("s", lambda e: e.dma_start(T.yw[:, :], T.ysw[:, 256:512]), ["ysw1"], ["yw"], (), "ds2", 16)
-    order, deps = _schedule(prog)
+            classes(v("eu"), v("ew"), v("ef"), v("eb"), 130)
+            act(v("ea"), v("eb"), ACT.Identity, None, -382.0)
+            tt(ind(v("TT"), v("uu")), v("ea"), v("ef"), A.add)
+
+        ts(v("fnd"), v("xr"), 32.0, A.is_lt, 2.0 ** 17, A.mult)
+        tt(v("barK"), v("barf"), v("fnd"), A.mult)
+        ts(v("dp1"), v("dq"), 1.0, A.add, -1.0, A.mult)
+        ts(v("sd2"), v("sd"), 2.0, A.add)
+        ts(v("sdZ"), v("sd"), -2047.0, A.add, 4096.0, A.mult)
+        ts(v("x64"), v("xr"), 64.0, A.mult)
+        ts(v("c33x"), v("xr"), -1.0, A.mult, 33.0, A.add)
+        fill(v("ps5", 0, 8), 0.0)
+        for h in range(8):
+            red(col("MBi", h), lanes("key", h), A.max)
+        tt(v("ret"), v("MBi"), v("barK"), A.is_lt)
+        tt(v("nr"), v("MBi"), v("barK"), A.is_ge)
+        tt(v("A1"), v("ret"), v("dp1"), A.mult)
+        tt(v("A2"), v("ret"), v("sd2"), A.mult)
+        affine(v("A3"), v("ret"), 6400.0)
+        tt(v("xb"), v("A3"), v("x64"), A.add)
+        for h in range(8):
+            act(lanes("ps2", h), v("kc1"), ACT.Abs, None, col("A1", h))
+            ts(lanes("e2p", h), lanes(KW, h, 512), 2049.0, A.add, col("A2", h), A.not_equal)
+        kept = v("ps4", 0, 256)
+        tt(kept, v("e2p"), v("ps2", 0, 256), A.min)
+        for h in range(8):
+            scan(lanes("sp", h), v("ONES32"), lanes("ps4", h), 1.0, A.add, A.subtract)
+            act(lanes("ps7", h), v("kc"), ACT.Relu, -64.0, col("xb", h))
+        tt(v("Dz"), v("sp"), v("ps7", 0, 256), A.min)
+        tt(v("ps5", 8, 264), v(KW, 768, 1024), kept, A.mult)
+        ts(v("cb"), v("MBi"), 4095, A.bitwise_and)
+        tt(v("v1"), v("cb"), v("sdZ"), A.add)
+        tt(v("v2"), v("v1"), v("nr"), A.mult)
+        for h in range(8):
+            act(lanes("al", h), lanes("cmZ", h), ACT.Identity, col("ret", h), col("v2", h))
+        tt(v("nx"), v("c33x"), v("sp", 248, 256), A.subtract)
+        tt(v("rn"), v("nx"), v("ret"), A.mult)
+        tt(v("f1"), v("rn"), v("xr"), A.add)
+        affine(v("nr99"), v("nr"), 99.0)
+        tt(v("f0"), v("f1"), v("nr99"), A.add)
+        for h in range(8):
+            ts(lanes("ps4", h, 256), v("kc"), col("f0", h), A.min, col("f1", h), A.is_equal)
+        tt(v("alY"), v("al"), v("ps4", 256, 512), A.mult)
+        for b in range(6):
+            s = 8 << b
+            m = 264 - s
+            tb = v("tb", b * 256, b * 256 + m)
+            ts(tb, v("Dz", s - 8, 256), b, A.arith_shift_right, 1, A.bitwise_and)
+            tt(v("tm", 0, m), tb, v("ps5", s, 264), A.mult)
+            tt(v("ps5", s, 264), v("ps5", s, 264), v("tm", 0, m), A.subtract)
+            tt(v("ps5", 0, m), v("ps5", 0, m), v("tm", 0, m), A.add)
+        Z = v(ZO, 512, 768)
+        tt(Z, v("alY"), v("ps5", 0, 256), A.add)
+        ts(v("nS"), Z, 4095, A.bitwise_and)
+        if not last:
+            cp(v("plo%d" % t), v("nS"))
+            send("p%d" % (t + 1), v("pl%d" % (t + 1)), v("plo%d" % t), PLAN_GO, 2.0)
+            tt(v(ZO, 0, 256), v("nS"), v("ps6", 0, 256), A.add)
+            ts(v(ZO, 256, 512), Z, 12, A.arith_shift_right)
+            send("q%d" % (t + 1), v("KW%d" % (t + 1), 256, 1024), v(ZO), PLAN_GO, 4.0)
+            cp(v("retb"), v("ret"))
+            mms(col("ps3", 392), [(ONE, col("retb", h)) for h in range(8)])
+            cp(col("ri", 0), col("ps3", 392))
+            ts(col("ri", 1), col("ri", 0), 1, A.bitwise_and)
+            ts(v("thr"), col("ri", 1), 1.5, A.add, 2.0 ** 16, A.mult)
+            affine(v("THR", 0, 64, 1, 64), v("ONE", 0, 64, 1, 64), col("thr", 0, 64))
+        else:
+            cp(v("ysw", 0, 256), v("nS"))
+            store("y", 1, T.ys[:, :], v("ysw", 0, 256))
+            ts(v(ZO, 256, 512), Z, 12, A.arith_shift_right)
+            ts(v("ysw", 256, 512), v(ZO, 256, 512), 2047.0, A.add)
+            store("s", 2, T.yw[:, :], v("ysw", 256, 512))
+
+    if not PLANNED:
+        PLANNED["plan"] = _schedule(prog)
+    order, queue, deps = PLANNED["plan"]
     tok = {}
     for i in order:
-        kind, q, fn, R, Wr, P, sem, inc = prog[i]
-        toks = [tok[j] for j in sorted(deps[i]) if not (q == "t" and prog[j][1] == "t")]
-        if kind == "op":
-            tok[i] = op_now(q, fn, toks, P, sem, inc)
-        elif kind == "send":
-            tok[i] = send_now(fn, toks, inc[0], inc[1])
+        e, q = prog[i], queue[i]
+        toks = [tok[j] for j in sorted(deps[i]) if not (q == "t" and queue[j] == "t")]
+        if e["kind"] == "op":
+            tok[i] = op_now(q, e["fn"][q], toks, e["P"], e["sem"], e["inc"])
+        elif e["kind"] == "send":
+            tok[i] = send_now(e["fn"], toks, e["sem"], e["inc"])
         else:
-            tok[i] = lands_now(inc[0], inc[1])
+            tok[i] = lands_now(e["sem"], e["inc"])
     finish()

@@ -8,14 +8,12 @@ PLAN_GO, STATE_GO = 3, 1
 H, F, I, U = "bfloat16", "float32", "int32", "uint16"
 
 SCRATCH = {}
+PART = {}
 
 
 def _buf(dtype, n, *names):
     for x in names:
         SCRATCH[x] = ("sbuf", [128, n], dtype)
-
-
-PART = {}
 
 
 def _pool(name, dtype, n, *names):
@@ -32,14 +30,15 @@ _buf(H, 128, "ID", "ONE", "MK16", "SCM", "SCZ", "DM", "LT", "vx", "wm", "CW", "M
 _buf(H, 7 * 128, "IS")
 _buf(H, 8, "G8", "G82", "HR", "retb")
 _buf(H, 32, "ONES32")
-_buf(H, 64, "THR", "CS")
-_buf(H, 256, "K2c", "hi", "e2p")
+_buf(H, 64, "THR")
+_buf(H, 256, "K2c", "hi", "e2p", "kept", "sg1", "far")
 _buf(F, 128, "RM", "kd")
 _buf(F, 512, "W4", "ysw")
-_buf(F, 256, "d0", "cmZ", "key", "sp", "al", "alY", "tm", "Kf")
+_buf(F, 256, "d0", "cmZ", "key", "Dc", "al", "Kf", "KQf")
+_buf(F, 264, "sp")
 _buf(F, 32, "kc", "kc1", "KAP")
-_pool("lf", F, 8, "Cv", "C32", "SG", "sxf", "bsf", "barf", "barK", "fnd", "ret", "nr", "A1", "A2", "A3", "xb", "x64", "dp1", "sd2", "sdZ", "c33x",
-      "nx", "rn", "f0", "f1", "nr99", "v1", "v2")
+_pool("lf", F, 8, "Cv", "C32", "SG", "sxf", "bsf", "barf", "barK", "fnd", "ret", "nr", "mul", "dp1", "sd1", "xn", "xh", "x40", "n40",
+      "mid", "rad", "vq", "v1", "v2", "v3", "v4", "v5")
 _buf(F, 1, "thr", "lc")
 _buf(I, 2, "ri")
 _buf(I, 6 * 256, "tb")
@@ -47,8 +46,8 @@ _buf(I, 256, "craw", "cm", "Dz", "nS", "wi")
 _buf(I, 128, "rd")
 _buf(I, 8, "bari")
 _pool("li", I, 8, "pi", "pb", "qq", "xr", "sx", "oi", "sd", "dq", "pr0", "bs", "MBi", "cb", "ui", "ua", "uo")
-_buf(I, 1024, "KW0", "KW1", "KW2")
-_buf(I, 768, "ZO0", "ZO1", "ZO2")
+_buf(I, 1032, "KW0", "KW1", "KW2")
+_buf(I, 776, "ZO0", "ZO1", "ZO2")
 _buf(U, 256, "pl0", "pl1", "pl2", "plo0", "plo1", "cu")
 _buf(U, 24, "ou")
 _buf(U, 8, "uu")
@@ -57,11 +56,12 @@ for _b in range(8):
 
 DMAS = ["ld%d" % k for k in range(12)] + ["ds%d" % k for k in range(4)]
 SEMAPHORES = ["qv", "qs", "qt", "qg"] + DMAS + ["ap1", "ap2", "aq1", "aq2", "as1", "as2", "lp1", "lp2", "lq1", "lq2", "ls1", "ls2"]
-NFUSE = 3
+FUSED = (1, 3, 5)
 DL = 2.0 ** -18
 B1, B2 = 49152, 98304
 WM, C0 = 760, 1304
 CYC, GATHER, SCATTER, WAKE = 0.83e-3, 1.56, 3.8, 0.1
+AHEAD, PASSES = (2.0,), 4
 SIZE = {H: 2, F: 4, I: 4, U: 2}
 
 
@@ -144,40 +144,57 @@ def _schedule(prog):
     rank = [0.0] * n
     for i in range(n - 1, -1, -1):
         rank[i] = min(prog[i]["cost"].values()) + prog[i]["lat"] + max([rank[j] + WAKE for j in nxt[i]] + [0.0])
-    left = [len(d) for d in deps]
-    at = [{} for _ in range(n)]
-    ready = set(i for i in range(n) if not left[i])
-    free, bank, queue, order = {}, {}, {}, []
 
-    def start(i, q):
-        s = max([free.get(q, 0.0) if q != "x" else 0.0] + [t + (0.0 if q == q2 == "t" else WAKE) for q2, t in at[i].items()])
-        for b in prog[i]["P"]:
-            s = max([s] + [t + WAKE for q2, t in bank.get(b, {}).items() if q2 != q])
-        return s
+    def one(before, after, rank, back, ahead):
+        left = [len(d) for d in before]
+        at = [{} for _ in range(n)]
+        ready = set(i for i in range(n) if not left[i])
+        free, bank, queue, order, done = {}, {}, {}, [], [0.0] * n
 
-    fifo = {q: [i for i in range(n) if q in prog[i]["cost"]] for q in ("g", "y")}
-    while ready:
-        c = [(start(i, q), i, q) for i in ready for q in prog[i]["cost"] if q not in fifo or fifo[q][0] == i]
-        first = {}
-        for s, i, q in c:
-            first[q] = min(first.get(q, s), s)
-        q = min(first, key=lambda x: first[x])
-        _, i, s = min((-rank[i], i, s) for s, i, q2 in c if q2 == q and s <= first[q] + 0.03)
-        ready.discard(i)
-        if q in fifo:
-            fifo[q].pop(0)
-        end = s + prog[i]["cost"][q]
-        free[q] = end
-        queue[i] = q
-        order.append(i)
-        for b in prog[i]["P"]:
-            bank.setdefault(b, {})[q] = end
-        for j in nxt[i]:
-            at[j][q] = max(at[j].get(q, 0.0), end + prog[i]["lat"])
-            left[j] -= 1
-            if not left[j]:
-                ready.add(j)
-    return order, queue, deps
+        def start(i, q):
+            s = max([0.0] + [t + (0.0 if q == q2 == "t" else WAKE) for q2, t in at[i].items()]) + (prog[i]["lat"] if back else 0.0)
+            s = max(s, free.get(q, 0.0) if q != "x" else 0.0)
+            for b in prog[i]["P"]:
+                s = max([s] + [t + WAKE for q2, t in bank.get(b, {}).items() if q2 != q])
+            return s
+
+        fifo = {q: [i for i in range(n) if q in prog[i]["cost"]][::-1 if back else 1] for q in ("g", "y")}
+        while ready:
+            c = [(start(i, q), i, q) for i in ready for q in ([back[i]] if back else prog[i]["cost"]) if q not in fifo or fifo[q][0] == i]
+            first = {}
+            for s, i, q in c:
+                first[q] = min(first.get(q, s), s)
+            q = min(first, key=lambda x: first[x])
+            _, i, s = min((-rank[i], i, s) for s, i, q2 in c if q2 == q and s <= first[q] + 0.03)
+            for s2, i2, q2 in c:
+                if q2 == q and rank[i2] > rank[i] and s + prog[i]["cost"][q] - s2 > ahead * (s2 - first[q]):
+                    i, s = i2, s2
+            ready.discard(i)
+            if q in fifo:
+                fifo[q].pop(0)
+            end = s + prog[i]["cost"][q]
+            free[q] = end
+            queue[i] = q
+            order.append(i)
+            done[i] = end + (0.0 if back else prog[i]["lat"])
+            for b in prog[i]["P"]:
+                bank.setdefault(b, {})[q] = end
+            for j in after[i]:
+                at[j][q] = max(at[j].get(q, 0.0), done[i])
+                left[j] -= 1
+                if not left[j]:
+                    ready.add(j)
+        return max(done), order, queue, done
+
+    best = None
+    for ahead in AHEAD:
+        urge = rank
+        for _ in range(PASSES):
+            fw = one(deps, nxt, urge, None, ahead)
+            if best is None or fw[0] < best[0]:
+                best = fw
+            urge = one(nxt, deps, fw[3], fw[2], ahead)[3]
+    return best[1], best[2], deps
 
 
 PLANNED = {}
@@ -223,7 +240,7 @@ def rank_program(g, core, T, topo):
         cost = {}
         for q in fns:
             if kind == "mm":
-                c = max(64, ins[1][2]) * CYC
+                c = max(64, ins[1][2]) * CYC * len(ins) / 2
             elif kind in ("dma", "g"):
                 c = 0.05 if kind == "dma" else 0.15 + 2 * n * CYC
             elif any(x[5] for x in sides):
@@ -274,11 +291,15 @@ def rank_program(g, core, T, topo):
         fns = {"v": ts_fn(out, a, scale, A.mult, bias, None if bias is None else A.add), "s": act_fn(out, a, ACT.Identity, scale, bias)}
         rec({q: fns[q] for q in qs}, out, [a, scale, bias], "ts")
 
-    def mms(out, pairs):
+    def mms(out, pairs, run=()):
         key = [("open" + out[1][0][0], 1)]
-        for k, (l, r) in enumerate(pairs):
-            first, last = k == 0, k == len(pairs) - 1
-            rec({"t": lambda e, l=l, r=r, first=first, last=last: e.matmul(out[0], l[0], r[0], first, last)}, out, [l, r], "mm", Wr=key)
+        parts = [[x] for x in pairs] + ([list(run)] if run else [])
+        for k, part in enumerate(parts):
+            def fn(e, k=k, part=part):
+                for j, (l, r) in enumerate(part):
+                    ins = e.matmul(out[0], l[0], r[0], k == 0 and j == 0, k == len(parts) - 1 and j == len(part) - 1)
+                return ins
+            rec({"t": fn}, out, [x for lr in part for x in lr], "mm", Wr=key)
 
     def gp(fn, out, ins):
         rec({"g": fn}, out, ins, "g")
@@ -291,7 +312,7 @@ def rank_program(g, core, T, topo):
         rec({q: lambda e: e.dma_start(out[0], src)}, out, [], "dma", "ld%d" % k, 16, lat)
 
     def store(q, k, dst, src):
-        rec({q: lambda e: e.dma_start(dst, src[0])}, (None, [("out%d" % k, 1)], 1, 4, False, None), [src], "dma", "ds%d" % k, 16, 3.0)
+        rec({q: lambda e: e.dma_start(dst, src[0])}, (None, [("out%d" % k, 1)], 1, 4, False, None), [src], "dma", "ds%d" % k, 16, 2.0 + src[2] * src[3] / 1200)
 
     def send(name, out, src, go, lat):
         dst = T.cores[(rank + go) % N]
@@ -324,16 +345,20 @@ def rank_program(g, core, T, topo):
     gp(lambda e: e.affine_select(G8[0], G8[0], [[16, 8]], A.is_ge, 0.0, 15, -1), G8, [G8])
     iota(v("pi"), [[0, 8]], 0, 1)
     iota(v("C32"), [[16, 8]], 0, 0)
-    iota(v("Kf"), [[4096, 256]], 0, 0)
+    iota(v("Kf"), [[-4096, 256]], -4096, 0)
+    iota(v("KQf"), [[-8192, 32], [0, 8]], -8192, 0)
     iota(v("kc"), [[1, 32]], 0, 0)
     iota(v("kc1"), [[1, 32]], 1, 0)
     iota(v("KAP"), [[113, 32]], 37, 0)
     iota(v("HR"), [[1, 8]], 0, 0)
-    iota(v("K2c"), [[-4096, 32], [0, 8]], 31 * 4096, 0)
+    iota(v("K2c"), [[-64, 32], [0, 8]], 31 * 64, 0)
     fill(v("SEL"), 0.0)
     fill(v("SEL2"), 0.0)
     fill(v("FL", W, W + B), B2 * DL)
-    fill(v("ONES32"), 1.0)
+    fill(v("ONES32"), 1 / 128)
+    fill(v("sp", 0, 8), 1 / 128)
+    for x in (v("KW0", 768, 776), v("ZO0", 512, 520), v("ZO1", 512, 520)):
+        fill(x, 0)
     fill(v("SCM"), 10000.0)
     fill(v("SCM", 0, 128, 16), -10000.0)
     fill(v("SCZ"), 1.0)
@@ -342,7 +367,7 @@ def rank_program(g, core, T, topo):
     fill(v("M130"), -130.0)
     fill(v("THR"), 96.0 * 2 ** 22)
     fill(v("THR", 0, 64, 1, 64), 1.5 * 2 ** 16)
-    fill(v("CS"), -32000.0 * 64)
+    fill(v("K2c", 0, 256, 1, 64), -32000.0 * 128)
     slope = -(2 * WM + 20) / ((B2 - B1 + 256) * DL)
     for k, w in enumerate((-7.5, 128.5, 1.0, WM + 12 - slope * (B1 - 256) * DL, 0.0)):
         fill(col("SG", k), w)
@@ -354,11 +379,12 @@ def rank_program(g, core, T, topo):
     affine(v("G82"), G8, 2.0)
     affine(v("HR"), v("HR"), 1 / 128)
     ts(v("pb"), v("pi"), 15, A.bitwise_and)
-    cp(v("lc"), col("pb", 0))
+    ts(v("lc"), col("pb", 0), -16.0, A.add)
     tt(v("C32"), v("C32"), v("pb"), A.add)
-    affine(v("Cv"), v("C32"), 33.0)
+    affine(v("Cv"), v("C32"), 33.0, -1.0)
     affine(v("C32"), v("C32"), 32.0)
     affine(v("ps6", 0, 256), v("Kf"), 1.0)
+    affine(v("ps6", 256, 512), v("KQf"), 1.0)
     ts(v("barf"), v("bari"), 16.0, A.add)
     tt(v("DM", 0, 64), v("ID", 0, 64), v("ID", 64, 128), A.add)
     tt(v("DM", 64, 96), v("DM", 0, 32), v("DM", 32, 64), A.add)
@@ -368,9 +394,8 @@ def rank_program(g, core, T, topo):
 
     cp(v("pl0"), v("craw"))
     tt(v("KW0", 256, 512), v("craw"), v("ps6", 0, 256), A.add)
-    ts(v("KW0", 512, 768), v("wi"), -2047.0, A.add)
-    ts(v("ps5", 256, 512), v("wi"), -2047.0, A.add, 4096.0, A.mult)
-    tt(v("KW0", 768, 1024), v("craw"), v("ps5", 256, 512), A.add)
+    ts(v("KW0", 512, 768), v("wi"), 1.0, A.add)
+    tt(v("KW0", 776, 1032), v("KW0", 512, 768), v("ps6", 256, 512), A.add)
 
     def classes(u, w, f, e, off):
         ts(u, e, 4.0 + off, A.is_ge, -1 / DL, A.mult)
@@ -387,7 +412,7 @@ def rank_program(g, core, T, topo):
         ts(v("ND", k * 1024, k * 1024 + 1024), v("PT", k * 1024, k * 1024 + 1024), 12.0, A.is_lt)
 
     def rows(dst, sel, src, a, n, first):
-        mms(dst, first + [(v(sel, k * 128, k * 128 + 128), v(src, a + k, a + n, 16)) for k in range(16)])
+        mms(dst, first, [(v(sel, k * 128, k * 128 + 128), v(src, a + k, a + n, 16)) for k in range(16)])
 
     for t in range(VI):
         pl, KW, s0, sv, ZO = "pl%d" % t, "KW%d" % t, v("sc%d" % t), v("so%d" % t), "ZO%d" % t
@@ -407,18 +432,18 @@ def rank_program(g, core, T, topo):
             cn = v("ps%d" % (c % 2), c * 64, c * 64 + 64)
             rows(cn, "SEL", "FL", c * 1024, 1024, [(ONE, v("THR"))])
             affine(v("hi", c * 64, c * 64 + 64), cn, 1.0)
-            tt(v("d0", c * 64, c * 64 + 64), cn, v("hi", c * 64, c * 64 + 64), A.subtract)
+            tt(v("d0", c * 64, c * 64 + 64), v("hi", c * 64, c * 64 + 64), cn, A.subtract)
         if last:
-            rec({"y": lambda e: e.dma_start(T.E2[:, :], T.E[:, :])}, v("E2"), [v("E"), v(pl)], "dma", "ds3", 16, 6.0)
+            rec({"y": lambda e: e.dma_start(T.E2[:, :], T.E[:, :])}, v("E2"), [v("E"), v(pl)], "dma", "ds3", 16, 8.0)
 
         for h in range(8):
-            scan(lanes(KW, h), v("d0", 248 + h, None, -8), v(KW, 504 + h, 255, -8), (256.0 + h) * 4096, A.min, A.max)
+            scan(lanes(KW, h), v("d0", 248 + h, None, -8), v(KW, 504 + h, 255, -8), -(257.0 + h) * 4096, A.max, A.min)
         r = v(KW, 248, 256)
         ts(v("qq"), r, 12, A.arith_shift_right)
         ts(v("xr"), r, 15, A.arith_shift_right)
         ts(v("sx"), r, 4095, A.bitwise_and)
-        ts(v("ou", 8, 16), v("qq"), 16.0, A.mult, v("lc"), A.add)
-        tt(v("oi"), v("xr"), v("Cv"), A.add)
+        ts(v("ou", 8, 16), v("qq"), -16.0, A.mult, v("lc"), A.add)
+        tt(v("oi"), v("Cv"), v("xr"), A.subtract)
         cp(v("ou", 0, 8), v("oi"))
         affine(v("vx"), ind(v("V0"), v("ou", 0, 8)), 1 / DL, 1022.5, "v")
         act(v("wm"), ind(v("FL"), v("ou", 8, 16)), ACT.Abs, slope, col("SG", 3))
@@ -448,10 +473,9 @@ def rank_program(g, core, T, topo):
             ts(v("cm", a, a + 128), v("craw", a, a + 128), 4095, A.bitwise_and)
             cp(v("cu", a, a + 128), v("cm", a, a + 128))
         ts(v("cmZ"), v("cm"), -2.0 ** 23, A.add)
-        fused = (1, 4, 6, 7)[:NFUSE]
         for c in range(8):
             a, src = c * 512, ind(v("E"), v("cu", c * 32, c * 32 + 32))
-            if c in fused:
+            if c in FUSED:
                 tt(v("FL", a, a + 512), src, v("W4"), A.add)
             else:
                 affine(v("EC", a, a + 512), src, 1.0, C0 + 0.5, "s")
@@ -460,7 +484,7 @@ def rank_program(g, core, T, topo):
             if c % 2:
                 x = (c // 2) * 64
                 cn = v("ps%d" % (c // 2 % 2), 256 + x, 320 + x)
-                rows(cn, "SEL2", "FL", a - 512, 1024, [(ONE, v("CS")), (ID, v("K2c", x, x + 64))])
+                rows(cn, "SEL2", "FL", a - 512, 1024, [(ONE, v("K2c", x, x + 64))])
                 tt(v("key", x, x + 64), v("cmZ", x, x + 64), cn, A.add)
 
         act(v("r4"), V32, ACT.Identity, 1 / DL, 1022.5)
@@ -490,64 +514,72 @@ def rank_program(g, core, T, topo):
             act(v("ea"), v("eb"), ACT.Identity, None, -382.0)
             tt(ind(v("TT"), v("uu")), v("ea"), v("ef"), A.add)
 
-        ts(v("fnd"), v("xr"), 32.0, A.is_lt, 2.0 ** 17, A.mult)
+        ts(v("fnd"), v("xr"), -32.0, A.is_ge, 2.0 ** 17, A.mult)
         tt(v("barK"), v("barf"), v("fnd"), A.mult)
-        ts(v("dp1"), v("dq"), 1.0, A.add, -1.0, A.mult)
-        ts(v("sd2"), v("sd"), 2.0, A.add)
-        ts(v("sdZ"), v("sd"), -2047.0, A.add, 4096.0, A.mult)
-        ts(v("x64"), v("xr"), 64.0, A.mult)
-        ts(v("c33x"), v("xr"), -1.0, A.mult, 33.0, A.add)
-        fill(v("ps5", 0, 8), 0.0)
+        cp(v("dp1"), v("dq"))
+        ts(v("sd1"), v("sd"), 1.0, A.add)
+        ts(v("xn"), v("xr"), 1.0, A.add)
+        ts(v("xh"), v("xr"), -1.0, A.mult, -1.5, A.add)
+        ts(v("x40"), v("xr"), -1.0, A.mult, -41.0, A.add)
+        for h in range(8):
+            act(lanes("sg1", h), v("kc"), ACT.Sign, -1.0, col("xh", h))
+            out = lanes("ps2", h, 256)
+            rec({"s": act_fn(out, v("kc1"), ACT.Abs, None, col("dp1", h)), "v": ts_fn(out, v("kc1"), col("dp1", h), A.add, 0.0, A.not_equal)},
+                out, [v("kc1"), col("dp1", h)], "act")
+            ts(lanes("e2p", h), lanes(KW, h, 512), col("sd1", h), A.not_equal, 1 / 128, A.mult)
+        act(v("ps7", 0, 256), v("sg1"), ACT.Relu)
+        tt(v("kept"), v("e2p"), v("ps2", 256, 512), A.min)
+        for h in range(8):
+            scan(lanes("sp", h, 8), v("ONES32"), lanes("kept", h), 1 / 128, A.add, A.subtract)
+        tt(v("Dc"), v("sp", 0, 256), v("ps7", 0, 256), A.add)
+        ts(v("n40"), v("sp", 256, 264), 128.0, A.mult, 7.0, A.add)
+        fill(r, 0)
         for h in range(8):
             red(col("MBi", h), lanes("key", h), A.max)
         tt(v("ret"), v("MBi"), v("barK"), A.is_lt)
         tt(v("nr"), v("MBi"), v("barK"), A.is_ge)
-        tt(v("A1"), v("ret"), v("dp1"), A.mult)
-        tt(v("A2"), v("ret"), v("sd2"), A.mult)
-        affine(v("A3"), v("ret"), 6400.0)
-        tt(v("xb"), v("A3"), v("x64"), A.add)
+        affine(v("mul"), v("ret"), 127.0, 1.0)
         for h in range(8):
-            act(lanes("ps2", h), v("kc1"), ACT.Abs, None, col("A1", h))
-            ts(lanes("e2p", h), lanes(KW, h, 512), 2049.0, A.add, col("A2", h), A.not_equal)
-        kept = v("ps4", 0, 256)
-        tt(kept, v("e2p"), v("ps2", 0, 256), A.min)
-        for h in range(8):
-            scan(lanes("sp", h), v("ONES32"), lanes("ps4", h), 1.0, A.add, A.subtract)
-            act(lanes("ps7", h), v("kc"), ACT.Relu, -64.0, col("xb", h))
-        tt(v("Dz"), v("sp"), v("ps7", 0, 256), A.min)
-        tt(v("ps5", 8, 264), v(KW, 768, 1024), kept, A.mult)
+            ts(lanes("Dz", h), lanes("Dc", h), col("mul", h), A.mult)
         ts(v("cb"), v("MBi"), 4095, A.bitwise_and)
-        tt(v("v1"), v("cb"), v("sdZ"), A.add)
+        ts(v("v1"), v("cb"), -2.0 ** 23, A.add)
         tt(v("v2"), v("v1"), v("nr"), A.mult)
+        tt(v("v3"), v("x40"), v("ret"), A.mult)
+        tt(v("mid"), v("v3"), v("xn"), A.add)
+        tt(v("v4"), v("n40"), v("ret"), A.mult)
+        affine(v("rad"), v("v4"), 1.0, 0.5)
+        tt(v("v5"), v("sd1"), v("nr"), A.mult)
+        affine(v("vq"), v("v5"), 1.0, -2.0 ** 23)
+        Fp = v("ps4", 0, 256)
         for h in range(8):
+            act(lanes("far", h), v("kc"), ACT.Abs, None, col("mid", h))
+            act(lanes("sg1", h), lanes("far", h), ACT.Sign, -1.0, col("rad", h))
             act(lanes("al", h), lanes("cmZ", h), ACT.Identity, col("ret", h), col("v2", h))
-        tt(v("nx"), v("c33x"), v("sp", 248, 256), A.subtract)
-        tt(v("rn"), v("nx"), v("ret"), A.mult)
-        tt(v("f1"), v("rn"), v("xr"), A.add)
-        affine(v("nr99"), v("nr"), 99.0)
-        tt(v("f0"), v("f1"), v("nr99"), A.add)
+        act(Fp, v("sg1"), ACT.Relu)
+        tt(v("ps2", 0, 256), v("al"), Fp, A.mult)
         for h in range(8):
-            ts(lanes("ps4", h, 256), v("kc"), col("f0", h), A.min, col("f1", h), A.is_equal)
-        tt(v("alY"), v("al"), v("ps4", 256, 512), A.mult)
+            act(lanes("ps1", h, 256), lanes("ps4", h), ACT.Identity, col("vq", h))
         for b in range(6):
             s = 8 << b
             m = 264 - s
             tb = v("tb", b * 256, b * 256 + m)
             ts(tb, v("Dz", s - 8, 256), b, A.arith_shift_right, 1, A.bitwise_and)
-            tt(v("tm", 0, m), tb, v("ps5", s, 264), A.mult)
-            tt(v("ps5", s, 264), v("ps5", s, 264), v("tm", 0, m), A.subtract)
-            tt(v("ps5", 0, m), v("ps5", 0, m), v("tm", 0, m), A.add)
-        Z = v(ZO, 512, 768)
-        tt(Z, v("alY"), v("ps5", 0, 256), A.add)
-        ts(v("nS"), Z, 4095, A.bitwise_and)
+            for a, mv in ((248, v("ps5", 0, m)), (768, v("ps7", 256, 256 + m))):
+                scan(mv, tb, v(KW, a + s, a + 264), 0.0, A.max, A.mult)
+                tt(v(KW, a, a + m), v(KW, a, a + m), mv, A.min)
+        tt(v(KW, 248, 504), v(KW, 248, 504), v("ps2", 0, 256), A.min)
+        ts(v("nS"), v(KW, 248, 504), 4095, A.bitwise_and)
+        tt(v(KW, 768, 1024), v(KW, 768, 1024), v("ps1", 256, 512), A.min)
+        nQ = v(ZO, 256, 512)
+        ts(nQ, v(KW, 768, 1024), 8191, A.bitwise_and)
         if not last:
             cp(v("plo%d" % t), v("nS"))
-            send("p%d" % (t + 1), v("pl%d" % (t + 1)), v("plo%d" % t), PLAN_GO, 2.0)
+            send("p%d" % (t + 1), v("pl%d" % (t + 1)), v("plo%d" % t), PLAN_GO, 2.5)
             tt(v(ZO, 0, 256), v("nS"), v("ps6", 0, 256), A.add)
-            ts(v(ZO, 256, 512), Z, 12, A.arith_shift_right)
-            send("q%d" % (t + 1), v("KW%d" % (t + 1), 256, 1024), v(ZO), PLAN_GO, 4.0)
+            tt(v(ZO, 520, 776), nQ, v("ps6", 256, 512), A.add)
+            send("q%d" % (t + 1), v("KW%d" % (t + 1), 256, 1032), v(ZO), PLAN_GO, 3.5)
             cp(v("retb"), v("ret"))
-            mms(col("ps3", 392), [(ONE, col("retb", h)) for h in range(8)])
+            mms(col("ps3", 392), [], [(ONE, col("retb", h)) for h in range(8)])
             cp(col("ri", 0), col("ps3", 392))
             ts(col("ri", 1), col("ri", 0), 1, A.bitwise_and)
             ts(v("thr"), col("ri", 1), 1.5, A.add, 2.0 ** 16, A.mult)
@@ -555,8 +587,7 @@ def rank_program(g, core, T, topo):
         else:
             cp(v("ysw", 0, 256), v("nS"))
             store("y", 1, T.ys[:, :], v("ysw", 0, 256))
-            ts(v(ZO, 256, 512), Z, 12, A.arith_shift_right)
-            ts(v("ysw", 256, 512), v(ZO, 256, 512), 2047.0, A.add)
+            ts(v("ysw", 256, 512), nQ, -1.0, A.add)
             store("s", 2, T.yw[:, :], v("ysw", 256, 512))
 
     if not PLANNED:

@@ -24,32 +24,34 @@ def _pool(name, dtype, n, *names):
 
 _buf(H, W, "E", "E2", "PT", "TT", "ND", "Gn", "EC")
 _buf(H, 33 * B, "D1", "V0", "FL")
-_buf(H, 2048, "SEL", "SEL2")
+_buf(H, 2048, "SEL2")
 _buf(H, 128, "ID", "ONE", "MK16", "SCM", "SCZ", "DM", "LT", "vx", "wm", "CW", "M130", "sg0", "r4", "sgn", "az", "iseq", "w8", "prw",
      "es", "eb", "ea", "eu", "ew", "ef", "sc0", "sc1", "sc2", "so0", "so1", "so2")
 _buf(H, 7 * 128, "IS")
-_buf(H, 8, "G8", "G82", "HR", "retb")
-_buf(H, 32, "ONES32")
-_buf(H, 64, "THR")
-_buf(H, 256, "K2c", "hi", "e2p", "kept", "sg1", "far")
+_buf(H, 8, "G8", "G82", "retb")
+_buf(H, 16, "G8B")
+_buf(H, 24, "G83")
+_buf(H, 32, "ONES32", "HR", "kneg")
+_buf(H, 256, "THR", "K2c", "e2p", "kept", "sg1", "far")
 _buf(F, 128, "RM", "kd")
 _buf(F, 512, "W4", "ysw")
-_buf(F, 256, "d0", "cmZ", "key", "Dc", "al", "Kf", "KQf")
+_buf(F, 256, "d0", "cmZ", "key", "Dc", "al", "Kf", "KQf", "xs")
 _buf(F, 264, "sp")
 _buf(F, 32, "kc", "kc1", "KAP")
 _pool("lf", F, 8, "Cv", "C32", "SG", "sxf", "bsf", "barf", "barK", "fnd", "ret", "nr", "mul", "dp1", "sd1", "xn", "xh", "x40", "n40",
       "mid", "rad", "vq", "v1", "v2", "v3", "v4", "v5")
-_buf(F, 1, "thr", "lc")
+_buf(F, 1, "thr")
+_buf(F, 2, "lc")
 _buf(I, 2, "ri")
 _buf(I, 6 * 256, "tb")
 _buf(I, 256, "craw", "cm", "Dz", "nS", "wi")
-_buf(I, 128, "rd")
+_buf(I, 128, "rd", "rx")
 _buf(I, 8, "bari")
 _pool("li", I, 8, "pi", "pb", "qq", "xr", "sx", "oi", "sd", "dq", "pr0", "bs", "MBi", "cb", "ui", "ua", "uo")
 _buf(I, 1032, "KW0", "KW1", "KW2")
 _buf(I, 776, "ZO0", "ZO1", "ZO2")
 _buf(U, 256, "pl0", "pl1", "pl2", "plo0", "plo1", "cu")
-_buf(U, 24, "ou")
+_buf(U, 32, "ou")
 _buf(U, 8, "uu")
 for _b in range(8):
     SCRATCH["ps%d" % _b] = ("psum", [128, 512], F)
@@ -57,11 +59,15 @@ for _b in range(8):
 DMAS = ["ld%d" % k for k in range(12)] + ["ds%d" % k for k in range(4)]
 SEMAPHORES = ["qv", "qs", "qt", "qg"] + DMAS + ["ap1", "ap2", "aq1", "aq2", "as1", "as2", "lp1", "lp2", "lq1", "lq2", "ls1", "ls2"]
 FUSED = (1, 3, 5)
+VADD = 2
 DL = 2.0 ** -18
 B1, B2 = 49152, 98304
 WM, C0 = 760, 1304
-CYC, GATHER, SCATTER, WAKE = 0.83e-3, 1.56, 3.8, 0.1
-AHEAD, PASSES = (2.0,), 4
+CYC, GATHER, SCATTER, WAKE = 0.83e-3, 1.56, 3.8, 0.15
+AHEAD, PASSES = (0.7, 1.0, 1.5, 2.5), 4
+FLY, LOAD, NEXT, EARLY = 1.3, 2.5, 0.9, 8.0
+ORDER = list(range(0, 32, 4))
+NEEDS_V = (4, 5)
 SIZE = {H: 2, F: 4, I: 4, U: 2}
 
 
@@ -187,10 +193,13 @@ def _schedule(prog):
         return max(done), order, queue, done
 
     best = None
+    const = []
+    for i in range(n):
+        const.append(prog[i]["sem"] is None and all(const[j] for j in deps[i]))
     for ahead in AHEAD:
         urge = rank
         for _ in range(PASSES):
-            fw = one(deps, nxt, urge, None, ahead)
+            fw = one(deps, nxt, [max(u, max(urge) - EARLY) if c else u for u, c in zip(urge, const)], None, ahead)
             if best is None or fw[0] < best[0]:
                 best = fw
             urge = one(nxt, deps, fw[3], fw[2], ahead)[3]
@@ -301,6 +310,16 @@ def rank_program(g, core, T, topo):
                 return ins
             rec({"t": fn}, out, [x for lr in part for x in lr], "mm", Wr=key)
 
+    def group(items, first, last, part="a"):
+        def fn(e):
+            for j, (o, l, r) in enumerate(items):
+                ins = e.matmul(o[0], l[0], r[0], first and j == 0, last and j == len(items) - 1)
+            return ins
+        out = items[0][0]
+        key = [("open" + out[1][0][0], 1)]
+        rec({"t": fn}, out, [x for o, l, r in items for x in (l, r)], "mm", R=key if part == "b" else [],
+            Wr=([] if part == "b" else key) + [o[1][0] for o, l, r in items])
+
     def gp(fn, out, ins):
         rec({"g": fn}, out, ins, "g")
 
@@ -329,14 +348,14 @@ def rank_program(g, core, T, topo):
     def IS(k):
         return v("IS", k * 128, k * 128 + 128)
 
-    load("s", 0, v("craw"), T.act[:, :], 3.0)
-    load("s", 2, v("sc0"), T.st0[:, :], 3.0)
-    load("s", 1, v("wi"), T.why[:, :], 3.5)
-    load("s", 3, v("bari"), T.bar[:, :], 3.5)
     for k in range(4):
-        load("y", 4 + k, v("E", k * 1024, k * 1024 + 1024), T.eff[:, k * 1024:k * 1024 + 1024], 3.5 + k)
+        load("y", 4 + k, v("E", k * 1024, k * 1024 + 1024), T.eff[:, k * 1024:k * 1024 + 1024], LOAD + NEXT * k)
+    load("y", 0, v("craw"), T.act[:, :], LOAD + NEXT * 4)
+    load("y", 2, v("sc0"), T.st0[:, :], LOAD + NEXT * 4)
     for k in range(4):
-        load("y", 8 + k, v("PT", k * 1024, k * 1024 + 1024), T.req[:, k * 1024:k * 1024 + 1024], 7.5 + k)
+        load("y", 8 + k, v("PT", k * 1024, k * 1024 + 1024), T.req[:, k * 1024:k * 1024 + 1024], LOAD + NEXT * (5.5 + k))
+    load("y", 1, v("wi"), T.why[:, :], LOAD + NEXT * 10)
+    load("y", 3, v("bari"), T.bar[:, :], LOAD + NEXT * 10)
 
     ID, ONE, G8 = v("ID"), v("ONE"), v("G8")
     fill(ONE, 1.0)
@@ -350,9 +369,7 @@ def rank_program(g, core, T, topo):
     iota(v("kc"), [[1, 32]], 0, 0)
     iota(v("kc1"), [[1, 32]], 1, 0)
     iota(v("KAP"), [[113, 32]], 37, 0)
-    iota(v("HR"), [[1, 8]], 0, 0)
     iota(v("K2c"), [[-64, 32], [0, 8]], 31 * 64, 0)
-    fill(v("SEL"), 0.0)
     fill(v("SEL2"), 0.0)
     fill(v("FL", W, W + B), B2 * DL)
     fill(v("ONES32"), 1 / 128)
@@ -365,8 +382,7 @@ def rank_program(g, core, T, topo):
     fill(v("SCZ", 0, 128, 16), 0.0)
     fill(v("CW"), -784.0)
     fill(v("M130"), -130.0)
-    fill(v("THR"), 96.0 * 2 ** 22)
-    fill(v("THR", 0, 64, 1, 64), 1.5 * 2 ** 16)
+    fill(v("THR"), -1.5 * 8)
     fill(v("K2c", 0, 256, 1, 64), -32000.0 * 128)
     slope = -(2 * WM + 20) / ((B2 - B1 + 256) * DL)
     for k, w in enumerate((-7.5, 128.5, 1.0, WM + 12 - slope * (B1 - 256) * DL, 0.0)):
@@ -374,14 +390,20 @@ def rank_program(g, core, T, topo):
     for k, w in enumerate((-1.0, 6.0, 8.0, 64.0, 1 / DL, -1 / DL, -3 / 32 / DL)):
         affine(IS(k), ID, w)
     for k in range(16):
-        affine(v("SEL", k * 128 + k, k * 128 + 128, 16), G8, 2.0 ** 32)
         affine(v("SEL2", k * 128 + k, k * 128 + 128, 16), G8, 2.0 ** 13)
     affine(v("G82"), G8, 2.0)
-    affine(v("HR"), v("HR"), 1 / 128)
+    affine(v("G8B", 0, 8), G8, 2.0 ** 20)
+    affine(v("G8B", 8, 16), G8, -2.0 ** 20)
+    for k, (w, a, b) in enumerate(((-1.0, 528, 0), (-128.0, 16, 0), (-8.0, 1, 8))):
+        affine(v("G83", 8 * k, 8 * k + 8), G8, w)
+        affine(v("HR", 8 * k, 8 * k + 8), v("kc", 0, 8), a / 128, b / 128)
+    affine(v("HR", 24, 32), v("kc", 0, 8), 1 / 128)
+    affine(v("kneg"), v("kc"), -1.0)
     ts(v("pb"), v("pi"), 15, A.bitwise_and)
-    ts(v("lc"), col("pb", 0), -16.0, A.add)
+    ts(col("lc", 0), col("pb", 0), 33.0, A.mult)
+    cp(col("lc", 1), col("pb", 0))
     tt(v("C32"), v("C32"), v("pb"), A.add)
-    affine(v("Cv"), v("C32"), 33.0, -1.0)
+    affine(v("Cv"), v("kc", 0, 8), 528.0, -1.0)
     affine(v("C32"), v("C32"), 32.0)
     affine(v("ps6", 0, 256), v("Kf"), 1.0)
     affine(v("ps6", 256, 512), v("KQf"), 1.0)
@@ -406,8 +428,12 @@ def rank_program(g, core, T, topo):
         a, b = c * 512, c * 512 + 512
         p = v(("ps0", "ps1", "ps2", "ps7")[c % 4])
         classes(v("Gn", a, b), v("EC", a, b), v("D1", a, b), v("E", a, b), 0)
-        mms(p, [(ID, v("E", a, b)), (ID, v("D1", a, b))])
-        act(v("TT", a, b), p, ACT.Identity, None, -252.0)
+        if c < 8 - VADD:
+            mms(p, [(ID, v("E", a, b)), (ID, v("D1", a, b))])
+            act(v("TT", a, b), p, ACT.Identity, None, -252.0)
+        else:
+            act(p, v("E", a, b), ACT.Identity, None, -252.0)
+            tt(v("TT", a, b), v("D1", a, b), p, A.add)
     for k in range(4):
         ts(v("ND", k * 1024, k * 1024 + 1024), v("PT", k * 1024, k * 1024 + 1024), 12.0, A.is_lt)
 
@@ -424,40 +450,49 @@ def rank_program(g, core, T, topo):
         for k in range(32):
             affine(v("D1", k + 1, None, 33), ind(v("TT"), v(pl, k * 8, k * 8 + 8)), DL, 4 * min(k, 30) * DL)
         for c in range(8):
-            affine(v("Gn", c * 512, c * 512 + 512), ind(v("ND"), v(pl, c * 32, c * 32 + 32)), (B2 - B1) * DL, B1 * DL)
+            affine(v("Gn", c * 512, c * 512 + 512), ind(v("ND"), v(pl, c * 32, c * 32 + 32)), (B2 - B1) * DL, B1 * DL, "v" if c in NEEDS_V else "s")
         scan(v("V0"), v("D1"), v("D1"), 0.0, A.mult, A.min)
-        for c in range(4):
-            for k in range(8 * c, 8 * c + 8):
+        group([(v("ps0", 0, 256), ONE, v("THR"))], True, False, "a")
+        for a in ORDER:
+            group([(v("ps0", k * 8, k * 8 + 8), v("Gn", k * 128, k * 128 + 128), v("G8B", 0, 8)) for k in range(a, a + 4)], False, False, "b")
+        for a in ORDER:
+            for k in range(a, a + 4):
                 scan(v("FL", k * 128, k * 128 + 128), v("V0", k, None, 33), v("Gn", k * 128, k * 128 + 128), 1.0, A.min, A.add)
-            cn = v("ps%d" % (c % 2), c * 64, c * 64 + 64)
-            rows(cn, "SEL", "FL", c * 1024, 1024, [(ONE, v("THR"))])
-            affine(v("hi", c * 64, c * 64 + 64), cn, 1.0)
-            tt(v("d0", c * 64, c * 64 + 64), v("hi", c * 64, c * 64 + 64), cn, A.subtract)
+            group([(v("ps0", k * 8, k * 8 + 8), v("FL", k * 128, k * 128 + 128), v("G8B", 8, 16)) for k in range(a, a + 4)],
+                  False, a == ORDER[-1], "c" if a == ORDER[-1] else "b")
         if last:
             rec({"y": lambda e: e.dma_start(T.E2[:, :], T.E[:, :])}, v("E2"), [v("E"), v(pl)], "dma", "ds3", 16, 8.0)
 
+        def turn(out, src, a, step, rhs, const):
+            for h in range(8):
+                affine(v("LT", h * 16, h * 16 + 16), v("MK16", 0, 16), col(src, a + h * step))
+            mms(out, [(ONE, const), (v("LT"), rhs)])
+
+        def pick(out, lst):
+            tt(v("kd"), ind(v(KW, 248, 520), lst), v("DM"), A.mult)
+            scan(v(out), v("SCZ"), v("kd"), 0.0, A.mult, A.add)
+            return v(out, 15, None, 16)
+
         for h in range(8):
-            scan(lanes(KW, h), v("d0", 248 + h, None, -8), v(KW, 504 + h, 255, -8), -(257.0 + h) * 4096, A.max, A.min)
-        r = v(KW, 248, 256)
-        ts(v("qq"), r, 12, A.arith_shift_right)
-        ts(v("xr"), r, 15, A.arith_shift_right)
-        ts(v("sx"), r, 4095, A.bitwise_and)
-        ts(v("ou", 8, 16), v("qq"), -16.0, A.mult, v("lc"), A.add)
-        tt(v("oi"), v("Cv"), v("xr"), A.subtract)
-        cp(v("ou", 0, 8), v("oi"))
+            scan(lanes("xs", h), v("ps0", 248 + h, None, -8), v("kneg", 31, None, -1), -32.0, A.max, A.min)
+        turn(v("ps4", 256, 280), "xs", 248, 1, v("G83"), v("HR", 0, 24))
+        ts(v("ou", 0, 8), v("ps4", 256, 264), col("lc", 0), A.add)
+        ts(v("ou", 8, 16), v("ps4", 264, 272), col("lc", 1), A.add)
+        cp(v("ou", 24, 32), v("ps4", 272, 280))
+        tt(v("xr"), v("Cv"), v("ps4", 256, 264), A.subtract)
         affine(v("vx"), ind(v("V0"), v("ou", 0, 8)), 1 / DL, 1022.5, "v")
         act(v("wm"), ind(v("FL"), v("ou", 8, 16)), ACT.Abs, slope, col("SG", 3))
+        r = v(KW, 248, 256)
+        rx = pick("rx", v("ou", 24, 32))
+        cp(r, rx)
+        ts(v("sx"), rx, 4095, A.bitwise_and)
 
         DT, D8 = v("ps2", 0, 128), v("ps2", 128, 136)
         mms(DT, [(v("CW"), IS(3)), (v("wm"), IS(3)), (v("vx"), ID)])
         scan(v("RM"), v("SCM"), DT, 0.0, A.min, A.max)
-        for h in range(8):
-            affine(v("LT", h * 16, h * 16 + 16), v("MK16", 0, 16), col("RM", h * 16 + 15))
-        mms(D8, [(ONE, v("HR")), (v("LT"), v("G82"))])
+        turn(D8, "RM", 15, 16, v("G82"), v("HR", 24, 32))
         cp(v("ou", 16, 24), D8)
-        tt(v("kd"), ind(v(KW, 248, 512), v("ou", 16, 24)), v("DM"), A.mult)
-        scan(v("rd"), v("SCZ"), v("kd"), 0.0, A.mult, A.add)
-        rd = v("rd", 15, None, 16)
+        rd = pick("rd", v("ou", 16, 24))
         ts(v("sd"), rd, 4095, A.bitwise_and)
         ts(v("dq"), rd, 15, A.arith_shift_right)
         cp(v("sxf"), v("sx"))
@@ -499,8 +534,9 @@ def rank_program(g, core, T, topo):
         act(sv, v("ps3", 256, 384), ACT.Identity, None, 1030.0)
         if not last:
             send("s%d" % (t + 1), v("sc%d" % (t + 1)), sv, STATE_GO, 2.0)
-        rows(v("ps3", 384, 392), "SEL", "so%d" % t, 0, 128, [])
-        ts(v("ui"), v("ps3", 384, 392), 2.0 ** -32, A.mult)
+        for a in range(0, 16, 4):
+            group([(v("ps3", 384, 392), v("SEL2", k * 128, k * 128 + 128), v("so%d" % t, k, 128, 16)) for k in range(a, a + 4)], a == 0, a == 12)
+        ts(v("ui"), v("ps3", 384, 392), 2.0 ** -13, A.mult)
         ts(v("ua"), v("ui"), 31, A.bitwise_and)
         tt(v("uo"), v("ua"), v("C32"), A.add)
         cp(v("uu"), v("uo"))
@@ -533,7 +569,6 @@ def rank_program(g, core, T, topo):
             scan(lanes("sp", h, 8), v("ONES32"), lanes("kept", h), 1 / 128, A.add, A.subtract)
         tt(v("Dc"), v("sp", 0, 256), v("ps7", 0, 256), A.add)
         ts(v("n40"), v("sp", 256, 264), 128.0, A.mult, 7.0, A.add)
-        fill(r, 0)
         for h in range(8):
             red(col("MBi", h), lanes("key", h), A.max)
         tt(v("ret"), v("MBi"), v("barK"), A.is_lt)
@@ -559,12 +594,15 @@ def rank_program(g, core, T, topo):
         tt(v("ps2", 0, 256), v("al"), Fp, A.mult)
         for h in range(8):
             act(lanes("ps1", h, 256), lanes("ps4", h), ACT.Identity, col("vq", h))
-        for b in range(6):
+        for b in (5, 0, 1, 2, 3, 4):
             s = 8 << b
             m = 264 - s
             tb = v("tb", b * 256, b * 256 + m)
             ts(tb, v("Dz", s - 8, 256), b, A.arith_shift_right, 1, A.bitwise_and)
             for a, mv in ((248, v("ps5", 0, m)), (768, v("ps7", 256, 256 + m))):
+                if b == 5:
+                    scan(v(KW, a, a + m), tb, v(KW, a + s, a + 264), 0.0, A.max, A.mult)
+                    continue
                 scan(mv, tb, v(KW, a + s, a + 264), 0.0, A.max, A.mult)
                 tt(v(KW, a, a + m), v(KW, a, a + m), mv, A.min)
         tt(v(KW, 248, 504), v(KW, 248, 504), v("ps2", 0, 256), A.min)
@@ -574,7 +612,7 @@ def rank_program(g, core, T, topo):
         ts(nQ, v(KW, 768, 1024), 8191, A.bitwise_and)
         if not last:
             cp(v("plo%d" % t), v("nS"))
-            send("p%d" % (t + 1), v("pl%d" % (t + 1)), v("plo%d" % t), PLAN_GO, 2.5)
+            send("p%d" % (t + 1), v("pl%d" % (t + 1)), v("plo%d" % t), PLAN_GO, FLY)
             tt(v(ZO, 0, 256), v("nS"), v("ps6", 0, 256), A.add)
             tt(v(ZO, 520, 776), nQ, v("ps6", 256, 512), A.add)
             send("q%d" % (t + 1), v("KW%d" % (t + 1), 256, 1032), v(ZO), PLAN_GO, 3.5)
@@ -582,8 +620,9 @@ def rank_program(g, core, T, topo):
             mms(col("ps3", 392), [], [(ONE, col("retb", h)) for h in range(8)])
             cp(col("ri", 0), col("ps3", 392))
             ts(col("ri", 1), col("ri", 0), 1, A.bitwise_and)
-            ts(v("thr"), col("ri", 1), 1.5, A.add, 2.0 ** 16, A.mult)
-            affine(v("THR", 0, 64, 1, 64), v("ONE", 0, 64, 1, 64), col("thr", 0, 64))
+            ts(v("thr"), col("ri", 1), 1.5, A.add, -8.0, A.mult)
+            for a in (0, 128):
+                affine(v("THR", a, a + 128), ONE, v("thr"), None, "s")
         else:
             cp(v("ysw", 0, 256), v("nS"))
             store("y", 1, T.ys[:, :], v("ysw", 0, 256))

@@ -1,3 +1,5 @@
+import numpy as np
+from concourse.bass import DstId, RemoteDMATransfer
 from concourse.mybir import AluOpType, AxisListType, ActivationFunctionType
 
 A = AluOpType
@@ -25,49 +27,60 @@ def _pool(name, dtype, n, *names):
 _buf(H, W, "E", "E2", "PT", "TT", "ND", "Gn", "EC")
 _buf(H, 33 * B, "D1", "V0", "FL")
 _buf(H, 2048, "SEL2")
-_buf(H, 128, "ID", "ONE", "MK16", "SCM", "SCZ", "DM", "LT", "vx", "wm", "CW", "M130", "sg0", "r4", "sgn", "az", "iseq", "w8", "prw",
+_buf(H, 128, "ID", "ONE", "MK16", "SCM", "SCZ", "DM", "LT", "vx", "CW", "M130", "sg0", "r4", "sgn", "az", "iseq", "w8", "prw",
      "es", "eb", "ea", "eu", "ew", "ef", "sc0", "sc1", "sc2", "so0", "so1", "so2")
-_buf(H, 7 * 128, "IS")
+_buf(H, 12 * 128, "IS")
 _buf(H, 8, "G8", "G82", "retb")
 _buf(H, 16, "G8B")
-_buf(H, 24, "G83")
-_buf(H, 32, "ONES32", "HR", "kneg")
-_buf(H, 256, "THR", "K2c", "e2p", "kept", "sg1", "far")
-_buf(F, 128, "RM", "kd")
-_buf(F, 512, "W4", "ysw")
-_buf(F, 256, "d0", "cmZ", "key", "Dc", "al", "Kf", "KQf", "xs")
-_buf(F, 264, "sp")
+_buf(H, 40, "G83")
+_buf(H, 48, "HR")
+_buf(H, 32, "ONES32")
+_buf(H, 264, "THR", "RST", "O264", "kneg")
+_buf(F, 264, "xs")
+_buf(H, 256, "K2c", "e2p", "kept", "sg1", "sg2", "far", "wm")
+_buf(F, 128, "RM", "krx", "krd", "krp", "DX")
+_buf(F, 1024, "W4")
+_buf(F, 512, "ysw")
+_buf(F, 256, "key", "Dc", "al")
+_buf(F, 128, "ID32")
+_buf(H, 256, "C192", "Db", "lt0")
+_buf(H, 4 * 256, "fb")
+_buf(H, 264, "sp")
 _buf(F, 32, "kc", "kc1", "KAP")
 _pool("lf", F, 8, "Cv", "C32", "SG", "sxf", "bsf", "barf", "barK", "fnd", "ret", "nr", "mul", "dp1", "sd1", "xn", "xh", "x40", "n40",
       "mid", "rad", "vq", "v1", "v2", "v3", "v4", "v5")
 _buf(F, 1, "thr")
-_buf(F, 2, "lc")
+_buf(H, 80, "LC")
 _buf(I, 2, "ri")
 _buf(I, 6 * 256, "tb")
-_buf(I, 256, "craw", "cm", "Dz", "nS", "wi")
-_buf(I, 128, "rd", "rx")
+_buf(I, 256, "craw", "cm", "Dz", "wi", "Kf", "KQf")
+_buf(I, 128, "rd", "rx", "rp")
 _buf(I, 8, "bari")
 _pool("li", I, 8, "pi", "pb", "qq", "xr", "sx", "oi", "sd", "dq", "pr0", "bs", "MBi", "cb", "ui", "ua", "uo")
-_buf(I, 1032, "KW0", "KW1", "KW2")
-_buf(I, 776, "ZO0", "ZO1", "ZO2")
+_buf(I, 1296, "KW0", "KW1", "KW2")
+_buf(I, 1040, "ZO0", "ZO1", "ZO2")
 _buf(U, 256, "pl0", "pl1", "pl2", "plo0", "plo1", "cu")
-_buf(U, 32, "ou")
+_buf(U, 40, "ou")
 _buf(U, 8, "uu")
 for _b in range(8):
     SCRATCH["ps%d" % _b] = ("psum", [128, 512], F)
 
-DMAS = ["ld%d" % k for k in range(12)] + ["ds%d" % k for k in range(4)]
-SEMAPHORES = ["qv", "qs", "qt", "qg"] + DMAS + ["ap1", "ap2", "aq1", "aq2", "as1", "as2", "lp1", "lp2", "lq1", "lq2", "ls1", "ls2"]
-FUSED = (1, 3, 5)
+DMAS = ["ld%d" % k for k in range(12) if k != 9] + ["ds%d" % k for k in range(4)]
+SEMAPHORES = ["qv", "qs", "qt", "qg"] + DMAS + [a + x + t for a in "al" for x in "pkqs" for t in "12"]
+FUSED = (1, 3, 6)
 VADD = 2
 DL = 2.0 ** -18
 B1, B2 = 49152, 98304
 WM, C0 = 760, 1304
-CYC, GATHER, SCATTER, WAKE = 0.83e-3, 1.56, 3.8, 0.15
-AHEAD, PASSES = (0.7, 1.0, 1.5, 2.5), 4
-FLY, LOAD, NEXT, EARLY = 1.3, 2.5, 0.9, 8.0
-ORDER = list(range(0, 32, 4))
-NEEDS_V = (4, 5)
+CYC, GATHER, SCATTER, WAKE = 0.83e-3, 1.4, 3.8, 0.22
+AHEAD, PASSES, SLACK, LAZY, SHAKE = (1.0, 1.5, 2.0), 5, 2.0, 0.6, 3.0
+TRIES, STRETCH, SFIX = 1300, 1.5, 0.05
+OTHERS = ((0.17, 1.25), (0.27, 0.85))
+FLY, LOAD, NEXT, LATE, EARLY = 1.3, 1.3, 1.25, 0.3, 8.0
+HIGH, HALF, PFIX = (5, 3), (True, True), 0.01
+STORE = 1000.0
+CUTS = (0, 512, 1536, 2560, 3584, 4096)
+NEEDS_V = {4: 2, 5: 4}
 SIZE = {H: 2, F: 4, I: 4, U: 2}
 
 
@@ -157,11 +170,19 @@ def _schedule(prog):
         ready = set(i for i in range(n) if not left[i])
         free, bank, queue, order, done = {}, {}, {}, [], [0.0] * n
 
+        met = {}
+
         def start(i, q):
-            s = max([0.0] + [t + (0.0 if q == q2 == "t" else WAKE) for q2, t in at[i].items()]) + (prog[i]["lat"] if back else 0.0)
-            s = max(s, free.get(q, 0.0) if q != "x" else 0.0)
+            s = met.get((i, q))
+            if s is None:
+                s = met[(i, q)] = max([0.0] + [t + (0.0 if q == q2 == "t" else WAKE) for q2, t in at[i].items()]) + (prog[i]["lat"] if back else 0.0)
+            f = free.get(q, 0.0) if q != "x" else 0.0
+            if f > s:
+                s = f
             for b in prog[i]["P"]:
-                s = max([s] + [t + WAKE for q2, t in bank.get(b, {}).items() if q2 != q])
+                for q2, t in bank.get(b, {}).items():
+                    if q2 != q and t + WAKE > s:
+                        s = t + WAKE
             return s
 
         fifo = {q: [i for i in range(n) if q in prog[i]["cost"]][::-1 if back else 1] for q in ("g", "y")}
@@ -173,7 +194,7 @@ def _schedule(prog):
             q = min(first, key=lambda x: first[x])
             _, i, s = min((-rank[i], i, s) for s, i, q2 in c if q2 == q and s <= first[q] + 0.03)
             for s2, i2, q2 in c:
-                if q2 == q and rank[i2] > rank[i] and s + prog[i]["cost"][q] - s2 > ahead * (s2 - first[q]):
+                if q2 == q and rank[i2] > rank[i] and s + prog[i]["cost"][q] - s2 > (ahead if rank[i2] < rank[i] + SLACK else LAZY) * (s2 - first[q]):
                     i, s = i2, s2
             ready.discard(i)
             if q in fifo:
@@ -195,15 +216,41 @@ def _schedule(prog):
     best = None
     const = []
     for i in range(n):
-        const.append(prog[i]["sem"] is None and all(const[j] for j in deps[i]))
+        const.append(prog[i]["sem"] is None and min(prog[i]["cost"].values()) < 1.0 and all(const[j] for j in deps[i]))
+
+    def replay(order, queue, wake, slow):
+        free, bank, done = {}, {}, [0.0] * n
+        for i in order:
+            q = queue[i]
+            s = max([free.get(q, 0.0) if q != "x" else 0.0] + [done[j] + (0.0 if q == queue[j] == "t" else wake) for j in deps[i]])
+            for b in prog[i]["P"]:
+                s = max([s] + [t + wake for q2, t in bank.get(b, {}).items() if q2 != q])
+            free[q] = s + prog[i]["cost"][q] * (slow if prog[i].get("by index") else 1.0)
+            done[i] = free[q] + prog[i]["lat"]
+            for b in prog[i]["P"]:
+                bank.setdefault(b, {})[q] = free[q]
+        return max(done)
+
+    def forward(urge, ahead):
+        top = max(urge) - EARLY
+        fw = one(deps, nxt, [max(u, top) if c else u for u, c in zip(urge, const)], None, ahead)
+        return (fw[0] + sum(replay(fw[1], fw[2], w, x) for w, x in OTHERS), fw[1], fw[2], fw[3], urge, ahead)
+
     for ahead in AHEAD:
         urge = rank
-        for _ in range(PASSES):
-            fw = one(deps, nxt, [max(u, max(urge) - EARLY) if c else u for u, c in zip(urge, const)], None, ahead)
+        for k in range(PASSES):
+            fw = forward(urge, ahead)
             if best is None or fw[0] < best[0]:
                 best = fw
             urge = one(nxt, deps, fw[3], fw[2], ahead)[3]
-    return best[1], best[2], deps
+    shake = np.random.default_rng(1)
+    for k in range(TRIES):
+        at = float(shake.uniform(0.0, max(best[3])))
+        noise = shake.uniform(-SHAKE, SHAKE, n) * shake.uniform(0.05, 1.0) * (shake.uniform(0.0, 1.0, n) < shake.uniform(0.1, 1.0))
+        fw = forward([u + (float(x) if abs(d - at) < STRETCH else 0.0) for u, x, d in zip(best[4], noise, best[3])], best[5])
+        if fw[0] <= best[0]:
+            best = fw
+    return best[1], best[2], deps, best[3]
 
 
 PLANNED = {}
@@ -249,18 +296,20 @@ def rank_program(g, core, T, topo):
         cost = {}
         for q in fns:
             if kind == "mm":
-                c = max(64, ins[1][2]) * CYC * len(ins) / 2
+                c = max(64, ins[1][2]) * CYC * len(ins) / 2 * (4 if ins[0][3] == 4 else 1)
             elif kind in ("dma", "g"):
                 c = 0.05 if kind == "dma" else 0.15 + 2 * n * CYC
             elif any(x[5] for x in sides):
                 c = (0.05 if q == "v" else 0.065) + n * CYC * (SCATTER if out[5] else GATHER)
+            elif q == "s":
+                c = SFIX + n * CYC
             elif kind == "tt":
                 c = max(64, n * (1 if any(x[4] for x in ins) else 2)) * CYC
             else:
                 c = max(64, n * (0.5 if q == "v" and kind == "ts" and all(x[3] == 2 for x in sides if x[2] > 1) else 1)) * CYC
-            cost[q] = c
+            cost[q] = c + (PFIX if q in "vs" and any(x[4] for x in sides) else 0.0)
         prog.append({"kind": "op", "fn": fns, "R": reads, "W": list(out[1]) + list(Wr), "P": sorted(set(x[1][0][0] for x in sides if x[4])),
-                     "sem": sem, "inc": inc, "cost": cost, "lat": lat})
+                     "sem": sem, "inc": inc, "cost": cost, "lat": lat, "by index": any(x[5] for x in sides)})
 
     def ts_fn(out, a, s1, o0, s2, o1):
         if o1 is None:
@@ -331,16 +380,25 @@ def rank_program(g, core, T, topo):
         rec({q: lambda e: e.dma_start(out[0], src)}, out, [], "dma", "ld%d" % k, 16, lat)
 
     def store(q, k, dst, src):
-        rec({q: lambda e: e.dma_start(dst, src[0])}, (None, [("out%d" % k, 1)], 1, 4, False, None), [src], "dma", "ds%d" % k, 16, 2.0 + src[2] * src[3] / 1200)
+        rec({q: lambda e: e.dma_start(dst, src[0])}, (None, [("out%d" % k, 1)], 1, 4, False, None), [src], "dma", "ds%d" % k, 16, 2.0 + src[2] * src[3] / STORE)
 
-    def send(name, out, src, go, lat):
+    def send(name, moves, go, lat):
         dst = T.cores[(rank + go) % N]
         rid, pid, _ = topo.addr(dst)
-        fn = lambda: g.remote_dma(out[0], src[0], T.sem["a" + name], T.sem["l" + name], pid, rid, topo.mask(core, dst))
-        prog.append({"kind": "send", "fn": fn, "R": src[1], "W": [("sent" + name, 1)], "P": [], "sem": "l" + name,
-                     "inc": len(topo.engines(core, dst)), "cost": {"g": 0.5}, "lat": 0.0})
-        prog.append({"kind": "lands", "fn": None, "R": [("sent" + name, 1)], "W": out[1], "P": [], "sem": "a" + name,
-                     "inc": len(topo.engines(T.cores[(rank - go) % N], core)), "cost": {"x": lat}, "lat": 0.0})
+        eng = topo.engines(core, dst)
+        if len(moves) == 1:
+            (out, (src,)), n = moves[0], len(eng)
+            fn = lambda: g.remote_dma(out[0], src[0], T.sem["a" + name], T.sem["l" + name], pid, rid, topo.mask(core, dst))
+        else:
+            k = len(eng) // len(moves)
+            n = k * len(moves)
+            fn = lambda: g.remote_dma_fused([RemoteDMATransfer(dst_ids=[DstId(rid=rid, pnc=pid)], dma_engine_mask=sum(1 << x for x in eng[j * k:j * k + k]),
+                                                               remote_sem=T.sem["a" + name], srcs=[x[0] for x in srcs], dsts=[out[0]], alu_op=int(len(srcs) > 1))
+                                             for j, (out, srcs) in enumerate(moves)], local_sem=T.sem["l" + name])
+        prog.append({"kind": "send", "fn": fn, "R": [k for _, srcs in moves for x in srcs for k in x[1]], "W": [("sent" + name, 1)], "P": [],
+                     "sem": "l" + name, "inc": n, "cost": {"g": 0.5}, "lat": 0.0})
+        prog.append({"kind": "lands", "fn": None, "R": [("sent" + name, 1)], "W": [k for out, _ in moves for k in out[1]], "P": [], "sem": "a" + name,
+                     "inc": n, "cost": {"x": lat}, "lat": 0.0})
 
     def lanes(name, h, a=0):
         return v(name, a + h, a + 256, 8)
@@ -348,34 +406,32 @@ def rank_program(g, core, T, topo):
     def IS(k):
         return v("IS", k * 128, k * 128 + 128)
 
-    for k in range(4):
-        load("y", 4 + k, v("E", k * 1024, k * 1024 + 1024), T.eff[:, k * 1024:k * 1024 + 1024], LOAD + NEXT * k)
-    load("y", 0, v("craw"), T.act[:, :], LOAD + NEXT * 4)
-    load("y", 2, v("sc0"), T.st0[:, :], LOAD + NEXT * 4)
-    for k in range(4):
-        load("y", 8 + k, v("PT", k * 1024, k * 1024 + 1024), T.req[:, k * 1024:k * 1024 + 1024], LOAD + NEXT * (5.5 + k))
-    load("y", 1, v("wi"), T.why[:, :], LOAD + NEXT * 10)
-    load("y", 3, v("bari"), T.bar[:, :], LOAD + NEXT * 10)
+    for k, (a, b) in enumerate(zip(CUTS, CUTS[1:])):
+        load("y", 4 + k, v("E", a, b), T.eff[:, a:b], LOAD + NEXT * b / 1024)
+    load("y", 0, v("KW0", 520, 776), T.act[:, :], LOAD + NEXT * 4.5)
+    load("y", 2, v("sc0"), T.st0[:, :], LOAD + NEXT * 4.7)
+    for k in range(2):
+        load("y", 10 + k, v("PT", k * 2048, k * 2048 + 2048), T.req[:, k * 2048:k * 2048 + 2048], LOAD + NEXT * (6.7 + 2 * k) + LATE)
+    load("y", 1, v("wi"), T.why[:, :], LOAD + NEXT * 10 + LATE)
+    load("y", 3, v("bari"), T.bar[:, :], LOAD + NEXT * 10 + LATE)
 
     ID, ONE, G8 = v("ID"), v("ONE"), v("G8")
     fill(ONE, 1.0)
     gp(lambda e: e.affine_select(ID[0], ONE[0], [[-1, 128]], A.is_equal, 0.0, 0, 1), ID, [ONE])
     gp(lambda e: e.affine_select(G8[0], v("ONE", 0, 8)[0], [[-16, 8]], A.is_ge, 0.0, 0, 1), G8, [ONE])
     gp(lambda e: e.affine_select(G8[0], G8[0], [[16, 8]], A.is_ge, 0.0, 15, -1), G8, [G8])
+    gp(lambda e: e.affine_select(v("LT")[0], ONE[0], [[0, 8], [-1, 16]], A.is_equal, 0.0, 0, 1), v("LT"), [ONE])
+    iota(v("kc"), [[1, 32]], 0, 0)
     iota(v("pi"), [[0, 8]], 0, 1)
     iota(v("C32"), [[16, 8]], 0, 0)
-    iota(v("Kf"), [[-4096, 256]], -4096, 0)
-    iota(v("KQf"), [[-8192, 32], [0, 8]], -8192, 0)
-    iota(v("kc"), [[1, 32]], 0, 0)
     iota(v("kc1"), [[1, 32]], 1, 0)
     iota(v("KAP"), [[113, 32]], 37, 0)
     iota(v("K2c"), [[-64, 32], [0, 8]], 31 * 64, 0)
-    fill(v("SEL2"), 0.0)
+    fill(v("K2c", 0, 256, 1, 64), -33024.0 * 128)
     fill(v("FL", W, W + B), B2 * DL)
     fill(v("ONES32"), 1 / 128)
     fill(v("sp", 0, 8), 1 / 128)
-    for x in (v("KW0", 768, 776), v("ZO0", 512, 520), v("ZO1", 512, 520)):
-        fill(x, 0)
+    fill(v("C192"), 192.0)
     fill(v("SCM"), 10000.0)
     fill(v("SCM", 0, 128, 16), -10000.0)
     fill(v("SCZ"), 1.0)
@@ -383,41 +439,56 @@ def rank_program(g, core, T, topo):
     fill(v("CW"), -784.0)
     fill(v("M130"), -130.0)
     fill(v("THR"), -1.5 * 8)
-    fill(v("K2c", 0, 256, 1, 64), -32000.0 * 128)
+    fill(v("O264"), 1.0)
+    fill(v("RST"), 0.0)
+    fill(v("RST", 32, 264, 33), 64.0)
+    iota(v("kneg"), [[0, 8], [-1, 33]], 0, 0)
     slope = -(2 * WM + 20) / ((B2 - B1 + 256) * DL)
-    for k, w in enumerate((-7.5, 128.5, 1.0, WM + 12 - slope * (B1 - 256) * DL, 0.0)):
+    for k, w in enumerate((-7.5, 128.5, 1.0, WM + 12 - slope * (B1 - 256) * DL, 0.0, -133.5, -141.5)):
         fill(col("SG", k), w)
-    for k, w in enumerate((-1.0, 6.0, 8.0, 64.0, 1 / DL, -1 / DL, -3 / 32 / DL)):
+    for k, w in enumerate((-1.0, 6.0, 8.0, 64.0, 1 / DL, -1 / DL, -3 / 32 / DL, -2.0, -2.0 ** 23, 2.0 ** 17, -2.0 ** 17, 58.0)):
         affine(IS(k), ID, w)
-    for k in range(16):
-        affine(v("SEL2", k * 128 + k, k * 128 + 128, 16), G8, 2.0 ** 13)
-    affine(v("G82"), G8, 2.0)
+    for j in range(2):
+        affine(v("G82", j, 8, 2), v("G8", 4 * j, 4 * j + 4), 2.0)
     affine(v("G8B", 0, 8), G8, 2.0 ** 20)
     affine(v("G8B", 8, 16), G8, -2.0 ** 20)
-    for k, (w, a, b) in enumerate(((-1.0, 528, 0), (-128.0, 16, 0), (-8.0, 1, 8))):
-        affine(v("G83", 8 * k, 8 * k + 8), G8, w)
-        affine(v("HR", 8 * k, 8 * k + 8), v("kc", 0, 8), a / 128, b / 128)
-    affine(v("HR", 24, 32), v("kc", 0, 8), 1 / 128)
-    affine(v("kneg"), v("kc"), -1.0)
+    o = 0
+    for w, a, b, hs in ((-1.0, 528, 0, (0, 1)), (-128.0, 16, 0, (0, 0, 1, 1)), (-8.0, 1, 8, None), (1.0, 0, 0, None)):
+        for x in [(j, 8, 2) for j in hs] if hs else [(0, 8, 1)]:
+            n = 8 // x[2]
+            affine(v("G83", o, o + n), v("G8", *x), w)
+            affine(v("HR", o, o + n), v("kc", *x), a / 128, b / 128)
+            o += n
+    affine(v("HR", 40, 48), v("kc", 0, 8), 1 / 128)
     ts(v("pb"), v("pi"), 15, A.bitwise_and)
-    ts(col("lc", 0), col("pb", 0), 33.0, A.mult)
-    cp(col("lc", 1), col("pb", 0))
+    fill(v("LC"), 0.0)
+    ts(v("LC", 0, 8), v("pb"), 32.0, A.mult)
+    for a in (8, 16, 40):
+        cp(v("LC", a, a + 8), v("pb"))
     tt(v("C32"), v("C32"), v("pb"), A.add)
-    affine(v("Cv"), v("kc", 0, 8), 528.0, -1.0)
     affine(v("C32"), v("C32"), 32.0)
-    affine(v("ps6", 0, 256), v("Kf"), 1.0)
-    affine(v("ps6", 256, 512), v("KQf"), 1.0)
-    ts(v("barf"), v("bari"), 16.0, A.add)
-    tt(v("DM", 0, 64), v("ID", 0, 64), v("ID", 64, 128), A.add)
-    tt(v("DM", 64, 96), v("DM", 0, 32), v("DM", 32, 64), A.add)
-    tt(v("MK16", 0, 16), v("DM", 64, 80), v("DM", 80, 96), A.add)
-    for h in range(8):
-        affine(v("DM", 16 * h, 16 * h + 16), v("MK16", 0, 16), 1.0)
+    affine(v("ID32"), ID, 1.0)
+    ts(v("barf"), v("bari"), 16.0, A.add, 2.0 ** 17, A.mult)
+    mms(v("ps3", 0, 128), [(v("LT"), v("LT"))])
+    act(v("DM"), v("ps3", 0, 128), ACT.Identity)
 
-    cp(v("pl0"), v("craw"))
-    tt(v("KW0", 256, 512), v("craw"), v("ps6", 0, 256), A.add)
-    ts(v("KW0", 512, 768), v("wi"), 1.0, A.add)
-    tt(v("KW0", 776, 1032), v("KW0", 512, 768), v("ps6", 256, 512), A.add)
+    cp(v("pl0"), v("KW0", 520, 776))
+    iota(v("al"), [[-4096, 256]], -4096, 0)
+    iota(v("Dc"), [[-8192, 32], [0, 8]], -8192, 0)
+    Kc, KQc = v("ps5", 256, 512), v("ps6", 0, 256)
+    act(Kc, v("al"), ACT.Identity)
+    act(KQc, v("Dc"), ACT.Identity)
+    tt(v("KW0", 256, 512), v("KW0", 520, 776), Kc, A.add)
+    ts(v("KW0", 776, 1032), v("wi"), 1.0, A.add)
+    tt(v("KW0", 1040, 1296), v("KW0", 776, 1032), KQc, A.add)
+    for t in range(VI):
+        fill(v("KW%d" % t, 512, 520), 0)
+    iota(v("SEL2"), [[0, 2048]], 0, 0)
+    prog[-1]["lat"] = 4.0
+    for k in range(16):
+        affine(v("SEL2", k * 128 + k, k * 128 + 128, 16), G8, 2.0 ** 13, None, "s")
+    iota(v("Kf"), [[-4096, 256]], -4096, 0)
+    iota(v("KQf"), [[-8192, 32], [0, 8]], -8192, 0)
 
     def classes(u, w, f, e, off):
         ts(u, e, 4.0 + off, A.is_ge, -1 / DL, A.mult)
@@ -435,7 +506,8 @@ def rank_program(g, core, T, topo):
             act(p, v("E", a, b), ACT.Identity, None, -252.0)
             tt(v("TT", a, b), v("D1", a, b), p, A.add)
     for k in range(4):
-        ts(v("ND", k * 1024, k * 1024 + 1024), v("PT", k * 1024, k * 1024 + 1024), 12.0, A.is_lt)
+        for a in (k * 1024, k * 1024 + 512):
+            affine(v("ND", a, a + 512), v("PT", a, a + 512), -1.0, 2083.5)
 
     def rows(dst, sel, src, a, n, first):
         mms(dst, first, [(v(sel, k * 128, k * 128 + 128), v(src, a + k, a + n, 16)) for k in range(16)])
@@ -449,78 +521,80 @@ def rank_program(g, core, T, topo):
         affine(X0, v("sg0"), 64 * DL, -192 * DL)
         for k in range(32):
             affine(v("D1", k + 1, None, 33), ind(v("TT"), v(pl, k * 8, k * 8 + 8)), DL, 4 * min(k, 30) * DL)
-        for c in range(8):
-            affine(v("Gn", c * 512, c * 512 + 512), ind(v("ND"), v(pl, c * 32, c * 32 + 32)), (B2 - B1) * DL, B1 * DL, "v" if c in NEEDS_V else "s")
         scan(v("V0"), v("D1"), v("D1"), 0.0, A.mult, A.min)
-        group([(v("ps0", 0, 256), ONE, v("THR"))], True, False, "a")
-        for a in ORDER:
-            group([(v("ps0", k * 8, k * 8 + 8), v("Gn", k * 128, k * 128 + 128), v("G8B", 0, 8)) for k in range(a, a + 4)], False, False, "b")
-        for a in ORDER:
+        group([(v("ps0", 0, 264), ONE, v("RST")), (v("ps0", 0, 264), ONE, v("THR"))], True, False, "a")
+        for c in range(8):
+            a = 4 * c
+            affine(v("Gn", c * 512, c * 512 + 512), ind(v("ND"), v(pl, c * 32, c * 32 + 32)), (B2 - B1) / 16 * DL, (B1 - 129 * (B2 - B1)) * DL, "v" if c in NEEDS_V else "s")
+            if c in NEEDS_V:
+                prog[-1]["R"] += v("FL", 0, NEEDS_V[c] * 512)[1]
+            group([(v("ps0", k, 264, 33), v("Gn", k * 128, k * 128 + 128), v("G8B", 0, 8)) for k in range(a, a + 4)], False, False, "b")
             for k in range(a, a + 4):
                 scan(v("FL", k * 128, k * 128 + 128), v("V0", k, None, 33), v("Gn", k * 128, k * 128 + 128), 1.0, A.min, A.add)
-            group([(v("ps0", k * 8, k * 8 + 8), v("FL", k * 128, k * 128 + 128), v("G8B", 8, 16)) for k in range(a, a + 4)],
-                  False, a == ORDER[-1], "c" if a == ORDER[-1] else "b")
+            group([(v("ps0", k, 264, 33), v("FL", k * 128, k * 128 + 128), v("G8B", 8, 16)) for k in range(a, a + 4)], False, c == 7, "c" if c == 7 else "b")
         if last:
-            rec({"y": lambda e: e.dma_start(T.E2[:, :], T.E[:, :])}, v("E2"), [v("E"), v(pl)], "dma", "ds3", 16, 8.0)
+            rec({"y": lambda e: e.dma_start(T.E2[:, :], T.E[:, :])}, v("E2"), [v("E"), v(pl)], "dma", "ds3", 16, 9.0)
 
         def turn(out, src, a, step, rhs, const):
             for h in range(8):
-                affine(v("LT", h * 16, h * 16 + 16), v("MK16", 0, 16), col(src, a + h * step))
-            mms(out, [(ONE, const), (v("LT"), rhs)])
+                affine(v("LT", h * 16, h * 16 + 16), v("DM", 0, 16), col(src, a + h * step))
+            mms(out, const + [(v("LT"), rhs)])
 
-        def pick(out, lst):
-            tt(v("kd"), ind(v(KW, 248, 520), lst), v("DM"), A.mult)
-            scan(v(out), v("SCZ"), v("kd"), 0.0, A.mult, A.add)
+        def pick(out, win, lst, mask):
+            tt(v("k" + out), ind(win, lst), v(mask), A.mult)
+            scan(v(out), v("SCZ"), v("k" + out), 0.0, A.mult, A.add)
             return v(out, 15, None, 16)
 
-        for h in range(8):
-            scan(lanes("xs", h), v("ps0", 248 + h, None, -8), v("kneg", 31, None, -1), -32.0, A.max, A.min)
-        turn(v("ps4", 256, 280), "xs", 248, 1, v("G83"), v("HR", 0, 24))
-        ts(v("ou", 0, 8), v("ps4", 256, 264), col("lc", 0), A.add)
-        ts(v("ou", 8, 16), v("ps4", 264, 272), col("lc", 1), A.add)
-        cp(v("ou", 24, 32), v("ps4", 272, 280))
-        tt(v("xr"), v("Cv"), v("ps4", 256, 264), A.subtract)
+        scan(v("xs", 263, None, -1), v("ps0", 263, None, -1), v("kneg", 263, None, -1), 0.0, A.max, A.min)
+        turn(v("ps4", 400, 440), "xs", 0, 33, v("G83"), [(ONE, v("HR", 0, 40)), (ID, v("LC", 0, 40)), (ID, v("LC", 40, 80))])
+        cp(v("ou", 0, 32), v("ps4", 400, 432))
+        affine(v("xn"), v("ps4", 432, 440), 1.0)
         affine(v("vx"), ind(v("V0"), v("ou", 0, 8)), 1 / DL, 1022.5, "v")
-        act(v("wm"), ind(v("FL"), v("ou", 8, 16)), ACT.Abs, slope, col("SG", 3))
+        for a in (64, 0, 192):
+            n = 128 if a == 64 else 64
+            act(v("wm", a, a + n), ind(v("FL"), v("ou", 8 + a // 16, 8 + (a + n) // 16)), ACT.Abs, slope, col("SG", 3))
         r = v(KW, 248, 256)
-        rx = pick("rx", v("ou", 24, 32))
+        rx = pick("rx", v(KW, 248, 520), v("ou", 24, 32), "DM")
         cp(r, rx)
-        ts(v("sx"), rx, 4095, A.bitwise_and)
+        sx = v(KW, 512, 520)
+        ts(sx, rx, 4095, A.bitwise_and)
+        cp(v("sxf"), sx)
+        for h in range(8):
+            affine(v("DX", h * 16, h * 16 + 16), v("DM", 0, 16), col("sxf", h))
 
         DT, D8 = v("ps2", 0, 128), v("ps2", 128, 136)
-        mms(DT, [(v("CW"), IS(3)), (v("wm"), IS(3)), (v("vx"), ID)])
+        mms(DT, [(v("CW"), IS(3)), (v("wm", 64, 192), IS(3)), (v("vx"), ID)])
         scan(v("RM"), v("SCM"), DT, 0.0, A.min, A.max)
-        turn(D8, "RM", 15, 16, v("G82"), v("HR", 24, 32))
-        cp(v("ou", 16, 24), D8)
-        rd = pick("rd", v("ou", 16, 24))
+        turn(D8, "RM", 15, 16, v("G82"), [(ONE, v("HR", 40, 48))])
+        cp(v("ou", 32, 40), D8)
+        pr0 = pick("rp", v(KW, 512, 776), v("ou", 32, 40), "DX")
+        rd = pick("rd", v(KW, 248, 512), v("ou", 32, 40), "DM")
         ts(v("sd"), rd, 4095, A.bitwise_and)
         ts(v("dq"), rd, 15, A.arith_shift_right)
-        cp(v("sxf"), v("sx"))
-        for k in range(4):
-            act(v("W4", k * 128, k * 128 + 128), v("wm"), ACT.Identity, None, C0 + 0.5)
+        for j in set(c // 4 for c in FUSED):
+            for k in range(4):
+                act(v("W4", j * 512 + k * 128, j * 512 + k * 128 + 128), v("wm", j * 128, j * 128 + 128), ACT.Identity, None, C0 + 0.5)
 
-        tt(v("pr0"), v("sx"), v("sd"), A.mult)
-        ts(v("bs"), v("pr0"), 5, A.arith_shift_right)
+        ts(v("bs"), pr0, 5, A.arith_shift_right)
         ts(v("bsf"), v("bs"), 97.0 * t, A.add)
-        for h in range(8):
-            ts(lanes("craw", h), v("KAP"), col("sxf", h), A.mult, col("bsf", h), A.add)
-        for a in (0, 128):
-            ts(v("cm", a, a + 128), v("craw", a, a + 128), 4095, A.bitwise_and)
-            cp(v("cu", a, a + 128), v("cm", a, a + 128))
-        ts(v("cmZ"), v("cm"), -2.0 ** 23, A.add)
+        for j in range(2):
+            for h in range(j, 8, 2):
+                ts(lanes("craw", h), v("KAP"), col("sxf", h), A.mult, col("bsf", h), A.add)
+            ts(v("cm", j, 256, 2), v("craw", j, 256, 2), 4095, A.bitwise_and)
+            cp(v("cu", j * 128, j * 128 + 128), v("cm", j, 256, 2))
         for c in range(8):
-            a, src = c * 512, ind(v("E"), v("cu", c * 32, c * 32 + 32))
+            a, j, src = c * 512, c // 4, ind(v("E"), v("cu", c * 32, c * 32 + 32))
             if c in FUSED:
-                tt(v("FL", a, a + 512), src, v("W4"), A.add)
+                tt(v("FL", a, a + 512), src, v("W4", j * 512, j * 512 + 512), A.add)
             else:
                 affine(v("EC", a, a + 512), src, 1.0, C0 + 0.5, "s")
                 for k in range(a, a + 512, 128):
-                    scan(v("FL", k, k + 128), v("EC", k, k + 128), v("wm"), 4000.0, A.min, A.add)
+                    scan(v("FL", k, k + 128), v("EC", k, k + 128), v("wm", j * 128, j * 128 + 128), 4000.0, A.min, A.add)
             if c % 2:
-                x = (c // 2) * 64
-                cn = v("ps%d" % (c // 2 % 2), 256 + x, 320 + x)
-                rows(cn, "SEL2", "FL", a - 512, 1024, [(ONE, v("K2c", x, x + 64))])
-                tt(v("key", x, x + 64), v("cmZ", x, x + 64), cn, A.add)
+                x = (c // 2 % 2) * 128 + j
+                cn = v("ps%d" % (c // 2 % 2), 256 + j * 64, 320 + j * 64)
+                rows(cn, "SEL2", "FL", a - 512, 1024, [(ONE, v("K2c", x, x - j + 128, 2))])
+                tt(v("key", x, x - j + 128, 2), v("cm", x, x - j + 128, 2), cn, A.add)
 
         act(v("r4"), V32, ACT.Identity, 1 / DL, 1022.5)
         act(v("sgn"), V32, ACT.Sign, 1 / DL, col("SG", 1))
@@ -533,7 +607,7 @@ def rank_program(g, core, T, topo):
         mms(v("ps3", 256, 384), [(IS(4), V32), (IS(0), v("r4")), (IS(1), v("sgn")), (IS(2), v("iseq")), (ID, v("prw"))])
         act(sv, v("ps3", 256, 384), ACT.Identity, None, 1030.0)
         if not last:
-            send("s%d" % (t + 1), v("sc%d" % (t + 1)), sv, STATE_GO, 2.0)
+            send("s%d" % (t + 1), [(v("sc%d" % (t + 1)), [sv])], STATE_GO, 2.0)
         for a in range(0, 16, 4):
             group([(v("ps3", 384, 392), v("SEL2", k * 128, k * 128 + 128), v("so%d" % t, k, 128, 16)) for k in range(a, a + 4)], a == 0, a == 12)
         ts(v("ui"), v("ps3", 384, 392), 2.0 ** -13, A.mult)
@@ -546,92 +620,109 @@ def rank_program(g, core, T, topo):
         if last:
             store("y", 0, T.ye[:, :], v("E2"))
         else:
-            classes(v("eu"), v("ew"), v("ef"), v("eb"), 130)
-            act(v("ea"), v("eb"), ACT.Identity, None, -382.0)
-            tt(ind(v("TT"), v("uu")), v("ea"), v("ef"), A.add)
+            act(v("eu"), v("eb"), ACT.Sign, None, col("SG", 5))
+            act(v("ew"), v("eb"), ACT.Sign, None, col("SG", 6))
+            mms(v("ps1", 0, 128), [(IS(9), v("eu")), (IS(10), v("ew")), (IS(11), v("ew")), (ID, v("eb"))])
+            act(v("ea"), v("ps1", 0, 128), ACT.Identity, None, -324.0)
+            cp(ind(v("TT"), v("uu")), v("ea"))
 
-        ts(v("fnd"), v("xr"), -32.0, A.is_ge, 2.0 ** 17, A.mult)
-        tt(v("barK"), v("barf"), v("fnd"), A.mult)
+        affine(v("fnd"), v("xn"), 2.0 ** 23, 2.0 ** 28, "s")
+        tt(v("barK"), v("barf"), v("fnd"), A.min)
         cp(v("dp1"), v("dq"))
         ts(v("sd1"), v("sd"), 1.0, A.add)
-        ts(v("xn"), v("xr"), 1.0, A.add)
-        ts(v("xh"), v("xr"), -1.0, A.mult, -1.5, A.add)
-        ts(v("x40"), v("xr"), -1.0, A.mult, -41.0, A.add)
+        affine(v("xh"), v("xn"), -1.0, -0.5, "s")
+        affine(v("x40"), v("xn"), -1.0, -40.0, "s")
         for h in range(8):
             act(lanes("sg1", h), v("kc"), ACT.Sign, -1.0, col("xh", h))
             out = lanes("ps2", h, 256)
             rec({"s": act_fn(out, v("kc1"), ACT.Abs, None, col("dp1", h)), "v": ts_fn(out, v("kc1"), col("dp1", h), A.add, 0.0, A.not_equal)},
                 out, [v("kc1"), col("dp1", h)], "act")
-            ts(lanes("e2p", h), lanes(KW, h, 512), col("sd1", h), A.not_equal, 1 / 128, A.mult)
+            ts(lanes("e2p", h), lanes(KW, h, 776), col("sd1", h), A.not_equal, 1 / 128, A.mult)
         act(v("ps7", 0, 256), v("sg1"), ACT.Relu)
         tt(v("kept"), v("e2p"), v("ps2", 256, 512), A.min)
         for h in range(8):
             scan(lanes("sp", h, 8), v("ONES32"), lanes("kept", h), 1 / 128, A.add, A.subtract)
         tt(v("Dc"), v("sp", 0, 256), v("ps7", 0, 256), A.add)
-        ts(v("n40"), v("sp", 256, 264), 128.0, A.mult, 7.0, A.add)
-        for h in range(8):
-            red(col("MBi", h), lanes("key", h), A.max)
-        tt(v("ret"), v("MBi"), v("barK"), A.is_lt)
-        tt(v("nr"), v("MBi"), v("barK"), A.is_ge)
-        affine(v("mul"), v("ret"), 127.0, 1.0)
-        for h in range(8):
-            ts(lanes("Dz", h), lanes("Dc", h), col("mul", h), A.mult)
-        ts(v("cb"), v("MBi"), 4095, A.bitwise_and)
-        ts(v("v1"), v("cb"), -2.0 ** 23, A.add)
-        tt(v("v2"), v("v1"), v("nr"), A.mult)
-        tt(v("v3"), v("x40"), v("ret"), A.mult)
-        tt(v("mid"), v("v3"), v("xn"), A.add)
-        tt(v("v4"), v("n40"), v("ret"), A.mult)
-        affine(v("rad"), v("v4"), 1.0, 0.5)
-        tt(v("v5"), v("sd1"), v("nr"), A.mult)
-        affine(v("vq"), v("v5"), 1.0, -2.0 ** 23)
-        Fp = v("ps4", 0, 256)
-        for h in range(8):
-            act(lanes("far", h), v("kc"), ACT.Abs, None, col("mid", h))
-            act(lanes("sg1", h), lanes("far", h), ACT.Sign, -1.0, col("rad", h))
-            act(lanes("al", h), lanes("cmZ", h), ACT.Identity, col("ret", h), col("v2", h))
-        act(Fp, v("sg1"), ACT.Relu)
-        tt(v("ps2", 0, 256), v("al"), Fp, A.mult)
-        for h in range(8):
-            act(lanes("ps1", h, 256), lanes("ps4", h), ACT.Identity, col("vq", h))
-        for b in (5, 0, 1, 2, 3, 4):
-            s = 8 << b
-            m = 264 - s
-            tb = v("tb", b * 256, b * 256 + m)
-            ts(tb, v("Dz", s - 8, 256), b, A.arith_shift_right, 1, A.bitwise_and)
-            for a, mv in ((248, v("ps5", 0, m)), (768, v("ps7", 256, 256 + m))):
-                if b == 5:
-                    scan(v(KW, a, a + m), tb, v(KW, a + s, a + 264), 0.0, A.max, A.mult)
+        affine(v("n40"), v("sp", 256, 264), 128.0, 7.0)
+        nS, nQ = v(ZO, 264, 520), v(ZO, 520, 776)
+
+        def whole(name, a, n):
+            return v(name, a, a + n)
+
+        for j in range(2):
+            hs = range(j, 8, 2)
+
+            def u(name, a=0, n=8):
+                return v(name, a + j, a + n, 2)
+
+            for h in hs:
+                red(col("MBi", h), lanes("key", h), A.max)
+            tt(u("ret"), u("MBi"), u("barK"), A.is_lt)
+            tt(u("nr"), u("MBi"), u("barK"), A.is_ge)
+            affine(u("mul"), u("ret"), 127.0, 1.0)
+            for h in hs:
+                ts(lanes("Dz", h), lanes("Dc", h), col("mul", h), A.mult)
+            tt(u("v2"), u("MBi"), u("nr"), A.mult)
+            tt(u("v3"), u("x40"), u("ret"), A.mult)
+            tt(u("mid"), u("v3"), u("xn"), A.add)
+            tt(u("v4"), u("n40"), u("ret"), A.mult)
+            affine(u("rad"), u("v4"), 1.0, 0.5, "s")
+            tt(u("v5"), u("sd1"), u("nr"), A.mult)
+            affine(u("vq"), u("v5"), 1.0, -2.0 ** 23, "s")
+            for h in hs:
+                act(lanes("far", h), v("kc"), ACT.Abs, None, col("mid", h))
+                act(lanes("sg2", h), lanes("far", h), ACT.Sign, -1.0, col("rad", h))
+                act(lanes("al", h), lanes("key", h), ACT.Identity, col("ret", h), col("v2", h))
+                act(lanes("ps3", h), lanes("sg2", h), ACT.Identity, -2.0 ** 23, col("vq", h))
+            mms(u("ps2", 0, 256), [(IS(8), ONE), (IS(8), u("sg2", 0, 256)), (v("ID32"), u("al", 0, 256))])
+            if HIGH[j] < 5:
+                for h in hs:
+                    act(lanes("Db", h), lanes("Dc", h), ACT.Identity, col("mul", h))
+                for b in range(HIGH[j], 6):
+                    act(u("fb", (b - 2) * 256, 256), u("Db", 0, 256), ACT.Identity, 0.5 ** b, 191.5 + 0.5 ** (b + 1))
+            for b in (5, 0, 1, 2, 3, 4):
+                s = 8 << b
+                m = 264 - s
+                tb, o = (("ps6", "ps6", "ps4")[b - 2], 256 * (b == 3)) if HIGH[j] <= b < 5 else ("tb", b * 256)
+                if tb != "tb":
+                    mms(u(tb, o, m), [(ID, v("C192", 0, m // 2)), (ID, u("fb", (b - 2) * 256 + s - 8, m)), (IS(7), u("fb", (b - 1) * 256 + s - 8, m))])
+                else:
+                    ts(u(tb, o, m), u("Dz", s - 8, m), b, A.arith_shift_right, 1, A.bitwise_and)
+                for a, mv, z, w in ((248, "ps5", 0, u if HALF[0] else whole), (1032, "ps7", 256, u if HALF[1] else whole)):
+                    if w is whole and j == 0:
+                        continue
+                    if b == 5:
+                        scan(w(KW, a, m), w(tb, o, m), w(KW, a + s, m), 0.0, A.max, A.mult)
+                    else:
+                        scan(w(mv, z, m), w(tb, o, m), w(KW, a + s, m), 0.0, A.max, A.mult)
+                        tt(w(KW, a, m), w(KW, a, m), w(mv, z, m), A.min)
+            for a, new, o, bits, w in ((248, "ps2", 264, 4095, u if HALF[0] else whole), (1032, "ps3", 520, 8191, u if HALF[1] else whole)):
+                if w is whole and j == 0:
                     continue
-                scan(mv, tb, v(KW, a + s, a + 264), 0.0, A.max, A.mult)
-                tt(v(KW, a, a + m), v(KW, a, a + m), mv, A.min)
-        tt(v(KW, 248, 504), v(KW, 248, 504), v("ps2", 0, 256), A.min)
-        ts(v("nS"), v(KW, 248, 504), 4095, A.bitwise_and)
-        tt(v(KW, 768, 1024), v(KW, 768, 1024), v("ps1", 256, 512), A.min)
-        nQ = v(ZO, 256, 512)
-        ts(nQ, v(KW, 768, 1024), 8191, A.bitwise_and)
+                tt(w(KW, a, 256), w(KW, a, 256), w(new, 0, 256), A.min)
+                ts(w(ZO, o, 256), w(KW, a, 256), bits, A.bitwise_and)
+                if not last and a == 248:
+                    cp(w("plo%d" % t, 0, 256), w(ZO, 264, 256))
         if not last:
-            cp(v("plo%d" % t), v("nS"))
-            send("p%d" % (t + 1), v("pl%d" % (t + 1)), v("plo%d" % t), PLAN_GO, FLY)
-            tt(v(ZO, 0, 256), v("nS"), v("ps6", 0, 256), A.add)
-            tt(v(ZO, 520, 776), nQ, v("ps6", 256, 512), A.add)
-            send("q%d" % (t + 1), v("KW%d" % (t + 1), 256, 1032), v(ZO), PLAN_GO, 3.5)
+            send("p%d" % (t + 1), [(v("pl%d" % (t + 1)), [v("plo%d" % t)])], PLAN_GO, FLY)
+            nx = "KW%d" % (t + 1)
+            send("k%d" % (t + 1), [(v(nx, 256, 512), [nS, v("Kf")]), (v(nx, 520, 776), [nS])], PLAN_GO, 6.0)
+            send("q%d" % (t + 1), [(v(nx, 776, 1032), [nQ]), (v(nx, 1040, 1296), [nQ, v("KQf")])], PLAN_GO, 6.0)
             cp(v("retb"), v("ret"))
             mms(col("ps3", 392), [], [(ONE, col("retb", h)) for h in range(8)])
             cp(col("ri", 0), col("ps3", 392))
             ts(col("ri", 1), col("ri", 0), 1, A.bitwise_and)
             ts(v("thr"), col("ri", 1), 1.5, A.add, -8.0, A.mult)
-            for a in (0, 128):
-                affine(v("THR", a, a + 128), ONE, v("thr"), None, "s")
+            affine(v("THR"), v("O264"), v("thr"), None, "s")
         else:
-            cp(v("ysw", 0, 256), v("nS"))
+            cp(v("ysw", 0, 256), nS)
             store("y", 1, T.ys[:, :], v("ysw", 0, 256))
             ts(v("ysw", 256, 512), nQ, -1.0, A.add)
             store("s", 2, T.yw[:, :], v("ysw", 256, 512))
 
     if not PLANNED:
         PLANNED["plan"] = _schedule(prog)
-    order, queue, deps = PLANNED["plan"]
+    order, queue, deps, done = PLANNED["plan"]
     tok = {}
     for i in order:
         e, q = prog[i], queue[i]

@@ -8,6 +8,7 @@ AX = AxisListType.X
 W, L, B, VI = 4096, 32, 128, 3
 PLAN_GO, STATE_GO = 3, 1
 H, F, I, U = "bfloat16", "float32", "int32", "uint16"
+BL = 33 * 16
 
 SCRATCH = {}
 PART = {}
@@ -15,7 +16,7 @@ PART = {}
 
 def _buf(dtype, n, *names):
     for x in names:
-        SCRATCH[x] = ("sbuf", [128, n], dtype)
+        SCRATCH[x] = ("sbuf", [128] + (list(n) if isinstance(n, tuple) else [n]), dtype)
 
 
 def _pool(name, dtype, n, *names):
@@ -24,63 +25,59 @@ def _pool(name, dtype, n, *names):
         PART[x] = (name, k * n, n)
 
 
-_buf(H, W, "E", "E2", "PT", "TT", "ND", "Gn", "EC")
-_buf(H, 33 * B, "D1", "V0", "FL")
+_buf(H, W, "E0", "E1", "E2", "PT", "TT", "EC", "FC")
+_buf(H, 8 * BL, "D1", "V0", "TM", "Gn", "FL")
 _buf(H, 2048, "SEL2")
-_buf(H, 128, "ID", "ONE", "MK16", "SCM", "SCZ", "DM", "LT", "vx", "CW", "M130", "sg0", "r4", "sgn", "az", "iseq", "w8", "prw",
-     "es", "eb", "ea", "eu", "ew", "ef", "sc0", "sc1", "sc2", "so0", "so1", "so2")
-_buf(H, 12 * 128, "IS")
-_buf(H, 8, "G8", "G82", "retb")
-_buf(H, 16, "G8B")
-_buf(H, 40, "G83")
-_buf(H, 48, "HR")
+_buf(H, 128, "ID", "ONE", "SCM", "DM", "LT", "vx", "fx", "dd", "CW", "M130", "sg0", "sgn",
+     "es", "eb", "ea", "eu", "ew", "sc0", "sc1", "sc2", "so0", "so1", "so2")
+_buf(H, 14 * 128, "IS")
+_buf(H, 8, "G8", "retb")
 _buf(H, 32, "ONES32")
-_buf(H, 264, "THR", "RST", "O264", "kneg")
-_buf(F, 264, "xs")
-_buf(H, 256, "K2c", "e2p", "kept", "sg1", "sg2", "far", "wm")
-_buf(F, 128, "RM", "krx", "krd", "krp", "DX")
-_buf(F, 1024, "W4")
+_buf(H, 132, "TP")
+_buf(H, 264, "THR", "CB", "O264", "TR", "HR")
+_buf(F, 264, "xs", "XC")
+_buf(H, 256, "K2c", "e2p", "kept", "sg1", "gt", "tl", "wm")
+_buf(F, 128, "RM")
 _buf(F, 512, "ysw")
-_buf(F, 256, "key", "Dc", "al")
-_buf(F, 128, "ID32")
-_buf(H, 256, "C192", "Db", "lt0")
-_buf(H, 4 * 256, "fb")
-_buf(H, 264, "sp")
-_buf(F, 32, "kc", "kc1", "KAP")
-_pool("lf", F, 8, "Cv", "C32", "SG", "sxf", "bsf", "barf", "barK", "fnd", "ret", "nr", "mul", "dp1", "sd1", "xn", "xh", "x40", "n40",
-      "mid", "rad", "vq", "v1", "v2", "v3", "v4", "v5")
+_buf(F, 256, "key", "al", "RQ", "IA", "IQ")
+_buf(F, 32, "kc1", "kcm", "KAP")
+_pool("lf", F, 8, "C32", "SG", "sxf", "sx32", "bsf", "barf", "barK", "fnd", "dcol", "Aq", "nf", "z", "ret", "zq", "vq", "p32", "MB", "pbf")
 _buf(F, 1, "thr")
-_buf(H, 80, "LC")
 _buf(I, 2, "ri")
-_buf(I, 6 * 256, "tb")
-_buf(I, 256, "craw", "cm", "Dz", "wi", "Kf", "KQf")
-_buf(I, 128, "rd", "rx", "rp")
+_buf(I, 5 * 256, "tb")
+_buf(I, 256, "craw", "cm", "wi", "Kf", "KQf", "YS", "YQ")
+_buf(I, 264, "kx", "kd", "Dz")
 _buf(I, 8, "bari")
-_pool("li", I, 8, "pi", "pb", "qq", "xr", "sx", "oi", "sd", "dq", "pr0", "bs", "MBi", "cb", "ui", "ua", "uo")
-_buf(I, 1296, "KW0", "KW1", "KW2")
-_buf(I, 1040, "ZO0", "ZO1", "ZO2")
+_pool("li", I, 8, "pi", "pb", "sx", "sd", "dq", "ui", "ua", "uo", "lo")
+_buf(I, 1056, "KW0", "KW1", "KW2")
+_buf(I, 512, "ZO0", "ZO1", "ZO2")
 _buf(U, 256, "pl0", "pl1", "pl2", "plo0", "plo1", "cu")
-_buf(U, 40, "ou")
-_buf(U, 8, "uu")
+_buf(U, 8, "ou", "uu", "LO", "FO")
 for _b in range(8):
     SCRATCH["ps%d" % _b] = ("psum", [128, 512], F)
+KS, RAWS, RAWQ, KQ = 0, 272, 536, 800
 
-DMAS = ["ld%d" % k for k in range(12) if k != 9] + ["ds%d" % k for k in range(4)]
-SEMAPHORES = ["qv", "qs", "qt", "qg"] + DMAS + [a + x + t for a in "al" for x in "pkqs" for t in "12"]
-FUSED = (1, 3, 6)
+DMAS = ["ld%d" % k for k in range(12)] + ["ds%d" % k for k in range(5)]
+SEMAPHORES = ["qv", "qs", "qt", "qg"] + DMAS + [a + x + t for a in "al" for x in "prkqs" for t in "12"]
 VADD = 2
 DL = 2.0 ** -18
-B1, B2 = 49152, 98304
-WM, C0 = 760, 1304
+SW, SC = -2.0 ** 31, -2.0 ** -16
+C0 = 1304
 CYC, GATHER, SCATTER, WAKE = 0.83e-3, 1.4, 3.8, 0.22
 AHEAD, PASSES, SLACK, LAZY, SHAKE = (1.0, 1.5, 2.0), 5, 2.0, 0.6, 3.0
-TRIES, STRETCH, SFIX = 1300, 1.5, 0.05
+TRIES, STRETCH, SFIX = 100, 1.5, 0.05
+POLISH, HEAT = 8000, 0.05
+TUNE, HOT, PERIOD = 0, 0.3, 25.0
 OTHERS = ((0.17, 1.25), (0.27, 0.85))
 FLY, LOAD, NEXT, LATE, EARLY = 1.3, 1.3, 1.25, 0.3, 8.0
-HIGH, HALF, PFIX = (5, 3), (True, True), 0.01
+PFIX = 0.01
+PULL = {"table": 3.0, "reasons": -3.0, "after": 0.0}
 STORE = 1000.0
 CUTS = (0, 512, 1536, 2560, 3584, 4096)
-NEEDS_V = {4: 2, 5: 4}
+QC = "ssssssss"
+KEEP = False
+RUN = (("T2 T3 R0 T5 T7 R1 N1 F0 F1 N3 F2 F3 M0 M1 F4 F5 M2 F6 F7 M3", "T0 T1 T4 T6 N0 N2 N4 N5 N6 N7"),
+       ("T2 T3 R0 T5 F0 F1 T7 R1 N3 F2 F3 M0 M1 F4 F5 N7 F6 F7 M2 M3", "T0 T1 N0 N1 T4 T6 N2 N4 N5 N6"))
 SIZE = {H: 2, F: 4, I: 4, U: 2}
 
 
@@ -160,12 +157,19 @@ def _schedule(prog):
     for i in range(n):
         for j in deps[i]:
             nxt[j].append(i)
+    behind = [e.get("behind", []) for e in prog]
+    ahead_of = [[] for _ in range(n)]
+    for i in range(n):
+        for j in behind[i]:
+            ahead_of[j].append(i)
     rank = [0.0] * n
-    for i in range(n - 1, -1, -1):
-        rank[i] = min(prog[i]["cost"].values()) + prog[i]["lat"] + max([rank[j] + WAKE for j in nxt[i]] + [0.0])
+    for k in range(3):
+        for i in range(n - 1, -1, -1):
+            rank[i] = min(prog[i]["cost"].values()) + max([prog[i]["lat"] + rank[j] + WAKE for j in nxt[i]] + [rank[j] for j in ahead_of[i]] + [prog[i]["lat"]])
 
     def one(before, after, rank, back, ahead):
-        left = [len(d) for d in before]
+        ob, oa = (ahead_of, behind) if back else (behind, ahead_of)
+        left = [len(d) + len(x) for d, x in zip(before, ob)]
         at = [{} for _ in range(n)]
         ready = set(i for i in range(n) if not left[i])
         free, bank, queue, order, done = {}, {}, {}, [], [0.0] * n
@@ -211,6 +215,10 @@ def _schedule(prog):
                 left[j] -= 1
                 if not left[j]:
                     ready.add(j)
+            for j in oa[i]:
+                left[j] -= 1
+                if not left[j]:
+                    ready.add(j)
         return max(done), order, queue, done
 
     best = None
@@ -233,7 +241,7 @@ def _schedule(prog):
 
     def forward(urge, ahead):
         top = max(urge) - EARLY
-        fw = one(deps, nxt, [max(u, top) if c else u for u, c in zip(urge, const)], None, ahead)
+        fw = one(deps, nxt, [(max(u, top) if c else u) + e.get("pull", 0.0) for u, c, e in zip(urge, const, prog)], None, ahead)
         return (fw[0] + sum(replay(fw[1], fw[2], w, x) for w, x in OTHERS), fw[1], fw[2], fw[3], urge, ahead)
 
     for ahead in AHEAD:
@@ -250,7 +258,191 @@ def _schedule(prog):
         fw = forward([u + (float(x) if abs(d - at) < STRETCH else 0.0) for u, x, d in zip(best[4], noise, best[3])], best[5])
         if fw[0] <= best[0]:
             best = fw
-    return best[1], best[2], deps, best[3]
+    return _polish(prog, deps, nxt, best[1], best[2]) + (deps,)
+
+
+def _polish(prog, deps, nxt, order, queue):
+    n = len(prog)
+    before = [set(d) for d in deps]
+    after = [set(x) for x in nxt]
+    for q in ("g", "y"):
+        ix = [i for i in range(n) if q in prog[i]["cost"]]
+        for a, b in zip(ix, ix[1:]):
+            before[b].add(a)
+            after[a].add(b)
+    for b in range(n):
+        for a in prog[b].get("behind", []) if KEEP else []:
+            before[b].add(a)
+            after[a].add(b)
+    dl = [sorted(d) for d in deps]
+    lat = [e["lat"] for e in prog]
+    banks = [e["P"] for e in prog]
+    ways = ((WAKE, 1.0),) + OTHERS
+    cost = [[{q: c * (x if e["by index"] else 1.0) for q, c in e["cost"].items()} if "by index" in e else e["cost"] for e in prog] for w, x in ways]
+
+    def run(order, queue, k):
+        wake, ck = ways[k][0], cost[k]
+        free, holder, bank, done, why = {}, {}, {}, [0.0] * n, [None] * n
+        for i in order:
+            q = queue[i]
+            s, w = free.get(q, 0.0), holder.get(q)
+            soft = True
+            if q == "t":
+                for j in dl[i]:
+                    x = done[j] if queue[j] == "t" else done[j] + wake
+                    if x > s:
+                        s, w, soft = x, j, False
+            else:
+                for j in dl[i]:
+                    x = done[j] + wake
+                    if x > s:
+                        s, w, soft = x, j, False
+            e = banks[i]
+            if e:
+                for b in e:
+                    for q2, (x, j) in bank.get(b, {}).items():
+                        if q2 != q and x + wake > s:
+                            s, w, soft = x + wake, j, True
+            s += ck[i][q]
+            if q != "x":
+                free[q], holder[q] = s, i
+            done[i] = s + lat[i]
+            why[i] = (w, soft)
+            if e:
+                for b in e:
+                    bank.setdefault(b, {})[q] = (s, i)
+        return max(done), done, why
+
+    def judge(order, queue):
+        r = [run(order, queue, k) for k in range(len(ways))]
+        return sum(x[0] for x in r), r
+
+    def links(r):
+        top, done, why = r
+        i, out = done.index(top), []
+        while why[i][0] is not None:
+            if why[i][1]:
+                out.append((why[i][0], i))
+            i = why[i][0]
+        return out
+
+    pick = np.random.default_rng(2)
+    order, queue = list(order), dict(queue)
+    now, res = judge(order, queue)
+
+    like = [e["like"] for e in prog]
+    visit = [e["visit"] for e in prog]
+    done = res[0][1]
+    base = [done[[i for i in range(n) if like[i] == "xs.0" and visit[i] == t][0]] for t in range(VI)]
+    when = {}
+    for t in (0, 2, 1):
+        when.update({like[i]: done[i] - base[t] for i in range(n) if visit[i] == t})
+    base = [base[0] + t * PERIOD for t in range(VI)]
+    kin = {}
+    for x in when:
+        kin.setdefault(x.split(".")[0], []).append(x)
+    alike = {}
+    for i in range(n):
+        alike.setdefault(like[i], []).append(i)
+    nb = [len(x) for x in before]
+    al = [sorted(x) for x in after]
+
+    def arrange(when):
+        at = [base[visit[i]] + when[like[i]] for i in range(n)]
+        for i in range(n - 1, -1, -1):
+            for j in al[i]:
+                if at[j] <= at[i]:
+                    at[i] = at[j] - 1e-4
+        o = sorted(range(n), key=lambda x: at[x])
+        left, seen, out, held = list(nb), [False] * n, [], []
+        for i in o:
+            held.append(i)
+            while held:
+                k = held.pop()
+                seen[k] = True
+                if not left[k]:
+                    left[k] = -1
+                    out.append(k)
+                    for j in al[k]:
+                        left[j] -= 1
+                        if not left[j] and seen[j]:
+                            held.append(j)
+        return out, at
+
+    o2, at = arrange(when)
+    new, r2 = judge(o2, queue)
+    cur = (new, o2, queue, r2, at, when)
+    top = cur
+    for step in range(TUNE):
+        new, o2, q2, r2, at, when = cur
+        lk = links(r2[int(pick.integers(len(ways)))])
+        j, i = lk[int(pick.integers(len(lk)))]
+        way = float(pick.uniform())
+        w2 = dict(when)
+        k = i if way < 0.5 else j
+        if pick.uniform() < 0.08 and len(prog[k]["cost"]) > 1:
+            q2 = dict(q2)
+            other = [q for q in prog[k]["cost"] if q != q2[k]][0]
+            q2.update({x: other for x in alike[like[k]] if other in prog[x]["cost"]})
+        else:
+            far = float(pick.exponential()) * (0.02, 0.2, 0.7, 2.0)[int(pick.integers(4))]
+            by = (at[j] - at[i] - far if k == i else at[i] - at[j] + far)
+            w2[like[k]] = at[k] - base[visit[k]]
+            for x in (kin[like[k].split(".")[0]] if pick.uniform() < 0.3 else [like[k]]):
+                if abs(w2[x] - w2[like[k]]) < 1.0 or x == like[k]:
+                    w2[x] = w2[x] + by if x != like[k] else w2[x]
+            w2[like[k]] += by
+        o3, a3 = arrange(w2)
+        n3, r3 = judge(o3, q2)
+        if n3 <= new + HOT * (1 - step / TUNE) * float(pick.exponential()):
+            cur = (n3, o3, q2, r3, a3, w2)
+            if n3 < top[0]:
+                top = cur
+    if top[0] < now:
+        now, order, queue, res = top[:4]
+    best = (now, order, queue, res[0][1])
+    soft = [links(r) for r in res]
+    for step in range(POLISH):
+        lk = soft[int(pick.integers(len(ways)))]
+        x = int(pick.integers(len(lk)))
+        j, i = lk[x]
+        way = float(pick.uniform())
+        q2 = queue
+        if way < 0.1:
+            k = j if way < 0.05 else i
+            if len(prog[k]["cost"]) < 2:
+                continue
+            q2 = dict(queue)
+            q2[k] = [q for q in prog[k]["cost"] if q != queue[k]][0]
+            o2 = order
+        else:
+            far = int(pick.geometric(0.45)) - 1
+            if way < 0.55:
+                while far and x + 1 < len(lk) and lk[x + 1][1] == j:
+                    x, far = x + 1, far - 1
+                    j = lk[x][0]
+            else:
+                while far and x > 0 and lk[x - 1][0] == i:
+                    x, far = x - 1, far - 1
+                    i = lk[x][1]
+            a, b = order.index(j), order.index(i)
+            mid = order[a:b + 1]
+            go, need = set(), ({i} if way < 0.55 else {j})
+            for k in (mid[::-1] if way < 0.55 else mid):
+                if k in need:
+                    go.add(k)
+                    need |= before[k] if way < 0.55 else after[k]
+            if (j if way < 0.55 else i) in go:
+                continue
+            stay, moved = [k for k in mid if k not in go], [k for k in mid if k in go]
+            o2 = order[:a] + (moved + stay if way < 0.55 else stay + moved) + order[b + 1:]
+        new, r2 = judge(o2, q2)
+        if new <= now + HEAT * (1 - step / POLISH) * float(pick.exponential()):
+            now, order, queue, res = new, o2, q2, r2
+            soft = [links(r) for r in res]
+            if now < best[0]:
+                best = (now, order, queue, res[0][1])
+    return best[1], best[2], best[3]
 
 
 PLANNED = {}
@@ -263,11 +455,24 @@ def rank_program(g, core, T, topo):
     N = len(T.cores)
     op_now, send_now, lands_now, finish = _tracker(g, T)
     prog = []
+    pull = [0.0]
+
+    named, starts = {}, []
+
+    def name(x):
+        named.setdefault(x, []).append(len(prog) - 1)
+
+    def line(names):
+        ix = [i for x in names.split() for i in named.pop(x)]
+        for a, b in zip(ix, ix[1:]):
+            prog[b].setdefault("behind", []).append(a)
 
     def v(name, a=0, b=None, step=1, p=0):
         if name in PART:
             name, o, n = PART[name]
             a, b = o + a, o + (n if b is None else b)
+        if b is not None and b < 0:
+            b = None
         n = SCRATCH[name][1][1]
         cols = range(n)[a:b:step]
         m = 0
@@ -296,7 +501,7 @@ def rank_program(g, core, T, topo):
         cost = {}
         for q in fns:
             if kind == "mm":
-                c = max(64, ins[1][2]) * CYC * len(ins) / 2 * (4 if ins[0][3] == 4 else 1)
+                c = sum(max(64, x[2]) for x in ins[1::2]) * CYC * (4 if ins[0][3] == 4 else 1)
             elif kind in ("dma", "g"):
                 c = 0.05 if kind == "dma" else 0.15 + 2 * n * CYC
             elif any(x[5] for x in sides):
@@ -309,7 +514,7 @@ def rank_program(g, core, T, topo):
                 c = max(64, n * (0.5 if q == "v" and kind == "ts" and all(x[3] == 2 for x in sides if x[2] > 1) else 1)) * CYC
             cost[q] = c + (PFIX if q in "vs" and any(x[4] for x in sides) else 0.0)
         prog.append({"kind": "op", "fn": fns, "R": reads, "W": list(out[1]) + list(Wr), "P": sorted(set(x[1][0][0] for x in sides if x[4])),
-                     "sem": sem, "inc": inc, "cost": cost, "lat": lat, "by index": any(x[5] for x in sides)})
+                     "sem": sem, "inc": inc, "cost": cost, "lat": lat, "by index": any(x[5] for x in sides), "pull": pull[0]})
 
     def ts_fn(out, a, s1, o0, s2, o1):
         if o1 is None:
@@ -382,6 +587,9 @@ def rank_program(g, core, T, topo):
     def store(q, k, dst, src):
         rec({q: lambda e: e.dma_start(dst, src[0])}, (None, [("out%d" % k, 1)], 1, 4, False, None), [src], "dma", "ds%d" % k, 16, 2.0 + src[2] * src[3] / STORE)
 
+    def copy(k, out, src):
+        rec({"y": lambda e: e.dma_start(out[0], src[0])}, out, [src], "dma", "ds%d" % k, 16, 9.0)
+
     def send(name, moves, go, lat):
         dst = T.cores[(rank + go) % N]
         rid, pid, _ = topo.addr(dst)
@@ -400,20 +608,24 @@ def rank_program(g, core, T, topo):
         prog.append({"kind": "lands", "fn": None, "R": [("sent" + name, 1)], "W": [k for out, _ in moves for k in out[1]], "P": [], "sem": "a" + name,
                      "inc": n, "cost": {"x": lat}, "lat": 0.0})
 
-    def lanes(name, h, a=0):
-        return v(name, a + h, a + 256, 8)
+    def lanes(name, h, a=0, n=32):
+        return v(name, a + h, a + 8 * n, 8)
+
+    def blk(h):
+        return 4 * (h % 2) + h // 2
 
     def IS(k):
         return v("IS", k * 128, k * 128 + 128)
 
     for k, (a, b) in enumerate(zip(CUTS, CUTS[1:])):
-        load("y", 4 + k, v("E", a, b), T.eff[:, a:b], LOAD + NEXT * b / 1024)
-    load("y", 0, v("KW0", 520, 776), T.act[:, :], LOAD + NEXT * 4.5)
+        load("y", 4 + k, v("E0", a, b), T.eff[:, a:b], LOAD + NEXT * b / 1024)
+    load("y", 0, v("KW0", RAWS + 8, RAWS + 264), T.act[:, :], LOAD + NEXT * 4.5)
     load("y", 2, v("sc0"), T.st0[:, :], LOAD + NEXT * 4.7)
     for k in range(2):
         load("y", 10 + k, v("PT", k * 2048, k * 2048 + 2048), T.req[:, k * 2048:k * 2048 + 2048], LOAD + NEXT * (6.7 + 2 * k) + LATE)
     load("y", 1, v("wi"), T.why[:, :], LOAD + NEXT * 10 + LATE)
     load("y", 3, v("bari"), T.bar[:, :], LOAD + NEXT * 10 + LATE)
+    load("y", 9, v("E1"), T.eff[:, :], LOAD + NEXT * 14 + LATE)
 
     ID, ONE, G8 = v("ID"), v("ONE"), v("G8")
     fill(ONE, 1.0)
@@ -421,233 +633,234 @@ def rank_program(g, core, T, topo):
     gp(lambda e: e.affine_select(G8[0], v("ONE", 0, 8)[0], [[-16, 8]], A.is_ge, 0.0, 0, 1), G8, [ONE])
     gp(lambda e: e.affine_select(G8[0], G8[0], [[16, 8]], A.is_ge, 0.0, 15, -1), G8, [G8])
     gp(lambda e: e.affine_select(v("LT")[0], ONE[0], [[0, 8], [-1, 16]], A.is_equal, 0.0, 0, 1), v("LT"), [ONE])
-    iota(v("kc"), [[1, 32]], 0, 0)
     iota(v("pi"), [[0, 8]], 0, 1)
-    iota(v("C32"), [[16, 8]], 0, 0)
+    for a in range(0, 2048, 256):
+        iota(v("SEL2", a, a + 256), [[0, 256]], 0, 0)
+    for k in range(16):
+        affine(v("SEL2", k * 128 + k, k * 128 + 128, 16), G8, SW, None, "s")
+    iota(v("TP"), [[0, 4], [-1, 33]], 40, 0)
+    iota(v("C32"), [[16, 2], [32, 4]], 0, 0)
     iota(v("kc1"), [[1, 32]], 1, 0)
-    iota(v("KAP"), [[113, 32]], 37, 0)
+    iota(v("KAP"), [[113, 32]], 37 - W, 0)
+    iota(v("lo"), [[16, 8]], 15, 0)
     iota(v("K2c"), [[-64, 32], [0, 8]], 31 * 64, 0)
-    fill(v("K2c", 0, 256, 1, 64), -33024.0 * 128)
-    fill(v("FL", W, W + B), B2 * DL)
-    fill(v("ONES32"), 1 / 128)
-    fill(v("sp", 0, 8), 1 / 128)
-    fill(v("C192"), 192.0)
+    fill(v("K2c", 0, 256, 1, 64), -33280.0 * 512)
+    for h in range(8):
+        fill(v("FL", h * BL + 512, h * BL + BL), -33024 * DL)
+        fill(v("Gn", h * BL + 512, h * BL + BL), -32768 * DL)
+    fill(v("ONES32"), 1.0)
     fill(v("SCM"), 10000.0)
     fill(v("SCM", 0, 128, 16), -10000.0)
-    fill(v("SCZ"), 1.0)
-    fill(v("SCZ", 0, 128, 16), 0.0)
-    fill(v("CW"), -784.0)
+    fill(v("CW"), -129.0)
     fill(v("M130"), -130.0)
-    fill(v("THR"), -1.5 * 8)
+    fill(v("THR"), -1.5 * 2 ** 14)
+    fill(v("CB"), -2.0 ** 25)
     fill(v("O264"), 1.0)
-    fill(v("RST"), 0.0)
-    fill(v("RST", 32, 264, 33), 64.0)
-    iota(v("kneg"), [[0, 8], [-1, 33]], 0, 0)
-    slope = -(2 * WM + 20) / ((B2 - B1 + 256) * DL)
-    for k, w in enumerate((-7.5, 128.5, 1.0, WM + 12 - slope * (B1 - 256) * DL, 0.0, -133.5, -141.5)):
+    for k, w in enumerate((-7.5, 128.0, -133.5, -141.5)):
         fill(col("SG", k), w)
-    for k, w in enumerate((-1.0, 6.0, 8.0, 64.0, 1 / DL, -1 / DL, -3 / 32 / DL, -2.0, -2.0 ** 23, 2.0 ** 17, -2.0 ** 17, 58.0)):
+    WS = (DL, 48 * DL, -0.5 / DL, -1.0, 1 / DL, -48.0, 2.0 ** 17, -2.0 ** 17, 48.0, 2.0 ** 24, 2.0 ** 25, -3 * 2.0 ** 24, 8192.0, -33 * 8192.0)
+    for k, w in enumerate(WS):
         affine(IS(k), ID, w)
-    for j in range(2):
-        affine(v("G82", j, 8, 2), v("G8", 4 * j, 4 * j + 4), 2.0)
-    affine(v("G8B", 0, 8), G8, 2.0 ** 20)
-    affine(v("G8B", 8, 16), G8, -2.0 ** 20)
-    o = 0
-    for w, a, b, hs in ((-1.0, 528, 0, (0, 1)), (-128.0, 16, 0, (0, 0, 1, 1)), (-8.0, 1, 8, None), (1.0, 0, 0, None)):
-        for x in [(j, 8, 2) for j in hs] if hs else [(0, 8, 1)]:
-            n = 8 // x[2]
-            affine(v("G83", o, o + n), v("G8", *x), w)
-            affine(v("HR", o, o + n), v("kc", *x), a / 128, b / 128)
-            o += n
-    affine(v("HR", 40, 48), v("kc", 0, 8), 1 / 128)
     ts(v("pb"), v("pi"), 15, A.bitwise_and)
-    fill(v("LC"), 0.0)
-    ts(v("LC", 0, 8), v("pb"), 32.0, A.mult)
-    for a in (8, 16, 40):
-        cp(v("LC", a, a + 8), v("pb"))
-    tt(v("C32"), v("C32"), v("pb"), A.add)
-    affine(v("C32"), v("C32"), 32.0)
-    affine(v("ID32"), ID, 1.0)
-    ts(v("barf"), v("bari"), 16.0, A.add, 2.0 ** 17, A.mult)
+    cp(v("pbf"), v("pb"))
+    cp(v("LO"), v("lo"))
+    iota(v("XC"), [[-BL, 8], [-16, 33]], 0, 0)
+    ts(v("XC"), v("XC"), col("pbf", 0), A.subtract)
+    ts(v("FO"), v("XC", 32, 264, 33), -1.0, A.mult)
+    iota(v("HR"), [[0, 8], [1, 33]], 0, 0)
+    affine(v("HR"), v("HR"), 8192.0, -40.5 * 8192)
+    for h in range(8):
+        ts(v("TR", 33 * h, 33 * h + 33), v("ONE", 0, 33), col("G8", blk(h)), A.mult, -2.0 ** 20, A.mult)
+    affine(v("kcm"), v("kc1"), 1.0, -32.5)
+    ts(v("C32"), v("C32"), col("pbf", 0), A.add, 32.0, A.mult)
+    ts(v("barf"), v("bari"), 2.0 ** 19, A.mult, -65536.0, A.add)
     mms(v("ps3", 0, 128), [(v("LT"), v("LT"))])
     act(v("DM"), v("ps3", 0, 128), ACT.Identity)
 
-    cp(v("pl0"), v("KW0", 520, 776))
-    iota(v("al"), [[-4096, 256]], -4096, 0)
-    iota(v("Dc"), [[-8192, 32], [0, 8]], -8192, 0)
+    for h in range(8):
+        cp(v("pl0", 32 * blk(h), 32 * blk(h) + 32), lanes("KW0", h, RAWS + 8))
+    iota(v("al"), [[-4096, 32], [0, 8]], -4096, 0)
     Kc, KQc = v("ps5", 256, 512), v("ps6", 0, 256)
     act(Kc, v("al"), ACT.Identity)
-    act(KQc, v("Dc"), ACT.Identity)
-    tt(v("KW0", 256, 512), v("KW0", 520, 776), Kc, A.add)
-    ts(v("KW0", 776, 1032), v("wi"), 1.0, A.add)
-    tt(v("KW0", 1040, 1296), v("KW0", 776, 1032), KQc, A.add)
+    act(KQc, v("al"), ACT.Identity, 2.0)
+    tt(v("KW0", KS + 8, KS + 264), v("KW0", RAWS + 8, RAWS + 264), Kc, A.add)
+    ts(v("KW0", RAWQ + 8, RAWQ + 264), v("wi"), 1.0, A.add)
+    tt(v("KW0", KQ, KQ + 256), v("KW0", RAWQ + 8, RAWQ + 264), KQc, A.add)
     for t in range(VI):
-        fill(v("KW%d" % t, 512, 520), 0)
-    iota(v("SEL2"), [[0, 2048]], 0, 0)
-    prog[-1]["lat"] = 4.0
-    for k in range(16):
-        affine(v("SEL2", k * 128 + k, k * 128 + 128, 16), G8, 2.0 ** 13, None, "s")
-    iota(v("Kf"), [[-4096, 256]], -4096, 0)
+        fill(v("KW%d" % t, KS + 264, KS + 272), -4096 * 33)
+        fill(v("KW%d" % t, RAWS, RAWS + 8), 0)
+        fill(v("KW%d" % t, RAWQ, RAWQ + 8), 0)
+    iota(v("Kf"), [[-4096, 32], [0, 8]], -4096, 0)
     iota(v("KQf"), [[-8192, 32], [0, 8]], -8192, 0)
-
-    def classes(u, w, f, e, off):
-        ts(u, e, 4.0 + off, A.is_ge, -1 / DL, A.mult)
-        ts(w, e, 12.0 + off, A.is_ge, 1 + 116 * DL, A.subtract)
-        scan(f, u, w, 0.0, A.min, A.mult)
 
     for c in range(8):
         a, b = c * 512, c * 512 + 512
         p = v(("ps0", "ps1", "ps2", "ps7")[c % 4])
-        classes(v("Gn", a, b), v("EC", a, b), v("D1", a, b), v("E", a, b), 0)
+        ts(v("FC", a, b), v("E0", a, b), 4.0, A.is_ge, -1 / DL, A.mult)
+        ts(v("EC", a, b), v("E0", a, b), 12.0, A.is_ge, 1 + 96 * DL, A.subtract)
+        scan(v("TM", a, b), v("FC", a, b), v("EC", a, b), 0.0, A.min, A.mult)
         if c < 8 - VADD:
-            mms(p, [(ID, v("E", a, b)), (ID, v("D1", a, b))])
-            act(v("TT", a, b), p, ACT.Identity, None, -252.0)
+            mms(p, [(ID, v("E0", a, b)), (ID, v("TM", a, b))])
+            act(v("TT", a, b), p, ACT.Identity, None, -192.0)
         else:
-            act(p, v("E", a, b), ACT.Identity, None, -252.0)
-            tt(v("TT", a, b), v("D1", a, b), p, A.add)
-    for k in range(4):
-        for a in (k * 1024, k * 1024 + 512):
-            affine(v("ND", a, a + 512), v("PT", a, a + 512), -1.0, 2083.5)
+            act(p, v("E0", a, b), ACT.Identity, None, -192.0)
+            tt(v("TT", a, b), v("TM", a, b), p, A.add)
 
-    def rows(dst, sel, src, a, n, first):
-        mms(dst, first, [(v(sel, k * 128, k * 128 + 128), v(src, a + k, a + n, 16)) for k in range(16)])
+    def SEL(k):
+        return v("SEL2", k * 128, k * 128 + 128)
 
     for t in range(VI):
-        pl, KW, s0, sv, ZO = "pl%d" % t, "KW%d" % t, v("sc%d" % t), v("so%d" % t), "ZO%d" % t
+        pl, KW, so, ZO = "pl%d" % t, "KW%d" % t, v("so%d" % t), "ZO%d" % t
         last = t == VI - 1
-        X0, V32 = v("D1", 0, None, 33), v("V0", 32, None, 33)
+        Et, En = "E%d" % t, "E%d" % ((t + 1) % 3)
 
-        act(v("sg0"), s0, ACT.Sign, None, col("SG", 0))
-        affine(X0, v("sg0"), 64 * DL, -192 * DL)
-        for k in range(32):
-            affine(v("D1", k + 1, None, 33), ind(v("TT"), v(pl, k * 8, k * 8 + 8)), DL, 4 * min(k, 30) * DL)
-        scan(v("V0"), v("D1"), v("D1"), 0.0, A.mult, A.min)
-        group([(v("ps0", 0, 264), ONE, v("RST")), (v("ps0", 0, 264), ONE, v("THR"))], True, False, "a")
-        for c in range(8):
-            a = 4 * c
-            affine(v("Gn", c * 512, c * 512 + 512), ind(v("ND"), v(pl, c * 32, c * 32 + 32)), (B2 - B1) / 16 * DL, (B1 - 129 * (B2 - B1)) * DL, "v" if c in NEEDS_V else "s")
-            if c in NEEDS_V:
-                prog[-1]["R"] += v("FL", 0, NEEDS_V[c] * 512)[1]
-            group([(v("ps0", k, 264, 33), v("Gn", k * 128, k * 128 + 128), v("G8B", 0, 8)) for k in range(a, a + 4)], False, False, "b")
-            for k in range(a, a + 4):
-                scan(v("FL", k * 128, k * 128 + 128), v("V0", k, None, 33), v("Gn", k * 128, k * 128 + 128), 1.0, A.min, A.add)
-            group([(v("ps0", k, 264, 33), v("FL", k * 128, k * 128 + 128), v("G8B", 8, 16)) for k in range(a, a + 4)], False, c == 7, "c" if c == 7 else "b")
-        if last:
-            rec({"y": lambda e: e.dma_start(T.E2[:, :], T.E[:, :])}, v("E2"), [v("E"), v(pl)], "dma", "ds3", 16, 9.0)
-
-        def turn(out, src, a, step, rhs, const):
-            for h in range(8):
-                affine(v("LT", h * 16, h * 16 + 16), v("DM", 0, 16), col(src, a + h * step))
-            mms(out, const + [(v("LT"), rhs)])
-
-        def pick(out, win, lst, mask):
-            tt(v("k" + out), ind(win, lst), v(mask), A.mult)
-            scan(v(out), v("SCZ"), v("k" + out), 0.0, A.mult, A.add)
-            return v(out, 15, None, 16)
-
-        scan(v("xs", 263, None, -1), v("ps0", 263, None, -1), v("kneg", 263, None, -1), 0.0, A.max, A.min)
-        turn(v("ps4", 400, 440), "xs", 0, 33, v("G83"), [(ONE, v("HR", 0, 40)), (ID, v("LC", 0, 40)), (ID, v("LC", 40, 80))])
-        cp(v("ou", 0, 32), v("ps4", 400, 432))
-        affine(v("xn"), v("ps4", 432, 440), 1.0)
-        affine(v("vx"), ind(v("V0"), v("ou", 0, 8)), 1 / DL, 1022.5, "v")
-        for a in (64, 0, 192):
-            n = 128 if a == 64 else 64
-            act(v("wm", a, a + n), ind(v("FL"), v("ou", 8 + a // 16, 8 + (a + n) // 16)), ACT.Abs, slope, col("SG", 3))
-        r = v(KW, 248, 256)
-        rx = pick("rx", v(KW, 248, 520), v("ou", 24, 32), "DM")
-        cp(r, rx)
-        sx = v(KW, 512, 520)
-        ts(sx, rx, 4095, A.bitwise_and)
-        cp(v("sxf"), sx)
+        pull[0] = 0.0
+        if t == 0:
+            act(v("sg0"), v("sc0"), ACT.Sign, None, col("SG", 0))
+            mms(v("ps1", 256, 384), [(IS(0), v("sc0")), (IS(1), v("sg0"))])
+        starts.append(len(prog))
         for h in range(8):
-            affine(v("DX", h * 16, h * 16 + 16), v("DM", 0, 16), col("sxf", h))
+            if t:
+                affine(v("D1", h * BL, h * BL + 16), v("sc%d" % t, 16 * h, 16 * h + 16), 1.0)
+            else:
+                affine(v("D1", blk(h) * BL, blk(h) * BL + 16), v("ps1", 256 + 16 * h, 272 + 16 * h), 1.0, -144 * DL)
+        run_v, run_s = RUN[min(t, 1)]
+        for c in range(8):
+            affine(v("D1", c * BL + 16, c * BL + BL), ind(v("TT"), v(pl, c * 32, c * 32 + 32)), DL, None, "v" if "T%d" % c in run_v else "s")
+            name("T%d" % c)
+        for j in range(2):
+            for k in range(16):
+                d = v("D1", 4 * j * BL + k, 4 * (j + 1) * BL, 16)
+                scan(v("V0", 4 * j * BL + k, 4 * (j + 1) * BL, 16), d, d, 0.0, A.mult, A.min)
+                name("R%d" % j)
+        for j in range(2):
+            for k in range(16):
+                scan(v("TM", 4 * j * BL + k, 4 * (j + 1) * BL, 16), v("D1", 4 * j * BL + k, 4 * (j + 1) * BL, 16), v("TP"), 0.0, A.mult, A.max)
+                name("M%d" % (2 * j + k // 8))
+        cnt = v("ps0", 0, 264)
+        group([(cnt, ONE, v("CB")), (cnt, ONE, v("THR"))], True, False, "a")
+        for c in range(8):
+            a = c * BL
+            affine(v("Gn", a, a + 512), ind(v("PT"), v(pl, c * 32, c * 32 + 32)), -DL, -32692.5 * DL, "v" if "N%d" % c in run_v else "s")
+            name("N%d" % c)
+            scan(v("FL", a, a + 512), v("V0", a, a + 512), v("Gn", a, a + 512), -1.0, A.max, A.add)
+            name("F%d" % c)
+            if c == 7:
+                line(run_v)
+                line(run_s)
+            if c % 2:
+                for k0 in range(0, 16, 4):
+                    end = c == 7 and k0 == 12
+                    group([(v("ps0", 33 * c - 33, 33 * c + 33), SEL(k), v("FL", a - BL + k, a + BL, 16)) for k in range(k0, k0 + 4)], False, end, "c" if end else "b")
 
-        DT, D8 = v("ps2", 0, 128), v("ps2", 128, 136)
-        mms(DT, [(v("CW"), IS(3)), (v("wm", 64, 192), IS(3)), (v("vx"), ID)])
+        pull[0] = PULL["table"]
+        affine(so, ind(v("V0"), v("FO")), 1.0)
+        if not last:
+            send("s%d" % (t + 1), [(v("sc%d" % (t + 1)), [so])], STATE_GO, 2.0)
+        act(v("sgn"), so, ACT.Sign, 1 / DL, col("SG", 1))
+        for a in range(0, 16, 4):
+            group([(v("ps4", 384, 392), SEL(k), v("so%d" % t, k, 128, 16)) for k in range(a, a + 4)], a == 0, a == 12)
+        ts(v("ui"), v("ps4", 384, 392), 1 / (SW * DL), A.mult)
+        ts(v("ua"), v("ui"), 31, A.bitwise_and)
+        tt(v("uo"), v("ua"), v("C32"), A.add)
+        cp(v("uu"), v("uo"))
+        act(v("es"), ind(v(Et), v("uu")), ACT.Identity)
+        mms(v("ps4", 256, 384), [(IS(4), so), (IS(5), v("sgn")), (ID, v("es"))])
+        act(v("eb"), v("ps4", 256, 384), ACT.Identity, 0.5, 129.75 + 72)
+        tt(ind(v(En), v("uu")), v("eb"), v("M130"), A.add)
+        if last:
+            store("y", 0, T.ye[:, :], v(En))
+        else:
+            copy(3 + t, v("E%d" % ((t + 2) % 3)), v(En))
+            act(v("eu"), v("eb"), ACT.Sign, None, col("SG", 2))
+            act(v("ew"), v("eb"), ACT.Sign, None, col("SG", 3))
+            mms(v("ps4", 128, 256), [(ID, v("eb")), (IS(6), v("eu")), (IS(7), v("ew")), (IS(8), v("ew"))])
+            act(v("ea"), v("ps4", 128, 256), ACT.Identity, None, -274.0)
+            cp(ind(v("TT"), v("uu")), v("ea"))
+        pull[0] = 0.0
+
+        scan(v("xs", 263, None, -1), v("ps0", 263, None, -1), v("XC", 263, None, -1), 0.0, A.max, A.min)
+        ts(v("ou"), v("xs", 0, 264, 33), -1.0, A.mult)
+        for h in range(8):
+            scan(v("kx", 33 * h + 32, 33 * h - 1, -1), v("ps0", 33 * blk(h) + 32, 33 * blk(h) - 1, -1), v(KW, KS + 264 + h, KS + h, -8), 0.0, A.max, A.min)
+        kx = v("kx", 0, 264, 33)
+        cp(v("vx"), ind(v("TM"), v("ou")))
+        act(v("fx"), ind(v("FL"), v("ou")), ACT.Identity)
+        act(v("dd"), ind(v("Gn"), v("ou")), ACT.Identity)
+        mms(v("ps3", 128, 256), [(ID, v("dd")), (IS(3), v("fx"))])
+        for a in range(4):
+            affine(v("wm", 64 * a, 64 * a + 64), v("ps3", 128 + 64 * (a // 2), 192 + 64 * (a // 2)), SC / (32 * DL), 764 * SC, "s")
+        ts(v(KW, KS, KS + 8), kx, 2.0 ** 18, A.add)
+        ts(v("sx"), kx, 4095, A.bitwise_and)
+        cp(v("sxf"), v("sx"))
+        affine(v("sx32"), v("sxf"), 1 / 32)
+        ts(v("fnd"), kx, 131072.5, A.add, 2.0 ** 26, A.mult)
+        tt(v("barK"), v("barf"), v("fnd"), A.min)
+        for h in range(8):
+            act(lanes("sg1", h), v("XC", 33 * blk(h), 33 * blk(h) + 32), ACT.Sign, -1.0, col("xs", 33 * blk(h)))
+        act(v("gt"), v("sg1"), ACT.Relu)
+        G = v("ps6", 0, 256)
+        mms(G, [(IS(9), v("O264", 0, 256)), (IS(10), v("sg1")), (IS(11), v("gt")), (IS(12), v("gt"))])
+
+        DT = v("ps1", 0, 128)
+        mms(DT, [(v("CW"), v("ONE")), (v("fx"), IS(2)), (v("vx"), IS(3))])
         scan(v("RM"), v("SCM"), DT, 0.0, A.min, A.max)
-        turn(D8, "RM", 15, 16, v("G82"), [(ONE, v("HR", 40, 48))])
-        cp(v("ou", 32, 40), D8)
-        pr0 = pick("rp", v(KW, 512, 776), v("ou", 32, 40), "DX")
-        rd = pick("rd", v(KW, 248, 512), v("ou", 32, 40), "DM")
-        ts(v("sd"), rd, 4095, A.bitwise_and)
-        ts(v("dq"), rd, 15, A.arith_shift_right)
-        for j in set(c // 4 for c in FUSED):
-            for k in range(4):
-                act(v("W4", j * 512 + k * 128, j * 512 + k * 128 + 128), v("wm", j * 128, j * 128 + 128), ACT.Identity, None, C0 + 0.5)
+        tt(v("LT"), ind(v("RM"), v("LO")), v("DM"), A.mult)
+        mms(v("ps2", 0, 264), [(ONE, v("HR")), (v("LT"), v("TR"))])
+        for h in range(8):
+            scan(v("kd", 33 * h, 33 * h + 33), v("ps2", 33 * h, 33 * h + 33), lanes(KW, h, KS, 33), 0.0, A.min, A.max)
+        kd = v("kd", 32, 264, 33)
+        ts(v("sd"), kd, 4095, A.bitwise_and)
+        ts(v("dq"), kd, 12, A.arith_shift_right, 63, A.bitwise_and)
+        tt(v("p32"), v("sd"), v("sx32"), A.mult)
+        ts(v("bsf"), v("p32"), -262016.484375, A.add, 2.0 ** 23 + 4096 + 262016 + 97 * t, A.add)
 
-        ts(v("bs"), pr0, 5, A.arith_shift_right)
-        ts(v("bsf"), v("bs"), 97.0 * t, A.add)
         for j in range(2):
             for h in range(j, 8, 2):
                 ts(lanes("craw", h), v("KAP"), col("sxf", h), A.mult, col("bsf", h), A.add)
             ts(v("cm", j, 256, 2), v("craw", j, 256, 2), 4095, A.bitwise_and)
             cp(v("cu", j * 128, j * 128 + 128), v("cm", j, 256, 2))
         for c in range(8):
-            a, j, src = c * 512, c // 4, ind(v("E"), v("cu", c * 32, c * 32 + 32))
-            if c in FUSED:
-                tt(v("FL", a, a + 512), src, v("W4", j * 512, j * 512 + 512), A.add)
-            else:
-                affine(v("EC", a, a + 512), src, 1.0, C0 + 0.5, "s")
-                for k in range(a, a + 512, 128):
-                    scan(v("FL", k, k + 128), v("EC", k, k + 128), v("wm", j * 128, j * 128 + 128), 4000.0, A.min, A.add)
+            a, j = c * 512, c // 4
+            affine(v("EC", a, a + 512), ind(v(Et), v("cu", c * 32, c * 32 + 32)), SC, (C0 + 0.5) * SC, QC[c])
+            for k in range(a, a + 512, 128):
+                scan(v("FC", k, k + 128), v("EC", k, k + 128), v("wm", j * 128, j * 128 + 128), -1.0, A.max, A.add)
             if c % 2:
                 x = (c // 2 % 2) * 128 + j
-                cn = v("ps%d" % (c // 2 % 2), 256 + j * 64, 320 + j * 64)
-                rows(cn, "SEL2", "FL", a - 512, 1024, [(ONE, v("K2c", x, x - j + 128, 2))])
+                cn = v("ps%d" % (3 + c // 2 % 2), j * 64, 64 + j * 64)
+                mms(cn, [(ONE, v("K2c", x, x - j + 128, 2))], [(SEL(k), v("FC", a - 512 + k, a + 512, 16)) for k in range(16)])
                 tt(v("key", x, x - j + 128, 2), v("cm", x, x - j + 128, 2), cn, A.add)
 
-        act(v("r4"), V32, ACT.Identity, 1 / DL, 1022.5)
-        act(v("sgn"), V32, ACT.Sign, 1 / DL, col("SG", 1))
-        mms(v("ps3", 0, 128), [(IS(4), V32), (IS(5), X0)])
-        mms(v("ps3", 128, 256), [(ID, s0), (IS(6), X0)])
-        act(v("az"), v("ps3", 0, 128), ACT.Abs, None, col("SG", 4))
-        act(v("w8"), v("ps3", 128, 256), ACT.Identity, None, -32.0)
-        act(v("iseq"), v("az"), ACT.Relu, -1.0, col("SG", 2))
-        scan(v("prw"), v("iseq"), v("w8"), 0.0, A.max, A.mult)
-        mms(v("ps3", 256, 384), [(IS(4), V32), (IS(0), v("r4")), (IS(1), v("sgn")), (IS(2), v("iseq")), (ID, v("prw"))])
-        act(sv, v("ps3", 256, 384), ACT.Identity, None, 1030.0)
-        if not last:
-            send("s%d" % (t + 1), [(v("sc%d" % (t + 1)), [sv])], STATE_GO, 2.0)
-        for a in range(0, 16, 4):
-            group([(v("ps3", 384, 392), v("SEL2", k * 128, k * 128 + 128), v("so%d" % t, k, 128, 16)) for k in range(a, a + 4)], a == 0, a == 12)
-        ts(v("ui"), v("ps3", 384, 392), 2.0 ** -13, A.mult)
-        ts(v("ua"), v("ui"), 31, A.bitwise_and)
-        tt(v("uo"), v("ua"), v("C32"), A.add)
-        cp(v("uu"), v("uo"))
-        tt(v("es"), ind(v("E"), v("uu")), sv, A.add)
-        act(v("eb"), v("es"), ACT.Identity, 0.5, 129.75)
-        tt(ind(v("E2" if last else "E"), v("uu")), v("eb"), v("M130"), A.add)
-        if last:
-            store("y", 0, T.ye[:, :], v("E2"))
-        else:
-            act(v("eu"), v("eb"), ACT.Sign, None, col("SG", 5))
-            act(v("ew"), v("eb"), ACT.Sign, None, col("SG", 6))
-            mms(v("ps1", 0, 128), [(IS(9), v("eu")), (IS(10), v("ew")), (IS(11), v("ew")), (ID, v("eb"))])
-            act(v("ea"), v("ps1", 0, 128), ACT.Identity, None, -324.0)
-            cp(ind(v("TT"), v("uu")), v("ea"))
-
-        affine(v("fnd"), v("xn"), 2.0 ** 23, 2.0 ** 28, "s")
-        tt(v("barK"), v("barf"), v("fnd"), A.min)
-        cp(v("dp1"), v("dq"))
-        ts(v("sd1"), v("sd"), 1.0, A.add)
-        affine(v("xh"), v("xn"), -1.0, -0.5, "s")
-        affine(v("x40"), v("xn"), -1.0, -40.0, "s")
+        pull[0] = 0.0
+        ts(v("dcol"), v("dq"), -64.0, A.add)
+        ts(v("Aq"), v("sd"), 16385.0, A.add)
         for h in range(8):
-            act(lanes("sg1", h), v("kc"), ACT.Sign, -1.0, col("xh", h))
-            out = lanes("ps2", h, 256)
-            rec({"s": act_fn(out, v("kc1"), ACT.Abs, None, col("dp1", h)), "v": ts_fn(out, v("kc1"), col("dp1", h), A.add, 0.0, A.not_equal)},
-                out, [v("kc1"), col("dp1", h)], "act")
-            ts(lanes("e2p", h), lanes(KW, h, 776), col("sd1", h), A.not_equal, 1 / 128, A.mult)
-        act(v("ps7", 0, 256), v("sg1"), ACT.Relu)
-        tt(v("kept"), v("e2p"), v("ps2", 256, 512), A.min)
+            act(lanes("ps7", h, 256), v("kc1"), ACT.Abs, None, col("dcol", h))
+            ts(lanes("e2p", h), lanes(KW, h, RAWQ + 8), 16384.0, A.add, col("Aq", h), A.not_equal)
+        tt(v("kept"), v("e2p"), v("ps7", 256, 512), A.min)
         for h in range(8):
-            scan(lanes("sp", h, 8), v("ONES32"), lanes("kept", h), 1 / 128, A.add, A.subtract)
-        tt(v("Dc"), v("sp", 0, 256), v("ps7", 0, 256), A.add)
-        affine(v("n40"), v("sp", 256, 264), 128.0, 7.0)
-        nS, nQ = v(ZO, 264, 520), v(ZO, 520, 776)
-
-        def whole(name, a, n):
-            return v(name, a, a + n)
+            scan(lanes("Dz", h, 8), v("ONES32"), lanes("kept", h), 0.0, A.add, A.subtract)
+        cp(v("nf"), v("Dz", 256, 264))
+        for h in range(8):
+            act(lanes("tl", h), v("kcm"), ACT.Sign, None, col("nf", h))
+        TL = v("ps6", 256, 512)
+        mms(TL, [(IS(13), v("tl"))])
+        for b in range(5):
+            s = 8 << b
+            m = 256 - s
+            tb = v("tb", b * 256, b * 256 + m)
+            ts(tb, v("Dz", s, 256), b, A.arith_shift_right, 1, A.bitwise_and)
+            for a, mv in ((KS + 8, "ps5"), (KQ, "ps7")):
+                pull[0] = PULL["reasons"] if a == KQ and not last else 0.0
+                scan(v(mv, 0, m), tb, v(KW, a + s, a + 256), 0.0, A.max, A.mult)
+                tt(v(KW, a, a + m), v(KW, a, a + m), v(mv, 0, m), A.min)
+            pull[0] = 0.0
+        tt(v("ps5", 256, 512), v("cm"), TL, A.add)
+        tt(v(KW, KS + 8, KS + 264), v(KW, KS + 8, KS + 264), v("ps5", 256, 512), A.min)
+        tt(v("RQ"), v(KW, KQ, KQ + 256), TL, A.min)
+        for a, tmp, out in ((RAWS, "ps0", "IA"), (RAWQ, "ps2", "IQ")):
+            tt(v(tmp, 0, 256), v(KW, a, a + 256), G, A.add)
+            tt(v(out), v(KW, a + 8, a + 264), v(tmp, 0, 256), A.max)
 
         for j in range(2):
             hs = range(j, 8, 2)
@@ -656,63 +869,34 @@ def rank_program(g, core, T, topo):
                 return v(name, a + j, a + n, 2)
 
             for h in hs:
-                red(col("MBi", h), lanes("key", h), A.max)
-            tt(u("ret"), u("MBi"), u("barK"), A.is_lt)
-            tt(u("nr"), u("MBi"), u("barK"), A.is_ge)
-            affine(u("mul"), u("ret"), 127.0, 1.0)
+                red(col("MB", h), lanes("key", h), A.max)
+            tt(u("z"), u("MB"), u("barK"), A.subtract)
             for h in hs:
-                ts(lanes("Dz", h), lanes("Dc", h), col("mul", h), A.mult)
-            tt(u("v2"), u("MBi"), u("nr"), A.mult)
-            tt(u("v3"), u("x40"), u("ret"), A.mult)
-            tt(u("mid"), u("v3"), u("xn"), A.add)
-            tt(u("v4"), u("n40"), u("ret"), A.mult)
-            affine(u("rad"), u("v4"), 1.0, 0.5, "s")
-            tt(u("v5"), u("sd1"), u("nr"), A.mult)
-            affine(u("vq"), u("v5"), 1.0, -2.0 ** 23, "s")
-            for h in hs:
-                act(lanes("far", h), v("kc"), ACT.Abs, None, col("mid", h))
-                act(lanes("sg2", h), lanes("far", h), ACT.Sign, -1.0, col("rad", h))
-                act(lanes("al", h), lanes("key", h), ACT.Identity, col("ret", h), col("v2", h))
-                act(lanes("ps3", h), lanes("sg2", h), ACT.Identity, -2.0 ** 23, col("vq", h))
-            mms(u("ps2", 0, 256), [(IS(8), ONE), (IS(8), u("sg2", 0, 256)), (v("ID32"), u("al", 0, 256))])
-            if HIGH[j] < 5:
+                ts(lanes("ps5", h), lanes(KW, h, KS + 8), col("z", h), A.max)
+            tt(u("YS", 0, 256), u("IA", 0, 256), u("ps5", 0, 256), A.min)
+            ts(u(ZO, 0, 256), u("YS", 0, 256), 4095, A.bitwise_and)
+            if not last:
                 for h in hs:
-                    act(lanes("Db", h), lanes("Dc", h), ACT.Identity, col("mul", h))
-                for b in range(HIGH[j], 6):
-                    act(u("fb", (b - 2) * 256, 256), u("Db", 0, 256), ACT.Identity, 0.5 ** b, 191.5 + 0.5 ** (b + 1))
-            for b in (5, 0, 1, 2, 3, 4):
-                s = 8 << b
-                m = 264 - s
-                tb, o = (("ps6", "ps6", "ps4")[b - 2], 256 * (b == 3)) if HIGH[j] <= b < 5 else ("tb", b * 256)
-                if tb != "tb":
-                    mms(u(tb, o, m), [(ID, v("C192", 0, m // 2)), (ID, u("fb", (b - 2) * 256 + s - 8, m)), (IS(7), u("fb", (b - 1) * 256 + s - 8, m))])
-                else:
-                    ts(u(tb, o, m), u("Dz", s - 8, m), b, A.arith_shift_right, 1, A.bitwise_and)
-                for a, mv, z, w in ((248, "ps5", 0, u if HALF[0] else whole), (1032, "ps7", 256, u if HALF[1] else whole)):
-                    if w is whole and j == 0:
-                        continue
-                    if b == 5:
-                        scan(w(KW, a, m), w(tb, o, m), w(KW, a + s, m), 0.0, A.max, A.mult)
-                    else:
-                        scan(w(mv, z, m), w(tb, o, m), w(KW, a + s, m), 0.0, A.max, A.mult)
-                        tt(w(KW, a, m), w(KW, a, m), w(mv, z, m), A.min)
-            for a, new, o, bits, w in ((248, "ps2", 264, 4095, u if HALF[0] else whole), (1032, "ps3", 520, 8191, u if HALF[1] else whole)):
-                if w is whole and j == 0:
-                    continue
-                tt(w(KW, a, 256), w(KW, a, 256), w(new, 0, 256), A.min)
-                ts(w(ZO, o, 256), w(KW, a, 256), bits, A.bitwise_and)
-                if not last and a == 248:
-                    cp(w("plo%d" % t, 0, 256), w(ZO, 264, 256))
+                    cp(v("plo%d" % t, 32 * blk(h), 32 * blk(h) + 32), lanes(ZO, h))
+                send("pr"[j] + str(t + 1), [(v("pl%d" % (t + 1), 128 * j, 128 * j + 128), [v("plo%d" % t, 128 * j, 128 * j + 128)])], PLAN_GO, FLY)
+        pull[0] = 0.0 if last else PULL["after"]
+        ts(v("ret"), v("z"), 0.0, A.is_lt)
+        tt(v("zq"), v("z"), v("Aq"), A.min)
+        act(v("vq"), v("zq"), ACT.Relu)
+        for h in range(8):
+            act(lanes("ps7", h), lanes("RQ", h), ACT.Identity, col("ret", h), col("vq", h))
+        tt(v("YQ"), v("IQ"), v("ps7", 0, 256), A.min)
+        ts(v(ZO, 256, 512), v("YQ"), 8191, A.bitwise_and)
+        nS, nQ = v(ZO, 0, 256), v(ZO, 256, 512)
         if not last:
-            send("p%d" % (t + 1), [(v("pl%d" % (t + 1)), [v("plo%d" % t)])], PLAN_GO, FLY)
             nx = "KW%d" % (t + 1)
-            send("k%d" % (t + 1), [(v(nx, 256, 512), [nS, v("Kf")]), (v(nx, 520, 776), [nS])], PLAN_GO, 6.0)
-            send("q%d" % (t + 1), [(v(nx, 776, 1032), [nQ]), (v(nx, 1040, 1296), [nQ, v("KQf")])], PLAN_GO, 6.0)
-            cp(v("retb"), v("ret"))
-            mms(col("ps3", 392), [], [(ONE, col("retb", h)) for h in range(8)])
-            cp(col("ri", 0), col("ps3", 392))
+            send("k%d" % (t + 1), [(v(nx, KS + 8, KS + 264), [nS, v("Kf")]), (v(nx, RAWS + 8, RAWS + 264), [nS])], PLAN_GO, 6.0)
+            send("q%d" % (t + 1), [(v(nx, RAWQ + 8, RAWQ + 264), [nQ]), (v(nx, KQ, KQ + 256), [nQ, v("KQf")])], PLAN_GO, 6.0)
+            affine(v("retb"), v("ret"), 1.0)
+            mms(col("ps1", 392), [], [(ONE, col("retb", h)) for h in range(8)])
+            cp(col("ri", 0), col("ps1", 392))
             ts(col("ri", 1), col("ri", 0), 1, A.bitwise_and)
-            ts(v("thr"), col("ri", 1), 1.5, A.add, -8.0, A.mult)
+            ts(v("thr"), col("ri", 1), 1.5, A.add, -2.0 ** 14, A.mult)
             affine(v("THR"), v("O264"), v("thr"), None, "s")
         else:
             cp(v("ysw", 0, 256), nS)
@@ -721,8 +905,16 @@ def rank_program(g, core, T, topo):
             store("s", 2, T.yw[:, :], v("ysw", 256, 512))
 
     if not PLANNED:
+        seen = {}
+        for i, e in enumerate(prog):
+            e["visit"] = sum(i >= x for x in starts[1:])
+            x = e["W"][0][0] if i >= starts[0] else "first%d" % i
+            x = x if x.startswith(("ps", "first", "out", "D1", "V0", "sg")) else x.rstrip("012")
+            seen[x, e["visit"]] = seen.get((x, e["visit"]), -1) + 1
+            e["like"] = "%s.%d" % (x, seen[x, e["visit"]])
         PLANNED["plan"] = _schedule(prog)
-    order, queue, deps, done = PLANNED["plan"]
+        PLANNED["prog"] = prog
+    order, queue, done, deps = PLANNED["plan"]
     tok = {}
     for i in order:
         e, q = prog[i], queue[i]

@@ -16,7 +16,7 @@ PART = {}
 
 def _buf(dtype, n, *names):
     for x in names:
-        SCRATCH[x] = ("sbuf", [128] + (list(n) if isinstance(n, tuple) else [n]), dtype)
+        SCRATCH[x] = ("sbuf", [128, n], dtype)
 
 
 def _pool(name, dtype, n, *names):
@@ -28,56 +28,59 @@ def _pool(name, dtype, n, *names):
 _buf(H, W, "E0", "E1", "E2", "PT", "TT", "EC", "FC")
 _buf(H, 8 * BL, "D1", "V0", "TM", "Gn", "FL")
 _buf(H, 2048, "SEL2")
-_buf(H, 128, "ID", "ONE", "SCM", "DM", "LT", "vx", "fx", "dd", "CW", "M130", "sg0", "sgn",
+_buf(H, 128, "ID", "ONE", "SCM", "DM", "LT0", "LT1", "vx0", "vx1", "fx0", "fx1", "dd", "CW", "M130", "sg0", "sgn", "K2c",
      "es", "eb", "ea", "eu", "ew", "sc0", "sc1", "sc2", "so0", "so1", "so2")
 _buf(H, 14 * 128, "IS")
 _buf(H, 8, "G8", "retb")
-_buf(H, 32, "ONES32")
-_buf(H, 132, "TP")
-_buf(H, 264, "THR", "CB", "O264", "TR", "HR")
-_buf(F, 264, "xs", "XC")
-_buf(H, 256, "K2c", "e2p", "kept", "sg1", "gt", "tl", "wm")
-_buf(F, 128, "RM")
+_buf(H, 132, "TP", "THR", "CB", "O132", "HR")
+_buf(H, 264, "TR")
+_buf(F, 264, "xs")
+_buf(F, 132, "XC")
+_buf(H, 256, "BAR", "e2p", "kept", "sg1", "gt", "tl", "wm")
+_buf(F, 128, "RM0", "RM1", "al")
 _buf(F, 512, "ysw")
-_buf(F, 256, "key", "al", "RQ", "IA", "IQ")
+_buf(F, 256, "key", "RQ", "IA", "IQ")
 _buf(F, 32, "kc1", "kcm", "KAP")
-_pool("lf", F, 8, "C32", "SG", "sxf", "sx32", "bsf", "barf", "barK", "fnd", "dcol", "Aq", "nf", "z", "ret", "zq", "vq", "p32", "MB", "pbf")
-_buf(F, 1, "thr")
+_pool("lf", F, 8, "C32", "SG", "sxf", "sx32", "bsf", "barf", "dcol", "Aq", "nf", "z", "ret", "zq", "vq", "p32", "pbf")
+_buf(F, 2, "thr")
 _buf(I, 2, "ri")
-_buf(I, 5 * 256, "tb")
-_buf(I, 256, "craw", "cm", "wi", "Kf", "KQf", "YS", "YQ")
+_buf(I, 10 * 128, "tb")
+_buf(I, 256, "craw", "cm", "wa", "wi", "YS", "YQ")
+_buf(I, 128, "Kf", "KQf")
 _buf(I, 264, "kx", "kd", "Dz")
 _buf(I, 8, "bari")
 _pool("li", I, 8, "pi", "pb", "sx", "sd", "dq", "ui", "ua", "uo", "lo")
-_buf(I, 1056, "KW0", "KW1", "KW2")
+HW, KS, RAWS, RAWQ, KQ = 536, 0, 136, 272, 408
+_buf(I, 2 * HW, "KW0", "KW1", "KW2")
 _buf(I, 512, "ZO0", "ZO1", "ZO2")
 _buf(U, 256, "pl0", "pl1", "pl2", "plo0", "plo1", "cu")
 _buf(U, 8, "ou", "uu", "LO", "FO")
 for _b in range(8):
     SCRATCH["ps%d" % _b] = ("psum", [128, 512], F)
-KS, RAWS, RAWQ, KQ = 0, 272, 536, 800
 
 DMAS = ["ld%d" % k for k in range(12)] + ["ds%d" % k for k in range(5)]
-SEMAPHORES = ["qv", "qs", "qt", "qg"] + DMAS + [a + x + t for a in "al" for x in "prkqs" for t in "12"]
+SEMAPHORES = ["qv", "qs", "qt", "qg"] + DMAS + [a + x + t for a in "al" for x in ("p0", "p1", "k0", "k1", "q0", "q1", "s") for t in "12"]
 VADD = 2
 DL = 2.0 ** -18
 SW, SC = -2.0 ** 31, -2.0 ** -16
 C0 = 1304
 CYC, GATHER, SCATTER, WAKE = 0.83e-3, 1.4, 3.8, 0.22
-AHEAD, PASSES, SLACK, LAZY, SHAKE = (1.0, 1.5, 2.0), 5, 2.0, 0.6, 3.0
-TRIES, STRETCH, SFIX = 100, 1.5, 0.05
-POLISH, HEAT = 8000, 0.05
-TUNE, HOT, PERIOD = 0, 0.3, 25.0
+AHEAD, PASSES, SLACK, LAZY, SFIX = (1.0, 1.5, 2.0), 5, 2.0, 0.6, 0.05
+POLISH, HEAT = 12000, 0.05
 OTHERS = ((0.17, 1.25), (0.27, 0.85))
-FLY, LOAD, NEXT, LATE, EARLY = 1.3, 1.3, 1.25, 0.3, 8.0
+FLY, FOLD, LOAD, NEXT, LATE, EARLY = 1.3, 4.5, 1.3, 1.25, 0.3, 8.0
 PFIX = 0.01
-PULL = {"table": 3.0, "reasons": -3.0, "after": 0.0}
+PULL = {"table": 0.0, "reasons": 0.0, "after": 0.0, "parity": 3.0}
 STORE = 1000.0
 CUTS = (0, 512, 1536, 2560, 3584, 4096)
 QC = "ssssssss"
-KEEP = False
-RUN = (("T2 T3 R0 T5 T7 R1 N1 F0 F1 N3 F2 F3 M0 M1 F4 F5 M2 F6 F7 M3", "T0 T1 T4 T6 N0 N2 N4 N5 N6 N7"),
-       ("T2 T3 R0 T5 F0 F1 T7 R1 N3 F2 F3 M0 M1 F4 F5 N7 F6 F7 M2 M3", "T0 T1 N0 N1 T4 T6 N2 N4 N5 N6"))
+RUN = (("T2 T3 R0 M0 M1 N1 F0 F1 N3 F2 F3 R1 F4 F5 F6 F7 M2 M3", "T0 T1 T4 T5 N0 N2 T6 T7 N4 N5 N6 N7 E0"),
+       ("R0 F0 F1 M0 F2 F3 M1 xs0 ou0 vx0 R1 F4 F5 M2 F6 F7 M3 xs1",
+        "T0 T1 T2 T3 N0 N1 N2 N3 T4 T5 T6 T7 dd0 sg0 N4 gt0 wm0 N5 N6 ab0 N7 E0 E1 tl0 E2 dd1 sg1 E3 gt1 wm1 ab1 E4"))
+LINES = ("E0 E1 E2 E3 E4 E5 E6 E7", "P0 P1 DT0 turn0 P2 P3 DT1 turn1", "S0 S1 S2 S3")
+QF = "v"
+MIDS = ("fill0 Q00", "fill1 Q10")
+ENDS = ()
 SIZE = {H: 2, F: 4, I: 4, U: 2}
 
 
@@ -189,9 +192,8 @@ def _schedule(prog):
                         s = t + WAKE
             return s
 
-        fifo = {q: [i for i in range(n) if q in prog[i]["cost"]][::-1 if back else 1] for q in ("g", "y")}
         while ready:
-            c = [(start(i, q), i, q) for i in ready for q in ([back[i]] if back else prog[i]["cost"]) if q not in fifo or fifo[q][0] == i]
+            c = [(start(i, q), i, q) for i in ready for q in ([back[i]] if back else prog[i]["cost"])]
             first = {}
             for s, i, q in c:
                 first[q] = min(first.get(q, s), s)
@@ -201,8 +203,6 @@ def _schedule(prog):
                 if q2 == q and rank[i2] > rank[i] and s + prog[i]["cost"][q] - s2 > (ahead if rank[i2] < rank[i] + SLACK else LAZY) * (s2 - first[q]):
                     i, s = i2, s2
             ready.discard(i)
-            if q in fifo:
-                fifo[q].pop(0)
             end = s + prog[i]["cost"][q]
             free[q] = end
             queue[i] = q
@@ -225,39 +225,14 @@ def _schedule(prog):
     const = []
     for i in range(n):
         const.append(prog[i]["sem"] is None and min(prog[i]["cost"].values()) < 1.0 and all(const[j] for j in deps[i]))
-
-    def replay(order, queue, wake, slow):
-        free, bank, done = {}, {}, [0.0] * n
-        for i in order:
-            q = queue[i]
-            s = max([free.get(q, 0.0) if q != "x" else 0.0] + [done[j] + (0.0 if q == queue[j] == "t" else wake) for j in deps[i]])
-            for b in prog[i]["P"]:
-                s = max([s] + [t + wake for q2, t in bank.get(b, {}).items() if q2 != q])
-            free[q] = s + prog[i]["cost"][q] * (slow if prog[i].get("by index") else 1.0)
-            done[i] = free[q] + prog[i]["lat"]
-            for b in prog[i]["P"]:
-                bank.setdefault(b, {})[q] = free[q]
-        return max(done)
-
-    def forward(urge, ahead):
-        top = max(urge) - EARLY
-        fw = one(deps, nxt, [(max(u, top) if c else u) + e.get("pull", 0.0) for u, c, e in zip(urge, const, prog)], None, ahead)
-        return (fw[0] + sum(replay(fw[1], fw[2], w, x) for w, x in OTHERS), fw[1], fw[2], fw[3], urge, ahead)
-
     for ahead in AHEAD:
         urge = rank
         for k in range(PASSES):
-            fw = forward(urge, ahead)
+            top = max(urge) - EARLY
+            fw = one(deps, nxt, [(max(u, top) if c else u) + e.get("pull", 0.0) for u, c, e in zip(urge, const, prog)], None, ahead)
             if best is None or fw[0] < best[0]:
                 best = fw
             urge = one(nxt, deps, fw[3], fw[2], ahead)[3]
-    shake = np.random.default_rng(1)
-    for k in range(TRIES):
-        at = float(shake.uniform(0.0, max(best[3])))
-        noise = shake.uniform(-SHAKE, SHAKE, n) * shake.uniform(0.05, 1.0) * (shake.uniform(0.0, 1.0, n) < shake.uniform(0.1, 1.0))
-        fw = forward([u + (float(x) if abs(d - at) < STRETCH else 0.0) for u, x, d in zip(best[4], noise, best[3])], best[5])
-        if fw[0] <= best[0]:
-            best = fw
     return _polish(prog, deps, nxt, best[1], best[2]) + (deps,)
 
 
@@ -265,20 +240,15 @@ def _polish(prog, deps, nxt, order, queue):
     n = len(prog)
     before = [set(d) for d in deps]
     after = [set(x) for x in nxt]
-    for q in ("g", "y"):
-        ix = [i for i in range(n) if q in prog[i]["cost"]]
-        for a, b in zip(ix, ix[1:]):
-            before[b].add(a)
-            after[a].add(b)
-    for b in range(n):
-        for a in prog[b].get("behind", []) if KEEP else []:
-            before[b].add(a)
-            after[a].add(b)
+    ix = [i for i in range(n) if "y" in prog[i]["cost"]]
+    for a, b in zip(ix, ix[1:]):
+        before[b].add(a)
+        after[a].add(b)
     dl = [sorted(d) for d in deps]
     lat = [e["lat"] for e in prog]
     banks = [e["P"] for e in prog]
     ways = ((WAKE, 1.0),) + OTHERS
-    cost = [[{q: c * (x if e["by index"] else 1.0) for q, c in e["cost"].items()} if "by index" in e else e["cost"] for e in prog] for w, x in ways]
+    cost = [[{q: c * (x if e.get("by index") else 1.0) for q, c in e["cost"].items()} for e in prog] for w, x in ways]
 
     def run(order, queue, k):
         wake, ck = ways[k][0], cost[k]
@@ -329,77 +299,6 @@ def _polish(prog, deps, nxt, order, queue):
     pick = np.random.default_rng(2)
     order, queue = list(order), dict(queue)
     now, res = judge(order, queue)
-
-    like = [e["like"] for e in prog]
-    visit = [e["visit"] for e in prog]
-    done = res[0][1]
-    base = [done[[i for i in range(n) if like[i] == "xs.0" and visit[i] == t][0]] for t in range(VI)]
-    when = {}
-    for t in (0, 2, 1):
-        when.update({like[i]: done[i] - base[t] for i in range(n) if visit[i] == t})
-    base = [base[0] + t * PERIOD for t in range(VI)]
-    kin = {}
-    for x in when:
-        kin.setdefault(x.split(".")[0], []).append(x)
-    alike = {}
-    for i in range(n):
-        alike.setdefault(like[i], []).append(i)
-    nb = [len(x) for x in before]
-    al = [sorted(x) for x in after]
-
-    def arrange(when):
-        at = [base[visit[i]] + when[like[i]] for i in range(n)]
-        for i in range(n - 1, -1, -1):
-            for j in al[i]:
-                if at[j] <= at[i]:
-                    at[i] = at[j] - 1e-4
-        o = sorted(range(n), key=lambda x: at[x])
-        left, seen, out, held = list(nb), [False] * n, [], []
-        for i in o:
-            held.append(i)
-            while held:
-                k = held.pop()
-                seen[k] = True
-                if not left[k]:
-                    left[k] = -1
-                    out.append(k)
-                    for j in al[k]:
-                        left[j] -= 1
-                        if not left[j] and seen[j]:
-                            held.append(j)
-        return out, at
-
-    o2, at = arrange(when)
-    new, r2 = judge(o2, queue)
-    cur = (new, o2, queue, r2, at, when)
-    top = cur
-    for step in range(TUNE):
-        new, o2, q2, r2, at, when = cur
-        lk = links(r2[int(pick.integers(len(ways)))])
-        j, i = lk[int(pick.integers(len(lk)))]
-        way = float(pick.uniform())
-        w2 = dict(when)
-        k = i if way < 0.5 else j
-        if pick.uniform() < 0.08 and len(prog[k]["cost"]) > 1:
-            q2 = dict(q2)
-            other = [q for q in prog[k]["cost"] if q != q2[k]][0]
-            q2.update({x: other for x in alike[like[k]] if other in prog[x]["cost"]})
-        else:
-            far = float(pick.exponential()) * (0.02, 0.2, 0.7, 2.0)[int(pick.integers(4))]
-            by = (at[j] - at[i] - far if k == i else at[i] - at[j] + far)
-            w2[like[k]] = at[k] - base[visit[k]]
-            for x in (kin[like[k].split(".")[0]] if pick.uniform() < 0.3 else [like[k]]):
-                if abs(w2[x] - w2[like[k]]) < 1.0 or x == like[k]:
-                    w2[x] = w2[x] + by if x != like[k] else w2[x]
-            w2[like[k]] += by
-        o3, a3 = arrange(w2)
-        n3, r3 = judge(o3, q2)
-        if n3 <= new + HOT * (1 - step / TUNE) * float(pick.exponential()):
-            cur = (n3, o3, q2, r3, a3, w2)
-            if n3 < top[0]:
-                top = cur
-    if top[0] < now:
-        now, order, queue, res = top[:4]
     best = (now, order, queue, res[0][1])
     soft = [links(r) for r in res]
     for step in range(POLISH):
@@ -456,16 +355,17 @@ def rank_program(g, core, T, topo):
     op_now, send_now, lands_now, finish = _tracker(g, T)
     prog = []
     pull = [0.0]
-
-    named, starts = {}, []
+    named, now = {}, [0]
 
     def name(x):
-        named.setdefault(x, []).append(len(prog) - 1)
+        named.setdefault((now[0], x), []).append(len(prog) - 1)
 
-    def line(names):
-        ix = [i for x in names.split() for i in named.pop(x)]
+    def chain(ix):
         for a, b in zip(ix, ix[1:]):
             prog[b].setdefault("behind", []).append(a)
+
+    def line(names, t):
+        chain([i for x in names.split() for i in named.get((t - (x[0] == "<"), x.strip("<")), [])])
 
     def v(name, a=0, b=None, step=1, p=0):
         if name in PART:
@@ -483,6 +383,9 @@ def rank_program(g, core, T, topo):
                 m |= 1 << c
         ap = T[name][p:128, a:b:step] if p else T[name][:, a:b:step]
         return (ap, [(name, m)], len(cols), SIZE[SCRATCH[name][2]], SCRATCH[name][0] == "psum", None)
+
+    def w(name, a, n):
+        return v(name, a, a + n)
 
     def col(name, c, p=0):
         return v(name, c, c + 1, 1, p)
@@ -594,7 +497,7 @@ def rank_program(g, core, T, topo):
         dst = T.cores[(rank + go) % N]
         rid, pid, _ = topo.addr(dst)
         eng = topo.engines(core, dst)
-        if len(moves) == 1:
+        if len(moves) == 1 and len(moves[0][1]) == 1:
             (out, (src,)), n = moves[0], len(eng)
             fn = lambda: g.remote_dma(out[0], src[0], T.sem["a" + name], T.sem["l" + name], pid, rid, topo.mask(core, dst))
         else:
@@ -608,18 +511,19 @@ def rank_program(g, core, T, topo):
         prog.append({"kind": "lands", "fn": None, "R": [("sent" + name, 1)], "W": [k for out, _ in moves for k in out[1]], "P": [], "sem": "a" + name,
                      "inc": n, "cost": {"x": lat}, "lat": 0.0})
 
-    def lanes(name, h, a=0, n=32):
-        return v(name, a + h, a + 8 * n, 8)
-
-    def blk(h):
-        return 4 * (h % 2) + h // 2
+    def lanes(name, c, a=0, n=32, size=128):
+        o = size * (c // 4) + a
+        return v(name, o + c % 4, o + 4 * n, 4)
 
     def IS(k):
         return v("IS", k * 128, k * 128 + 128)
 
+    def SEL(k):
+        return v("SEL2", k * 128, k * 128 + 128)
+
     for k, (a, b) in enumerate(zip(CUTS, CUTS[1:])):
         load("y", 4 + k, v("E0", a, b), T.eff[:, a:b], LOAD + NEXT * b / 1024)
-    load("y", 0, v("KW0", RAWS + 8, RAWS + 264), T.act[:, :], LOAD + NEXT * 4.5)
+    load("y", 0, v("wa"), T.act[:, :], LOAD + NEXT * 4.5)
     load("y", 2, v("sc0"), T.st0[:, :], LOAD + NEXT * 4.7)
     for k in range(2):
         load("y", 10 + k, v("PT", k * 2048, k * 2048 + 2048), T.req[:, k * 2048:k * 2048 + 2048], LOAD + NEXT * (6.7 + 2 * k) + LATE)
@@ -632,7 +536,7 @@ def rank_program(g, core, T, topo):
     gp(lambda e: e.affine_select(ID[0], ONE[0], [[-1, 128]], A.is_equal, 0.0, 0, 1), ID, [ONE])
     gp(lambda e: e.affine_select(G8[0], v("ONE", 0, 8)[0], [[-16, 8]], A.is_ge, 0.0, 0, 1), G8, [ONE])
     gp(lambda e: e.affine_select(G8[0], G8[0], [[16, 8]], A.is_ge, 0.0, 15, -1), G8, [G8])
-    gp(lambda e: e.affine_select(v("LT")[0], ONE[0], [[0, 8], [-1, 16]], A.is_equal, 0.0, 0, 1), v("LT"), [ONE])
+    gp(lambda e: e.affine_select(v("LT0")[0], ONE[0], [[0, 8], [-1, 16]], A.is_equal, 0.0, 0, 1), v("LT0"), [ONE])
     iota(v("pi"), [[0, 8]], 0, 1)
     for a in range(0, 2048, 256):
         iota(v("SEL2", a, a + 256), [[0, 256]], 0, 0)
@@ -643,55 +547,64 @@ def rank_program(g, core, T, topo):
     iota(v("kc1"), [[1, 32]], 1, 0)
     iota(v("KAP"), [[113, 32]], 37 - W, 0)
     iota(v("lo"), [[16, 8]], 15, 0)
-    iota(v("K2c"), [[-64, 32], [0, 8]], 31 * 64, 0)
-    fill(v("K2c", 0, 256, 1, 64), -33280.0 * 512)
-    for h in range(8):
-        fill(v("FL", h * BL + 512, h * BL + BL), -33024 * DL)
-        fill(v("Gn", h * BL + 512, h * BL + BL), -32768 * DL)
-    fill(v("ONES32"), 1.0)
+    iota(v("K2c"), [[-64, 32], [0, 4]], 31 * 64, 0)
+    fill(v("K2c", 0, 128, 1, 64), -33280.0 * 512)
+    for c in range(8):
+        fill(v("FL", c * BL + 512, c * BL + BL), -33024 * DL)
+        fill(v("Gn", c * BL + 512, c * BL + BL), -31744 * DL)
     fill(v("SCM"), 10000.0)
     fill(v("SCM", 0, 128, 16), -10000.0)
     fill(v("CW"), -129.0)
     fill(v("M130"), -130.0)
     fill(v("THR"), -1.5 * 2 ** 14)
     fill(v("CB"), -2.0 ** 25)
-    fill(v("O264"), 1.0)
-    for k, w in enumerate((-7.5, 128.0, -133.5, -141.5)):
-        fill(col("SG", k), w)
+    fill(v("O132"), 1.0)
+    for j in range(2):
+        fill(w("vx%d" % j, 64 - 64 * j, 64), 0.0)
+        fill(w("fx%d" % j, 64 - 64 * j, 64), 0.0)
+    for k, x in enumerate((-7.5, 128.0, -133.5, -141.5)):
+        fill(col("SG", k), x)
     WS = (DL, 48 * DL, -0.5 / DL, -1.0, 1 / DL, -48.0, 2.0 ** 17, -2.0 ** 17, 48.0, 2.0 ** 24, 2.0 ** 25, -3 * 2.0 ** 24, 8192.0, -33 * 8192.0)
-    for k, w in enumerate(WS):
-        affine(IS(k), ID, w)
+    for k, x in enumerate(WS):
+        affine(IS(k), ID, x)
     ts(v("pb"), v("pi"), 15, A.bitwise_and)
     cp(v("pbf"), v("pb"))
     cp(v("LO"), v("lo"))
-    iota(v("XC"), [[-BL, 8], [-16, 33]], 0, 0)
+    iota(v("XC"), [[-BL, 4], [-16, 33]], 0, 0)
     ts(v("XC"), v("XC"), col("pbf", 0), A.subtract)
-    ts(v("FO"), v("XC", 32, 264, 33), -1.0, A.mult)
-    iota(v("HR"), [[0, 8], [1, 33]], 0, 0)
+    for j in range(2):
+        ts(w("FO", 4 * j, 4), v("XC", 32, 132, 33), -1.0, A.mult, 4.0 * BL * j, A.add)
+    iota(v("HR"), [[0, 4], [1, 33]], 0, 0)
     affine(v("HR"), v("HR"), 8192.0, -40.5 * 8192)
-    for h in range(8):
-        ts(v("TR", 33 * h, 33 * h + 33), v("ONE", 0, 33), col("G8", blk(h)), A.mult, -2.0 ** 20, A.mult)
+    for c in range(8):
+        ts(w("TR", 33 * c, 33), v("ONE", 0, 33), col("G8", c), A.mult, -2.0 ** 20, A.mult)
     affine(v("kcm"), v("kc1"), 1.0, -32.5)
     ts(v("C32"), v("C32"), col("pbf", 0), A.add, 32.0, A.mult)
-    ts(v("barf"), v("bari"), 2.0 ** 19, A.mult, -65536.0, A.add)
-    mms(v("ps3", 0, 128), [(v("LT"), v("LT"))])
+    for j in range(2):
+        ts(w("barf", 4 * j, 4), v("bari", j, 8, 2), -2.0 ** 19, A.mult, 65536.0, A.add)
+    for c in range(8):
+        affine(lanes("BAR", c), v("ONE", 0, 32), col("barf", c), None, "s")
+    mms(v("ps3", 0, 128), [(v("LT0"), v("LT0"))])
     act(v("DM"), v("ps3", 0, 128), ACT.Identity)
 
-    for h in range(8):
-        cp(v("pl0", 32 * blk(h), 32 * blk(h) + 32), lanes("KW0", h, RAWS + 8))
-    iota(v("al"), [[-4096, 32], [0, 8]], -4096, 0)
-    Kc, KQc = v("ps5", 256, 512), v("ps6", 0, 256)
+    for c in range(8):
+        cp(w("pl0", 32 * c, 32), v("wa", 2 * (c % 4) + c // 4, 256, 8))
+    iota(v("al"), [[-4096, 32], [0, 4]], -4096, 0)
+    Kc, KQc = v("ps6", 0, 128), v("ps6", 128, 256)
     act(Kc, v("al"), ACT.Identity)
     act(KQc, v("al"), ACT.Identity, 2.0)
-    tt(v("KW0", KS + 8, KS + 264), v("KW0", RAWS + 8, RAWS + 264), Kc, A.add)
-    ts(v("KW0", RAWQ + 8, RAWQ + 264), v("wi"), 1.0, A.add)
-    tt(v("KW0", KQ, KQ + 256), v("KW0", RAWQ + 8, RAWQ + 264), KQc, A.add)
-    for t in range(VI):
-        fill(v("KW%d" % t, KS + 264, KS + 272), -4096 * 33)
-        fill(v("KW%d" % t, RAWS, RAWS + 8), 0)
-        fill(v("KW%d" % t, RAWQ, RAWQ + 8), 0)
-    iota(v("Kf"), [[-4096, 32], [0, 8]], -4096, 0)
-    iota(v("KQf"), [[-8192, 32], [0, 8]], -8192, 0)
+    for j in range(2):
+        o = j * HW
+        tt(w("KW0", o + KS + 4, 128), v("wa", j, 256, 2), Kc, A.add)
+        cp(w("KW0", o + RAWS + 4, 128), v("wa", j, 256, 2))
+        ts(w("KW0", o + RAWQ + 4, 128), v("wi", j, 256, 2), 1.0, A.add)
+        tt(w("KW0", o + KQ, 128), w("KW0", o + RAWQ + 4, 128), KQc, A.add)
+        for t in range(VI):
+            fill(w("KW%d" % t, o + KS + 132, 4), -4096 * 33)
+            fill(w("KW%d" % t, o + RAWS, 4), 0)
+            fill(w("KW%d" % t, o + RAWQ, 4), 0)
+    iota(v("Kf"), [[-4096, 32], [0, 4]], -4096, 0)
+    iota(v("KQf"), [[-8192, 32], [0, 4]], -8192, 0)
 
     for c in range(8):
         a, b = c * 512, c * 512 + 512
@@ -705,28 +618,24 @@ def rank_program(g, core, T, topo):
         else:
             act(p, v("E0", a, b), ACT.Identity, None, -192.0)
             tt(v("TT", a, b), v("TM", a, b), p, A.add)
-
-    def SEL(k):
-        return v("SEL2", k * 128, k * 128 + 128)
+    act(v("sg0"), v("sc0"), ACT.Sign, None, col("SG", 0))
+    mms(v("ps1", 256, 384), [(IS(0), v("sc0")), (IS(1), v("sg0"))])
 
     for t in range(VI):
         pl, KW, so, ZO = "pl%d" % t, "KW%d" % t, v("so%d" % t), "ZO%d" % t
         last = t == VI - 1
         Et, En = "E%d" % t, "E%d" % ((t + 1) % 3)
-
+        now[0] = t
         pull[0] = 0.0
-        if t == 0:
-            act(v("sg0"), v("sc0"), ACT.Sign, None, col("SG", 0))
-            mms(v("ps1", 256, 384), [(IS(0), v("sc0")), (IS(1), v("sg0"))])
-        starts.append(len(prog))
-        for h in range(8):
-            if t:
-                affine(v("D1", h * BL, h * BL + 16), v("sc%d" % t, 16 * h, 16 * h + 16), 1.0)
-            else:
-                affine(v("D1", blk(h) * BL, blk(h) * BL + 16), v("ps1", 256 + 16 * h, 272 + 16 * h), 1.0, -144 * DL)
-        run_v, run_s = RUN[min(t, 1)]
+
         for c in range(8):
-            affine(v("D1", c * BL + 16, c * BL + BL), ind(v("TT"), v(pl, c * 32, c * 32 + 32)), DL, None, "v" if "T%d" % c in run_v else "s")
+            if t:
+                affine(w("D1", c * BL, 16), w("sc%d" % t, 16 * c, 16), 1.0, None, "s")
+            else:
+                affine(w("D1", c * BL, 16), w("ps1", 256 + 32 * (c % 4) + 16 * (c // 4), 16), 1.0, -144 * DL)
+        run_v = RUN[min(t, 1)][0].split()
+        for c in range(8):
+            affine(w("D1", c * BL + 16, 512), ind(v("TT"), w(pl, c * 32, 32)), DL, None, "v" if "T%d" % c in run_v else "s")
             name("T%d" % c)
         for j in range(2):
             for k in range(16):
@@ -737,21 +646,22 @@ def rank_program(g, core, T, topo):
             for k in range(16):
                 scan(v("TM", 4 * j * BL + k, 4 * (j + 1) * BL, 16), v("D1", 4 * j * BL + k, 4 * (j + 1) * BL, 16), v("TP"), 0.0, A.mult, A.max)
                 name("M%d" % (2 * j + k // 8))
-        cnt = v("ps0", 0, 264)
-        group([(cnt, ONE, v("CB")), (cnt, ONE, v("THR"))], True, False, "a")
         for c in range(8):
-            a = c * BL
-            affine(v("Gn", a, a + 512), ind(v("PT"), v(pl, c * 32, c * 32 + 32)), -DL, -32692.5 * DL, "v" if "N%d" % c in run_v else "s")
+            a, cnt = c * BL, ("ps0", "ps5")[c // 4]
+            if c % 4 == 0:
+                group([(v(cnt, 0, 132), ONE, v("CB"))], True, False, "a")
+                group([(v(cnt, 0, 132), ONE, v("THR"))], False, False, "b")
+            affine(w("Gn", a, 512), ind(v("PT"), w(pl, c * 32, 32)), -DL, -32692.5 * DL, "v" if "N%d" % c in run_v else "s")
             name("N%d" % c)
-            scan(v("FL", a, a + 512), v("V0", a, a + 512), v("Gn", a, a + 512), -1.0, A.max, A.add)
+            scan(w("FL", a, 512), w("V0", a, 512), w("Gn", a, 512), -1.0, A.max, A.add)
             name("F%d" % c)
-            if c == 7:
-                line(run_v)
-                line(run_s)
             if c % 2:
                 for k0 in range(0, 16, 4):
-                    end = c == 7 and k0 == 12
-                    group([(v("ps0", 33 * c - 33, 33 * c + 33), SEL(k), v("FL", a - BL + k, a + BL, 16)) for k in range(k0, k0 + 4)], False, end, "c" if end else "b")
+                    end = c % 4 == 3 and k0 == 12
+                    group([(w(cnt, 33 * (c % 4) - 33, 66), SEL(k), v("FL", a - BL + k, a + BL, 16)) for k in range(k0, k0 + 4)], False, end, "c" if end else "b")
+                    name("P%d" % (c // 2))
+                    if end:
+                        prog[-1]["W"] += v(cnt, 0, 132)[1]
 
         pull[0] = PULL["table"]
         affine(so, ind(v("V0"), v("FO")), 1.0)
@@ -760,158 +670,222 @@ def rank_program(g, core, T, topo):
         act(v("sgn"), so, ACT.Sign, 1 / DL, col("SG", 1))
         for a in range(0, 16, 4):
             group([(v("ps4", 384, 392), SEL(k), v("so%d" % t, k, 128, 16)) for k in range(a, a + 4)], a == 0, a == 12)
+            name("us")
         ts(v("ui"), v("ps4", 384, 392), 1 / (SW * DL), A.mult)
         ts(v("ua"), v("ui"), 31, A.bitwise_and)
         tt(v("uo"), v("ua"), v("C32"), A.add)
         cp(v("uu"), v("uo"))
+        name("uu")
         act(v("es"), ind(v(Et), v("uu")), ACT.Identity)
-        mms(v("ps4", 256, 384), [(IS(4), so), (IS(5), v("sgn")), (ID, v("es"))])
-        act(v("eb"), v("ps4", 256, 384), ACT.Identity, 0.5, 129.75 + 72)
+        name("es")
+        mms(v("ps7", 0, 128), [(IS(4), so), (IS(5), v("sgn")), (ID, v("es"))])
+        act(v("eb"), v("ps7", 0, 128), ACT.Identity, 0.5, 129.75 + 72)
         tt(ind(v(En), v("uu")), v("eb"), v("M130"), A.add)
+        name("En")
         if last:
             store("y", 0, T.ye[:, :], v(En))
         else:
             copy(3 + t, v("E%d" % ((t + 2) % 3)), v(En))
             act(v("eu"), v("eb"), ACT.Sign, None, col("SG", 2))
             act(v("ew"), v("eb"), ACT.Sign, None, col("SG", 3))
-            mms(v("ps4", 128, 256), [(ID, v("eb")), (IS(6), v("eu")), (IS(7), v("ew")), (IS(8), v("ew"))])
-            act(v("ea"), v("ps4", 128, 256), ACT.Identity, None, -274.0)
+            mms(v("ps7", 128, 256), [(ID, v("eb")), (IS(6), v("eu")), (IS(7), v("ew")), (IS(8), v("ew"))])
+            act(v("ea"), v("ps7", 128, 256), ACT.Identity, None, -274.0)
+            name("ea")
             cp(ind(v("TT"), v("uu")), v("ea"))
+            name("TT")
         pull[0] = 0.0
-
-        scan(v("xs", 263, None, -1), v("ps0", 263, None, -1), v("XC", 263, None, -1), 0.0, A.max, A.min)
-        ts(v("ou"), v("xs", 0, 264, 33), -1.0, A.mult)
-        for h in range(8):
-            scan(v("kx", 33 * h + 32, 33 * h - 1, -1), v("ps0", 33 * blk(h) + 32, 33 * blk(h) - 1, -1), v(KW, KS + 264 + h, KS + h, -8), 0.0, A.max, A.min)
-        kx = v("kx", 0, 264, 33)
-        cp(v("vx"), ind(v("TM"), v("ou")))
-        act(v("fx"), ind(v("FL"), v("ou")), ACT.Identity)
-        act(v("dd"), ind(v("Gn"), v("ou")), ACT.Identity)
-        mms(v("ps3", 128, 256), [(ID, v("dd")), (IS(3), v("fx"))])
-        for a in range(4):
-            affine(v("wm", 64 * a, 64 * a + 64), v("ps3", 128 + 64 * (a // 2), 192 + 64 * (a // 2)), SC / (32 * DL), 764 * SC, "s")
-        ts(v(KW, KS, KS + 8), kx, 2.0 ** 18, A.add)
-        ts(v("sx"), kx, 4095, A.bitwise_and)
-        cp(v("sxf"), v("sx"))
-        affine(v("sx32"), v("sxf"), 1 / 32)
-        ts(v("fnd"), kx, 131072.5, A.add, 2.0 ** 26, A.mult)
-        tt(v("barK"), v("barf"), v("fnd"), A.min)
-        for h in range(8):
-            act(lanes("sg1", h), v("XC", 33 * blk(h), 33 * blk(h) + 32), ACT.Sign, -1.0, col("xs", 33 * blk(h)))
-        act(v("gt"), v("sg1"), ACT.Relu)
-        G = v("ps6", 0, 256)
-        mms(G, [(IS(9), v("O264", 0, 256)), (IS(10), v("sg1")), (IS(11), v("gt")), (IS(12), v("gt"))])
-
-        DT = v("ps1", 0, 128)
-        mms(DT, [(v("CW"), v("ONE")), (v("fx"), IS(2)), (v("vx"), IS(3))])
-        scan(v("RM"), v("SCM"), DT, 0.0, A.min, A.max)
-        tt(v("LT"), ind(v("RM"), v("LO")), v("DM"), A.mult)
-        mms(v("ps2", 0, 264), [(ONE, v("HR")), (v("LT"), v("TR"))])
-        for h in range(8):
-            scan(v("kd", 33 * h, 33 * h + 33), v("ps2", 33 * h, 33 * h + 33), lanes(KW, h, KS, 33), 0.0, A.min, A.max)
-        kd = v("kd", 32, 264, 33)
-        ts(v("sd"), kd, 4095, A.bitwise_and)
-        ts(v("dq"), kd, 12, A.arith_shift_right, 63, A.bitwise_and)
-        tt(v("p32"), v("sd"), v("sx32"), A.mult)
-        ts(v("bsf"), v("p32"), -262016.484375, A.add, 2.0 ** 23 + 4096 + 262016 + 97 * t, A.add)
 
         for j in range(2):
-            for h in range(j, 8, 2):
-                ts(lanes("craw", h), v("KAP"), col("sxf", h), A.mult, col("bsf", h), A.add)
-            ts(v("cm", j, 256, 2), v("craw", j, 256, 2), 4095, A.bitwise_and)
-            cp(v("cu", j * 128, j * 128 + 128), v("cm", j, 256, 2))
-        for c in range(8):
-            a, j = c * 512, c // 4
-            affine(v("EC", a, a + 512), ind(v(Et), v("cu", c * 32, c * 32 + 32)), SC, (C0 + 0.5) * SC, QC[c])
-            for k in range(a, a + 512, 128):
-                scan(v("FC", k, k + 128), v("EC", k, k + 128), v("wm", j * 128, j * 128 + 128), -1.0, A.max, A.add)
-            if c % 2:
-                x = (c // 2 % 2) * 128 + j
-                cn = v("ps%d" % (3 + c // 2 % 2), j * 64, 64 + j * 64)
-                mms(cn, [(ONE, v("K2c", x, x - j + 128, 2))], [(SEL(k), v("FC", a - 512 + k, a + 512, 16)) for k in range(16)])
-                tt(v("key", x, x - j + 128, 2), v("cm", x, x - j + 128, 2), cn, A.add)
+            cs, o, y, x4 = range(4 * j, 4 * j + 4), j * HW, 128 * j, 4 * j
+            cnt, vx, fx, RM, LT = ("ps0", "ps5")[j], "vx%d" % j, "fx%d" % j, v("RM%d" % j), v("LT%d" % j)
 
-        pull[0] = 0.0
-        ts(v("dcol"), v("dq"), -64.0, A.add)
-        ts(v("Aq"), v("sd"), 16385.0, A.add)
-        for h in range(8):
-            act(lanes("ps7", h, 256), v("kc1"), ACT.Abs, None, col("dcol", h))
-            ts(lanes("e2p", h), lanes(KW, h, RAWQ + 8), 16384.0, A.add, col("Aq", h), A.not_equal)
-        tt(v("kept"), v("e2p"), v("ps7", 256, 512), A.min)
-        for h in range(8):
-            scan(lanes("Dz", h, 8), v("ONES32"), lanes("kept", h), 0.0, A.add, A.subtract)
-        cp(v("nf"), v("Dz", 256, 264))
-        for h in range(8):
-            act(lanes("tl", h), v("kcm"), ACT.Sign, None, col("nf", h))
-        TL = v("ps6", 256, 512)
-        mms(TL, [(IS(13), v("tl"))])
-        for b in range(5):
-            s = 8 << b
-            m = 256 - s
-            tb = v("tb", b * 256, b * 256 + m)
-            ts(tb, v("Dz", s, 256), b, A.arith_shift_right, 1, A.bitwise_and)
-            for a, mv in ((KS + 8, "ps5"), (KQ, "ps7")):
-                pull[0] = PULL["reasons"] if a == KQ and not last else 0.0
-                scan(v(mv, 0, m), tb, v(KW, a + s, a + 256), 0.0, A.max, A.mult)
-                tt(v(KW, a, a + m), v(KW, a, a + m), v(mv, 0, m), A.min)
+            def s4(name):
+                return w(name, x4, 4)
+
+            def hv(name, a=0, n=128):
+                return w(name, y + a, n)
+
+            def nm(x):
+                name("%s%d" % (x, j))
+
+            scan(v("xs", 132 * j + 131, 132 * j - 1, -1), v(cnt, 131, None, -1), v("XC", 131, None, -1), 0.0, A.max, A.min)
+            nm("xs")
+            ts(s4("ou"), v("xs", 132 * j, 132 * j + 132, 33), -1.0, A.mult)
+            nm("ou")
+            for c in cs:
+                scan(v("kx", 33 * c + 32, 33 * c - 1, -1), v(cnt, 33 * (c % 4) + 32, 33 * (c % 4) - 1, -1), v(KW, o + KS + 132 + c % 4, o + KS + c % 4, -4), 0.0, A.max, A.min)
+                nm("kx")
+            kx = v("kx", 132 * j, 132 * j + 132, 33)
+            cp(w(vx, 64 * j, 64), ind(w("TM", 4 * BL * j, 4 * BL), s4("ou")))
+            nm("vx")
+            affine(w(fx, 64 * j, 64), ind(w("FL", 4 * BL * j, 4 * BL), s4("ou")), 1.0, None, QF)
+            nm("fx")
+            act(w("dd", 64 * j, 64), ind(w("Gn", 4 * BL * j, 4 * BL), s4("ou")), ACT.Identity)
+            nm("dd")
+            mms(w("ps3", 128 + 64 * j, 64), [(ID, w("dd", 64 * j, 64)), (IS(3), w(fx, 64 * j, 64))])
+            nm("dm")
+            for a in range(2):
+                affine(hv("wm", 64 * a, 64), w("ps3", 128 + 64 * j, 64), SC / (32 * DL), 764 * SC, "s")
+                nm("wm")
+            ts(w(KW, o + KS, 4), kx, 2.0 ** 18, A.add)
+            ts(s4("sx"), kx, 4095, A.bitwise_and)
+            cp(s4("sxf"), s4("sx"))
+            affine(s4("sx32"), s4("sxf"), 1 / 32, None, "s")
+            for c in cs:
+                act(lanes("sg1", c), w("XC", 33 * (c % 4), 32), ACT.Sign, -1.0, col("xs", 33 * c))
+                nm("sg")
+            act(hv("gt"), hv("sg1"), ACT.Relu)
+            nm("gt")
+            G = hv("ps6")
+            mms(G, [(IS(9), ONE), (IS(10), hv("sg1")), (IS(11), hv("gt")), (IS(12), hv("gt"))])
+            nm("G")
+
+            DT = hv("ps1")
+            mms(DT, [(v("CW"), ONE), (v(fx), IS(2)), (v(vx), IS(3))])
+            nm("DT")
+            scan(RM, v("SCM"), DT, 0.0, A.min, A.max)
+            nm("RM")
+            tt(LT, ind(RM, v("LO")), v("DM"), A.mult)
+            nm("LT")
+            mms(w("ps2", 132 * j, 132), [(ONE, v("HR")), (LT, w("TR", 132 * j, 132))])
+            nm("turn")
+            for c in cs:
+                scan(w("kd", 33 * c, 33), w("ps2", 33 * c, 33), lanes(KW, c, KS, 33, HW), 0.0, A.min, A.max)
+                nm("kd")
+            kd = v("kd", 132 * j + 32, 132 * j + 132, 33)
+            ts(s4("sd"), kd, 4095, A.bitwise_and)
+            nm("sd")
+            ts(s4("dq"), kd, 12, A.arith_shift_right, 63, A.bitwise_and)
+            tt(s4("p32"), s4("sd"), s4("sx32"), A.mult)
+            ts(s4("bsf"), s4("p32"), -262016.484375, A.add, 2.0 ** 23 + 4096 + 262016 + 97 * t, A.add)
+
+            for c in cs:
+                ts(lanes("craw", c), v("KAP"), col("sxf", c), A.mult, col("bsf", c), A.add)
+                nm("c")
+            ts(hv("cm"), hv("craw"), 4095, A.bitwise_and)
+            nm("cm")
+            cp(hv("cu"), hv("cm"))
+            nm("cu")
+            for c in cs:
+                a = c * 512
+                affine(w("EC", a, 512), ind(v(Et), w("cu", c * 32, 32)), SC, (C0 + 0.5) * SC, QC[c])
+                name("E%d" % c)
+                for k in range(a, a + 512, 128):
+                    scan(w("FC", k, 128), w("EC", k, 128), hv("wm"), -1.0, A.max, A.add)
+                    name("C%d" % c)
+                if c % 2:
+                    x = (c // 2 % 2) * 64
+                    cn = w("ps%d" % (3 + c // 2 % 2), j * 64, 64)
+                    mms(cn, [(ONE, w("K2c", x, 64)), (ID, hv("BAR", x, 64))], [(SEL(k), v("FC", a - 512 + k, a + 512, 16)) for k in range(16)])
+                    name("S%d" % (c // 2))
+                    tt(hv("key", x, 64), hv("cm", x, 64), cn, A.add)
+                    name("key%d" % (c // 2))
+
+            ts(s4("dcol"), s4("dq"), -64.0, A.add)
+            ts(s4("Aq"), s4("sd"), 16385.0, A.add)
+            for c in cs:
+                act(lanes("ps7", c, 256), v("kc1"), ACT.Abs, None, col("dcol", c))
+                nm("ab")
+                ts(lanes("e2p", c), lanes(KW, c, RAWQ + 4, 32, HW), 16384.0, A.add, col("Aq", c), A.not_equal)
+                nm("e")
+            tt(hv("kept"), hv("e2p"), hv("ps7", 256), A.min)
+            nm("kept")
+            for c in cs:
+                scan(lanes("Dz", c, 4, 32, 132), v("ONE", 0, 32), lanes("kept", c), 0.0, A.add, A.subtract)
+                nm("D")
+            cp(s4("nf"), w("Dz", 132 * j + 128, 4))
+            for c in cs:
+                act(lanes("tl", c), v("kcm"), ACT.Sign, None, col("nf", c))
+                nm("tl")
+            TL = hv("ps6", 256)
+            mms(TL, [(IS(13), hv("tl"))])
+            nm("TL")
+            for b in range(5):
+                s = 4 << b
+                m = 128 - s
+                tb = w("tb", 640 * j + 128 * b, m)
+                ts(tb, w("Dz", 132 * j + s, m), b, A.arith_shift_right, 1, A.bitwise_and)
+                name("b%d%d" % (j, b))
+                scan(hv("ps0", 256, m), tb, w(KW, o + KS + 4 + s, m), 0.0, A.max, A.mult)
+                name("m%d%d" % (j, b))
+                tt(w(KW, o + KS + 4, m), w(KW, o + KS + 4, m), hv("ps0", 256, m), A.min)
+                name("r%d%d" % (j, b))
+            tt(hv("ps5", 256), hv("cm"), TL, A.add)
+            nm("cT")
+            tt(w(KW, o + KS + 4, 128), w(KW, o + KS + 4, 128), hv("ps5", 256), A.min)
+            nm("fill")
+            pull[0] = 0.0 if last else PULL["reasons"]
+            for b in range(5):
+                s = 4 << b
+                m = 128 - s
+                scan(hv("ps7", 0, m), w("tb", 640 * j + 128 * b, m), w(KW, o + KQ + s, m), 0.0, A.max, A.mult)
+                name("Q%d%d" % (j, b))
+                tt(w(KW, o + KQ, m), w(KW, o + KQ, m), hv("ps7", 0, m), A.min)
+                name("q%d%d" % (j, b))
+            tt(hv("RQ"), w(KW, o + KQ, 128), TL, A.min)
+            nm("RQ")
             pull[0] = 0.0
-        tt(v("ps5", 256, 512), v("cm"), TL, A.add)
-        tt(v(KW, KS + 8, KS + 264), v(KW, KS + 8, KS + 264), v("ps5", 256, 512), A.min)
-        tt(v("RQ"), v(KW, KQ, KQ + 256), TL, A.min)
-        for a, tmp, out in ((RAWS, "ps0", "IA"), (RAWQ, "ps2", "IQ")):
-            tt(v(tmp, 0, 256), v(KW, a, a + 256), G, A.add)
-            tt(v(out), v(KW, a + 8, a + 264), v(tmp, 0, 256), A.max)
+            for a, tmp, out in ((RAWS, "ps0", "IA"), (RAWQ, "ps1", "IQ")):
+                tt(hv(tmp, 256), w(KW, o + a, 128), G, A.add)
+                nm("t" + out)
+                tt(hv(out), w(KW, o + a + 4, 128), hv(tmp, 256), A.max)
+                nm(out)
 
-        for j in range(2):
-            hs = range(j, 8, 2)
-
-            def u(name, a=0, n=8):
-                return v(name, a + j, a + n, 2)
-
-            for h in hs:
-                red(col("MB", h), lanes("key", h), A.max)
-            tt(u("z"), u("MB"), u("barK"), A.subtract)
-            for h in hs:
-                ts(lanes("ps5", h), lanes(KW, h, KS + 8), col("z", h), A.max)
-            tt(u("YS", 0, 256), u("IA", 0, 256), u("ps5", 0, 256), A.min)
-            ts(u(ZO, 0, 256), u("YS", 0, 256), 4095, A.bitwise_and)
+            for c in cs:
+                red(col("z", c), lanes("key", c), A.max)
+                nm("z")
+            for c in cs:
+                ts(lanes("ps0", c, 256), lanes(KW, c, KS + 4, 32, HW), col("z", c), A.max)
+                nm("g")
+            tt(hv("YS"), hv("IA"), hv("ps0", 256), A.min)
+            nm("Y")
+            nS, nQ, nx = hv(ZO), hv(ZO, 256), "KW%d" % (t + 1)
+            ts(nS, hv("YS"), 4095, A.bitwise_and)
+            nm("Z")
             if not last:
-                for h in hs:
-                    cp(v("plo%d" % t, 32 * blk(h), 32 * blk(h) + 32), lanes(ZO, h))
-                send("pr"[j] + str(t + 1), [(v("pl%d" % (t + 1), 128 * j, 128 * j + 128), [v("plo%d" % t, 128 * j, 128 * j + 128)])], PLAN_GO, FLY)
-        pull[0] = 0.0 if last else PULL["after"]
-        ts(v("ret"), v("z"), 0.0, A.is_lt)
-        tt(v("zq"), v("z"), v("Aq"), A.min)
-        act(v("vq"), v("zq"), ACT.Relu)
-        for h in range(8):
-            act(lanes("ps7", h), lanes("RQ", h), ACT.Identity, col("ret", h), col("vq", h))
-        tt(v("YQ"), v("IQ"), v("ps7", 0, 256), A.min)
-        ts(v(ZO, 256, 512), v("YQ"), 8191, A.bitwise_and)
-        nS, nQ = v(ZO, 0, 256), v(ZO, 256, 512)
+                for c in cs:
+                    cp(w("plo%d" % t, 32 * c, 32), lanes(ZO, c))
+                    nm("L")
+                send("p%d%d" % (j, t + 1), [(hv("pl%d" % (t + 1)), [hv("plo%d" % t)])], PLAN_GO, FLY)
+                send("k%d%d" % (j, t + 1), [(w(nx, o + KS + 4, 128), [nS, v("Kf")]), (w(nx, o + RAWS + 4, 128), [nS])], PLAN_GO, FOLD)
+            else:
+                cp(v("ysw", j, 256, 2), nS)
+            pull[0] = 0.0 if last else PULL["after"]
+            ts(s4("ret"), s4("z"), 0.0, A.is_lt)
+            tt(s4("zq"), s4("z"), s4("Aq"), A.min)
+            act(s4("vq"), s4("zq"), ACT.Relu)
+            nm("vq")
+            for c in cs:
+                act(lanes("ps7", c), lanes("RQ", c), ACT.Identity, col("ret", c), col("vq", c))
+                nm("gq")
+            tt(hv("YQ"), hv("IQ"), hv("ps7"), A.min)
+            nm("YQ")
+            ts(nQ, hv("YQ"), 8191, A.bitwise_and)
+            nm("ZQ")
+            if not last:
+                send("q%d%d" % (j, t + 1), [(w(nx, o + RAWQ + 4, 128), [nQ]), (w(nx, o + KQ, 128), [nQ, v("KQf")])], PLAN_GO, FOLD)
+            else:
+                ts(v("ysw", 256 + j, 512, 2), nQ, -1.0, A.add)
+            pull[0] = 0.0
         if not last:
-            nx = "KW%d" % (t + 1)
-            send("k%d" % (t + 1), [(v(nx, KS + 8, KS + 264), [nS, v("Kf")]), (v(nx, RAWS + 8, RAWS + 264), [nS])], PLAN_GO, 6.0)
-            send("q%d" % (t + 1), [(v(nx, RAWQ + 8, RAWQ + 264), [nQ]), (v(nx, KQ, KQ + 256), [nQ, v("KQf")])], PLAN_GO, 6.0)
-            affine(v("retb"), v("ret"), 1.0)
-            mms(col("ps1", 392), [], [(ONE, col("retb", h)) for h in range(8)])
-            cp(col("ri", 0), col("ps1", 392))
-            ts(col("ri", 1), col("ri", 0), 1, A.bitwise_and)
-            ts(v("thr"), col("ri", 1), 1.5, A.add, -2.0 ** 14, A.mult)
-            affine(v("THR"), v("O264"), v("thr"), None, "s")
+            pull[0] = PULL["parity"]
+            ts(v("retb"), v("z"), 0.0, A.is_lt)
+            mms(col("ps6", 0), [], [(ONE, col("retb", c)) for c in range(8)])
+            ts(col("ri", 0), col("ps6", 0), -0.5, A.add, 0.5, A.mult)
+            ts(col("thr", 0), col("ps6", 0), -2.0 ** 14, A.mult)
+            ts(col("thr", 1), col("ri", 0), 2.0 ** 15, A.mult, -1.5 * 2 ** 14, A.add)
+            affine(v("THR"), v("O132"), col("thr", 0), col("thr", 1))
+            name("THR")
+            pull[0] = 0.0
         else:
-            cp(v("ysw", 0, 256), nS)
             store("y", 1, T.ys[:, :], v("ysw", 0, 256))
-            ts(v("ysw", 256, 512), nQ, -1.0, A.add)
             store("s", 2, T.yw[:, :], v("ysw", 256, 512))
 
+    chain([i for i, e in enumerate(prog) if "y" in e["cost"]])
+    for t in range(VI):
+        for x in RUN[min(t, 1)] + LINES + (ENDS if t == VI - 1 else MIDS):
+            line(x, t)
     if not PLANNED:
-        seen = {}
-        for i, e in enumerate(prog):
-            e["visit"] = sum(i >= x for x in starts[1:])
-            x = e["W"][0][0] if i >= starts[0] else "first%d" % i
-            x = x if x.startswith(("ps", "first", "out", "D1", "V0", "sg")) else x.rstrip("012")
-            seen[x, e["visit"]] = seen.get((x, e["visit"]), -1) + 1
-            e["like"] = "%s.%d" % (x, seen[x, e["visit"]])
         PLANNED["plan"] = _schedule(prog)
         PLANNED["prog"] = prog
     order, queue, done, deps = PLANNED["plan"]

@@ -9,6 +9,7 @@ W, L, B, VI = 4096, 32, 128, 3
 PLAN_GO, STATE_GO = 3, 1
 H, F, I, U = "bfloat16", "float32", "int32", "uint16"
 BL = 33 * 16
+LW = 34
 
 SCRATCH = {}
 PART = {}
@@ -25,62 +26,70 @@ def _pool(name, dtype, n, *names):
         PART[x] = (name, k * n, n)
 
 
-_buf(H, W, "E0", "E1", "E2", "PT", "TT", "EC", "FC")
-_buf(H, 8 * BL, "D1", "V0", "TM", "Gn", "FL")
-_buf(H, 2048, "SEL2")
-_buf(H, 128, "ID", "ONE", "SCM", "DM", "LT0", "LT1", "vx0", "vx1", "fx0", "fx1", "dd", "CW", "M130", "sg0", "sgn", "K2c",
-     "es", "eb", "ea", "eu", "ew", "sc0", "sc1", "sc2", "so0", "so1", "so2")
-_buf(H, 14 * 128, "IS")
-_buf(H, 8, "G8", "retb")
-_buf(H, 132, "TP", "THR", "CB", "O132", "HR")
-_buf(H, 264, "TR")
-_buf(F, 264, "xs")
-_buf(F, 132, "XC")
-_buf(H, 256, "BAR", "e2p", "kept", "sg1", "gt", "tl", "wm")
-_buf(F, 128, "RM0", "RM1", "al")
-_buf(F, 512, "ysw")
-_buf(F, 256, "key", "RQ", "IA", "IQ")
-_buf(F, 32, "kc1", "kcm", "KAP")
-_pool("lf", F, 8, "C32", "SG", "sxf", "sx32", "bsf", "barf", "dcol", "Aq", "nf", "z", "ret", "zq", "vq", "p32", "pbf")
+_buf(H, W, "E0", "E1", "PT", "EC", "FC")
+_buf(H, W + VI * B, "TT")
+_buf(H, 8 * BL, "D1", "V0", "Gn", "FL")
+_buf(H, 288, "SEL")
+_buf(H, 128, "ID", "ONE", "fx", "dd", "M130", "K2c", "K3c", "es", "eb", "ea", "eu", "ew", "st", "so0", "so1", "so2")
+_buf(H, 1024, "WT")
+_buf(H, 6 * 128, "IS")
+_buf(H, 8, "G8", "retb", "UB")
+_buf(H, 66, "THR")
+_buf(H, 64, "PERM")
+_buf(H, 512, "wm", "hit")
+_buf(F, 264, "xs", "kx")
+_buf(F, 66, "XC", "XC8")
+_buf(F, 64, "kc1")
+_buf(H, 264, "sg1")
+_buf(H, 256, "BAR", "e2p", "kept", "tl")
+_buf(F, 128, "al", "aq")
+_buf(F, 512, "ysw", "RK")
+_buf(F, 256, "RQ", "IA", "IQ")
+_buf(F, 32, "kcm", "KAP")
+_pool("lf", F, 8, "C32", "SG", "sxf", "sx32", "bsf", "barf", "dcol", "Aq", "nf", "ret", "zq", "vq", "p32", "pbf", "kx0", "pb16", "sgz")
 _buf(F, 2, "thr")
 _buf(I, 2, "ri")
 _buf(I, 10 * 128, "tb")
-_buf(I, 256, "craw", "cm", "wa", "wi", "YS", "YQ")
+_buf(I, 256, "craw", "cm", "wa", "wi", "YS", "YQ", "kd")
 _buf(I, 128, "Kf", "KQf")
-_buf(I, 264, "kx", "kd", "Dz")
+_buf(I, 264, "Dz")
 _buf(I, 8, "bari")
-_pool("li", I, 8, "pi", "pb", "sx", "sd", "dq", "ui", "ua", "uo", "lo")
-HW, KS, RAWS, RAWQ, KQ = 536, 0, 136, 272, 408
+_pool("li", I, 8, "pi", "pb", "sx", "sd", "dq", "ui", "ua", "uo", "wo", "xi", "fo")
+HW, KS, RAWQ, KQ = 396, 4, 136, 268
 _buf(I, 2 * HW, "KW0", "KW1", "KW2")
 _buf(I, 512, "ZO0", "ZO1", "ZO2")
-_buf(U, 256, "pl0", "pl1", "pl2", "plo0", "plo1", "cu")
-_buf(U, 8, "ou", "uu", "LO", "FO")
+_buf(U, 8 * LW, "pl0", "pl1", "pl2", "plo0", "plo1")
+_buf(U, 256, "cu")
+_buf(U, 8, "ou", "uu", "WO", "FO")
 for _b in range(8):
     SCRATCH["ps%d" % _b] = ("psum", [128, 512], F)
 
 DMAS = ["ld%d" % k for k in range(12)] + ["ds%d" % k for k in range(5)]
 SEMAPHORES = ["qv", "qs", "qt", "qg"] + DMAS + [a + x + t for a in "al" for x in ("p0", "p1", "k0", "k1", "q0", "q1", "s") for t in "12"]
-VADD = 2
-DL = 2.0 ** -18
+TAB = "ttvtvttv"
+BIG = 2.0 ** 19
 SW, SC = -2.0 ** 31, -2.0 ** -16
 C0 = 1304
 CYC, GATHER, SCATTER, WAKE = 0.83e-3, 1.4, 3.8, 0.22
-AHEAD, PASSES, SLACK, LAZY, SFIX = (1.0, 1.5, 2.0), 5, 2.0, 0.6, 0.05
-POLISH, HEAT = 12000, 0.05
-OTHERS = ((0.17, 1.25), (0.27, 0.85))
+AHEAD, PASSES, SLACK, LAZY, SFIX = (0.8, 3.0), 120, (0.5, 3.0), (0.3, 1.0), 0.05
+BLUR, STRAY, SPARE = (0.0, 0.05, 0.15, 0.4), 2.0, 0.1
+POLISH, HEAT, SNAP, FLIP = ((6, 2000), (2, 5000), (1, 24000)), 0.06, 48, 0.13
+WAYS = ((0.2, 1.0), (0.16, 1.33), (0.26, 0.8))
+FOLD1, MEAN = 3.0, 0.3
 FLY, FOLD, LOAD, NEXT, LATE, EARLY = 1.3, 4.5, 1.3, 1.25, 0.3, 8.0
 PFIX = 0.01
 PULL = {"table": 0.0, "reasons": 0.0, "after": 0.0, "parity": 3.0}
 STORE = 1000.0
 CUTS = (0, 512, 1536, 2560, 3584, 4096)
 QC = "ssssssss"
-RUN = (("T2 T3 R0 M0 M1 N1 F0 F1 N3 F2 F3 R1 F4 F5 F6 F7 M2 M3", "T0 T1 T4 T5 N0 N2 T6 T7 N4 N5 N6 N7 E0"),
-       ("R0 F0 F1 M0 F2 F3 M1 xs0 ou0 vx0 R1 F4 F5 M2 F6 F7 M3 xs1",
-        "T0 T1 T2 T3 N0 N1 N2 N3 T4 T5 T6 T7 dd0 sg0 N4 gt0 wm0 N5 N6 ab0 N7 E0 E1 tl0 E2 dd1 sg1 E3 gt1 wm1 ab1 E4"))
-LINES = ("E0 E1 E2 E3 E4 E5 E6 E7", "P0 P1 DT0 turn0 P2 P3 DT1 turn1", "S0 S1 S2 S3")
+RUN = (("T2 T3 R0 T6 T7 R1 N1 F0 F1 N3 F2 F3 N5 F4 F5 F6 F7", "T0 T1 T4 T5 N0 N2 N4 N6 N7 E0"),
+       ("R0 R1", "T0 T1 T2 T3 N0 N1 N2 N3 T4 T5 T6 T7 N4 N5 N6 N7 E0"))
+LINES = ("E0 E1 E2 E3 E4 E5 E6 E7", "P0 P1 H0 turn0 H1 turn1 P2 P3 H2 turn2 H3 turn3", "S0 S1 S2 S3")
 QF = "v"
-MIDS = ("fill0 Q00", "fill1 Q10")
+GQ = "ssv"
+MIDS = ()
 ENDS = ()
+WHOLE = ("ps1", "ps2", "ps6")
 SIZE = {H: 2, F: 4, I: 4, U: 2}
 
 
@@ -170,7 +179,10 @@ def _schedule(prog):
         for i in range(n - 1, -1, -1):
             rank[i] = min(prog[i]["cost"].values()) + max([prog[i]["lat"] + rank[j] + WAKE for j in nxt[i]] + [rank[j] for j in ahead_of[i]] + [prog[i]["lat"]])
 
-    def one(before, after, rank, back, ahead):
+    run, costs = _timer(prog, deps)
+
+    def one(before, after, rank, back, way, ahead, slack, lazy):
+        wake, cost = WAYS[way][0], costs[way]
         ob, oa = (ahead_of, behind) if back else (behind, ahead_of)
         left = [len(d) + len(x) for d, x in zip(before, ob)]
         at = [{} for _ in range(n)]
@@ -182,28 +194,28 @@ def _schedule(prog):
         def start(i, q):
             s = met.get((i, q))
             if s is None:
-                s = met[(i, q)] = max([0.0] + [t + (0.0 if q == q2 == "t" else WAKE) for q2, t in at[i].items()]) + (prog[i]["lat"] if back else 0.0)
+                s = met[(i, q)] = max([0.0] + [t + (0.0 if q == q2 == "t" else wake) for q2, t in at[i].items()]) + (prog[i]["lat"] if back else 0.0)
             f = free.get(q, 0.0) if q != "x" else 0.0
             if f > s:
                 s = f
             for b in prog[i]["P"]:
                 for q2, t in bank.get(b, {}).items():
-                    if q2 != q and t + WAKE > s:
-                        s = t + WAKE
+                    if q2 != q and t + wake > s:
+                        s = t + wake
             return s
 
         while ready:
-            c = [(start(i, q), i, q) for i in ready for q in ([back[i]] if back else prog[i]["cost"])]
+            c = [(start(i, q), i, q) for i in ready for q in ([back[i]] if back else prog[i].get("first") or prog[i]["cost"])]
             first = {}
             for s, i, q in c:
                 first[q] = min(first.get(q, s), s)
             q = min(first, key=lambda x: first[x])
             _, i, s = min((-rank[i], i, s) for s, i, q2 in c if q2 == q and s <= first[q] + 0.03)
             for s2, i2, q2 in c:
-                if q2 == q and rank[i2] > rank[i] and s + prog[i]["cost"][q] - s2 > (ahead if rank[i2] < rank[i] + SLACK else LAZY) * (s2 - first[q]):
+                if q2 == q and rank[i2] > rank[i] and s + cost[i][q] - s2 > (ahead if rank[i2] < rank[i] + slack else lazy) * (s2 - first[q]):
                     i, s = i2, s2
             ready.discard(i)
-            end = s + prog[i]["cost"][q]
+            end = s + cost[i][q]
             free[q] = end
             queue[i] = q
             order.append(i)
@@ -221,102 +233,127 @@ def _schedule(prog):
                     ready.add(j)
         return max(done), order, queue, done
 
-    best = None
+    best, found = None, []
     const = []
     for i in range(n):
         const.append(prog[i]["sem"] is None and min(prog[i]["cost"].values()) < 1.0 and all(const[j] for j in deps[i]))
-    for ahead in AHEAD:
-        urge = rank
-        for k in range(PASSES):
-            top = max(urge) - EARLY
-            fw = one(deps, nxt, [(max(u, top) if c else u) + e.get("pull", 0.0) for u, c, e in zip(urge, const, prog)], None, ahead)
-            if best is None or fw[0] < best[0]:
-                best = fw
-            urge = one(nxt, deps, fw[3], fw[2], ahead)[3]
-    return _polish(prog, deps, nxt, best[1], best[2]) + (deps,)
+    const = [c and "g" not in e["cost"] for c, e in zip(const, prog)]
+    pick = np.random.default_rng(1)
+    urge = rank
+    for k in range(PASSES):
+        way, ahead, slack, lazy = int(pick.integers(len(WAYS))), float(pick.uniform(*AHEAD)), float(pick.uniform(*SLACK)), float(pick.uniform(*LAZY))
+        blur = pick.normal(0.0, 1.0, n) * float(pick.choice(BLUR))
+        top = max(urge) - EARLY
+        fw = one(deps, nxt, [(max(u, top) if c else u) + e.get("pull", 0.0) + float(x) for u, c, e, x in zip(urge, const, prog, blur)], None, way, ahead, slack, lazy)
+        now = sum(run(fw[1], fw[2], x)[0] for x in range(len(WAYS)))
+        urge = one(nxt, deps, fw[3], fw[2], way, ahead, slack, lazy)[3]
+        found.append((now, fw[1], fw[2]))
+        if best is None or now < best[0]:
+            best = (now, fw[1], fw[2], urge)
+        elif now > best[0] + STRAY:
+            urge = best[3] if pick.uniform() < 0.8 else rank
+    found.sort(key=lambda x: x[0])
+    for keep, steps in POLISH:
+        found = sorted((_polish(prog, deps, nxt, x[1], x[2], run, steps, k) for k, x in enumerate(found[:keep])), key=lambda x: x[0])
+    return found[0][1:] + (deps,)
 
 
-def _polish(prog, deps, nxt, order, queue):
+def _timer(prog, deps):
     n = len(prog)
-    before = [set(d) for d in deps]
-    after = [set(x) for x in nxt]
-    ix = [i for i in range(n) if "y" in prog[i]["cost"]]
-    for a, b in zip(ix, ix[1:]):
-        before[b].add(a)
-        after[a].add(b)
     dl = [sorted(d) for d in deps]
     lat = [e["lat"] for e in prog]
     banks = [e["P"] for e in prog]
-    ways = ((WAKE, 1.0),) + OTHERS
+    ways = WAYS
     cost = [[{q: c * (x if e.get("by index") else 1.0) for q, c in e["cost"].items()} for e in prog] for w, x in ways]
 
-    def run(order, queue, k):
+    def run(order, queue, k, a=0, old=None, to=0, room=0.0):
         wake, ck = ways[k][0], cost[k]
-        free, holder, bank, done, why = {}, {}, {}, [0.0] * n, [None] * n
-        for i in order:
-            q = queue[i]
-            s, w = free.get(q, 0.0), holder.get(q)
-            soft = True
-            if q == "t":
-                for j in dl[i]:
-                    x = done[j] if queue[j] == "t" else done[j] + wake
-                    if x > s:
-                        s, w, soft = x, j, False
-            else:
-                for j in dl[i]:
-                    x = done[j] + wake
-                    if x > s:
-                        s, w, soft = x, j, False
-            e = banks[i]
-            if e:
-                for b in e:
-                    for q2, (x, j) in bank.get(b, {}).items():
-                        if q2 != q and x + wake > s:
-                            s, w, soft = x + wake, j, True
-            s += ck[i][q]
-            if q != "x":
-                free[q], holder[q] = s, i
-            done[i] = s + lat[i]
-            why[i] = (w, soft)
-            if e:
-                for b in e:
-                    bank.setdefault(b, {})[q] = (s, i)
-        return max(done), done, why
+        if old is None:
+            free, holder, bank, done, why, kept = {}, {}, {}, [0.0] * n, [None] * n, []
+        else:
+            kept = old[3][:a // SNAP + 1]
+            free, holder, bank = dict(kept[-1][0]), dict(kept[-1][1]), {b: dict(x) for b, x in kept[-1][2].items()}
+            done, why = list(old[1]), list(old[2])
+        for p in range(a // SNAP * SNAP, n, SNAP):
+            if old and p > to + 2 * SNAP and min(free[q] - old[3][p // SNAP][0][q] for q in "vst") > room:
+                return None
+            if p // SNAP == len(kept):
+                kept.append((dict(free), dict(holder), {b: dict(x) for b, x in bank.items()}))
+            for i in order[p:p + SNAP]:
+                q = queue[i]
+                s, w = free.get(q, 0.0), holder.get(q)
+                soft = True
+                if q == "t":
+                    for j in dl[i]:
+                        x = done[j] if queue[j] == "t" else done[j] + wake
+                        if x > s:
+                            s, w, soft = x, j, False
+                else:
+                    for j in dl[i]:
+                        x = done[j] + wake
+                        if x > s:
+                            s, w, soft = x, j, False
+                e = banks[i]
+                if e:
+                    for b in e:
+                        for q2, (x, j) in bank.get(b, {}).items():
+                            if q2 != q and x + wake > s:
+                                s, w, soft = x + wake, j, True
+                s += ck[i][q]
+                if q != "x":
+                    free[q], holder[q] = s, i
+                done[i] = s + lat[i]
+                why[i] = (w, soft)
+                if e:
+                    for b in e:
+                        bank.setdefault(b, {})[q] = (s, i)
+        return max(done) + MEAN * sum(done) / n, done, why, kept
 
-    def judge(order, queue):
-        r = [run(order, queue, k) for k in range(len(ways))]
-        return sum(x[0] for x in r), r
+    return run, cost
+
+
+def _polish(prog, deps, nxt, order, queue, run, steps, seed):
+    ways = WAYS
+    before = [set(d) for d in deps]
+    after = [set(x) for x in nxt]
+    ix = [i for i in range(len(prog)) if "y" in prog[i]["cost"]]
+    for a, b in zip(ix, ix[1:]):
+        before[b].add(a)
+        after[a].add(b)
 
     def links(r):
-        top, done, why = r
-        i, out = done.index(top), []
+        done, why = r[1:3]
+        i, out = done.index(max(done)), []
         while why[i][0] is not None:
             if why[i][1]:
                 out.append((why[i][0], i))
             i = why[i][0]
         return out
 
-    pick = np.random.default_rng(2)
+    pick = np.random.default_rng(seed + steps)
     order, queue = list(order), dict(queue)
-    now, res = judge(order, queue)
+    res = [run(order, queue, k) for k in range(len(ways))]
+    now = sum(x[0] for x in res)
     best = (now, order, queue, res[0][1])
     soft = [links(r) for r in res]
-    for step in range(POLISH):
+    for step in range(steps):
         lk = soft[int(pick.integers(len(ways)))]
         x = int(pick.integers(len(lk)))
         j, i = lk[x]
         way = float(pick.uniform())
         q2 = queue
-        if way < 0.1:
-            k = j if way < 0.05 else i
+        if way < FLIP:
+            k = j if way < FLIP / 2 else i
             if len(prog[k]["cost"]) < 2:
                 continue
             q2 = dict(queue)
             q2[k] = [q for q in prog[k]["cost"] if q != queue[k]][0]
             o2 = order
+            a = b = order.index(k)
         else:
+            fore = way < (1 + FLIP) / 2
             far = int(pick.geometric(0.45)) - 1
-            if way < 0.55:
+            if fore:
                 while far and x + 1 < len(lk) and lk[x + 1][1] == j:
                     x, far = x + 1, far - 1
                     j = lk[x][0]
@@ -326,22 +363,28 @@ def _polish(prog, deps, nxt, order, queue):
                     i = lk[x][1]
             a, b = order.index(j), order.index(i)
             mid = order[a:b + 1]
-            go, need = set(), ({i} if way < 0.55 else {j})
-            for k in (mid[::-1] if way < 0.55 else mid):
+            go, need = set(), ({i} if fore else {j})
+            for k in (mid[::-1] if fore else mid):
                 if k in need:
                     go.add(k)
-                    need |= before[k] if way < 0.55 else after[k]
-            if (j if way < 0.55 else i) in go:
+                    need |= before[k] if fore else after[k]
+            if (j if fore else i) in go:
                 continue
             stay, moved = [k for k in mid if k not in go], [k for k in mid if k in go]
-            o2 = order[:a] + (moved + stay if way < 0.55 else stay + moved) + order[b + 1:]
-        new, r2 = judge(o2, q2)
-        if new <= now + HEAT * (1 - step / POLISH) * float(pick.exponential()):
+            o2 = order[:a] + (moved + stay if fore else stay + moved) + order[b + 1:]
+        limit = now + HEAT * (1 - step / steps) * float(pick.exponential())
+        r2, new = [], now
+        for k in range(len(ways)):
+            r2.append(run(o2, q2, k, a, res[k], max(b, 200), limit - new + SPARE * (len(ways) - 1 - k)))
+            new += r2[k][0] - res[k][0] if r2[k] else 1e9
+            if new > limit + SPARE * (len(ways) - 1 - k):
+                break
+        if new <= limit:
             now, order, queue, res = new, o2, q2, r2
             soft = [links(r) for r in res]
             if now < best[0]:
                 best = (now, order, queue, res[0][1])
-    return best[1], best[2], best[3]
+    return best
 
 
 PLANNED = {}
@@ -367,7 +410,7 @@ def rank_program(g, core, T, topo):
     def line(names, t):
         chain([i for x in names.split() for i in named.get((t - (x[0] == "<"), x.strip("<")), [])])
 
-    def v(name, a=0, b=None, step=1, p=0):
+    def v(name, a=0, b=None, step=1, p=0, q=128):
         if name in PART:
             name, o, n = PART[name]
             a, b = o + a, o + (n if b is None else b)
@@ -381,8 +424,7 @@ def rank_program(g, core, T, topo):
         else:
             for c in cols:
                 m |= 1 << c
-        ap = T[name][p:128, a:b:step] if p else T[name][:, a:b:step]
-        return (ap, [(name, m)], len(cols), SIZE[SCRATCH[name][2]], SCRATCH[name][0] == "psum", None)
+        return (T[name][p:q, a:b:step], [(name, m)], len(cols), SIZE[SCRATCH[name][2]], SCRATCH[name][0] == "psum", None)
 
     def w(name, a, n):
         return v(name, a, a + n)
@@ -396,7 +438,7 @@ def rank_program(g, core, T, topo):
     def ap(x):
         return x[0] if isinstance(x, tuple) else x
 
-    def rec(fns, out, ins, kind, sem=None, inc=1, lat=0.0, R=(), Wr=()):
+    def rec(fns, out, ins, kind, sem=None, inc=1, lat=0.0, R=(), Wr=(), first=None):
         ins = [x for x in ins if isinstance(x, tuple)]
         sides = [out] + ins
         reads = [k for x in ins for k in x[1]] + [k for x in sides if x[5] for k in x[5][1]] + list(R)
@@ -404,9 +446,11 @@ def rank_program(g, core, T, topo):
         cost = {}
         for q in fns:
             if kind == "mm":
-                c = sum(max(64, x[2]) for x in ins[1::2]) * CYC * (4 if ins[0][3] == 4 else 1)
-            elif kind in ("dma", "g"):
-                c = 0.05 if kind == "dma" else 0.15 + 2 * n * CYC
+                c = sum(max(min(64, l[2]), x[2]) * (4 if x[3] == 4 else 1) for l, x in zip(ins[::2], ins[1::2])) * CYC
+            elif kind == "dma":
+                c = 0.05
+            elif q == "g":
+                c = 0.15 + 2 * n * CYC
             elif any(x[5] for x in sides):
                 c = (0.05 if q == "v" else 0.065) + n * CYC * (SCATTER if out[5] else GATHER)
             elif q == "s":
@@ -417,7 +461,7 @@ def rank_program(g, core, T, topo):
                 c = max(64, n * (0.5 if q == "v" and kind == "ts" and all(x[3] == 2 for x in sides if x[2] > 1) else 1)) * CYC
             cost[q] = c + (PFIX if q in "vs" and any(x[4] for x in sides) else 0.0)
         prog.append({"kind": "op", "fn": fns, "R": reads, "W": list(out[1]) + list(Wr), "P": sorted(set(x[1][0][0] for x in sides if x[4])),
-                     "sem": sem, "inc": inc, "cost": cost, "lat": lat, "by index": any(x[5] for x in sides), "pull": pull[0]})
+                     "sem": sem, "inc": inc, "cost": cost, "lat": lat, "by index": any(x[5] for x in sides), "pull": pull[0], "first": first})
 
     def ts_fn(out, a, s1, o0, s2, o1):
         if o1 is None:
@@ -434,10 +478,7 @@ def rank_program(g, core, T, topo):
         rec({"v": lambda e: e.tensor_copy(out[0], a[0])}, out, [a], "ts")
 
     def scan(out, a, b, init, o0, o1):
-        rec({"v": lambda e: e.tensor_tensor_scan(out[0], a[0], b[0], init, o0, o1)}, out, [a, b], "ts")
-
-    def red(out, a, o):
-        rec({"v": lambda e: e.tensor_reduce(out[0], a[0], AX, o)}, out, [a], "red")
+        rec({"v": lambda e: e.tensor_tensor_scan(out[0], a[0], b[0], ap(init), o0, o1)}, out, [a, b, init], "ts")
 
     def fill(out, c):
         rec({"v": lambda e: e.memset(out[0], c)}, out, [], "ts")
@@ -453,13 +494,14 @@ def rank_program(g, core, T, topo):
     def act(out, a, fn, scale=None, bias=None):
         rec({"s": act_fn(out, a, fn, scale, bias)}, out, [a, scale, bias], "act")
 
-    def affine(out, a, scale, bias=None, qs="vs"):
+    def affine(out, a, scale, bias=None, qs="vs", first=None):
         fns = {"v": ts_fn(out, a, scale, A.mult, bias, None if bias is None else A.add), "s": act_fn(out, a, ACT.Identity, scale, bias)}
-        rec({q: fns[q] for q in qs}, out, [a, scale, bias], "ts")
+        rec({q: fns[q] for q in qs}, out, [a, scale, bias], "ts", first=first)
 
     def mms(out, pairs, run=()):
-        key = [("open" + out[1][0][0], 1)]
-        parts = [[x] for x in pairs] + ([list(run)] if run else [])
+        whole = out[1][0][0] in WHOLE
+        key = [] if whole else [("open" + out[1][0][0], 1)]
+        parts = [list(pairs) + list(run)] if whole else [[x] for x in pairs] + ([list(run)] if run else [])
         for k, part in enumerate(parts):
             def fn(e, k=k, part=part):
                 for j, (l, r) in enumerate(part):
@@ -477,12 +519,24 @@ def rank_program(g, core, T, topo):
         rec({"t": fn}, out, [x for o, l, r in items for x in (l, r)], "mm", R=key if part == "b" else [],
             Wr=([] if part == "b" else key) + [o[1][0] for o, l, r in items])
 
+    def singles(items):
+        def fn(e):
+            for o, l, r in items:
+                ins = e.matmul(o[0], l[0], r[0], True, True)
+            return ins
+        out = items[0][0]
+        rec({"t": fn}, out, [x for o, l, r in items for x in (l, r)], "mm", Wr=[o[1][0] for o, l, r in items])
+
     def gp(fn, out, ins):
         rec({"g": fn}, out, ins, "g")
 
     def iota(out, pattern, base, cmul):
         flag = {} if SCRATCH[out[1][0][0]][2] == I else {"allow_small_or_imprecise_dtypes": True}
         gp(lambda e: e.iota(out[0], pattern, base, cmul, **flag), out, [])
+
+    def whole(out, c):
+        flag = {} if SCRATCH[out[1][0][0]][2] == I else {"allow_small_or_imprecise_dtypes": True}
+        rec({"v": lambda e: e.memset(out[0], c if not flag else float(c)), "g": lambda e: e.iota(out[0], [[0, out[2]]], c, 0, **flag)}, out, [], "ts", first="g")
 
     def load(q, k, out, src, lat):
         rec({q: lambda e: e.dma_start(out[0], src)}, out, [], "dma", "ld%d" % k, 16, lat)
@@ -511,193 +565,184 @@ def rank_program(g, core, T, topo):
         prog.append({"kind": "lands", "fn": None, "R": [("sent" + name, 1)], "W": [k for out, _ in moves for k in out[1]], "P": [], "sem": "a" + name,
                      "inc": n, "cost": {"x": lat}, "lat": 0.0})
 
+    def at(c):
+        return c // 4 * 4 + c % 2 * 2 + c % 4 // 2
+
+    def again(out, a):
+        rec({"g": lambda e: e.affine_select(out[0], a[0], [[0, out[2]]], A.is_equal, 0.0, 0, 0), "s": act_fn(out, a, ACT.Identity, None, None)}, out, [a], "ts", first="g")
+
     def lanes(name, c, a=0, n=32, size=128):
         o = size * (c // 4) + a
-        return v(name, o + c % 4, o + 4 * n, 4)
+        return v(name, o + at(c) % 4, o + 4 * n, 4)
 
     def IS(k):
         return v("IS", k * 128, k * 128 + 128)
 
-    def SEL(k):
-        return v("SEL2", k * 128, k * 128 + 128)
+    def SEL(k, a=0):
+        return w("SEL", a + 15 - k, 128)
 
     for k, (a, b) in enumerate(zip(CUTS, CUTS[1:])):
         load("y", 4 + k, v("E0", a, b), T.eff[:, a:b], LOAD + NEXT * b / 1024)
     load("y", 0, v("wa"), T.act[:, :], LOAD + NEXT * 4.5)
-    load("y", 2, v("sc0"), T.st0[:, :], LOAD + NEXT * 4.7)
+    load("y", 2, v("st"), T.st0[:, :], LOAD + NEXT * 4.7)
     for k in range(2):
         load("y", 10 + k, v("PT", k * 2048, k * 2048 + 2048), T.req[:, k * 2048:k * 2048 + 2048], LOAD + NEXT * (6.7 + 2 * k) + LATE)
     load("y", 1, v("wi"), T.why[:, :], LOAD + NEXT * 10 + LATE)
     load("y", 3, v("bari"), T.bar[:, :], LOAD + NEXT * 10 + LATE)
-    load("y", 9, v("E1"), T.eff[:, :], LOAD + NEXT * 14 + LATE)
 
     ID, ONE, G8 = v("ID"), v("ONE"), v("G8")
     fill(ONE, 1.0)
     gp(lambda e: e.affine_select(ID[0], ONE[0], [[-1, 128]], A.is_equal, 0.0, 0, 1), ID, [ONE])
     gp(lambda e: e.affine_select(G8[0], v("ONE", 0, 8)[0], [[-16, 8]], A.is_ge, 0.0, 0, 1), G8, [ONE])
     gp(lambda e: e.affine_select(G8[0], G8[0], [[16, 8]], A.is_ge, 0.0, 15, -1), G8, [G8])
-    gp(lambda e: e.affine_select(v("LT0")[0], ONE[0], [[0, 8], [-1, 16]], A.is_equal, 0.0, 0, 1), v("LT0"), [ONE])
+    gp(lambda e: e.affine_select(v("PERM")[0], v("ONE", 0, 64)[0], [[-1, 32], [-32, 2]], A.is_equal, 0.0, 0, 1), v("PERM"), [ONE])
+    affine(v("PERM"), v("PERM"), BIG)
     iota(v("pi"), [[0, 8]], 0, 1)
-    for a in range(0, 2048, 256):
-        iota(v("SEL2", a, a + 256), [[0, 256]], 0, 0)
-    for k in range(16):
-        affine(v("SEL2", k * 128 + k, k * 128 + 128, 16), G8, SW, None, "s")
-    iota(v("TP"), [[0, 4], [-1, 33]], 40, 0)
-    iota(v("C32"), [[16, 2], [32, 4]], 0, 0)
-    iota(v("kc1"), [[1, 32]], 1, 0)
+    iota(v("SEL"), [[0, 288]], 0, 0)
+    affine(v("SEL", 15, 143, 16), G8, SW)
+    affine(v("SEL", 159, 287, 16), G8, 1.5 * SW)
+    for a in range(0, 1024, 256):
+        iota(v("WT", a, a + 256), [[0, 256]], 0, 0)
+    iota(v("C32"), [[16, 2], [32, 2], [64, 2]], 0, 0)
+    iota(v("kc1"), [[33, 2], [1, 32]], 1, 0)
+    whole(col("kc1", 63), 1)
     iota(v("KAP"), [[113, 32]], 37 - W, 0)
-    iota(v("lo"), [[16, 8]], 15, 0)
+    iota(v("wo"), [[0, 2], [128, 4]], 0, 1)
+    iota(v("xi"), [[16, 8]], W + 16, 0)
     iota(v("K2c"), [[-64, 32], [0, 4]], 31 * 64, 0)
-    fill(v("K2c", 0, 128, 1, 64), -33280.0 * 512)
+    fill(v("K2c", 0, 128, 1, 64), -33280.0 * 768)
+    iota(v("K3c"), [[-8192, 32], [0, 4]], 31 * 8192, 0)
     for c in range(8):
-        fill(v("FL", c * BL + 512, c * BL + BL), -33024 * DL)
-        fill(v("Gn", c * BL + 512, c * BL + BL), -31744 * DL)
-    fill(v("SCM"), 10000.0)
-    fill(v("SCM", 0, 128, 16), -10000.0)
-    fill(v("CW"), -129.0)
+        whole(v("FL", c * BL + 512, c * BL + BL), -8256)
+        whole(v("Gn", c * BL + 512, c * BL + BL), -7936)
     fill(v("M130"), -130.0)
-    fill(v("THR"), -1.5 * 2 ** 14)
-    fill(v("CB"), -2.0 ** 25)
-    fill(v("O132"), 1.0)
-    for j in range(2):
-        fill(w("vx%d" % j, 64 - 64 * j, 64), 0.0)
-        fill(w("fx%d" % j, 64 - 64 * j, 64), 0.0)
-    for k, x in enumerate((-7.5, 128.0, -133.5, -141.5)):
+    fill(v("THR", 0, 66, 1, 0, 32), -1.5 * 2 ** 32)
+    fill(v("THR", 0, 66, 1, 32, 64), -2.0 ** 43)
+    for k, x in enumerate((-7.5, 24.0, -137.5)):
         fill(col("SG", k), x)
-    WS = (DL, 48 * DL, -0.5 / DL, -1.0, 1 / DL, -48.0, 2.0 ** 17, -2.0 ** 17, 48.0, 2.0 ** 24, 2.0 ** 25, -3 * 2.0 ** 24, 8192.0, -33 * 8192.0)
+    WS = (64.0, -1.0, BIG, -206 * 2.0 ** 15, 208 * 2.0 ** 15, -BIG)
     for k, x in enumerate(WS):
         affine(IS(k), ID, x)
     ts(v("pb"), v("pi"), 15, A.bitwise_and)
     cp(v("pbf"), v("pb"))
-    cp(v("LO"), v("lo"))
-    iota(v("XC"), [[-BL, 4], [-16, 33]], 0, 0)
-    ts(v("XC"), v("XC"), col("pbf", 0), A.subtract)
-    for j in range(2):
-        ts(w("FO", 4 * j, 4), v("XC", 32, 132, 33), -1.0, A.mult, 4.0 * BL * j, A.add)
-    iota(v("HR"), [[0, 4], [1, 33]], 0, 0)
-    affine(v("HR"), v("HR"), 8192.0, -40.5 * 8192)
-    for c in range(8):
-        ts(w("TR", 33 * c, 33), v("ONE", 0, 33), col("G8", c), A.mult, -2.0 ** 20, A.mult)
-    affine(v("kcm"), v("kc1"), 1.0, -32.5)
+    cp(v("WO"), v("wo"))
+    iota(v("XC"), [[-4096, 66]], -4096, 0)
+    iota(v("XC8"), [[-4096, 66]], -2048, 0)
+    affine(col("pb16", 0), col("pbf", 0), 1.0, -16.0)
+    iota(v("fo"), [[BL, 8]], 512, 0)
+    ts(v("FO"), v("fo"), col("pbf", 0), A.add)
+    affine(v("kcm"), v("kc1", 0, 32), 1.0, -32.5)
+    affine(v("UB"), v("C32"), -32 * SW, -384 * SW)
     ts(v("C32"), v("C32"), col("pbf", 0), A.add, 32.0, A.mult)
     for j in range(2):
-        ts(w("barf", 4 * j, 4), v("bari", j, 8, 2), -2.0 ** 19, A.mult, 65536.0, A.add)
+        ts(w("barf", 4 * j, 4), v("bari", j, 8, 2), -1.5 * 2 ** 19, A.mult, 2.0 ** 17, A.add)
     for c in range(8):
-        affine(lanes("BAR", c), v("ONE", 0, 32), col("barf", c), None, "s")
-    mms(v("ps3", 0, 128), [(v("LT0"), v("LT0"))])
-    act(v("DM"), v("ps3", 0, 128), ACT.Identity)
+        affine(lanes("BAR", c), v("ONE", 0, 32), col("barf", at(c)), None, "s")
+    for t in range(1, VI):
+        for k in range(2):
+            ts(v("plo%d" % (t - 1), 32 + k, None, LW), v("xi"), col("pbf", 0), A.add, float(B * t), A.add)
 
     for c in range(8):
-        cp(w("pl0", 32 * c, 32), v("wa", 2 * (c % 4) + c // 4, 256, 8))
-    iota(v("al"), [[-4096, 32], [0, 4]], -4096, 0)
+        cp(w("pl0", LW * c, 32), v("wa", 2 * (at(c) % 4) + c // 4, 256, 8))
+    ts(v("pl0", 32, 7 * LW, LW), v("C32", 1, 8), 1 / 32, A.mult, float(W), A.add)
+    affine(w("TT", W, B), v("st"), -1.0, 24.0)
+    iota(v("al"), [[1, 32], [33, 2], [0, 2]], 1, 0)
+    iota(v("aq"), [[-8192, 32], [0, 4]], -8192, 0)
     Kc, KQc = v("ps6", 0, 128), v("ps6", 128, 256)
-    act(Kc, v("al"), ACT.Identity)
-    act(KQc, v("al"), ACT.Identity, 2.0)
+    affine(Kc, v("al"), -4096.0)
+    affine(KQc, v("aq"), 1.0)
     for j in range(2):
         o = j * HW
-        tt(w("KW0", o + KS + 4, 128), v("wa", j, 256, 2), Kc, A.add)
-        cp(w("KW0", o + RAWS + 4, 128), v("wa", j, 256, 2))
-        ts(w("KW0", o + RAWQ + 4, 128), v("wi", j, 256, 2), 1.0, A.add)
-        tt(w("KW0", o + KQ, 128), w("KW0", o + RAWQ + 4, 128), KQc, A.add)
+        tt(w("KW0", o + KS, 128), v("wa", j, 256, 2), Kc, A.add)
+        ts(w("KW0", o + RAWQ, 128), v("wi", j, 256, 2), 1.0, A.add)
+        tt(w("KW0", o + KQ, 128), w("KW0", o + RAWQ, 128), KQc, A.add)
         for t in range(VI):
-            fill(w("KW%d" % t, o + KS + 132, 4), -4096 * 33)
-            fill(w("KW%d" % t, o + RAWS, 4), 0)
-            fill(w("KW%d" % t, o + RAWQ, 4), 0)
-    iota(v("Kf"), [[-4096, 32], [0, 4]], -4096, 0)
+            for a in (KS - 4, KQ - 4):
+                whole(w("KW%d" % t, o + a, 4), -2 ** 19)
+            for k in range(2):
+                whole(w("KW%d" % t, o + KS + 128 + 2 * k, 2), -4096 * 33 * (k + 1))
+    ts(v("Kf"), v("al"), -4096.0, A.mult)
     iota(v("KQf"), [[-8192, 32], [0, 4]], -8192, 0)
 
     for c in range(8):
         a, b = c * 512, c * 512 + 512
-        p = v(("ps0", "ps1", "ps2", "ps7")[c % 4])
-        ts(v("FC", a, b), v("E0", a, b), 4.0, A.is_ge, -1 / DL, A.mult)
-        ts(v("EC", a, b), v("E0", a, b), 12.0, A.is_ge, 1 + 96 * DL, A.subtract)
-        scan(v("TM", a, b), v("FC", a, b), v("EC", a, b), 0.0, A.min, A.mult)
-        if c < 8 - VADD:
-            mms(p, [(ID, v("E0", a, b)), (ID, v("TM", a, b))])
-            act(v("TT", a, b), p, ACT.Identity, None, -192.0)
+        if TAB[c] == "t":
+            p = v(("ps0", "ps1", "ps2", "ps7")[c % 4])
+            ts(v("EC", a, b), v("E0", a, b), 1024.5, A.add)
+            ts(v("FC", a, b), v("EC", a, b), 1032.0, A.is_equal, 64.0, A.mult)
+            mms(p, [(ID, v("E0", a, b)), (ID, v("FC", a, b))])
+            act(v("TT", a, b), p, ACT.Relu, -1.0, col("SG", 1))
         else:
-            act(p, v("E0", a, b), ACT.Identity, None, -192.0)
-            tt(v("TT", a, b), v("TM", a, b), p, A.add)
-    act(v("sg0"), v("sc0"), ACT.Sign, None, col("SG", 0))
-    mms(v("ps1", 256, 384), [(IS(0), v("sc0")), (IS(1), v("sg0"))])
+            act(v("EC", a, b), v("E0", a, b), ACT.Abs, None, col("SG", 0))
+            ts(v("V0", a, b), v("E0", a, b), -24.0, A.add)
+            ts(v("FC", a, b), v("EC", a, b), 4.0, A.is_gt, -1.0, A.mult)
+            scan(v("TT", a, b), v("FC", a, b), v("V0", a, b), 0.0, A.min, A.mult)
 
     for t in range(VI):
         pl, KW, so, ZO = "pl%d" % t, "KW%d" % t, v("so%d" % t), "ZO%d" % t
         last = t == VI - 1
-        Et, En = "E%d" % t, "E%d" % ((t + 1) % 3)
+        Et = "E0"
         now[0] = t
         pull[0] = 0.0
 
-        for c in range(8):
-            if t:
-                affine(w("D1", c * BL, 16), w("sc%d" % t, 16 * c, 16), 1.0, None, "s")
-            else:
-                affine(w("D1", c * BL, 16), w("ps1", 256 + 32 * (c % 4) + 16 * (c // 4), 16), 1.0, -144 * DL)
+        affine(w("D1", 0, 16), w("TT", W + B * t, 16), -2.0, 1.0)
         run_v = RUN[min(t, 1)][0].split()
         for c in range(8):
-            affine(w("D1", c * BL + 16, 512), ind(v("TT"), w(pl, c * 32, 32)), DL, None, "v" if "T%d" % c in run_v else "s")
+            n = 32 if c == 7 else 33
+            affine(w("D1", c * BL + 16, 16 * n), ind(v("TT", 0, W + B * t + B), w(pl, c * LW, n)), -2.0, 1.0, first="v" if "T%d" % c in run_v else "s")
             name("T%d" % c)
         for j in range(2):
             for k in range(16):
                 d = v("D1", 4 * j * BL + k, 4 * (j + 1) * BL, 16)
                 scan(v("V0", 4 * j * BL + k, 4 * (j + 1) * BL, 16), d, d, 0.0, A.mult, A.min)
                 name("R%d" % j)
-        for j in range(2):
-            for k in range(16):
-                scan(v("TM", 4 * j * BL + k, 4 * (j + 1) * BL, 16), v("D1", 4 * j * BL + k, 4 * (j + 1) * BL, 16), v("TP"), 0.0, A.mult, A.max)
-                name("M%d" % (2 * j + k // 8))
         for c in range(8):
-            a, cnt = c * BL, ("ps0", "ps5")[c // 4]
-            if c % 4 == 0:
-                group([(v(cnt, 0, 132), ONE, v("CB"))], True, False, "a")
-                group([(v(cnt, 0, 132), ONE, v("THR"))], False, False, "b")
-            affine(w("Gn", a, 512), ind(v("PT"), w(pl, c * 32, 32)), -DL, -32692.5 * DL, "v" if "N%d" % c in run_v else "s")
+            a = c * BL
+            affine(w("Gn", a, 512), ind(v("PT"), w(pl, c * LW, 32)), -2.0, -8153.0, first="v" if "N%d" % c in run_v else "s")
             name("N%d" % c)
-            scan(w("FL", a, 512), w("V0", a, 512), w("Gn", a, 512), -1.0, A.max, A.add)
+            scan(w("FL", a, 512), w("V0", a, 512), w("Gn", a, 512), -1e4, A.max, A.add)
             name("F%d" % c)
             if c % 2:
+                sums = w(("ps3", "ps4")[c // 2 % 2], 66 * (c // 4), 66)
                 for k0 in range(0, 16, 4):
-                    end = c % 4 == 3 and k0 == 12
-                    group([(w(cnt, 33 * (c % 4) - 33, 66), SEL(k), v("FL", a - BL + k, a + BL, 16)) for k in range(k0, k0 + 4)], False, end, "c" if end else "b")
+                    group([(sums, SEL(k), v("FL", a - BL + k, a + BL, 16)) for k in range(k0, k0 + 4)]
+                          + [(sums, v("ONE", 0, 128, 1, 0, 64), v("THR", 0, 66, 1, 0, 64))] * (k0 == 12), k0 == 0, k0 == 12)
                     name("P%d" % (c // 2))
-                    if end:
-                        prog[-1]["W"] += v(cnt, 0, 132)[1]
 
         pull[0] = PULL["table"]
-        affine(so, ind(v("V0"), v("FO")), 1.0)
+        affine(so, ind(v("V0"), v("FO")), -0.5, 0.5)
         if not last:
-            send("s%d" % (t + 1), [(v("sc%d" % (t + 1)), [so])], STATE_GO, 2.0)
-        act(v("sgn"), so, ACT.Sign, 1 / DL, col("SG", 1))
+            send("s%d" % (t + 1), [(w("TT", W + B * t + B, B), [so])], STATE_GO, 2.0)
         for a in range(0, 16, 4):
-            group([(v("ps4", 384, 392), SEL(k), v("so%d" % t, k, 128, 16)) for k in range(a, a + 4)], a == 0, a == 12)
+            group([(v("ps7", 256, 264), ID, v("UB"))] * (a == 0) + [(v("ps7", 256, 264), SEL(k), v("so%d" % t, k, 128, 16)) for k in range(a, a + 4)], a == 0, a == 12)
             name("us")
-        ts(v("ui"), v("ps4", 384, 392), 1 / (SW * DL), A.mult)
-        ts(v("ua"), v("ui"), 31, A.bitwise_and)
-        tt(v("uo"), v("ua"), v("C32"), A.add)
-        cp(v("uu"), v("uo"))
+        ts(v("ui"), v("ps7", 256, 264), -1 / SW, A.mult)
+        ts(v("ua"), v("ui"), 31 + 7 * 512, A.bitwise_and)
+        ts(v("uu"), v("ua"), col("C32", 0), A.add)
         name("uu")
-        act(v("es"), ind(v(Et), v("uu")), ACT.Identity)
+        affine(v("es"), ind(v(Et), v("uu")), 1.0, first="s")
         name("es")
-        mms(v("ps7", 0, 128), [(IS(4), so), (IS(5), v("sgn")), (ID, v("es"))])
-        act(v("eb"), v("ps7", 0, 128), ACT.Identity, 0.5, 129.75 + 72)
-        tt(ind(v(En), v("uu")), v("eb"), v("M130"), A.add)
-        name("En")
+        mms(v("ps1", 384, 512), [(IS(1), so), (ID, v("es"))])
+        affine(v("eb"), v("ps1", 384, 512), 0.5, 141.75, first="s")
+
+        def change(E):
+            tt(ind(v(E), v("uu")), v("eb"), v("M130"), A.add)
+            name("En")
+
         if last:
-            store("y", 0, T.ye[:, :], v(En))
+            change("E1")
+            store("y", 0, T.ye[:, :], v("E1"))
         else:
-            copy(3 + t, v("E%d" % ((t + 2) % 3)), v(En))
-            act(v("eu"), v("eb"), ACT.Sign, None, col("SG", 2))
-            act(v("ew"), v("eb"), ACT.Sign, None, col("SG", 3))
-            mms(v("ps7", 128, 256), [(ID, v("eb")), (IS(6), v("eu")), (IS(7), v("ew")), (IS(8), v("ew"))])
-            act(v("ea"), v("ps7", 128, 256), ACT.Identity, None, -274.0)
+            act(v("eu"), v("eb"), ACT.Abs, None, col("SG", 2))
+            affine(v("ew"), v("eb"), -1.0, 154.0)
+            ts(v("ea"), v("eu"), 4.0, A.is_gt)
             name("ea")
-            cp(ind(v("TT"), v("uu")), v("ea"))
+            tt(ind(v("TT", 0, W), v("uu")), v("ea"), v("ew"), A.mult)
             name("TT")
         pull[0] = 0.0
 
         for j in range(2):
             cs, o, y, x4 = range(4 * j, 4 * j + 4), j * HW, 128 * j, 4 * j
-            cnt, vx, fx, RM, LT = ("ps0", "ps5")[j], "vx%d" % j, "fx%d" % j, v("RM%d" % j), v("LT%d" % j)
 
             def s4(name):
                 return w(name, x4, 4)
@@ -705,176 +750,211 @@ def rank_program(g, core, T, topo):
             def hv(name, a=0, n=128):
                 return w(name, y + a, n)
 
+            def tmp(a=0, n=128):
+                return w("ps0", 2 * y + a, n)
+
             def nm(x):
                 name("%s%d" % (x, j))
 
-            scan(v("xs", 132 * j + 131, 132 * j - 1, -1), v(cnt, 131, None, -1), v("XC", 131, None, -1), 0.0, A.max, A.min)
-            nm("xs")
-            ts(s4("ou"), v("xs", 132 * j, 132 * j + 132, 33), -1.0, A.mult)
-            nm("ou")
-            for c in cs:
-                scan(v("kx", 33 * c + 32, 33 * c - 1, -1), v(cnt, 33 * (c % 4) + 32, 33 * (c % 4) - 1, -1), v(KW, o + KS + 132 + c % 4, o + KS + c % 4, -4), 0.0, A.max, A.min)
-                nm("kx")
-            kx = v("kx", 132 * j, 132 * j + 132, 33)
-            cp(w(vx, 64 * j, 64), ind(w("TM", 4 * BL * j, 4 * BL), s4("ou")))
-            nm("vx")
-            affine(w(fx, 64 * j, 64), ind(w("FL", 4 * BL * j, 4 * BL), s4("ou")), 1.0, None, QF)
-            nm("fx")
-            act(w("dd", 64 * j, 64), ind(w("Gn", 4 * BL * j, 4 * BL), s4("ou")), ACT.Identity)
-            nm("dd")
-            mms(w("ps3", 128 + 64 * j, 64), [(ID, w("dd", 64 * j, 64)), (IS(3), w(fx, 64 * j, 64))])
-            nm("dm")
-            for a in range(2):
-                affine(hv("wm", 64 * a, 64), w("ps3", 128 + 64 * j, 64), SC / (32 * DL), 764 * SC, "s")
-                nm("wm")
-            ts(w(KW, o + KS, 4), kx, 2.0 ** 18, A.add)
-            ts(s4("sx"), kx, 4095, A.bitwise_and)
-            cp(s4("sxf"), s4("sx"))
-            affine(s4("sx32"), s4("sxf"), 1 / 32, None, "s")
-            for c in cs:
-                act(lanes("sg1", c), w("XC", 33 * (c % 4), 32), ACT.Sign, -1.0, col("xs", 33 * c))
-                nm("sg")
-            act(hv("gt"), hv("sg1"), ACT.Relu)
-            nm("gt")
+            gt, ge = w("sg1", 132 * j, 128), w("sg1", 132 * j + 4, 128)
+            for h in range(2):
+                a, k, cnt, bank = 66 * j, 2 * j + h, ("ps3", "ps4")[h], ("ps1", "ps2")[h]
+                pair = (2 * k, 2 * k + 1)
+
+                def s2(name):
+                    return v(name, x4 + h, x4 + 4, 2)
+
+                def pv(name, a=0):
+                    return v(name, y + a + h, y + a + 128, 2)
+
+                def nk(x):
+                    name("%s%d" % (x, k))
+
+                xs, kx = v("xs", 66 * k, 66 * k + 66, 33), v("kx", 66 * k, 66 * k + 66, 33)
+                fx, dd = w("fx", 32 * k, 32), w("dd", 32 * k, 32)
+                scan(v("xs", 66 * k + 65, 66 * k - 1, -1), v(cnt, a + 65, a - 1, -1), v("XC", 65, None, -1), 0.0, A.max, A.min)
+                nk("xs")
+                ts(w("ou", 2 * k, 2), xs, -1 / 256, A.mult, col("pb16", 0), A.add)
+                nk("ou")
+                affine(fx, ind(w("FL", 2 * BL * k, 2 * BL), w("ou", 2 * k, 2)), -1 / 64, -128.0, first=QF)
+                nk("fx")
+                cp(ind(w("WT", 256 * k, 256), v("WO", 0, 2)), fx)
+                nk("W")
+                affine(dd, ind(w("Gn", 2 * BL * k, 2 * BL), w("ou", 2 * k, 2)), 1.0, first="s")
+                nk("dd")
+                for c in pair:
+                    b = a + 33 * (c % 2)
+                    scan(v("kx", 33 * c + 32, 33 * c - 1, -1), v(cnt, b + 32, b - 1, -1), v(KW, o + KS + 128 + at(c) % 4, o + KS - 4 + at(c) % 4, -4), 0.0, A.max, A.min)
+                    nk("kx")
+                    act(lanes("sg1", c, 0, 33, 132), w("XC8", 33 * (c % 2), 33), ACT.Sign, -1.0, col("xs", 33 * c))
+                    nk("sg")
+                mms(w(bank, 192, 32), [(ID, dd), (IS(0), fx)])
+                nk("dm")
+                affine(w("wm", 128 * k, 32), w(bank, 192, 32), SC / 8, 1788 * SC, first="s")
+                nk("wm")
+                for n in (32, 64):
+                    again(w("wm", 128 * k + n, n), w("wm", 128 * k, n))
+                    nk("wm")
+                affine(s2("kx0"), kx, 1.0, 2.0 ** 18, first="s")
+                tt(s2("sxf"), kx, xs, A.subtract)
+                affine(s2("sx32"), s2("sxf"), 1 / 32, first="s")
+
+                for c in pair:
+                    singles([(v(bank, l, 128, 16, 32 * (c % 2), 32 * (c % 2) + 32), v("D1", c * BL + 16 + l, c * BL + BL, 16), v("WT", 128 * c + l, 128 * c + 128, 16))
+                             for l in range(16)])
+                    nk("H")
+                hit, sums = v("hit", 128 * k, 128 * k + 128, 1, 0, 64), v(bank, 0, 128, 1, 0, 64)
+                rec({"v": ts_fn(hit, sums, 0.0, A.max, None, None), "s": act_fn(hit, sums, ACT.Relu, None, None)}, hit, [sums], "ts")
+                nk("hit")
+                mms(w(bank, 128, 64), [(IS(2), v("sg1", 132 * j + 4 + h, 132 * j + 132, 2)), (hit, v("PERM", 0, 64, 1, 0, 64))])
+                nk("turn")
+                for c in pair:
+                    scan(w("kd", 32 * at(c), 32), v(bank, 128 + c % 2, 192, 2), lanes(KW, c, KS, 32, HW), col("kx0", at(c)), A.min, A.max)
+                    nk("kd")
+                ts(s2("sd"), v("kd", y + 32 * h + 31, y + 128, 64), 4095, A.bitwise_and)
+                nk("sd")
+                tt(s2("p32"), s2("sd"), s2("sx32"), A.mult)
+                ts(s2("bsf"), s2("p32"), -262016.484375, A.add, 2.0 ** 23 + 4096 + 262016 + 97 * t, A.add)
+
+                for c in pair:
+                    ts(lanes("craw", c), v("KAP"), col("sxf", at(c)), A.mult, col("bsf", at(c)), A.add)
+                    nk("c")
+                ts(pv("cm"), pv("craw"), 4095, A.bitwise_and)
+                nk("cm")
+                cp(w("cu", 64 * k, 64), pv("cm"))
+                nk("cu")
+                for c in pair:
+                    b = c * 512
+                    affine(w("EC", b, 512), ind(v(Et), w("cu", c * 32, 32)), SC, (C0 + 0.5) * SC, first=QC[c])
+                    name("E%d" % c)
+                    for x in range(b, b + 512, 128):
+                        scan(w("FC", x, 128), w("EC", x, 128), w("wm", 128 * k, 128), -1.0, A.max, A.add)
+                        name("C%d" % c)
+                cn = w(cnt, 256 + j * 64, 64)
+                mms(cn, [(ONE, v("K2c", 0, 128, 2)), (ID, pv("BAR"))], [(SEL(x, 144), v("FC", 1024 * k + x, 1024 * k + 1024, 16)) for x in range(16)])
+                nk("S")
+                tt(pv("RK", y + 128), pv("cm"), cn, A.add)
+                nk("key")
+
             G = hv("ps6")
-            mms(G, [(IS(9), ONE), (IS(10), hv("sg1")), (IS(11), hv("gt")), (IS(12), hv("gt"))])
+            mms(G, [(IS(3), gt), (IS(4), ge)])
             nm("G")
-
-            DT = hv("ps1")
-            mms(DT, [(v("CW"), ONE), (v(fx), IS(2)), (v(vx), IS(3))])
-            nm("DT")
-            scan(RM, v("SCM"), DT, 0.0, A.min, A.max)
-            nm("RM")
-            tt(LT, ind(RM, v("LO")), v("DM"), A.mult)
-            nm("LT")
-            mms(w("ps2", 132 * j, 132), [(ONE, v("HR")), (LT, w("TR", 132 * j, 132))])
-            nm("turn")
-            for c in cs:
-                scan(w("kd", 33 * c, 33), w("ps2", 33 * c, 33), lanes(KW, c, KS, 33, HW), 0.0, A.min, A.max)
-                nm("kd")
-            kd = v("kd", 132 * j + 32, 132 * j + 132, 33)
-            ts(s4("sd"), kd, 4095, A.bitwise_and)
-            nm("sd")
-            ts(s4("dq"), kd, 12, A.arith_shift_right, 63, A.bitwise_and)
-            tt(s4("p32"), s4("sd"), s4("sx32"), A.mult)
-            ts(s4("bsf"), s4("p32"), -262016.484375, A.add, 2.0 ** 23 + 4096 + 262016 + 97 * t, A.add)
-
-            for c in cs:
-                ts(lanes("craw", c), v("KAP"), col("sxf", c), A.mult, col("bsf", c), A.add)
-                nm("c")
-            ts(hv("cm"), hv("craw"), 4095, A.bitwise_and)
-            nm("cm")
-            cp(hv("cu"), hv("cm"))
-            nm("cu")
-            for c in cs:
-                a = c * 512
-                affine(w("EC", a, 512), ind(v(Et), w("cu", c * 32, 32)), SC, (C0 + 0.5) * SC, QC[c])
-                name("E%d" % c)
-                for k in range(a, a + 512, 128):
-                    scan(w("FC", k, 128), w("EC", k, 128), hv("wm"), -1.0, A.max, A.add)
-                    name("C%d" % c)
-                if c % 2:
-                    x = (c // 2 % 2) * 64
-                    cn = w("ps%d" % (3 + c // 2 % 2), j * 64, 64)
-                    mms(cn, [(ONE, w("K2c", x, 64)), (ID, hv("BAR", x, 64))], [(SEL(k), v("FC", a - 512 + k, a + 512, 16)) for k in range(16)])
-                    name("S%d" % (c // 2))
-                    tt(hv("key", x, 64), hv("cm", x, 64), cn, A.add)
-                    name("key%d" % (c // 2))
-
+            for a, out in ((KS, "IA"), (KQ, "IQ")):
+                tt(hv("ps5", 256), w(KW, o + a - 4, 128), G, A.add)
+                nm("t" + out)
+                tt(hv(out), w(KW, o + a, 128), hv("ps5", 256), A.max)
+                nm(out)
+            ts(s4("dq"), v("kd", y + 31, y + 128, 32), 12, A.arith_shift_right, 63, A.bitwise_and)
             ts(s4("dcol"), s4("dq"), -64.0, A.add)
-            ts(s4("Aq"), s4("sd"), 16385.0, A.add)
+            ts(s4("Aq"), s4("sd"), 65537.0, A.add)
             for c in cs:
-                act(lanes("ps7", c, 256), v("kc1"), ACT.Abs, None, col("dcol", c))
+                act(lanes("ps7", c), w("kc1", 32 * (c % 2), 32), ACT.Abs, None, col("dcol", at(c)))
                 nm("ab")
-                ts(lanes("e2p", c), lanes(KW, c, RAWQ + 4, 32, HW), 16384.0, A.add, col("Aq", c), A.not_equal)
+                ts(lanes("e2p", c), lanes(KW, c, RAWQ, 32, HW), 65536.0, A.add, col("Aq", at(c)), A.not_equal)
                 nm("e")
-            tt(hv("kept"), hv("e2p"), hv("ps7", 256), A.min)
+            tt(hv("kept"), hv("e2p"), hv("ps7"), A.min)
             nm("kept")
             for c in cs:
                 scan(lanes("Dz", c, 4, 32, 132), v("ONE", 0, 32), lanes("kept", c), 0.0, A.add, A.subtract)
                 nm("D")
             cp(s4("nf"), w("Dz", 132 * j + 128, 4))
             for c in cs:
-                act(lanes("tl", c), v("kcm"), ACT.Sign, None, col("nf", c))
+                act(lanes("tl", c), v("kcm"), ACT.Sign, None, col("nf", at(c)))
                 nm("tl")
-            TL = hv("ps6", 256)
-            mms(TL, [(IS(13), hv("tl"))])
-            nm("TL")
+            TS = hv("ps6", 256)
+            mms(TS, [(ID, v("K3c")), (IS(5), hv("tl"))])
+            nm("TS")
+            tt(tmp(128), hv("cm"), TS, A.add)
+            nm("cT")
             for b in range(5):
                 s = 4 << b
                 m = 128 - s
                 tb = w("tb", 640 * j + 128 * b, m)
                 ts(tb, w("Dz", 132 * j + s, m), b, A.arith_shift_right, 1, A.bitwise_and)
                 name("b%d%d" % (j, b))
-                scan(hv("ps0", 256, m), tb, w(KW, o + KS + 4 + s, m), 0.0, A.max, A.mult)
+                scan(tmp(0, m), tb, w(KW, o + KS + s, m), 0.0, A.max, A.mult)
                 name("m%d%d" % (j, b))
-                tt(w(KW, o + KS + 4, m), w(KW, o + KS + 4, m), hv("ps0", 256, m), A.min)
+                there = w(KW, o + KS, m)
+                if b == 4:
+                    tt(w("RK", 2 * y, 128), w(KW, o + KS, 128), tmp(128), A.min)
+                    nm("fill")
+                    there = w("RK", 2 * y, m)
+                tt(there, there, tmp(0, m), A.min)
                 name("r%d%d" % (j, b))
-            tt(hv("ps5", 256), hv("cm"), TL, A.add)
-            nm("cT")
-            tt(w(KW, o + KS + 4, 128), w(KW, o + KS + 4, 128), hv("ps5", 256), A.min)
-            nm("fill")
             pull[0] = 0.0 if last else PULL["reasons"]
             for b in range(5):
                 s = 4 << b
                 m = 128 - s
-                scan(hv("ps7", 0, m), w("tb", 640 * j + 128 * b, m), w(KW, o + KQ + s, m), 0.0, A.max, A.mult)
+                scan(hv("ps5", 0, m), w("tb", 640 * j + 128 * b, m), w(KW, o + KQ + s, m), 0.0, A.max, A.mult)
                 name("Q%d%d" % (j, b))
-                tt(w(KW, o + KQ, m), w(KW, o + KQ, m), hv("ps7", 0, m), A.min)
+                tt(w(KW, o + KQ, m), w(KW, o + KQ, m), hv("ps5", 0, m), A.min)
                 name("q%d%d" % (j, b))
-            tt(hv("RQ"), w(KW, o + KQ, 128), TL, A.min)
+            tt(hv("RQ"), w(KW, o + KQ, 128), TS, A.min)
             nm("RQ")
             pull[0] = 0.0
-            for a, tmp, out in ((RAWS, "ps0", "IA"), (RAWQ, "ps1", "IQ")):
-                tt(hv(tmp, 256), w(KW, o + a, 128), G, A.add)
-                nm("t" + out)
-                tt(hv(out), w(KW, o + a + 4, 128), hv(tmp, 256), A.max)
-                nm(out)
 
             for c in cs:
-                red(col("z", c), lanes("key", c), A.max)
-                nm("z")
-            for c in cs:
-                ts(lanes("ps0", c, 256), lanes(KW, c, KS + 4, 32, HW), col("z", c), A.max)
+                k = c % 4
+                back = v("RK", 2 * y + 252 + k, 2 * y + k - 4, -4)
+                scan(v("ps0", 2 * y + 252 + k, 2 * y + k - 4, -4), back, back, -1e9, A.max, A.max)
                 nm("g")
-            tt(hv("YS"), hv("IA"), hv("ps0", 256), A.min)
+            z = tmp(128, 4)
+            tt(hv("YS"), hv("IA"), tmp(), A.min)
             nm("Y")
             nS, nQ, nx = hv(ZO), hv(ZO, 256), "KW%d" % (t + 1)
             ts(nS, hv("YS"), 4095, A.bitwise_and)
             nm("Z")
             if not last:
                 for c in cs:
-                    cp(w("plo%d" % t, 32 * c, 32), lanes(ZO, c))
+                    cp(w("plo%d" % t, LW * c, 32), lanes(ZO, c))
                     nm("L")
-                send("p%d%d" % (j, t + 1), [(hv("pl%d" % (t + 1)), [hv("plo%d" % t)])], PLAN_GO, FLY)
-                send("k%d%d" % (j, t + 1), [(w(nx, o + KS + 4, 128), [nS, v("Kf")]), (w(nx, o + RAWS + 4, 128), [nS])], PLAN_GO, FOLD)
+                send("p%d%d" % (j, t + 1), [(w("pl%d" % (t + 1), 4 * LW * j, 4 * LW), [w("plo%d" % t, 4 * LW * j, 4 * LW)])], PLAN_GO, FLY)
+                send("k%d%d" % (j, t + 1), [(w(nx, o + KS, 128), [nS, v("Kf")])], PLAN_GO, FOLD1)
+                prog[-2]["R"] += prog[-4]["W"]
             else:
                 cp(v("ysw", j, 256, 2), nS)
             pull[0] = 0.0 if last else PULL["after"]
-            ts(s4("ret"), s4("z"), 0.0, A.is_lt)
-            tt(s4("zq"), s4("z"), s4("Aq"), A.min)
-            act(s4("vq"), s4("zq"), ACT.Relu)
-            nm("vq")
-            for c in cs:
-                act(lanes("ps7", c), lanes("RQ", c), ACT.Identity, col("ret", c), col("vq", c))
-                nm("gq")
-            tt(hv("YQ"), hv("IQ"), hv("ps7"), A.min)
+            tt(s4("zq"), z, s4("Aq"), A.min)
+            if GQ[t] == "s":
+                act(s4("sgz"), z, ACT.Sign)
+                affine(s4("ret"), s4("sgz"), -0.5, 0.5, first="s")
+                act(s4("vq"), s4("zq"), ACT.Relu)
+                nm("vq")
+                for c in cs:
+                    act(lanes("ps7", c), lanes("RQ", c), ACT.Identity, col("ret", at(c)), col("vq", at(c)))
+                    nm("gq")
+                tt(hv("YQ"), hv("IQ"), hv("ps7"), A.min)
+            else:
+                if not last:
+                    ts(s4("retb"), z, 0.0, A.is_lt)
+                for c in cs:
+                    k = c % 4
+                    back = v("RQ", y + 124 + k, y + k - 4, -4)
+                    scan(v("ps5", y + 124 + k, y + k - 4, -4), back, back, col("zq", c), A.max, A.max)
+                    nm("gq")
+                tt(hv("YQ"), hv("IQ"), hv("ps5"), A.min)
             nm("YQ")
             ts(nQ, hv("YQ"), 8191, A.bitwise_and)
             nm("ZQ")
             if not last:
-                send("q%d%d" % (j, t + 1), [(w(nx, o + RAWQ + 4, 128), [nQ]), (w(nx, o + KQ, 128), [nQ, v("KQf")])], PLAN_GO, FOLD)
+                send("q%d%d" % (j, t + 1), [(w(nx, o + RAWQ, 128), [nQ]), (w(nx, o + KQ, 128), [nQ, v("KQf")])], PLAN_GO, FOLD)
             else:
                 ts(v("ysw", 256 + j, 512, 2), nQ, -1.0, A.add)
             pull[0] = 0.0
         if not last:
+            change("E0")
+            if t == VI - 2:
+                copy(3, v("E1"), v("E0"))
             pull[0] = PULL["parity"]
-            ts(v("retb"), v("z"), 0.0, A.is_lt)
-            mms(col("ps6", 0), [], [(ONE, col("retb", c)) for c in range(8)])
-            ts(col("ri", 0), col("ps6", 0), -0.5, A.add, 0.5, A.mult)
-            ts(col("thr", 0), col("ps6", 0), -2.0 ** 14, A.mult)
-            ts(col("thr", 1), col("ri", 0), 2.0 ** 15, A.mult, -1.5 * 2 ** 14, A.add)
-            affine(v("THR"), v("O132"), col("thr", 0), col("thr", 1))
+            if GQ[t] == "s":
+                affine(v("retb"), v("sgz"), -0.5, 0.5, first="s")
+            def top(name, a=0, n=1):
+                return v(name, a, a + n, 1, 0, 32)
+            mms(top("ps7", 272), [], [(v("ONE", 0, 32), col("retb", c)) for c in range(8)])
+            ts(top("ri"), top("ps7", 272), -0.5, A.add, 0.5, A.mult)
+            ts(top("thr"), top("ps7", 272), -2.0 ** 32, A.mult)
+            ts(top("thr", 1), top("ri"), 2.0 ** 33, A.mult, -1.5 * 2 ** 32, A.add)
+            affine(top("THR", 0, 66), top("ONE", 0, 66), top("thr"), top("thr", 1))
             name("THR")
             pull[0] = 0.0
         else:
@@ -886,8 +966,8 @@ def rank_program(g, core, T, topo):
         for x in RUN[min(t, 1)] + LINES + (ENDS if t == VI - 1 else MIDS):
             line(x, t)
     if not PLANNED:
+        PLANNED["prog"], PLANNED["named"] = prog, named
         PLANNED["plan"] = _schedule(prog)
-        PLANNED["prog"] = prog
     order, queue, done, deps = PLANNED["plan"]
     tok = {}
     for i in order:

import numpy as np
from concourse.bass import DstId, RemoteDMATransfer
from concourse.mybir import AluOpType, AxisListType, ActivationFunctionType

A = AluOpType
ACT = ActivationFunctionType
AX = AxisListType.X
W, L, B, VI = 4096, 32, 128, 3
PLAN_GO, STATE_GO = 3, 1
H, F, I, U = "bfloat16", "float32", "int32", "uint16"
BL = 33 * 16
LW = 34

SCRATCH = {}
PART = {}


def _buf(dtype, n, *names):
    for x in names:
        SCRATCH[x] = ("sbuf", [128, n], dtype)


def _pool(name, dtype, n, *names):
    _buf(dtype, n * len(names), name)
    for k, x in enumerate(names):
        PART[x] = (name, k * n, n)


_buf(H, W, "E0", "E1", "PT", "EC", "FC")
_buf(H, W + VI * B, "TT")
_buf(H, 8 * BL, "D1", "V0", "Gn", "FL")
_buf(H, 288, "SEL")
_buf(H, 128, "ID", "ONE", "fx", "dd", "M130", "K2c", "K3c", "es", "eb", "ea", "eu", "ew", "st", "so0", "so1", "so2")
_buf(H, 1024, "WT")
_buf(H, 6 * 128, "IS")
_buf(H, 8, "G8", "retb", "UB")
_buf(H, 66, "THR")
_buf(H, 64, "PERM")
_buf(H, 512, "wm", "hit")
_buf(F, 264, "xs", "kx")
_buf(F, 66, "XC", "XC8")
_buf(F, 64, "kc1")
_buf(H, 264, "sg1")
_buf(H, 256, "BAR", "e2p", "kept", "tl")
_buf(F, 128, "al", "aq")
_buf(F, 512, "ysw", "RK")
_buf(F, 256, "RQ", "IA", "IQ")
_buf(F, 32, "kcm", "KAP")
_pool("lf", F, 8, "C32", "SG", "sxf", "sx32", "bsf", "barf", "dcol", "Aq", "nf", "ret", "zq", "vq", "p32", "pbf", "kx0", "pb16", "sgz")
_buf(F, 2, "thr")
_buf(I, 2, "ri")
_buf(I, 10 * 128, "tb")
_buf(I, 256, "craw", "cm", "wa", "wi", "YS", "YQ", "kd")
_buf(I, 128, "Kf", "KQf")
_buf(I, 264, "Dz")
_buf(I, 8, "bari")
_pool("li", I, 8, "pi", "pb", "sx", "sd", "dq", "ui", "ua", "uo", "wo", "xi", "fo")
HW, KS, RAWQ, KQ = 396, 4, 136, 268
_buf(I, 2 * HW, "KW0", "KW1", "KW2")
_buf(I, 512, "ZO0", "ZO1", "ZO2")
_buf(U, 8 * LW, "pl0", "pl1", "pl2", "plo0", "plo1")
_buf(U, 256, "cu")
_buf(U, 8, "ou", "uu", "WO", "FO")
for _b in range(8):
    SCRATCH["ps%d" % _b] = ("psum", [128, 512], F)

DMAS = ["ld%d" % k for k in range(12)] + ["ds%d" % k for k in range(5)]
SEMAPHORES = ["qv", "qs", "qt", "qg"] + DMAS + [a + x + t for a in "al" for x in ("p0", "p1", "k0", "k1", "q0", "q1", "s") for t in "12"]
TAB = "ttvtvttv"
BIG = 2.0 ** 19
SW, SC = -2.0 ** 31, -2.0 ** -16
C0 = 1304
CYC, GATHER, SCATTER, WAKE = 0.83e-3, 1.4, 3.8, 0.22
AHEAD, PASSES, SLACK, LAZY, SFIX = (0.8, 3.0), 120, (0.5, 3.0), (0.3, 1.0), 0.05
BLUR, STRAY, SPARE = (0.0, 0.05, 0.15, 0.4), 2.0, 0.1
POLISH, HEAT, SNAP, FLIP = ((6, 2000), (2, 5000), (1, 24000)), 0.06, 48, 0.13
WAYS = ((0.2, 1.0), (0.16, 1.33), (0.26, 0.8))
FOLD1, MEAN = 3.0, 0.3
FLY, FOLD, LOAD, NEXT, LATE, EARLY = 1.3, 4.5, 1.3, 1.25, 0.3, 8.0
PFIX = 0.01
PULL = {"table": 0.0, "reasons": 0.0, "after": 0.0, "parity": 3.0}
STORE = 1000.0
CUTS = (0, 512, 1536, 2560, 3584, 4096)
QC = "ssssssss"
RUN = (("T2 T3 R0 T6 T7 R1 N1 F0 F1 N3 F2 F3 N5 F4 F5 F6 F7", "T0 T1 T4 T5 N0 N2 N4 N6 N7 E0"),
       ("R0 R1", "T0 T1 T2 T3 N0 N1 N2 N3 T4 T5 T6 T7 N4 N5 N6 N7 E0"))
LINES = ("E0 E1 E2 E3 E4 E5 E6 E7", "P0 P1 H0 turn0 H1 turn1 P2 P3 H2 turn2 H3 turn3", "S0 S1 S2 S3")
QF = "v"
GQ = "ssv"
MIDS = ()
ENDS = ()
WHOLE = ("ps1", "ps2", "ps6")
SIZE = {H: 2, F: 4, I: 4, U: 2}


def _tracker(g, T):
    eng = {"v": g.vector, "s": g.scalar, "t": g.tensor, "g": g, "y": g.sync}
    cnt, bank = {}, {}
    known = {q: {} for q in eng}

    def settle(q, toks):
        best = {}
        for sem, c, clk in toks:
            if known[q].get(sem, 0) < c and (sem not in best or best[sem][0] < c):
                best[sem] = (c, clk)
        todo = sorted(best.items(), key=lambda x: -len(x[1][1]))
        for sem, (c, clk) in todo:
            if known[q].get(sem, 0) >= c:
                continue
            if any(s2 != sem and known[q].get(s2, 0) < c2 and k2.get(sem, 0) >= c for s2, (c2, k2) in todo):
                continue
            eng[q].wait_ge(T.sem[sem], c)
            known[q][sem] = c
            for s2, c2 in clk.items():
                if known[q].get(s2, 0) < c2:
                    known[q][s2] = c2

    def op(q, fn, toks, P, sem, inc):
        for b in P:
            toks = toks + [t for q2, t in bank.get(b, {}).items() if q2 != q]
        settle(q, toks)
        ins = fn(eng[q])
        name = sem or "q" + q
        cnt[name] = cnt.get(name, 0) + inc
        ins.then_inc(T.sem[name], inc)
        tok = (name, cnt[name], dict(known[q]))
        for b in P:
            bank.setdefault(b, {})[q] = tok
        return tok

    def send(fn, toks, local, n):
        settle("g", toks)
        fn()
        cnt[local] = n
        return (local, n, dict(known["g"]))

    def lands(sem, n):
        cnt[sem] = n
        return (sem, n, {})

    def finish():
        settle("g", [(s, c, {}) for s, c in cnt.items()])

    return op, send, lands, finish


def _depends(prog):
    seen = {}
    deps = []
    for i, e in enumerate(prog):
        d = set()
        for name, m in e["R"]:
            d.update(j for m2, j, w in seen.get(name, ()) if w and m2 & m)
        for name, m in e["W"]:
            d.update(j for m2, j, w in seen.get(name, ()) if m2 & m)
        for name, m in e["W"]:
            seen[name] = [x for x in seen.get(name, ()) if x[0] & ~m] + [(m, i, True)]
        for name, m in e["R"]:
            seen.setdefault(name, []).append((m, i, False))
        d.discard(i)
        deps.append(d)
    return deps


def _schedule(prog):
    deps = _depends(prog)
    n = len(prog)
    nxt = [[] for _ in range(n)]
    for i in range(n):
        for j in deps[i]:
            nxt[j].append(i)
    behind = [e.get("behind", []) for e in prog]
    ahead_of = [[] for _ in range(n)]
    for i in range(n):
        for j in behind[i]:
            ahead_of[j].append(i)
    rank = [0.0] * n
    for k in range(3):
        for i in range(n - 1, -1, -1):
            rank[i] = min(prog[i]["cost"].values()) + max([prog[i]["lat"] + rank[j] + WAKE for j in nxt[i]] + [rank[j] for j in ahead_of[i]] + [prog[i]["lat"]])

    run, costs = _timer(prog, deps)

    def one(before, after, rank, back, way, ahead, slack, lazy):
        wake, cost = WAYS[way][0], costs[way]
        ob, oa = (ahead_of, behind) if back else (behind, ahead_of)
        left = [len(d) + len(x) for d, x in zip(before, ob)]
        at = [{} for _ in range(n)]
        ready = set(i for i in range(n) if not left[i])
        free, bank, queue, order, done = {}, {}, {}, [], [0.0] * n

        met = {}

        def start(i, q):
            s = met.get((i, q))
            if s is None:
                s = met[(i, q)] = max([0.0] + [t + (0.0 if q == q2 == "t" else wake) for q2, t in at[i].items()]) + (prog[i]["lat"] if back else 0.0)
            f = free.get(q, 0.0) if q != "x" else 0.0
            if f > s:
                s = f
            for b in prog[i]["P"]:
                for q2, t in bank.get(b, {}).items():
                    if q2 != q and t + wake > s:
                        s = t + wake
            return s

        while ready:
            c = [(start(i, q), i, q) for i in ready for q in ([back[i]] if back else prog[i].get("first") or prog[i]["cost"])]
            first = {}
            for s, i, q in c:
                first[q] = min(first.get(q, s), s)
            q = min(first, key=lambda x: first[x])
            _, i, s = min((-rank[i], i, s) for s, i, q2 in c if q2 == q and s <= first[q] + 0.03)
            for s2, i2, q2 in c:
                if q2 == q and rank[i2] > rank[i] and s + cost[i][q] - s2 > (ahead if rank[i2] < rank[i] + slack else lazy) * (s2 - first[q]):
                    i, s = i2, s2
            ready.discard(i)
            end = s + cost[i][q]
            free[q] = end
            queue[i] = q
            order.append(i)
            done[i] = end + (0.0 if back else prog[i]["lat"])
            for b in prog[i]["P"]:
                bank.setdefault(b, {})[q] = end
            for j in after[i]:
                at[j][q] = max(at[j].get(q, 0.0), done[i])
                left[j] -= 1
                if not left[j]:
                    ready.add(j)
            for j in oa[i]:
                left[j] -= 1
                if not left[j]:
                    ready.add(j)
        return max(done), order, queue, done

    best, found = None, []
    const = []
    for i in range(n):
        const.append(prog[i]["sem"] is None and min(prog[i]["cost"].values()) < 1.0 and all(const[j] for j in deps[i]))
    const = [c and "g" not in e["cost"] for c, e in zip(const, prog)]
    pick = np.random.default_rng(1)
    urge = rank
    for k in range(PASSES):
        way, ahead, slack, lazy = int(pick.integers(len(WAYS))), float(pick.uniform(*AHEAD)), float(pick.uniform(*SLACK)), float(pick.uniform(*LAZY))
        blur = pick.normal(0.0, 1.0, n) * float(pick.choice(BLUR))
        top = max(urge) - EARLY
        fw = one(deps, nxt, [(max(u, top) if c else u) + e.get("pull", 0.0) + float(x) for u, c, e, x in zip(urge, const, prog, blur)], None, way, ahead, slack, lazy)
        now = sum(run(fw[1], fw[2], x)[0] for x in range(len(WAYS)))
        urge = one(nxt, deps, fw[3], fw[2], way, ahead, slack, lazy)[3]
        found.append((now, fw[1], fw[2]))
        if best is None or now < best[0]:
            best = (now, fw[1], fw[2], urge)
        elif now > best[0] + STRAY:
            urge = best[3] if pick.uniform() < 0.8 else rank
    found.sort(key=lambda x: x[0])
    for keep, steps in POLISH:
        found = sorted((_polish(prog, deps, nxt, x[1], x[2], run, steps, k) for k, x in enumerate(found[:keep])), key=lambda x: x[0])
    return found[0][1:] + (deps,)


def _timer(prog, deps):
    n = len(prog)
    dl = [sorted(d) for d in deps]
    lat = [e["lat"] for e in prog]
    banks = [e["P"] for e in prog]
    ways = WAYS
    cost = [[{q: c * (x if e.get("by index") else 1.0) for q, c in e["cost"].items()} for e in prog] for w, x in ways]

    def run(order, queue, k, a=0, old=None, to=0, room=0.0):
        wake, ck = ways[k][0], cost[k]
        if old is None:
            free, holder, bank, done, why, kept = {}, {}, {}, [0.0] * n, [None] * n, []
        else:
            kept = old[3][:a // SNAP + 1]
            free, holder, bank = dict(kept[-1][0]), dict(kept[-1][1]), {b: dict(x) for b, x in kept[-1][2].items()}
            done, why = list(old[1]), list(old[2])
        for p in range(a // SNAP * SNAP, n, SNAP):
            if old and p > to + 2 * SNAP and min(free[q] - old[3][p // SNAP][0][q] for q in "vst") > room:
                return None
            if p // SNAP == len(kept):
                kept.append((dict(free), dict(holder), {b: dict(x) for b, x in bank.items()}))
            for i in order[p:p + SNAP]:
                q = queue[i]
                s, w = free.get(q, 0.0), holder.get(q)
                soft = True
                if q == "t":
                    for j in dl[i]:
                        x = done[j] if queue[j] == "t" else done[j] + wake
                        if x > s:
                            s, w, soft = x, j, False
                else:
                    for j in dl[i]:
                        x = done[j] + wake
                        if x > s:
                            s, w, soft = x, j, False
                e = banks[i]
                if e:
                    for b in e:
                        for q2, (x, j) in bank.get(b, {}).items():
                            if q2 != q and x + wake > s:
                                s, w, soft = x + wake, j, True
                s += ck[i][q]
                if q != "x":
                    free[q], holder[q] = s, i
                done[i] = s + lat[i]
                why[i] = (w, soft)
                if e:
                    for b in e:
                        bank.setdefault(b, {})[q] = (s, i)
        return max(done) + MEAN * sum(done) / n, done, why, kept

    return run, cost


def _polish(prog, deps, nxt, order, queue, run, steps, seed):
    ways = WAYS
    before = [set(d) for d in deps]
    after = [set(x) for x in nxt]
    ix = [i for i in range(len(prog)) if "y" in prog[i]["cost"]]
    for a, b in zip(ix, ix[1:]):
        before[b].add(a)
        after[a].add(b)

    def links(r):
        done, why = r[1:3]
        i, out = done.index(max(done)), []
        while why[i][0] is not None:
            if why[i][1]:
                out.append((why[i][0], i))
            i = why[i][0]
        return out

    pick = np.random.default_rng(seed + steps)
    order, queue = list(order), dict(queue)
    res = [run(order, queue, k) for k in range(len(ways))]
    now = sum(x[0] for x in res)
    best = (now, order, queue, res[0][1])
    soft = [links(r) for r in res]
    for step in range(steps):
        lk = soft[int(pick.integers(len(ways)))]
        x = int(pick.integers(len(lk)))
        j, i = lk[x]
        way = float(pick.uniform())
        q2 = queue
        if way < FLIP:
            k = j if way < FLIP / 2 else i
            if len(prog[k]["cost"]) < 2:
                continue
            q2 = dict(queue)
            q2[k] = [q for q in prog[k]["cost"] if q != queue[k]][0]
            o2 = order
            a = b = order.index(k)
        else:
            fore = way < (1 + FLIP) / 2
            far = int(pick.geometric(0.45)) - 1
            if fore:
                while far and x + 1 < len(lk) and lk[x + 1][1] == j:
                    x, far = x + 1, far - 1
                    j = lk[x][0]
            else:
                while far and x > 0 and lk[x - 1][0] == i:
                    x, far = x - 1, far - 1
                    i = lk[x][1]
            a, b = order.index(j), order.index(i)
            mid = order[a:b + 1]
            go, need = set(), ({i} if fore else {j})
            for k in (mid[::-1] if fore else mid):
                if k in need:
                    go.add(k)
                    need |= before[k] if fore else after[k]
            if (j if fore else i) in go:
                continue
            stay, moved = [k for k in mid if k not in go], [k for k in mid if k in go]
            o2 = order[:a] + (moved + stay if fore else stay + moved) + order[b + 1:]
        limit = now + HEAT * (1 - step / steps) * float(pick.exponential())
        r2, new = [], now
        for k in range(len(ways)):
            r2.append(run(o2, q2, k, a, res[k], max(b, 200), limit - new + SPARE * (len(ways) - 1 - k)))
            new += r2[k][0] - res[k][0] if r2[k] else 1e9
            if new > limit + SPARE * (len(ways) - 1 - k):
                break
        if new <= limit:
            now, order, queue, res = new, o2, q2, r2
            soft = [links(r) for r in res]
            if now < best[0]:
                best = (now, order, queue, res[0][1])
    return best


PLANNED = {}


def rank_program(g, core, T, topo):
    rank = T.rank_of(core)
    if rank is None:
        return
    N = len(T.cores)
    op_now, send_now, lands_now, finish = _tracker(g, T)
    prog = []
    pull = [0.0]
    named, now = {}, [0]

    def name(x):
        named.setdefault((now[0], x), []).append(len(prog) - 1)

    def chain(ix):
        for a, b in zip(ix, ix[1:]):
            prog[b].setdefault("behind", []).append(a)

    def line(names, t):
        chain([i for x in names.split() for i in named.get((t - (x[0] == "<"), x.strip("<")), [])])

    def v(name, a=0, b=None, step=1, p=0, q=128):
        if name in PART:
            name, o, n = PART[name]
            a, b = o + a, o + (n if b is None else b)
        if b is not None and b < 0:
            b = None
        n = SCRATCH[name][1][1]
        cols = range(n)[a:b:step]
        m = 0
        if step == 1:
            m = ((1 << len(cols)) - 1) << a
        else:
            for c in cols:
                m |= 1 << c
        return (T[name][p:q, a:b:step], [(name, m)], len(cols), SIZE[SCRATCH[name][2]], SCRATCH[name][0] == "psum", None)

    def w(name, a, n):
        return v(name, a, a + n)

    def col(name, c, p=0):
        return v(name, c, c + 1, 1, p)

    def ind(win, off):
        return (win[0].indirect(off[0]), win[1], 16 * off[2], win[3], False, off)

    def ap(x):
        return x[0] if isinstance(x, tuple) else x

    def rec(fns, out, ins, kind, sem=None, inc=1, lat=0.0, R=(), Wr=(), first=None):
        ins = [x for x in ins if isinstance(x, tuple)]
        sides = [out] + ins
        reads = [k for x in ins for k in x[1]] + [k for x in sides if x[5] for k in x[5][1]] + list(R)
        n = max(x[2] for x in sides)
        cost = {}
        for q in fns:
            if kind == "mm":
                c = sum(max(min(64, l[2]), x[2]) * (4 if x[3] == 4 else 1) for l, x in zip(ins[::2], ins[1::2])) * CYC
            elif kind == "dma":
                c = 0.05
            elif q == "g":
                c = 0.15 + 2 * n * CYC
            elif any(x[5] for x in sides):
                c = (0.05 if q == "v" else 0.065) + n * CYC * (SCATTER if out[5] else GATHER)
            elif q == "s":
                c = SFIX + n * CYC
            elif kind == "tt":
                c = max(64, n * (1 if any(x[4] for x in ins) else 2)) * CYC
            else:
                c = max(64, n * (0.5 if q == "v" and kind == "ts" and all(x[3] == 2 for x in sides if x[2] > 1) else 1)) * CYC
            cost[q] = c + (PFIX if q in "vs" and any(x[4] for x in sides) else 0.0)
        prog.append({"kind": "op", "fn": fns, "R": reads, "W": list(out[1]) + list(Wr), "P": sorted(set(x[1][0][0] for x in sides if x[4])),
                     "sem": sem, "inc": inc, "cost": cost, "lat": lat, "by index": any(x[5] for x in sides), "pull": pull[0], "first": first})

    def ts_fn(out, a, s1, o0, s2, o1):
        if o1 is None:
            return lambda e: e.tensor_scalar(out[0], a[0], ap(s1), None, o0)
        return lambda e: e.tensor_scalar(out[0], a[0], ap(s1), ap(s2), o0, o1)

    def ts(out, a, s1, o0, s2=None, o1=None):
        rec({"v": ts_fn(out, a, s1, o0, s2, o1)}, out, [a, s1, s2], "ts")

    def tt(out, a, b, o):
        rec({"v": lambda e: e.tensor_tensor(out[0], a[0], b[0], o)}, out, [a, b], "tt")

    def cp(out, a):
        rec({"v": lambda e: e.tensor_copy(out[0], a[0])}, out, [a], "ts")

    def scan(out, a, b, init, o0, o1):
        rec({"v": lambda e: e.tensor_tensor_scan(out[0], a[0], b[0], ap(init), o0, o1)}, out, [a, b, init], "ts")

    def fill(out, c):
        rec({"v": lambda e: e.memset(out[0], c)}, out, [], "ts")

    def act_fn(out, a, fn, scale, bias):
        kw = {}
        if scale is not None:
            kw["scale"] = ap(scale)
        if bias is not None:
            kw["bias"] = ap(bias)
        return lambda e: e.activation(out[0], a[0], fn, **kw)

    def act(out, a, fn, scale=None, bias=None):
        rec({"s": act_fn(out, a, fn, scale, bias)}, out, [a, scale, bias], "act")

    def affine(out, a, scale, bias=None, qs="vs", first=None):
        fns = {"v": ts_fn(out, a, scale, A.mult, bias, None if bias is None else A.add), "s": act_fn(out, a, ACT.Identity, scale, bias)}
        rec({q: fns[q] for q in qs}, out, [a, scale, bias], "ts", first=first)

    def mms(out, pairs, run=()):
        whole = out[1][0][0] in WHOLE
        key = [] if whole else [("open" + out[1][0][0], 1)]
        parts = [list(pairs) + list(run)] if whole else [[x] for x in pairs] + ([list(run)] if run else [])
        for k, part in enumerate(parts):
            def fn(e, k=k, part=part):
                for j, (l, r) in enumerate(part):
                    ins = e.matmul(out[0], l[0], r[0], k == 0 and j == 0, k == len(parts) - 1 and j == len(part) - 1)
                return ins
            rec({"t": fn}, out, [x for lr in part for x in lr], "mm", Wr=key)

    def group(items, first, last, part="a"):
        def fn(e):
            for j, (o, l, r) in enumerate(items):
                ins = e.matmul(o[0], l[0], r[0], first and j == 0, last and j == len(items) - 1)
            return ins
        out = items[0][0]
        key = [("open" + out[1][0][0], 1)]
        rec({"t": fn}, out, [x for o, l, r in items for x in (l, r)], "mm", R=key if part == "b" else [],
            Wr=([] if part == "b" else key) + [o[1][0] for o, l, r in items])

    def singles(items):
        def fn(e):
            for o, l, r in items:
                ins = e.matmul(o[0], l[0], r[0], True, True)
            return ins
        out = items[0][0]
        rec({"t": fn}, out, [x for o, l, r in items for x in (l, r)], "mm", Wr=[o[1][0] for o, l, r in items])

    def gp(fn, out, ins):
        rec({"g": fn}, out, ins, "g")

    def iota(out, pattern, base, cmul):
        flag = {} if SCRATCH[out[1][0][0]][2] == I else {"allow_small_or_imprecise_dtypes": True}
        gp(lambda e: e.iota(out[0], pattern, base, cmul, **flag), out, [])

    def whole(out, c):
        flag = {} if SCRATCH[out[1][0][0]][2] == I else {"allow_small_or_imprecise_dtypes": True}
        rec({"v": lambda e: e.memset(out[0], c if not flag else float(c)), "g": lambda e: e.iota(out[0], [[0, out[2]]], c, 0, **flag)}, out, [], "ts", first="g")

    def load(q, k, out, src, lat):
        rec({q: lambda e: e.dma_start(out[0], src)}, out, [], "dma", "ld%d" % k, 16, lat)

    def store(q, k, dst, src):
        rec({q: lambda e: e.dma_start(dst, src[0])}, (None, [("out%d" % k, 1)], 1, 4, False, None), [src], "dma", "ds%d" % k, 16, 2.0 + src[2] * src[3] / STORE)

    def copy(k, out, src):
        rec({"y": lambda e: e.dma_start(out[0], src[0])}, out, [src], "dma", "ds%d" % k, 16, 9.0)

    def send(name, moves, go, lat):
        dst = T.cores[(rank + go) % N]
        rid, pid, _ = topo.addr(dst)
        eng = topo.engines(core, dst)
        if len(moves) == 1 and len(moves[0][1]) == 1:
            (out, (src,)), n = moves[0], len(eng)
            fn = lambda: g.remote_dma(out[0], src[0], T.sem["a" + name], T.sem["l" + name], pid, rid, topo.mask(core, dst))
        else:
            k = len(eng) // len(moves)
            n = k * len(moves)
            fn = lambda: g.remote_dma_fused([RemoteDMATransfer(dst_ids=[DstId(rid=rid, pnc=pid)], dma_engine_mask=sum(1 << x for x in eng[j * k:j * k + k]),
                                                               remote_sem=T.sem["a" + name], srcs=[x[0] for x in srcs], dsts=[out[0]], alu_op=int(len(srcs) > 1))
                                             for j, (out, srcs) in enumerate(moves)], local_sem=T.sem["l" + name])
        prog.append({"kind": "send", "fn": fn, "R": [k for _, srcs in moves for x in srcs for k in x[1]], "W": [("sent" + name, 1)], "P": [],
                     "sem": "l" + name, "inc": n, "cost": {"g": 0.5}, "lat": 0.0})
        prog.append({"kind": "lands", "fn": None, "R": [("sent" + name, 1)], "W": [k for out, _ in moves for k in out[1]], "P": [], "sem": "a" + name,
                     "inc": n, "cost": {"x": lat}, "lat": 0.0})

    def at(c):
        return c // 4 * 4 + c % 2 * 2 + c % 4 // 2

    def again(out, a):
        rec({"g": lambda e: e.affine_select(out[0], a[0], [[0, out[2]]], A.is_equal, 0.0, 0, 0), "s": act_fn(out, a, ACT.Identity, None, None)}, out, [a], "ts", first="g")

    def lanes(name, c, a=0, n=32, size=128):
        o = size * (c // 4) + a
        return v(name, o + at(c) % 4, o + 4 * n, 4)

    def IS(k):
        return v("IS", k * 128, k * 128 + 128)

    def SEL(k, a=0):
        return w("SEL", a + 15 - k, 128)

    for k, (a, b) in enumerate(zip(CUTS, CUTS[1:])):
        load("y", 4 + k, v("E0", a, b), T.eff[:, a:b], LOAD + NEXT * b / 1024)
    load("y", 0, v("wa"), T.act[:, :], LOAD + NEXT * 4.5)
    load("y", 2, v("st"), T.st0[:, :], LOAD + NEXT * 4.7)
    for k in range(2):
        load("y", 10 + k, v("PT", k * 2048, k * 2048 + 2048), T.req[:, k * 2048:k * 2048 + 2048], LOAD + NEXT * (6.7 + 2 * k) + LATE)
    load("y", 1, v("wi"), T.why[:, :], LOAD + NEXT * 10 + LATE)
    load("y", 3, v("bari"), T.bar[:, :], LOAD + NEXT * 10 + LATE)

    ID, ONE, G8 = v("ID"), v("ONE"), v("G8")
    fill(ONE, 1.0)
    gp(lambda e: e.affine_select(ID[0], ONE[0], [[-1, 128]], A.is_equal, 0.0, 0, 1), ID, [ONE])
    gp(lambda e: e.affine_select(G8[0], v("ONE", 0, 8)[0], [[-16, 8]], A.is_ge, 0.0, 0, 1), G8, [ONE])
    gp(lambda e: e.affine_select(G8[0], G8[0], [[16, 8]], A.is_ge, 0.0, 15, -1), G8, [G8])
    gp(lambda e: e.affine_select(v("PERM")[0], v("ONE", 0, 64)[0], [[-1, 32], [-32, 2]], A.is_equal, 0.0, 0, 1), v("PERM"), [ONE])
    affine(v("PERM"), v("PERM"), BIG)
    iota(v("pi"), [[0, 8]], 0, 1)
    iota(v("SEL"), [[0, 288]], 0, 0)
    affine(v("SEL", 15, 143, 16), G8, SW)
    affine(v("SEL", 159, 287, 16), G8, 1.5 * SW)
    for a in range(0, 1024, 256):
        iota(v("WT", a, a + 256), [[0, 256]], 0, 0)
    iota(v("C32"), [[16, 2], [32, 2], [64, 2]], 0, 0)
    iota(v("kc1"), [[33, 2], [1, 32]], 1, 0)
    whole(col("kc1", 63), 1)
    iota(v("KAP"), [[113, 32]], 37 - W, 0)
    iota(v("wo"), [[0, 2], [128, 4]], 0, 1)
    iota(v("xi"), [[16, 8]], W + 16, 0)
    iota(v("K2c"), [[-64, 32], [0, 4]], 31 * 64, 0)
    fill(v("K2c", 0, 128, 1, 64), -33280.0 * 768)
    iota(v("K3c"), [[-8192, 32], [0, 4]], 31 * 8192, 0)
    for c in range(8):
        whole(v("FL", c * BL + 512, c * BL + BL), -8256)
        whole(v("Gn", c * BL + 512, c * BL + BL), -7936)
    fill(v("M130"), -130.0)
    fill(v("THR", 0, 66, 1, 0, 32), -1.5 * 2 ** 32)
    fill(v("THR", 0, 66, 1, 32, 64), -2.0 ** 43)
    for k, x in enumerate((-7.5, 24.0, -137.5)):
        fill(col("SG", k), x)
    WS = (64.0, -1.0, BIG, -206 * 2.0 ** 15, 208 * 2.0 ** 15, -BIG)
    for k, x in enumerate(WS):
        affine(IS(k), ID, x)
    ts(v("pb"), v("pi"), 15, A.bitwise_and)
    cp(v("pbf"), v("pb"))
    cp(v("WO"), v("wo"))
    iota(v("XC"), [[-4096, 66]], -4096, 0)
    iota(v("XC8"), [[-4096, 66]], -2048, 0)
    affine(col("pb16", 0), col("pbf", 0), 1.0, -16.0)
    iota(v("fo"), [[BL, 8]], 512, 0)
    ts(v("FO"), v("fo"), col("pbf", 0), A.add)
    affine(v("kcm"), v("kc1", 0, 32), 1.0, -32.5)
    affine(v("UB"), v("C32"), -32 * SW, -384 * SW)
    ts(v("C32"), v("C32"), col("pbf", 0), A.add, 32.0, A.mult)
    for j in range(2):
        ts(w("barf", 4 * j, 4), v("bari", j, 8, 2), -1.5 * 2 ** 19, A.mult, 2.0 ** 17, A.add)
    for c in range(8):
        affine(lanes("BAR", c), v("ONE", 0, 32), col("barf", at(c)), None, "s")
    for t in range(1, VI):
        for k in range(2):
            ts(v("plo%d" % (t - 1), 32 + k, None, LW), v("xi"), col("pbf", 0), A.add, float(B * t), A.add)

    for c in range(8):
        cp(w("pl0", LW * c, 32), v("wa", 2 * (at(c) % 4) + c // 4, 256, 8))
    ts(v("pl0", 32, 7 * LW, LW), v("C32", 1, 8), 1 / 32, A.mult, float(W), A.add)
    affine(w("TT", W, B), v("st"), -1.0, 24.0)
    iota(v("al"), [[1, 32], [33, 2], [0, 2]], 1, 0)
    iota(v("aq"), [[-8192, 32], [0, 4]], -8192, 0)
    Kc, KQc = v("ps6", 0, 128), v("ps6", 128, 256)
    affine(Kc, v("al"), -4096.0)
    affine(KQc, v("aq"), 1.0)
    for j in range(2):
        o = j * HW
        tt(w("KW0", o + KS, 128), v("wa", j, 256, 2), Kc, A.add)
        ts(w("KW0", o + RAWQ, 128), v("wi", j, 256, 2), 1.0, A.add)
        tt(w("KW0", o + KQ, 128), w("KW0", o + RAWQ, 128), KQc, A.add)
        for t in range(VI):
            for a in (KS - 4, KQ - 4):
                whole(w("KW%d" % t, o + a, 4), -2 ** 19)
            for k in range(2):
                whole(w("KW%d" % t, o + KS + 128 + 2 * k, 2), -4096 * 33 * (k + 1))
    ts(v("Kf"), v("al"), -4096.0, A.mult)
    iota(v("KQf"), [[-8192, 32], [0, 4]], -8192, 0)

    for c in range(8):
        a, b = c * 512, c * 512 + 512
        if TAB[c] == "t":
            p = v(("ps0", "ps1", "ps2", "ps7")[c % 4])
            ts(v("EC", a, b), v("E0", a, b), 1024.5, A.add)
            ts(v("FC", a, b), v("EC", a, b), 1032.0, A.is_equal, 64.0, A.mult)
            mms(p, [(ID, v("E0", a, b)), (ID, v("FC", a, b))])
            act(v("TT", a, b), p, ACT.Relu, -1.0, col("SG", 1))
        else:
            act(v("EC", a, b), v("E0", a, b), ACT.Abs, None, col("SG", 0))
            ts(v("V0", a, b), v("E0", a, b), -24.0, A.add)
            ts(v("FC", a, b), v("EC", a, b), 4.0, A.is_gt, -1.0, A.mult)
            scan(v("TT", a, b), v("FC", a, b), v("V0", a, b), 0.0, A.min, A.mult)

    for t in range(VI):
        pl, KW, so, ZO = "pl%d" % t, "KW%d" % t, v("so%d" % t), "ZO%d" % t
        last = t == VI - 1
        Et = "E0"
        now[0] = t
        pull[0] = 0.0

        affine(w("D1", 0, 16), w("TT", W + B * t, 16), -2.0, 1.0)
        run_v = RUN[min(t, 1)][0].split()
        for c in range(8):
            n = 32 if c == 7 else 33
            affine(w("D1", c * BL + 16, 16 * n), ind(v("TT", 0, W + B * t + B), w(pl, c * LW, n)), -2.0, 1.0, first="v" if "T%d" % c in run_v else "s")
            name("T%d" % c)
        for j in range(2):
            for k in range(16):
                d = v("D1", 4 * j * BL + k, 4 * (j + 1) * BL, 16)
                scan(v("V0", 4 * j * BL + k, 4 * (j + 1) * BL, 16), d, d, 0.0, A.mult, A.min)
                name("R%d" % j)
        for c in range(8):
            a = c * BL
            affine(w("Gn", a, 512), ind(v("PT"), w(pl, c * LW, 32)), -2.0, -8153.0, first="v" if "N%d" % c in run_v else "s")
            name("N%d" % c)
            scan(w("FL", a, 512), w("V0", a, 512), w("Gn", a, 512), -1e4, A.max, A.add)
            name("F%d" % c)
            if c % 2:
                sums = w(("ps3", "ps4")[c // 2 % 2], 66 * (c // 4), 66)
                for k0 in range(0, 16, 4):
                    group([(sums, SEL(k), v("FL", a - BL + k, a + BL, 16)) for k in range(k0, k0 + 4)]
                          + [(sums, v("ONE", 0, 128, 1, 0, 64), v("THR", 0, 66, 1, 0, 64))] * (k0 == 12), k0 == 0, k0 == 12)
                    name("P%d" % (c // 2))

        pull[0] = PULL["table"]
        affine(so, ind(v("V0"), v("FO")), -0.5, 0.5)
        if not last:
            send("s%d" % (t + 1), [(w("TT", W + B * t + B, B), [so])], STATE_GO, 2.0)
        for a in range(0, 16, 4):
            group([(v("ps7", 256, 264), ID, v("UB"))] * (a == 0) + [(v("ps7", 256, 264), SEL(k), v("so%d" % t, k, 128, 16)) for k in range(a, a + 4)], a == 0, a == 12)
            name("us")
        ts(v("ui"), v("ps7", 256, 264), -1 / SW, A.mult)
        ts(v("ua"), v("ui"), 31 + 7 * 512, A.bitwise_and)
        ts(v("uu"), v("ua"), col("C32", 0), A.add)
        name("uu")
        affine(v("es"), ind(v(Et), v("uu")), 1.0, first="s")
        name("es")
        mms(v("ps1", 384, 512), [(IS(1), so), (ID, v("es"))])
        affine(v("eb"), v("ps1", 384, 512), 0.5, 141.75, first="s")

        def change(E):
            tt(ind(v(E), v("uu")), v("eb"), v("M130"), A.add)
            name("En")

        if last:
            change("E1")
            store("y", 0, T.ye[:, :], v("E1"))
        else:
            act(v("eu"), v("eb"), ACT.Abs, None, col("SG", 2))
            affine(v("ew"), v("eb"), -1.0, 154.0)
            ts(v("ea"), v("eu"), 4.0, A.is_gt)
            name("ea")
            tt(ind(v("TT", 0, W), v("uu")), v("ea"), v("ew"), A.mult)
            name("TT")
        pull[0] = 0.0

        for j in range(2):
            cs, o, y, x4 = range(4 * j, 4 * j + 4), j * HW, 128 * j, 4 * j

            def s4(name):
                return w(name, x4, 4)

            def hv(name, a=0, n=128):
                return w(name, y + a, n)

            def tmp(a=0, n=128):
                return w("ps0", 2 * y + a, n)

            def nm(x):
                name("%s%d" % (x, j))

            gt, ge = w("sg1", 132 * j, 128), w("sg1", 132 * j + 4, 128)
            for h in range(2):
                a, k, cnt, bank = 66 * j, 2 * j + h, ("ps3", "ps4")[h], ("ps1", "ps2")[h]
                pair = (2 * k, 2 * k + 1)

                def s2(name):
                    return v(name, x4 + h, x4 + 4, 2)

                def pv(name, a=0):
                    return v(name, y + a + h, y + a + 128, 2)

                def nk(x):
                    name("%s%d" % (x, k))

                xs, kx = v("xs", 66 * k, 66 * k + 66, 33), v("kx", 66 * k, 66 * k + 66, 33)
                fx, dd = w("fx", 32 * k, 32), w("dd", 32 * k, 32)
                scan(v("xs", 66 * k + 65, 66 * k - 1, -1), v(cnt, a + 65, a - 1, -1), v("XC", 65, None, -1), 0.0, A.max, A.min)
                nk("xs")
                ts(w("ou", 2 * k, 2), xs, -1 / 256, A.mult, col("pb16", 0), A.add)
                nk("ou")
                affine(fx, ind(w("FL", 2 * BL * k, 2 * BL), w("ou", 2 * k, 2)), -1 / 64, -128.0, first=QF)
                nk("fx")
                cp(ind(w("WT", 256 * k, 256), v("WO", 0, 2)), fx)
                nk("W")
                affine(dd, ind(w("Gn", 2 * BL * k, 2 * BL), w("ou", 2 * k, 2)), 1.0, first="s")
                nk("dd")
                for c in pair:
                    b = a + 33 * (c % 2)
                    scan(v("kx", 33 * c + 32, 33 * c - 1, -1), v(cnt, b + 32, b - 1, -1), v(KW, o + KS + 128 + at(c) % 4, o + KS - 4 + at(c) % 4, -4), 0.0, A.max, A.min)
                    nk("kx")
                    act(lanes("sg1", c, 0, 33, 132), w("XC8", 33 * (c % 2), 33), ACT.Sign, -1.0, col("xs", 33 * c))
                    nk("sg")
                mms(w(bank, 192, 32), [(ID, dd), (IS(0), fx)])
                nk("dm")
                affine(w("wm", 128 * k, 32), w(bank, 192, 32), SC / 8, 1788 * SC, first="s")
                nk("wm")
                for n in (32, 64):
                    again(w("wm", 128 * k + n, n), w("wm", 128 * k, n))
                    nk("wm")
                affine(s2("kx0"), kx, 1.0, 2.0 ** 18, first="s")
                tt(s2("sxf"), kx, xs, A.subtract)
                affine(s2("sx32"), s2("sxf"), 1 / 32, first="s")

                for c in pair:
                    singles([(v(bank, l, 128, 16, 32 * (c % 2), 32 * (c % 2) + 32), v("D1", c * BL + 16 + l, c * BL + BL, 16), v("WT", 128 * c + l, 128 * c + 128, 16))
                             for l in range(16)])
                    nk("H")
                hit, sums = v("hit", 128 * k, 128 * k + 128, 1, 0, 64), v(bank, 0, 128, 1, 0, 64)
                rec({"v": ts_fn(hit, sums, 0.0, A.max, None, None), "s": act_fn(hit, sums, ACT.Relu, None, None)}, hit, [sums], "ts")
                nk("hit")
                mms(w(bank, 128, 64), [(IS(2), v("sg1", 132 * j + 4 + h, 132 * j + 132, 2)), (hit, v("PERM", 0, 64, 1, 0, 64))])
                nk("turn")
                for c in pair:
                    scan(w("kd", 32 * at(c), 32), v(bank, 128 + c % 2, 192, 2), lanes(KW, c, KS, 32, HW), col("kx0", at(c)), A.min, A.max)
                    nk("kd")
                ts(s2("sd"), v("kd", y + 32 * h + 31, y + 128, 64), 4095, A.bitwise_and)
                nk("sd")
                tt(s2("p32"), s2("sd"), s2("sx32"), A.mult)
                ts(s2("bsf"), s2("p32"), -262016.484375, A.add, 2.0 ** 23 + 4096 + 262016 + 97 * t, A.add)

                for c in pair:
                    ts(lanes("craw", c), v("KAP"), col("sxf", at(c)), A.mult, col("bsf", at(c)), A.add)
                    nk("c")
                ts(pv("cm"), pv("craw"), 4095, A.bitwise_and)
                nk("cm")
                cp(w("cu", 64 * k, 64), pv("cm"))
                nk("cu")
                for c in pair:
                    b = c * 512
                    affine(w("EC", b, 512), ind(v(Et), w("cu", c * 32, 32)), SC, (C0 + 0.5) * SC, first=QC[c])
                    name("E%d" % c)
                    for x in range(b, b + 512, 128):
                        scan(w("FC", x, 128), w("EC", x, 128), w("wm", 128 * k, 128), -1.0, A.max, A.add)
                        name("C%d" % c)
                cn = w(cnt, 256 + j * 64, 64)
                mms(cn, [(ONE, v("K2c", 0, 128, 2)), (ID, pv("BAR"))], [(SEL(x, 144), v("FC", 1024 * k + x, 1024 * k + 1024, 16)) for x in range(16)])
                nk("S")
                tt(pv("RK", y + 128), pv("cm"), cn, A.add)
                nk("key")

            G = hv("ps6")
            mms(G, [(IS(3), gt), (IS(4), ge)])
            nm("G")
            for a, out in ((KS, "IA"), (KQ, "IQ")):
                tt(hv("ps5", 256), w(KW, o + a - 4, 128), G, A.add)
                nm("t" + out)
                tt(hv(out), w(KW, o + a, 128), hv("ps5", 256), A.max)
                nm(out)
            ts(s4("dq"), v("kd", y + 31, y + 128, 32), 12, A.arith_shift_right, 63, A.bitwise_and)
            ts(s4("dcol"), s4("dq"), -64.0, A.add)
            ts(s4("Aq"), s4("sd"), 65537.0, A.add)
            for c in cs:
                act(lanes("ps7", c), w("kc1", 32 * (c % 2), 32), ACT.Abs, None, col("dcol", at(c)))
                nm("ab")
                ts(lanes("e2p", c), lanes(KW, c, RAWQ, 32, HW), 65536.0, A.add, col("Aq", at(c)), A.not_equal)
                nm("e")
            tt(hv("kept"), hv("e2p"), hv("ps7"), A.min)
            nm("kept")
            for c in cs:
                scan(lanes("Dz", c, 4, 32, 132), v("ONE", 0, 32), lanes("kept", c), 0.0, A.add, A.subtract)
                nm("D")
            cp(s4("nf"), w("Dz", 132 * j + 128, 4))
            for c in cs:
                act(lanes("tl", c), v("kcm"), ACT.Sign, None, col("nf", at(c)))
                nm("tl")
            TS = hv("ps6", 256)
            mms(TS, [(ID, v("K3c")), (IS(5), hv("tl"))])
            nm("TS")
            tt(tmp(128), hv("cm"), TS, A.add)
            nm("cT")
            for b in range(5):
                s = 4 << b
                m = 128 - s
                tb = w("tb", 640 * j + 128 * b, m)
                ts(tb, w("Dz", 132 * j + s, m), b, A.arith_shift_right, 1, A.bitwise_and)
                name("b%d%d" % (j, b))
                scan(tmp(0, m), tb, w(KW, o + KS + s, m), 0.0, A.max, A.mult)
                name("m%d%d" % (j, b))
                there = w(KW, o + KS, m)
                if b == 4:
                    tt(w("RK", 2 * y, 128), w(KW, o + KS, 128), tmp(128), A.min)
                    nm("fill")
                    there = w("RK", 2 * y, m)
                tt(there, there, tmp(0, m), A.min)
                name("r%d%d" % (j, b))
            pull[0] = 0.0 if last else PULL["reasons"]
            for b in range(5):
                s = 4 << b
                m = 128 - s
                scan(hv("ps5", 0, m), w("tb", 640 * j + 128 * b, m), w(KW, o + KQ + s, m), 0.0, A.max, A.mult)
                name("Q%d%d" % (j, b))
                tt(w(KW, o + KQ, m), w(KW, o + KQ, m), hv("ps5", 0, m), A.min)
                name("q%d%d" % (j, b))
            tt(hv("RQ"), w(KW, o + KQ, 128), TS, A.min)
            nm("RQ")
            pull[0] = 0.0

            for c in cs:
                k = c % 4
                back = v("RK", 2 * y + 252 + k, 2 * y + k - 4, -4)
                scan(v("ps0", 2 * y + 252 + k, 2 * y + k - 4, -4), back, back, -1e9, A.max, A.max)
                nm("g")
            z = tmp(128, 4)
            tt(hv("YS"), hv("IA"), tmp(), A.min)
            nm("Y")
            nS, nQ, nx = hv(ZO), hv(ZO, 256), "KW%d" % (t + 1)
            ts(nS, hv("YS"), 4095, A.bitwise_and)
            nm("Z")
            if not last:
                for c in cs:
                    cp(w("plo%d" % t, LW * c, 32), lanes(ZO, c))
                    nm("L")
                send("p%d%d" % (j, t + 1), [(w("pl%d" % (t + 1), 4 * LW * j, 4 * LW), [w("plo%d" % t, 4 * LW * j, 4 * LW)])], PLAN_GO, FLY)
                send("k%d%d" % (j, t + 1), [(w(nx, o + KS, 128), [nS, v("Kf")])], PLAN_GO, FOLD1)
                prog[-2]["R"] += prog[-4]["W"]
            else:
                cp(v("ysw", j, 256, 2), nS)
            pull[0] = 0.0 if last else PULL["after"]
            tt(s4("zq"), z, s4("Aq"), A.min)
            if GQ[t] == "s":
                act(s4("sgz"), z, ACT.Sign)
                affine(s4("ret"), s4("sgz"), -0.5, 0.5, first="s")
                act(s4("vq"), s4("zq"), ACT.Relu)
                nm("vq")
                for c in cs:
                    act(lanes("ps7", c), lanes("RQ", c), ACT.Identity, col("ret", at(c)), col("vq", at(c)))
                    nm("gq")
                tt(hv("YQ"), hv("IQ"), hv("ps7"), A.min)
            else:
                if not last:
                    ts(s4("retb"), z, 0.0, A.is_lt)
                for c in cs:
                    k = c % 4
                    back = v("RQ", y + 124 + k, y + k - 4, -4)
                    scan(v("ps5", y + 124 + k, y + k - 4, -4), back, back, col("zq", c), A.max, A.max)
                    nm("gq")
                tt(hv("YQ"), hv("IQ"), hv("ps5"), A.min)
            nm("YQ")
            ts(nQ, hv("YQ"), 8191, A.bitwise_and)
            nm("ZQ")
            if not last:
                send("q%d%d" % (j, t + 1), [(w(nx, o + RAWQ, 128), [nQ]), (w(nx, o + KQ, 128), [nQ, v("KQf")])], PLAN_GO, FOLD)
            else:
                ts(v("ysw", 256 + j, 512, 2), nQ, -1.0, A.add)
            pull[0] = 0.0
        if not last:
            change("E0")
            if t == VI - 2:
                copy(3, v("E1"), v("E0"))
            pull[0] = PULL["parity"]
            if GQ[t] == "s":
                affine(v("retb"), v("sgz"), -0.5, 0.5, first="s")
            def top(name, a=0, n=1):
                return v(name, a, a + n, 1, 0, 32)
            mms(top("ps7", 272), [], [(v("ONE", 0, 32), col("retb", c)) for c in range(8)])
            ts(top("ri"), top("ps7", 272), -0.5, A.add, 0.5, A.mult)
            ts(top("thr"), top("ps7", 272), -2.0 ** 32, A.mult)
            ts(top("thr", 1), top("ri"), 2.0 ** 33, A.mult, -1.5 * 2 ** 32, A.add)
            affine(top("THR", 0, 66), top("ONE", 0, 66), top("thr"), top("thr", 1))
            name("THR")
            pull[0] = 0.0
        else:
            store("y", 1, T.ys[:, :], v("ysw", 0, 256))
            store("s", 2, T.yw[:, :], v("ysw", 256, 512))

    chain([i for i, e in enumerate(prog) if "y" in e["cost"]])
    for t in range(VI):
        for x in RUN[min(t, 1)] + LINES + (ENDS if t == VI - 1 else MIDS):
            line(x, t)
    if not PLANNED:
        PLANNED["prog"], PLANNED["named"] = prog, named
        PLANNED["plan"] = _schedule(prog)
    order, queue, done, deps = PLANNED["plan"]
    tok = {}
    for i in order:
        e, q = prog[i], queue[i]
        toks = [tok[j] for j in sorted(deps[i]) if not (q == "t" and queue[j] == "t")]
        if e["kind"] == "op":
            tok[i] = op_now(q, e["fn"][q], toks, e["P"], e["sem"], e["inc"])
        elif e["kind"] == "send":
            tok[i] = send_now(e["fn"], toks, e["sem"], e["inc"])
        else:
            tok[i] = lands_now(e["sem"], e["inc"])
    finish()
